import numpy as np
import ml_dtypes


def mxq(x, axis, fmt="e4m3"):
    dtype, down = {"e4m3": (ml_dtypes.float8_e4m3fn, 7), "e5m2": (ml_dtypes.float8_e5m2, 14)}[fmt]
    v = np.moveaxis(np.asarray(x, np.float32).astype(ml_dtypes.bfloat16).astype(np.float64), axis, -1)
    blocks = v.reshape(v.shape[:-1] + (-1, 32))
    amax = np.abs(blocks).max(-1, keepdims=True)
    byte = np.maximum(np.where(amax > 0, np.frexp(amax)[1] - 1 + 127, 0) - down, 1)
    scale = np.exp2(byte - 127.0)
    codes = (blocks / scale).astype(np.float32).astype(dtype).astype(np.float64)
    return np.moveaxis((codes * scale).reshape(v.shape), -1, axis)


WIDE = False


def mx_kscale(k):
    if not WIDE:
        return np.ones(k)
    levels = np.array([10, -10, 5, -5, 0])
    if k % 512:
        return np.exp2(np.random.permutation(np.resize(levels, k // 32))).repeat(32)
    a = np.empty((k // 512, 16))
    for p in range(k // 512):
        a[p, :8] = np.random.permutation(np.resize(levels, 8))
        for g in range(8):
            far = levels[np.abs(levels - a[p, g]) >= 10]
            a[p, g + 8] = far[np.random.randint(len(far))]
    return np.exp2(a.ravel()).repeat(32)


BF16 = ml_dtypes.bfloat16


def bf(x):
    return np.asarray(x, np.float32).astype(BF16)


def f64(x):
    return np.asarray(x).astype(np.float64)


E2M1 = np.array([0.0, 0.5, 1.0, 1.5, 2.0, 3.0, 4.0, 6.0, -0.0, -0.5, -1.0, -1.5, -2.0, -3.0, -4.0, -6.0])


def pack_weight(w, fmt):
    k, n = w.shape
    w = f64(bf(w)).reshape(k // 32, 32, n)
    amax = np.abs(w).max(1)
    if fmt == "e4m3":
        byte = np.frexp(amax)[1] - 1 + 127 - 7
    else:
        mant, ex = np.frexp(amax / 6.0)
        byte = np.where(mant > 0.5, ex, ex - 1) + 127
    byte = np.clip(np.where(amax > 0, byte, 1), 1, 254)
    scaled = (w * np.exp2(127.0 - byte)[:, None, :]).reshape(k, n).astype(np.float32)
    by_word = np.ascontiguousarray(scaled.reshape(k // 512, 128, 4, n).transpose(0, 1, 3, 2))
    if fmt == "e4m3":
        words = by_word.astype(ml_dtypes.float8_e4m3fn).view(np.uint8)
    else:
        c = by_word.astype(ml_dtypes.float4_e2m1fn).view(np.uint8) & 0xF
        words = c[..., 0::2] | (c[..., 1::2] << 4)
    return np.ascontiguousarray(words), np.ascontiguousarray(byte.astype(np.uint8).reshape(k // 512, 16, n))


def unpack_weight(words, scales, fmt):
    g, p, n, _ = words.shape
    if fmt == "e4m3":
        vals = np.ascontiguousarray(words).view(ml_dtypes.float8_e4m3fn).astype(np.float64)
    else:
        nib = np.empty((g, p, n, 4), np.uint8)
        nib[..., 0::2] = words & 0xF
        nib[..., 1::2] = words >> 4
        vals = E2M1[nib]
    vals = vals * np.repeat(np.exp2(scales.astype(np.float64) - 127.0), 8, axis=1)[..., None]
    return vals.transpose(0, 1, 3, 2).reshape(g * 512, n)

def planes(Y):
    n, m = Y.shape
    b = f64(bf(Y)).reshape(n // 32, 32, m)
    amax = np.abs(b).max(1)
    byte = np.clip(np.where(amax > 0, np.frexp(amax)[1] - 1 + 127 - 7, 1), 1, 254)
    codes = (b * np.exp2(127.0 - byte)[:, None, :]).reshape(n, m).astype(np.float32).astype(ml_dtypes.float8_e4m3fn).view(np.uint8)
    words = codes.reshape(n // 512, 128, 4, m).transpose(0, 1, 3, 2)
    return np.ascontiguousarray(words), np.ascontiguousarray(byte.astype(np.uint8).reshape(n // 512, 16, m))


T, D, F = 1024, 1024, 1024

DIV = 32.0


def setup_inputs():
    s, u = mx_kscale(D), mx_kscale(T)
    x = bf(np.random.standard_normal((T, D)) * s)
    y = bf(np.random.standard_normal((T, D)) * s)
    words, scales = pack_weight(np.random.standard_normal((D, F)) / np.sqrt(D) / s[:, None], "e4m3")
    return {"x": x,
            "y": y,
            "w_words": words,
            "w_scales": scales,
            "b": bf(np.random.standard_normal(F) * 0.2 * np.sqrt(DIV / np.sqrt(T))),
            "p": bf((1.0 + 0.1 * np.random.standard_normal(T)) * u),
            "q": bf((1.0 + 0.1 * np.random.standard_normal(T)) / u)}


def weighted_observables(states, wq, b, weights):
    h = (mxq(f64(states), 1, "e4m3") @ wq) + f64(b)[None, :]
    return f64(weights)[:, None] * np.tanh(h)


def core(x, y, w_words, w_scales, b, p, q):
    wq = unpack_weight(w_words, w_scales, "e4m3")
    fx = weighted_observables(x, wq, b, p)
    fy = weighted_observables(y, wq, b, q)
    return (mxq(fx, 0, "e4m3").T @ mxq(fy, 0, "e4m3")) / DIV


def reference(x, y, w_words, w_scales, b, p, q):
    R_out = core(x, y, w_words, w_scales, b, p, q)
    words, scales = planes(R_out.T)
    return R_out, words, scales

@@ -1,0 +1,477 @@
+from contextlib import ExitStack
+
+import concourse.mybir as mybir
+from concourse.masks import make_identity
+
+SIZE = 1024
+P = 128
+FLOPS = 3 * 2 * SIZE * SIZE * SIZE
+INV_DIV = 1.0 / 32.0
+
+F32 = mybir.dt.float32
+BF16 = mybir.dt.bfloat16
+U32 = mybir.dt.uint32
+I32 = mybir.dt.int32
+U8 = mybir.dt.uint8
+FP8X4 = mybir.dt.float8_e4m3fn_x4
+ACT = mybir.ActivationFunctionType
+ALU = mybir.AluOpType
+
+SUM_BANKS = 4
+TURN_BANKS = 4
+
+SCORE = """
+turn.y.0.0 turn.y.0.1 lift.y.0.0.S spread_bias encode_y.0.0.1 lift_bias.S lift.y.0.1.V dot_y.0.0.0 add_y.0.0.0
+turn.y.0.3 encode_y.0.1.1 turn.y.0.2 lift.y.0.3.V dot_y.0.0.1 lift.y.0.2.S turn.y.1.0 widen_bias add_y.0.0.1
+turn.y.1.1 encode_y.0.2.2 lift.y.1.0.S turn.y.1.2 lift.y.1.1.S dot_y.0.0.2 lift.y.1.2.V tanh_y.0.0.0 dot_y.0.0.3
+encode_y.1.0.2 turn.y.1.3 add_y.0.0.3 turn.x.0.0 add_y.0.0.2 lift.y.1.3.S dot_y.0.1.0 scale_y.0.0.0 encode_y.1.2.2
+dot_y.0.1.1 tanh_y.0.0.1 add_y.0.1.0 dot_y.0.1.2 add_y.0.1.1 dot_y.0.1.3 scale_y.0.0.2 add_y.0.1.2 dot_y.1.0.3
+scale_y.0.0.3 add_y.0.1.3 dot_y.1.0.2 scale_y.0.0.1 add_y.1.0.3 turn.x.0.1 lift.x.0.0.S weave_y.0.0 turn.x.0.3
+lift.x.0.1.S turn.x.1.2 tanh_y.0.1.1 turn.x.0.2 encode_x.0.0 dot_y.1.0.0 add_y.1.0.2 lift.x.1.2.S dot_y.1.1.2
+encode_fy.0.0 lift.x.0.2.S dot_y.1.1.0 add_y.1.0.0 lift.x.0.3.S dot_y.1.1.3 add_y.1.1.0 tanh_y.0.1.0 dot_y.1.0.1
+add_y.1.1.3 turn.x.1.3 scale_y.0.1.3 encode_x.0.2 dot_y.1.1.1 lift.x.1.3.S add_y.1.0.1 turn_bias scale_y.0.1.0
+encode_x.1.2 dot_x.2.0.0 scale_y.0.1.1 add_y.1.1.1 turn.x.1.0 scale_y.0.1.2 add_y.1.1.2 turn.x.1.1 lift.x.1.0.S
+weave_y.0.1 dot_obs.1.0.1 lift_bias_column lift.x.1.1.S dot_obs.1.0.0 tanh_obs.1.0.1 dot_obs.0.0.0 encode_x.1.0
+tanh_obs.1.0.0 dot_obs.0.0.1 add_x.2.0.0 tanh_y.1.0.1 turn_obs.1.0.0 encode_fy.0.1 dot_x.2.0.1 weigh_obs.1.0.0
+tanh_y.1.0.0 turn_obs.1.0.1 add_x.2.0.1 dot_obs.1.1.0 weigh_obs.1.0.1 tanh_obs.0.0.0 dot_obs.1.1.1 weigh_y.1.0
+tanh_obs.1.1.0 dot_obs.0.1.0 tanh_obs.1.1.1 turn_obs.1.1.0 turn_obs.0.0.0 tanh_obs.0.1.0 dot_obs.0.1.1 tanh_obs.0.0.1
+weigh_obs.0.0.0 dot_x.3.0.0 tanh_y.1.1.1 turn_obs.1.1.1 weigh_obs.1.1.0 turn_obs.0.0.1 weigh_obs.1.1.1 dot_x.2.1.0
+tanh_obs.0.1.1 weigh_obs.0.0.1 turn_obs.0.1.0 tanh_x.2.0 encode_fx.1 turn_obs.0.1.1 dot_x.2.1.1 weigh_obs.0.1.1
+tanh_y.1.1.0 cross_t.0.2 weigh_obs.0.1.0 cross.3.0 add_x.2.1.1 lift_cross_t.0.2.S cross_t.0.3 encode_fx.0
+store_cross.3.0.S dot_x.3.0.1 add_x.2.1.0 lift_cross_t.0.3.S cross.1.0 weigh_y.1.1 tanh_x.2.1 cross_t.0.1 cross_t.0.0
+lift_cross_t.0.1.S cross.2.0 lift_cross_t.0.0.S cross.0.0 encode_fy.1.0 store_cross.2.0.S dot_x.3.1.1 encode_fy.1.1
+store_cross.0.0.S add_x.3.0.1 cross.2.1 store_cross.1.0.S add_x.3.0.0 cross.3.1 store_cross.2.1.S weigh_x.2.1
+cross.0.1 tanh_x.3.0 cross_t.1.0 weigh_x.2.0 dot_x.3.1.0 store_cross.0.1.S cross_t.1.2 lift_cross_t.1.0.S add_x.3.1.0
+cross_t.1.1 lift_cross_t.1.2.S encode_fx.2 cross.1.1 store_cross.3.1.S weigh_x.3.0 cross_t.1.3 lift_cross_t.1.1.S
+cross.4.0 store_cross.1.1.S add_x.3.1.1 cross_t.0.4 store_cross.4.0.S lift_cross_t.1.3.V cross.5.0 tanh_x.3.1
+store_plane.1.0 cross_t.0.5 store_cross.5.0.V cross.4.1 lift_cross_t.0.5.S weigh_x.3.1 cross_t.1.5 lift_cross_t.0.4.S
+cross.5.1 store_cross.4.1.S encode_fx.3 cross_t.1.4 store_cross.5.1.S store_plane.0.0 cross_t.1.6 store_plane.1.1
+lift_cross_t.1.5.S cross.6.0 lift_cross_t.1.6.V lift_cross_t.1.4.S cross.6.1 store_plane.0.2 store_cross.6.0.S
+store_plane.0.1 store_scales.0 cross_t.0.7 store_plane.1.2 store_cross.6.1.S cross_t.1.7 lift_cross_t.0.7.S cross.7.1
+cross.7.0 store_cross.7.1.V cross_t.0.6 store_cross.7.0.S lift_cross_t.1.7.V lift_cross_t.0.6.S store_plane.1.3
+store_plane.0.3 store_scales.1
+"""
+
+
+def tile_extendeddmdkoopmancrossmoment_x2_kernel(
+    tc, x, y, w_words, w_scales, b, p, q, out_0, out_1, out_2
+):
+    nc = tc.nc
+    with ExitStack() as ctx:
+        keep = ctx.enter_context(tc.tile_pool(name="keep", bufs=1))
+        work = ctx.enter_context(tc.tile_pool(name="work", bufs=3))
+        psum = ctx.enter_context(tc.psum_pool(name="psum", bufs=1))
+        ctx.enter_context(tc.manual_schedule())
+
+        made = {}
+
+
+        ident = keep.tile([P, P], F32, name="ident", align_bytes=64)
+        make_identity(nc, ident[:])
+
+        w_scale = keep.tile([P, SIZE], U8, name="w_scale", align_bytes=64)
+        nc.vector.memset(w_scale[:].bitcast(I32), 0)
+        zero = keep.tile([P, 1], F32, name="zero")
+        nc.vector.memset(zero[:], 0.0)
+
+        b_rows = keep.tile([P, 8], BF16, name="b_rows", align_bytes=64)
+        nc.scalar.dma_start(out=b_rows[:], in_=b.rearrange("(n w) -> n w", w=8))
+        for quad in range(4):
+            nc.scalar.dma_start(
+                out=w_scale[32 * quad : 32 * quad + 8, :].bitcast(I32),
+                in_=w_scales[:, 4 * quad : 4 * quad + 4, :].bitcast(I32),
+            )
+        tanh_warm_up = keep.tile([P, 1], F32, name="tanh_warm_up")
+        nc.scalar.activation(out=tanh_warm_up[:], in_=zero[:], func=ACT.Tanh)
+
+        row_words = {}
+
+        def load_rows(op, source, g, j, n):
+            rows = keep.tile([P, n, SIZE], BF16, name=f"rows_{op}{g}{j}", align_bytes=64)
+            nc.sync.dma_start(
+                out=rows[:], in_=source.rearrange("(g p j) d -> g p j d", g=2, j=4)[g, :, j : j + n, :]
+            )
+            for k in range(n):
+                row_words[op, g, j + k] = rows[:, k, :].bitcast(F32)
+
+        w_code = keep.tile([P, 2, SIZE], U32, name="w_code", align_bytes=64)
+        w_source = w_words.rearrange("c p n t -> p c (n t)")
+
+        def load_w(h):
+            nc.sync.dma_start(
+                out=w_code[:, :, 512 * h : 512 * h + 512].bitcast(I32),
+                in_=w_source[:, :, 2048 * h : 2048 * h + 2048].bitcast(I32),
+            )
+
+        weight = {}
+        weight_f32 = {}
+
+        def load_weights(op, source):
+            weight[op] = keep.tile([P, 2, 4], BF16, name=f"weight_{op}", align_bytes=64)
+            nc.sync.dma_start(out=weight[op][:], in_=source.rearrange("(g p j) -> p g j", g=2, j=4))
+            weight_f32[op] = keep.tile([P, 2, 4], F32, name=f"weight_f32_{op}", align_bytes=64)
+            nc.gpsimd.tensor_copy(out=weight_f32[op][:], in_=weight[op][:])
+
+        load_rows("y", y, 0, 0, 1)
+        load_rows("y", y, 0, 1, 1)
+        load_w(0)
+        load_rows("y", y, 0, 2, 2)
+        load_rows("y", y, 1, 0, 2)
+        load_rows("y", y, 1, 2, 2)
+        load_weights("y", q)
+        load_weights("x", p)
+        load_rows("x", x, 0, 0, 4)
+        load_rows("x", x, 1, 0, 4)
+        load_w(1)
+
+        def turn_bank():
+            bank = psum.tile([P, 4, P], F32, name="turn_bank", tag="turn_bank", bufs=TURN_BANKS)
+            return bank
+
+        def sum_bank():
+            bank = psum.tile([P, 512], F32, name="sum_bank", tag="sum_bank", bufs=SUM_BANKS)
+            return bank
+
+        for n in range(3):
+            bank = turn_bank()
+            for m in range(4):
+                nc.tensor.transpose(bank[:, m, :], ident[:], ident[:])
+
+
+        row_dims = {"y": [P, 4, 2, P], "x": [P, 2, 4, P]}
+        row_code = {}
+        row_scale = {}
+        for op in ("y", "x"):
+            for g in range(2):
+                row_code[op, g] = keep.tile(row_dims[op], U32, name=f"row_code_{op}{g}", align_bytes=64)
+                row_scale[op, g] = keep.tile(row_dims[op], U8, name=f"row_scale_{op}{g}", align_bytes=64)
+
+        def stationary_rows(op, g, j, c):
+            if op == "y":
+                return row_code[op, g][:, j, c, :].bitcast(FP8X4), row_scale[op, g][:, j, c, :]
+            return row_code[op, g][:, c, j, :].bitcast(FP8X4), row_scale[op, g][:, c, j, :]
+
+        def copy(engine, out, in_):
+            if engine == "S":
+                nc.scalar.copy(out=out, in_=in_)
+            else:
+                nc.vector.tensor_copy(out=out, in_=in_)
+
+        def turn(op, g, j):
+            bank = turn_bank()
+            words = row_words[op, g, j]
+            for c in range(2):
+                for e in range(2):
+                    nc.tensor.transpose(bank[:, 2 * c + e, :], words[:, 256 * c + e : 256 * (c + 1) : 2], ident[:])
+            made["turn", op, g, j] = bank
+
+        def lift(op, g, j, engine):
+            if ("lift", op, g, j // 2) not in made:
+                pair_dims = [P, 2, 2, P, 2]
+                made["lift", op, g, j // 2] = work.tile(pair_dims, F32, name="pair", tag="pair", align_bytes=64)
+            pair = made["lift", op, g, j // 2]
+            out = pair[:, j % 2] if op == "y" else pair[:, :, j % 2]
+            copy(engine, out, made["turn", op, g, j][:].rearrange("p (c e) r -> p c r e", e=2))
+
+        def encode_y(g, j, n):
+            pair = made["lift", "y", g, j // 2]
+            nc.vector.quantize_mx(
+                out=row_code["y", g][:, j : j + n].rearrange("p j c r -> p (j c r)").bitcast(FP8X4),
+                scales=row_scale["y", g][:, j : j + n].rearrange("p j c r -> p (j c r)"),
+                in_=pair[:, j % 2 : j % 2 + n].rearrange("p j c r e -> p (j c r e)").bitcast(BF16),
+            )
+
+        def encode_x(g, j):
+            for c in range(2):
+                nc.vector.quantize_mx(
+                    out=row_code["x", g][:, c, j : j + 2].rearrange("p j r -> p (j r)").bitcast(FP8X4),
+                    scales=row_scale["x", g][:, c, j : j + 2].rearrange("p j r -> p (j r)"),
+                    in_=made["lift", "x", g, j // 2][:, c].rearrange("p j r e -> p (j r e)").bitcast(BF16),
+                )
+
+
+        bias_words = keep.tile([P, P, 4], F32, name="bias_words", align_bytes=64)
+        bias_row = bias_words[:].rearrange("p n m -> p (n m)").bitcast(BF16)
+        bias_f32 = keep.tile([P, 4, P], F32, name="bias_f32", align_bytes=64)
+        bias_column = keep.tile([P, 4], F32, name="bias_column", align_bytes=64)
+
+        def spread_bias():
+            made["spread_bias"] = turn_bank()
+            words = b_rows[:].bitcast(F32)
+            for m in range(4):
+                nc.tensor.transpose(made["spread_bias"][:, m, :], words[:, m : m + 1].to_broadcast([P, P]), ident[:])
+
+        def lift_bias(engine):
+            copy(engine, bias_words[:], made["spread_bias"][:].rearrange("p m n -> p n m"))
+
+        def widen_bias():
+            nc.scalar.copy(out=bias_f32[:].rearrange("p m n -> p (m n)"), in_=bias_row[:, 0:512])
+
+        def turn_bias():
+            made["turn_bias"] = turn_bank()
+            for m in range(4):
+                nc.tensor.transpose(made["turn_bias"][:, m, :], bias_f32[:, m, :], ident[:])
+
+        def lift_bias_column():
+            nc.scalar.copy(out=bias_column[:], in_=made["turn_bias"][:, :, 0])
+
+
+        fy_code = {}
+        fy_scale = {}
+        for h in range(2):
+            for g in range(2):
+                fy_code[h, g] = keep.tile([P, 4, P], U32, name=f"fy_code{h}{g}", align_bytes=64)
+                fy_scale[h, g] = keep.tile([P, 4, P], U8, name=f"fy_scale{h}{g}", align_bytes=64)
+        fx_code = []
+        fx_scale = []
+        for c in range(4):
+            code = keep.tile([P, 2, 256], U32, name=f"fx_code{c}", align_bytes=64)
+            scale = keep.tile([P, 2, 256], U8, name=f"fx_scale{c}", align_bytes=64)
+            fx_code.append(code)
+            fx_scale.append(scale)
+
+        def work_tile(name, key, dims, dtype, bufs):
+            if (name, key) not in made:
+                made[name, key] = work.tile(dims, dtype, name=name, tag=name, bufs=bufs, align_bytes=64)
+            return made[name, key]
+
+        def project(op, g, j, col, n, out):
+            for c in range(2):
+                code, scale = stationary_rows(op, g, j, c)
+                nc.tensor.matmul_mx(
+                    out=out,
+                    lhsT=code,
+                    lhsT_scale=scale,
+                    rhs=w_code[:, c, col : col + n].bitcast(FP8X4),
+                    rhs_scale=w_scale[4 * c : P, col : col + n],
+                    start=(c == 0),
+                    stop=(c == 1),
+                )
+
+
+        def dot_y(h, g, j):
+            bank = sum_bank()
+            project("y", g, j, 512 * h, 512, bank[:])
+            made["dot_y", h, g, j] = bank
+
+        def add_y(h, g, j):
+            z = work_tile("z", ("y", h, g), [P, 2048], F32, 3)
+            nc.vector.tensor_tensor(
+                out=z[:, 512 * j : 512 * j + 512].rearrange("p (t a) -> p t a", t=4),
+                in0=made["dot_y", h, g, j][:].rearrange("p (a t) -> p t a", t=4),
+                in1=bias_row[:, 512 * h : 512 * h + 512].rearrange("p (a t) -> p t a", t=4),
+                op=ALU.add,
+            )
+
+        def tanh(key, part):
+            span = slice(1024 * part, 1024 * part + 1024)
+            th = work_tile("th", key, [P, 2048], F32, 3)
+            nc.scalar.activation(out=th[:, span], in_=made["z", key][:, span], func=ACT.Tanh)
+
+        def tanh_y(h, g, part):
+            tanh(("y", h, g), part)
+
+        def weave(f, th, weights, n):
+            nc.vector.tensor_tensor(
+                out=f.rearrange("p (o i) j -> p o j i", i=4),
+                in0=th.rearrange("p j (o i) -> p o j i", i=4),
+                in1=weights.unsqueeze(1).unsqueeze(3).to_broadcast([P, n // 4, 4, 4]),
+                op=ALU.mult,
+            )
+
+        def weigh_y(h, g):
+            f = work_tile("f", ("y", h, g), [P, 512, 4], BF16, 3)
+            weave(f[:], made["th", ("y", h, g)][:].rearrange("p (j o) -> p j o", j=4), weight["y"][:, g, :], 512)
+
+
+        def scale_y(h, g, j):
+            v = work_tile("v", ("y", h, g), [P, 4, 512], BF16, 2)
+            nc.scalar.activation(
+                out=v[:, j, :],
+                in_=made["th", ("y", h, g)][:, 512 * j : 512 * j + 512],
+                func=ACT.Copy,
+                scale=weight_f32["y"][:, g, j : j + 1],
+            )
+
+        def weave_y(h, g):
+            f = work_tile("f", ("y", h, g), [P, 512, 4], BF16, 3)
+            nc.vector.tensor_copy(
+                out=f[:].rearrange("p (o i) j -> p o j i", i=4),
+                in_=made["v", ("y", h, g)][:].rearrange("p j (o i) -> p o j i", i=4),
+            )
+
+        def encode_fy(h, g):
+            nc.vector.quantize_mx(
+                out=fy_code[h, g][:].rearrange("p t a -> p (t a)").bitcast(FP8X4),
+                scales=fy_scale[h, g][:].rearrange("p t a -> p (t a)"),
+                in_=made["f", ("y", h, g)][:].rearrange("p o j -> p (o j)"),
+            )
+
+
+        def dot_x(c, g, i):
+            bank = sum_bank()
+            for k in range(2):
+                project("x", g, 2 * i + k, 256 * c, 256, bank[:, 256 * k : 256 * k + 256])
+            made["dot_x", c, g, i] = bank
+
+        def add_x(c, g, i):
+            z = work_tile("z", ("x", c), [P, 2048], F32, 3)
+            first = 1024 * g + 512 * i
+            nc.vector.tensor_tensor(
+                out=z[:, first : first + 512].rearrange("p (k o) -> p k o", k=2),
+                in0=made["dot_x", c, g, i][:].rearrange("p (k o) -> p k o", k=2),
+                in1=bias_row[:, 256 * c : 256 * c + 256].unsqueeze(1).to_broadcast([P, 2, 256]),
+                op=ALU.add,
+            )
+
+        def tanh_x(c, g):
+            tanh(("x", c), g)
+
+        def weigh_x(c, g):
+            f = work_tile("f", ("x", c), [P, 512, 4], BF16, 3)
+            th = made["th", ("x", c)][:, 1024 * g : 1024 * g + 1024].rearrange("p (j o) -> p j o", j=4)
+            weave(f[:, 256 * g : 256 * g + 256, :], th, weight["x"][:, g, :], 256)
+
+
+        def dot_obs(c, g, i):
+            col = 256 * c + 128 * i
+            bank = sum_bank()
+            for k in range(2):
+                nc.tensor.matmul_mx(
+                    out=bank[:],
+                    lhsT=w_code[:, k, col : col + P].bitcast(FP8X4),
+                    lhsT_scale=w_scale[4 * k : P, col : col + P],
+                    rhs=row_code["x", g][:, k].rearrange("p j r -> p (j r)").bitcast(FP8X4),
+                    rhs_scale=row_scale["x", g][:, k].rearrange("p j r -> p (j r)"),
+                    start=(k == 0),
+                    stop=(k == 1),
+                )
+            made["dot_obs", c, g, i] = bank
+
+        def tanh_obs(c, g, i):
+            t = work_tile("t", (c, g, i), [P, 4, P], F32, 3)
+            nc.scalar.activation(
+                out=t[:].rearrange("p j r -> p (j r)"),
+                in_=made["dot_obs", c, g, i][:],
+                func=ACT.Tanh,
+                bias=bias_column[:, 2 * c + i : 2 * c + i + 1],
+            )
+
+        def turn_obs(c, g, i):
+            bank = turn_bank()
+            for j in range(4):
+                nc.tensor.transpose(bank[:, j, :], made["t", (c, g, i)][:, j, :], ident[:])
+            made["turn_obs", c, g, i] = bank
+
+        def weigh_obs(c, g, i):
+            f = work_tile("f", ("x", c), [P, 512, 4], BF16, 3)
+            first = 256 * g + 128 * i
+            nc.vector.tensor_tensor(
+                out=f[:, first : first + P, :],
+                in0=made["turn_obs", c, g, i][:].rearrange("p j o -> p o j"),
+                in1=weight["x"][:, g, :].unsqueeze(1).to_broadcast([P, P, 4]),
+                op=ALU.mult,
+            )
+
+        def encode_fx(c):
+            nc.vector.quantize_mx(
+                out=fx_code[c][:].rearrange("p g o -> p (g o)").bitcast(FP8X4),
+                scales=fx_scale[c][:].rearrange("p g o -> p (g o)"),
+                in_=made["f", ("x", c)][:].rearrange("p o j -> p (o j)"),
+            )
+
+
+        plane_code = []
+        for h in range(2):
+            code = keep.tile([P, SIZE], U32, name=f"plane_code{h}", align_bytes=64)
+            plane_code.append(code)
+        plane_scale = keep.tile([P, SIZE], U8, name="plane_scale", align_bytes=64)
+        plane_words = out_1.rearrange("g p m t -> g p (m t)")
+
+        def fx_tile(tile, g):
+            c, first = tile // 2, P * (tile % 2)
+            return fx_code[c][:, g, first : first + P].bitcast(FP8X4), fx_scale[c][:, g, first : first + P]
+
+        def divide(engine, out, in_):
+            if engine == "S":
+                nc.scalar.activation(out=out, in_=in_, func=ACT.Copy, scale=INV_DIV)
+            else:
+                nc.vector.tensor_scalar(out=out, in0=in_, scalar1=INV_DIV, scalar2=None, op0=ALU.mult)
+
+        def cross(tile, h):
+            bank = turn_bank()
+            for g in range(2):
+                code, scale = fx_tile(tile, g)
+                nc.tensor.matmul_mx(
+                    out=bank[:].rearrange("p t a -> p (t a)"),
+                    lhsT=code,
+                    lhsT_scale=scale,
+                    rhs=fy_code[h, g][:].rearrange("p t a -> p (t a)").bitcast(FP8X4),
+                    rhs_scale=fy_scale[h, g][:].rearrange("p t a -> p (t a)"),
+                    start=(g == 0),
+                    stop=(g == 1),
+                )
+            made["cross", tile, h] = bank
+
+        def store_cross(tile, h, engine):
+            r = work.tile([P, 512], F32, name="r", tag="r", bufs=6, align_bytes=64)
+            divide(engine, r[:].rearrange("p (a t) -> p a t", t=4), made["cross", tile, h][:].rearrange("p t a -> p a t"))
+            nc.sync.dma_start(out=out_0[P * tile : P * tile + P, 512 * h : 512 * h + 512], in_=r[:])
+
+        def cross_t(h, tile):
+            bank = turn_bank()
+            for t in range(4):
+                for g in range(2):
+                    code, scale = fx_tile(tile, g)
+                    nc.tensor.matmul_mx(
+                        out=bank[:, t, :],
+                        lhsT=fy_code[h, g][:, t, :].bitcast(FP8X4),
+                        lhsT_scale=fy_scale[h, g][:, t, :],
+                        rhs=code,
+                        rhs_scale=scale,
+                        start=(g == 0),
+                        stop=(g == 1),
+                    )
+            made["cross_t", h, tile] = bank
+
+        def lift_cross_t(h, tile, engine):
+            s = work_tile("s", (h, tile // 2), [P, 256, 4], BF16, 4)
+            first = P * (tile % 2)
+            divide(engine, s[:, first : first + P, :], made["cross_t", h, tile][:].rearrange("p t i -> p i t"))
+
+        def store_plane(h, c):
+            cols = slice(256 * c, 256 * c + 256)
+            nc.vector.quantize_mx(
+                out=plane_code[h][:, cols].bitcast(FP8X4),
+                scales=plane_scale[4 * h : P, cols],
+                in_=made["s", (h, c)][:].rearrange("p i t -> p (i t)"),
+            )
+            nc.sync.dma_start(
+                out=plane_words[h][:, 1024 * c : 1024 * c + 1024].bitcast(I32),
+                in_=plane_code[h][:, cols].bitcast(I32),
+            )
+
+        def store_scales(part):
+            cols = slice(512 * part, 512 * part + 512)
+            for quad in range(4):
+                nc.sync.dma_start(
+                    out=out_2[:, 4 * quad : 4 * quad + 4, cols].bitcast(I32),
+                    in_=plane_scale[32 * quad : 32 * quad + 8, cols].bitcast(I32),
+                )
+
+
+        steps = {
+            "turn": turn, "lift": lift, "encode_y": encode_y, "encode_x": encode_x,
+            "spread_bias": spread_bias, "lift_bias": lift_bias, "widen_bias": widen_bias,
+            "turn_bias": turn_bias, "lift_bias_column": lift_bias_column,
+            "dot_y": dot_y, "add_y": add_y, "tanh_y": tanh_y, "weigh_y": weigh_y,
+            "scale_y": scale_y, "weave_y": weave_y, "encode_fy": encode_fy,
+            "dot_x": dot_x, "add_x": add_x, "tanh_x": tanh_x, "weigh_x": weigh_x,
+            "dot_obs": dot_obs, "tanh_obs": tanh_obs, "turn_obs": turn_obs, "weigh_obs": weigh_obs,
+            "encode_fx": encode_fx,
+            "cross": cross, "store_cross": store_cross, "cross_t": cross_t, "lift_cross_t": lift_cross_t,
+            "store_plane": store_plane, "store_scales": store_scales,
+        }
+        for step in SCORE.split():
+            parts = step.split(".")
+            steps[parts[0]](*[int(a) if a in "01234567" else a for a in parts[1:]])

@@ -17,40 +17,10 @@ FP8X4 = mybir.dt.float8_e4m3fn_x4
 ACT = mybir.ActivationFunctionType
 ALU = mybir.AluOpType
 
-SUM_BANKS = 4
-TURN_BANKS = 4
+BANKS = 8
+SCALE_STORES = {4: 0, 8: 4}
 
-SCORE = """
-turn.y.0.0 turn.y.0.1 lift.y.0.0.S spread_bias encode_y.0.0.1 lift_bias.S lift.y.0.1.V dot_y.0.0.0 add_y.0.0.0
-turn.y.0.3 encode_y.0.1.1 turn.y.0.2 lift.y.0.3.V dot_y.0.0.1 lift.y.0.2.S turn.y.1.0 widen_bias add_y.0.0.1
-turn.y.1.1 encode_y.0.2.2 lift.y.1.0.S turn.y.1.2 lift.y.1.1.S dot_y.0.0.2 lift.y.1.2.V tanh_y.0.0.0 dot_y.0.0.3
-encode_y.1.0.2 turn.y.1.3 add_y.0.0.3 turn.x.0.0 add_y.0.0.2 lift.y.1.3.S dot_y.0.1.0 scale_y.0.0.0 encode_y.1.2.2
-dot_y.0.1.1 tanh_y.0.0.1 add_y.0.1.0 dot_y.0.1.2 add_y.0.1.1 dot_y.0.1.3 scale_y.0.0.2 add_y.0.1.2 dot_y.1.0.3
-scale_y.0.0.3 add_y.0.1.3 dot_y.1.0.2 scale_y.0.0.1 add_y.1.0.3 turn.x.0.1 lift.x.0.0.S weave_y.0.0 turn.x.0.3
-lift.x.0.1.S turn.x.1.2 tanh_y.0.1.1 turn.x.0.2 encode_x.0.0 dot_y.1.0.0 add_y.1.0.2 lift.x.1.2.S dot_y.1.1.2
-encode_fy.0.0 lift.x.0.2.S dot_y.1.1.0 add_y.1.0.0 lift.x.0.3.S dot_y.1.1.3 add_y.1.1.0 tanh_y.0.1.0 dot_y.1.0.1
-add_y.1.1.3 turn.x.1.3 scale_y.0.1.3 encode_x.0.2 dot_y.1.1.1 lift.x.1.3.S add_y.1.0.1 turn_bias scale_y.0.1.0
-encode_x.1.2 dot_x.2.0.0 scale_y.0.1.1 add_y.1.1.1 turn.x.1.0 scale_y.0.1.2 add_y.1.1.2 turn.x.1.1 lift.x.1.0.S
-weave_y.0.1 dot_obs.1.0.1 lift_bias_column lift.x.1.1.S dot_obs.1.0.0 tanh_obs.1.0.1 dot_obs.0.0.0 encode_x.1.0
-tanh_obs.1.0.0 dot_obs.0.0.1 add_x.2.0.0 tanh_y.1.0.1 turn_obs.1.0.0 encode_fy.0.1 dot_x.2.0.1 weigh_obs.1.0.0
-tanh_y.1.0.0 turn_obs.1.0.1 add_x.2.0.1 dot_obs.1.1.0 weigh_obs.1.0.1 tanh_obs.0.0.0 dot_obs.1.1.1 weigh_y.1.0
-tanh_obs.1.1.0 dot_obs.0.1.0 tanh_obs.1.1.1 turn_obs.1.1.0 turn_obs.0.0.0 tanh_obs.0.1.0 dot_obs.0.1.1 tanh_obs.0.0.1
-weigh_obs.0.0.0 dot_x.3.0.0 tanh_y.1.1.1 turn_obs.1.1.1 weigh_obs.1.1.0 turn_obs.0.0.1 weigh_obs.1.1.1 dot_x.2.1.0
-tanh_obs.0.1.1 weigh_obs.0.0.1 turn_obs.0.1.0 tanh_x.2.0 encode_fx.1 turn_obs.0.1.1 dot_x.2.1.1 weigh_obs.0.1.1
-tanh_y.1.1.0 cross_t.0.2 weigh_obs.0.1.0 cross.3.0 add_x.2.1.1 lift_cross_t.0.2.S cross_t.0.3 encode_fx.0
-store_cross.3.0.S dot_x.3.0.1 add_x.2.1.0 lift_cross_t.0.3.S cross.1.0 weigh_y.1.1 tanh_x.2.1 cross_t.0.1 cross_t.0.0
-lift_cross_t.0.1.S cross.2.0 lift_cross_t.0.0.S cross.0.0 encode_fy.1.0 store_cross.2.0.S dot_x.3.1.1 encode_fy.1.1
-store_cross.0.0.S add_x.3.0.1 cross.2.1 store_cross.1.0.S add_x.3.0.0 cross.3.1 store_cross.2.1.S weigh_x.2.1
-cross.0.1 tanh_x.3.0 cross_t.1.0 weigh_x.2.0 dot_x.3.1.0 store_cross.0.1.S cross_t.1.2 lift_cross_t.1.0.S add_x.3.1.0
-cross_t.1.1 lift_cross_t.1.2.S encode_fx.2 cross.1.1 store_cross.3.1.S weigh_x.3.0 cross_t.1.3 lift_cross_t.1.1.S
-cross.4.0 store_cross.1.1.S add_x.3.1.1 cross_t.0.4 store_cross.4.0.S lift_cross_t.1.3.V cross.5.0 tanh_x.3.1
-store_plane.1.0 cross_t.0.5 store_cross.5.0.V cross.4.1 lift_cross_t.0.5.S weigh_x.3.1 cross_t.1.5 lift_cross_t.0.4.S
-cross.5.1 store_cross.4.1.S encode_fx.3 cross_t.1.4 store_cross.5.1.S store_plane.0.0 cross_t.1.6 store_plane.1.1
-lift_cross_t.1.5.S cross.6.0 lift_cross_t.1.6.V lift_cross_t.1.4.S cross.6.1 store_plane.0.2 store_cross.6.0.S
-store_plane.0.1 store_scales.0 cross_t.0.7 store_plane.1.2 store_cross.6.1.S cross_t.1.7 lift_cross_t.0.7.S cross.7.1
-cross.7.0 store_cross.7.1.V cross_t.0.6 store_cross.7.0.S lift_cross_t.1.7.V lift_cross_t.0.6.S store_plane.1.3
-store_plane.0.3 store_scales.1
-"""
+OBS_HALF = {"y": 1, "x": 1}
 
 
 def tile_extendeddmdkoopmancrossmoment_x2_kernel(
@@ -71,8 +41,8 @@ def tile_extendeddmdkoopmancrossmoment_x2_kernel(
 
         w_scale = keep.tile([P, SIZE], U8, name="w_scale", align_bytes=64)
         nc.vector.memset(w_scale[:].bitcast(I32), 0)
-        zero = keep.tile([P, 1], F32, name="zero")
-        nc.vector.memset(zero[:], 0.0)
+        b_square = keep.tile([P, P], F32, name="b_square", align_bytes=64)
+        nc.gpsimd.memset(b_square[:], 0.0)
 
         b_rows = keep.tile([P, 8], BF16, name="b_rows", align_bytes=64)
         nc.scalar.dma_start(out=b_rows[:], in_=b.rearrange("(n w) -> n w", w=8))
@@ -81,8 +51,6 @@ def tile_extendeddmdkoopmancrossmoment_x2_kernel(
                 out=w_scale[32 * quad : 32 * quad + 8, :].bitcast(I32),
                 in_=w_scales[:, 4 * quad : 4 * quad + 4, :].bitcast(I32),
             )
-        tanh_warm_up = keep.tile([P, 1], F32, name="tanh_warm_up")
-        nc.scalar.activation(out=tanh_warm_up[:], in_=zero[:], func=ACT.Tanh)
 
         row_words = {}
 
@@ -104,52 +72,37 @@ def tile_extendeddmdkoopmancrossmoment_x2_kernel(
             )
 
         weight = {}
-        weight_f32 = {}
 
         def load_weights(op, source):
             weight[op] = keep.tile([P, 2, 4], BF16, name=f"weight_{op}", align_bytes=64)
             nc.sync.dma_start(out=weight[op][:], in_=source.rearrange("(g p j) -> p g j", g=2, j=4))
-            weight_f32[op] = keep.tile([P, 2, 4], F32, name=f"weight_f32_{op}", align_bytes=64)
-            nc.gpsimd.tensor_copy(out=weight_f32[op][:], in_=weight[op][:])
+
+        b_tiles = keep.tile([8, P], BF16, name="b_tiles", align_bytes=64)
 
         load_rows("y", y, 0, 0, 1)
         load_rows("y", y, 0, 1, 1)
-        load_w(0)
         load_rows("y", y, 0, 2, 2)
-        load_rows("y", y, 1, 0, 2)
-        load_rows("y", y, 1, 2, 2)
+        load_w(0)
         load_weights("y", q)
-        load_weights("x", p)
-        load_rows("x", x, 0, 0, 4)
-        load_rows("x", x, 1, 0, 4)
+        load_rows("y", y, 1, 0, 2)
         load_w(1)
+        load_rows("y", y, 1, 2, 2)
+        nc.sync.dma_start(out=b_tiles[:], in_=b.rearrange("(m n) -> m n", n=P))
+        nc.gpsimd.tensor_copy(out=b_square[0:8, :], in_=b_tiles[:])
+        load_weights("x", p)
+        for g in range(2):
+            for j in range(0, 4, 2):
+                load_rows("x", x, g, j, 2)
 
-        def turn_bank():
-            bank = psum.tile([P, 4, P], F32, name="turn_bank", tag="turn_bank", bufs=TURN_BANKS)
+        def new_bank(*key):
+            bank = psum.tile([P, 4, P], F32, name="bank", tag="bank", bufs=BANKS)
+            made["bank", key] = bank
             return bank
 
-        def sum_bank():
-            bank = psum.tile([P, 512], F32, name="sum_bank", tag="sum_bank", bufs=SUM_BANKS)
-            return bank
-
-        for n in range(3):
-            bank = turn_bank()
-            for m in range(4):
-                nc.tensor.transpose(bank[:, m, :], ident[:], ident[:])
-
-
-        row_dims = {"y": [P, 4, 2, P], "x": [P, 2, 4, P]}
-        row_code = {}
-        row_scale = {}
-        for op in ("y", "x"):
-            for g in range(2):
-                row_code[op, g] = keep.tile(row_dims[op], U32, name=f"row_code_{op}{g}", align_bytes=64)
-                row_scale[op, g] = keep.tile(row_dims[op], U8, name=f"row_scale_{op}{g}", align_bytes=64)
-
-        def stationary_rows(op, g, j, c):
-            if op == "y":
-                return row_code[op, g][:, j, c, :].bitcast(FP8X4), row_scale[op, g][:, j, c, :]
-            return row_code[op, g][:, c, j, :].bitcast(FP8X4), row_scale[op, g][:, c, j, :]
+        def work_tile(name, key, dims, dtype, bufs):
+            if (name, key) not in made:
+                made[name, key] = work.tile(dims, dtype, name=name, tag=name, bufs=bufs, align_bytes=64)
+            return made[name, key]
 
         def copy(engine, out, in_):
             if engine == "S":
@@ -157,71 +110,78 @@ def tile_extendeddmdkoopmancrossmoment_x2_kernel(
             else:
                 nc.vector.tensor_copy(out=out, in_=in_)
 
-        def turn(op, g, j):
-            bank = turn_bank()
+        def quantize(code, scale, in_):
+            nc.vector.quantize_mx(out=code.bitcast(FP8X4), scales=scale, in_=in_)
+
+
+        row_code = {}
+        row_scale = {}
+        for op in ("y", "x"):
+            for g in range(2):
+                dims = [P, 2, 4, P] if g == OBS_HALF[op] else [P, 4, 2, P]
+                row_code[op, g] = keep.tile(dims, U32, name=f"row_code_{op}{g}", align_bytes=64)
+                row_scale[op, g] = keep.tile(dims, U8, name=f"row_scale_{op}{g}", align_bytes=64)
+
+        def turn_rows(op, g, j):
+            bank = new_bank("rows", op, g, j)
             words = row_words[op, g, j]
             for c in range(2):
                 for e in range(2):
                     nc.tensor.transpose(bank[:, 2 * c + e, :], words[:, 256 * c + e : 256 * (c + 1) : 2], ident[:])
-            made["turn", op, g, j] = bank
 
-        def lift(op, g, j, engine):
-            if ("lift", op, g, j // 2) not in made:
-                pair_dims = [P, 2, 2, P, 2]
-                made["lift", op, g, j // 2] = work.tile(pair_dims, F32, name="pair", tag="pair", align_bytes=64)
-            pair = made["lift", op, g, j // 2]
-            out = pair[:, j % 2] if op == "y" else pair[:, :, j % 2]
-            copy(engine, out, made["turn", op, g, j][:].rearrange("p (c e) r -> p c r e", e=2))
+        def lift_rows(op, g, j, engine):
+            bank = made["bank", ("rows", op, g, j)]
+            pair = work_tile("pair", (op, g, j // 2), [P, 2, 2, P, 2], F32, 3)
+            out = pair[:, :, j % 2] if g == OBS_HALF[op] else pair[:, j % 2]
+            copy(engine, out, bank[:].rearrange("p (c e) r -> p c r e", e=2))
 
-        def encode_y(g, j, n):
-            pair = made["lift", "y", g, j // 2]
-            nc.vector.quantize_mx(
-                out=row_code["y", g][:, j : j + n].rearrange("p j c r -> p (j c r)").bitcast(FP8X4),
-                scales=row_scale["y", g][:, j : j + n].rearrange("p j c r -> p (j c r)"),
-                in_=pair[:, j % 2 : j % 2 + n].rearrange("p j c r e -> p (j c r e)").bitcast(BF16),
-            )
-
-        def encode_x(g, j):
-            for c in range(2):
-                nc.vector.quantize_mx(
-                    out=row_code["x", g][:, c, j : j + 2].rearrange("p j r -> p (j r)").bitcast(FP8X4),
-                    scales=row_scale["x", g][:, c, j : j + 2].rearrange("p j r -> p (j r)"),
-                    in_=made["lift", "x", g, j // 2][:, c].rearrange("p j r e -> p (j r e)").bitcast(BF16),
+        def encode_rows(op, g, i):
+            j = 2 * i
+            pair = made["pair", (op, g, i)]
+            if g == OBS_HALF[op]:
+                for c in range(2):
+                    quantize(
+                        row_code[op, g][:, c, j : j + 2].rearrange("p j r -> p (j r)"),
+                        row_scale[op, g][:, c, j : j + 2].rearrange("p j r -> p (j r)"),
+                        pair[:, c].rearrange("p j r e -> p (j r e)").bitcast(BF16),
+                    )
+            else:
+                quantize(
+                    row_code[op, g][:, j : j + 2].rearrange("p j c r -> p (j c r)"),
+                    row_scale[op, g][:, j : j + 2].rearrange("p j c r -> p (j c r)"),
+                    pair[:].rearrange("p j c r e -> p (j c r e)").bitcast(BF16),
                 )
 
 
         bias_words = keep.tile([P, P, 4], F32, name="bias_words", align_bytes=64)
         bias_row = bias_words[:].rearrange("p n m -> p (n m)").bitcast(BF16)
-        bias_f32 = keep.tile([P, 4, P], F32, name="bias_f32", align_bytes=64)
-        bias_column = keep.tile([P, 4], F32, name="bias_column", align_bytes=64)
+        bias_column = keep.tile([P, 8], F32, name="bias_column", align_bytes=64)
 
         def spread_bias():
-            made["spread_bias"] = turn_bank()
+            bank = new_bank("bias_row")
             words = b_rows[:].bitcast(F32)
             for m in range(4):
-                nc.tensor.transpose(made["spread_bias"][:, m, :], words[:, m : m + 1].to_broadcast([P, P]), ident[:])
+                nc.tensor.transpose(bank[:, m, :], words[:, m : m + 1].to_broadcast([P, P]), ident[:])
 
-        def lift_bias(engine):
-            copy(engine, bias_words[:], made["spread_bias"][:].rearrange("p m n -> p n m"))
-
-        def widen_bias():
-            nc.scalar.copy(out=bias_f32[:].rearrange("p m n -> p (m n)"), in_=bias_row[:, 0:512])
+        def lift_bias_row():
+            bank = made["bank", ("bias_row",)]
+            nc.scalar.copy(out=bias_words[:], in_=bank[:].rearrange("p m n -> p n m"))
 
         def turn_bias():
-            made["turn_bias"] = turn_bank()
-            for m in range(4):
-                nc.tensor.transpose(made["turn_bias"][:, m, :], bias_f32[:, m, :], ident[:])
+            bank = new_bank("bias_column")
+            nc.tensor.transpose(bank[:, 0, :], b_square[:], ident[:])
 
         def lift_bias_column():
-            nc.scalar.copy(out=bias_column[:], in_=made["turn_bias"][:, :, 0])
+            bank = made["bank", ("bias_column",)]
+            nc.scalar.copy(out=bias_column[:], in_=bank[:, 0, 0:8])
 
 
         fy_code = {}
         fy_scale = {}
-        for h in range(2):
-            for g in range(2):
-                fy_code[h, g] = keep.tile([P, 4, P], U32, name=f"fy_code{h}{g}", align_bytes=64)
-                fy_scale[h, g] = keep.tile([P, 4, P], U8, name=f"fy_scale{h}{g}", align_bytes=64)
+        for g in range(2):
+            for h in range(2):
+                fy_code[g, h] = keep.tile([P, 512], U32, name=f"fy_code{g}{h}", align_bytes=64)
+                fy_scale[g, h] = keep.tile([P, 512], U8, name=f"fy_scale{g}{h}", align_bytes=64)
         fx_code = []
         fx_scale = []
         for c in range(4):
@@ -230,248 +190,313 @@ def tile_extendeddmdkoopmancrossmoment_x2_kernel(
             fx_code.append(code)
             fx_scale.append(scale)
 
-        def work_tile(name, key, dims, dtype, bufs):
-            if (name, key) not in made:
-                made[name, key] = work.tile(dims, dtype, name=name, tag=name, bufs=bufs, align_bytes=64)
-            return made[name, key]
-
-        def project(op, g, j, col, n, out):
-            for c in range(2):
-                code, scale = stationary_rows(op, g, j, c)
-                nc.tensor.matmul_mx(
-                    out=out,
-                    lhsT=code,
-                    lhsT_scale=scale,
-                    rhs=w_code[:, c, col : col + n].bitcast(FP8X4),
-                    rhs_scale=w_scale[4 * c : P, col : col + n],
-                    start=(c == 0),
-                    stop=(c == 1),
-                )
-
-
-        def dot_y(h, g, j):
-            bank = sum_bank()
-            project("y", g, j, 512 * h, 512, bank[:])
-            made["dot_y", h, g, j] = bank
-
-        def add_y(h, g, j):
-            z = work_tile("z", ("y", h, g), [P, 2048], F32, 3)
-            nc.vector.tensor_tensor(
-                out=z[:, 512 * j : 512 * j + 512].rearrange("p (t a) -> p t a", t=4),
-                in0=made["dot_y", h, g, j][:].rearrange("p (a t) -> p t a", t=4),
-                in1=bias_row[:, 512 * h : 512 * h + 512].rearrange("p (a t) -> p t a", t=4),
-                op=ALU.add,
-            )
-
-        def tanh(key, part):
-            span = slice(1024 * part, 1024 * part + 1024)
-            th = work_tile("th", key, [P, 2048], F32, 3)
-            nc.scalar.activation(out=th[:, span], in_=made["z", key][:, span], func=ACT.Tanh)
-
-        def tanh_y(h, g, part):
-            tanh(("y", h, g), part)
-
-        def weave(f, th, weights, n):
-            nc.vector.tensor_tensor(
-                out=f.rearrange("p (o i) j -> p o j i", i=4),
-                in0=th.rearrange("p j (o i) -> p o j i", i=4),
-                in1=weights.unsqueeze(1).unsqueeze(3).to_broadcast([P, n // 4, 4, 4]),
-                op=ALU.mult,
-            )
-
-        def weigh_y(h, g):
-            f = work_tile("f", ("y", h, g), [P, 512, 4], BF16, 3)
-            weave(f[:], made["th", ("y", h, g)][:].rearrange("p (j o) -> p j o", j=4), weight["y"][:, g, :], 512)
-
-
-        def scale_y(h, g, j):
-            v = work_tile("v", ("y", h, g), [P, 4, 512], BF16, 2)
-            nc.scalar.activation(
-                out=v[:, j, :],
-                in_=made["th", ("y", h, g)][:, 512 * j : 512 * j + 512],
-                func=ACT.Copy,
-                scale=weight_f32["y"][:, g, j : j + 1],
-            )
-
-        def weave_y(h, g):
-            f = work_tile("f", ("y", h, g), [P, 512, 4], BF16, 3)
-            nc.vector.tensor_copy(
-                out=f[:].rearrange("p (o i) j -> p o j i", i=4),
-                in_=made["v", ("y", h, g)][:].rearrange("p j (o i) -> p o j i", i=4),
-            )
-
-        def encode_fy(h, g):
-            nc.vector.quantize_mx(
-                out=fy_code[h, g][:].rearrange("p t a -> p (t a)").bitcast(FP8X4),
-                scales=fy_scale[h, g][:].rearrange("p t a -> p (t a)"),
-                in_=made["f", ("y", h, g)][:].rearrange("p o j -> p (o j)"),
-            )
-
-
-        def dot_x(c, g, i):
-            bank = sum_bank()
-            for k in range(2):
-                project("x", g, 2 * i + k, 256 * c, 256, bank[:, 256 * k : 256 * k + 256])
-            made["dot_x", c, g, i] = bank
-
-        def add_x(c, g, i):
-            z = work_tile("z", ("x", c), [P, 2048], F32, 3)
-            first = 1024 * g + 512 * i
-            nc.vector.tensor_tensor(
-                out=z[:, first : first + 512].rearrange("p (k o) -> p k o", k=2),
-                in0=made["dot_x", c, g, i][:].rearrange("p (k o) -> p k o", k=2),
-                in1=bias_row[:, 256 * c : 256 * c + 256].unsqueeze(1).to_broadcast([P, 2, 256]),
-                op=ALU.add,
-            )
-
-        def tanh_x(c, g):
-            tanh(("x", c), g)
-
-        def weigh_x(c, g):
-            f = work_tile("f", ("x", c), [P, 512, 4], BF16, 3)
-            th = made["th", ("x", c)][:, 1024 * g : 1024 * g + 1024].rearrange("p (j o) -> p j o", j=4)
-            weave(f[:, 256 * g : 256 * g + 256, :], th, weight["x"][:, g, :], 256)
-
-
-        def dot_obs(c, g, i):
-            col = 256 * c + 128 * i
-            bank = sum_bank()
-            for k in range(2):
-                nc.tensor.matmul_mx(
-                    out=bank[:],
-                    lhsT=w_code[:, k, col : col + P].bitcast(FP8X4),
-                    lhsT_scale=w_scale[4 * k : P, col : col + P],
-                    rhs=row_code["x", g][:, k].rearrange("p j r -> p (j r)").bitcast(FP8X4),
-                    rhs_scale=row_scale["x", g][:, k].rearrange("p j r -> p (j r)"),
-                    start=(k == 0),
-                    stop=(k == 1),
-                )
-            made["dot_obs", c, g, i] = bank
-
-        def tanh_obs(c, g, i):
-            t = work_tile("t", (c, g, i), [P, 4, P], F32, 3)
-            nc.scalar.activation(
-                out=t[:].rearrange("p j r -> p (j r)"),
-                in_=made["dot_obs", c, g, i][:],
-                func=ACT.Tanh,
-                bias=bias_column[:, 2 * c + i : 2 * c + i + 1],
-            )
-
-        def turn_obs(c, g, i):
-            bank = turn_bank()
-            for j in range(4):
-                nc.tensor.transpose(bank[:, j, :], made["t", (c, g, i)][:, j, :], ident[:])
-            made["turn_obs", c, g, i] = bank
-
-        def weigh_obs(c, g, i):
-            f = work_tile("f", ("x", c), [P, 512, 4], BF16, 3)
-            first = 256 * g + 128 * i
-            nc.vector.tensor_tensor(
-                out=f[:, first : first + P, :],
-                in0=made["turn_obs", c, g, i][:].rearrange("p j o -> p o j"),
-                in1=weight["x"][:, g, :].unsqueeze(1).to_broadcast([P, P, 4]),
-                op=ALU.mult,
-            )
-
-        def encode_fx(c):
-            nc.vector.quantize_mx(
-                out=fx_code[c][:].rearrange("p g o -> p (g o)").bitcast(FP8X4),
-                scales=fx_scale[c][:].rearrange("p g o -> p (g o)"),
-                in_=made["f", ("x", c)][:].rearrange("p o j -> p (o j)"),
-            )
-
-
-        plane_code = []
-        for h in range(2):
-            code = keep.tile([P, SIZE], U32, name=f"plane_code{h}", align_bytes=64)
-            plane_code.append(code)
-        plane_scale = keep.tile([P, SIZE], U8, name="plane_scale", align_bytes=64)
-        plane_words = out_1.rearrange("g p m t -> g p (m t)")
-
-        def fx_tile(tile, g):
-            c, first = tile // 2, P * (tile % 2)
-            return fx_code[c][:, g, first : first + P].bitcast(FP8X4), fx_scale[c][:, g, first : first + P]
-
-        def divide(engine, out, in_):
-            if engine == "S":
-                nc.scalar.activation(out=out, in_=in_, func=ACT.Copy, scale=INV_DIV)
+        def f_part(op, g, col, n):
+            if op == "y":
+                key, first = (op, g, col // 512), col % 512
             else:
-                nc.vector.tensor_scalar(out=out, in0=in_, scalar1=INV_DIV, scalar2=None, op0=ALU.mult)
+                key, first = (op, col // 256), 256 * g + col % 256
+            f = work_tile("f", key, [P, 512, 4], BF16, 4)
+            return f[:, first : first + n, :]
 
-        def cross(tile, h):
-            bank = turn_bank()
-            for g in range(2):
-                code, scale = fx_tile(tile, g)
+        def encode_f(*key):
+            values = made["f", key][:].rearrange("p o j -> p (o j)")
+            if key[0] == "y":
+                quantize(fy_code[key[1], key[2]][:], fy_scale[key[1], key[2]][:], values)
+            else:
+                quantize(
+                    fx_code[key[1]][:].rearrange("p g o -> p (g o)"),
+                    fx_scale[key[1]][:].rearrange("p g o -> p (g o)"),
+                    values,
+                )
+
+        def dot_snap(op, c, i):
+            g = 1 - OBS_HALF[op]
+            bank = new_bank("snap", op, c, i)
+            sums = bank[:].rearrange("p (k a) r -> p k (a r)", k=2)
+            for k in range(2):
+                for n in range(2):
+                    nc.tensor.matmul_mx(
+                        out=sums[:, k, :],
+                        lhsT=row_code[op, g][:, 2 * i + k, n, :].bitcast(FP8X4),
+                        lhsT_scale=row_scale[op, g][:, 2 * i + k, n, :],
+                        rhs=w_code[:, n, 256 * c : 256 * c + 256].bitcast(FP8X4),
+                        rhs_scale=w_scale[4 * n : P, 256 * c : 256 * c + 256],
+                        start=(n == 0),
+                        stop=(n == 1),
+                    )
+
+        def add_bias(op, c, i):
+            sums = made["bank", ("snap", op, c, i)][:].rearrange("p (k a) r -> p k (a r)", k=2)
+            z = work_tile("z", (op, c), [P, 2, 256, 2], F32, 4)
+            nc.vector.tensor_tensor(
+                out=z[:, i],
+                in0=sums.rearrange("p k o -> p o k"),
+                in1=bias_row[:, 256 * c : 256 * c + 256].unsqueeze(2).to_broadcast([P, 256, 2]),
+                op=ALU.add,
+            )
+
+        def tanh_snap(op, c):
+            z = made["z", (op, c)]
+            th = work_tile("th", (op, c), [P, 2, 256, 2], F32, 4)
+            nc.scalar.activation(
+                out=th[:].rearrange("p i o k -> p (i o k)"), in_=z[:].rearrange("p i o k -> p (i o k)"), func=ACT.Tanh
+            )
+
+        def weigh_snap(op, c):
+            th = made["th", (op, c)]
+            g = 1 - OBS_HALF[op]
+            weights = weight[op][:, g, :].rearrange("p (i k) -> p i k", i=2)
+            nc.vector.tensor_tensor(
+                out=f_part(op, g, 256 * c, 256).rearrange("p o (i k) -> p o i k", i=2),
+                in0=th[:].rearrange("p i o k -> p o i k"),
+                in1=weights.unsqueeze(1).to_broadcast([P, 256, 2, 2]),
+                op=ALU.mult,
+            )
+
+        def dot_obs(op, m):
+            g = OBS_HALF[op]
+            bank = new_bank("obs", op, m)
+            sums = bank[:].rearrange("p j r -> p (j r)")
+            for n in range(2):
                 nc.tensor.matmul_mx(
-                    out=bank[:].rearrange("p t a -> p (t a)"),
-                    lhsT=code,
-                    lhsT_scale=scale,
-                    rhs=fy_code[h, g][:].rearrange("p t a -> p (t a)").bitcast(FP8X4),
-                    rhs_scale=fy_scale[h, g][:].rearrange("p t a -> p (t a)"),
+                    out=sums,
+                    lhsT=w_code[:, n, P * m : P * m + P].bitcast(FP8X4),
+                    lhsT_scale=w_scale[4 * n : P, P * m : P * m + P],
+                    rhs=row_code[op, g][:, n].rearrange("p j r -> p (j r)").bitcast(FP8X4),
+                    rhs_scale=row_scale[op, g][:, n].rearrange("p j r -> p (j r)"),
+                    start=(n == 0),
+                    stop=(n == 1),
+                )
+
+        def tanh_obs(op, m):
+            sums = made["bank", ("obs", op, m)][:].rearrange("p j r -> p (j r)")
+            t = work_tile("t", (op, m), [P, 4, P], F32, 6)
+            nc.scalar.activation(
+                out=t[:].rearrange("p j r -> p (j r)"), in_=sums, func=ACT.Tanh, bias=bias_column[:, m : m + 1]
+            )
+
+        def turn_obs(op, m):
+            t = made["t", (op, m)]
+            bank = new_bank("turned", op, m)
+            for j in range(4):
+                nc.tensor.transpose(bank[:, j, :], t[:, j, :], ident[:])
+
+        def weigh_obs(op, m):
+            bank = made["bank", ("turned", op, m)]
+            g = OBS_HALF[op]
+            nc.vector.tensor_tensor(
+                out=f_part(op, g, P * m, P),
+                in0=bank[:].rearrange("p j o -> p o j"),
+                in1=weight[op][:, g, :].unsqueeze(1).to_broadcast([P, P, 4]),
+                op=ALU.mult,
+            )
+
+
+        plane_code = keep.tile([P, 2, SIZE], U32, name="plane_code", align_bytes=64)
+        plane_scale = keep.tile([P, 2, SIZE], U8, name="plane_scale", align_bytes=64)
+        plane_words = out_1.rearrange("g p m t -> p g (m t)")
+
+        def cross(m, h):
+            c, first = m // 2, P * (m % 2)
+            bank = new_bank("cross", m, h)
+            sums = bank[:].rearrange("p t a -> p (t a)")
+            for g in range(2):
+                nc.tensor.matmul_mx(
+                    out=sums,
+                    lhsT=fx_code[c][:, g, first : first + P].bitcast(FP8X4),
+                    lhsT_scale=fx_scale[c][:, g, first : first + P],
+                    rhs=fy_code[g, h][:].bitcast(FP8X4),
+                    rhs_scale=fy_scale[g, h][:],
                     start=(g == 0),
                     stop=(g == 1),
                 )
-            made["cross", tile, h] = bank
 
-        def store_cross(tile, h, engine):
-            r = work.tile([P, 512], F32, name="r", tag="r", bufs=6, align_bytes=64)
-            divide(engine, r[:].rearrange("p (a t) -> p a t", t=4), made["cross", tile, h][:].rearrange("p t a -> p a t"))
-            nc.sync.dma_start(out=out_0[P * tile : P * tile + P, 512 * h : 512 * h + 512], in_=r[:])
+        def store_cross(m, h, engine):
+            sums = made["bank", ("cross", m, h)][:].rearrange("p t a -> p (t a)")
+            r = work_tile("r", m, [P, 2, 512], F32, 5)
+            if engine == "S":
+                nc.scalar.activation(out=r[:, h, :], in_=sums, func=ACT.Copy, scale=INV_DIV)
+            else:
+                nc.vector.tensor_scalar(out=r[:, h, :], in0=sums, scalar1=INV_DIV, scalar2=None, op0=ALU.mult)
+            nc.sync.dma_start(out=out_0[P * m : P * m + P, 512 * h : 512 * h + 512], in_=r[:, h, :])
 
-        def cross_t(h, tile):
-            bank = turn_bank()
-            for t in range(4):
-                for g in range(2):
-                    code, scale = fx_tile(tile, g)
-                    nc.tensor.matmul_mx(
-                        out=bank[:, t, :],
-                        lhsT=fy_code[h, g][:, t, :].bitcast(FP8X4),
-                        lhsT_scale=fy_scale[h, g][:, t, :],
-                        rhs=code,
-                        rhs_scale=scale,
-                        start=(g == 0),
-                        stop=(g == 1),
-                    )
-            made["cross_t", h, tile] = bank
+        def round_cross(m):
+            r = made["r", m]
+            s = work_tile("s", m, [P, 2, 2, P, 2], BF16, 5)
+            nc.vector.tensor_copy(out=s[:], in_=r[:].rearrange("p h (a e s) -> p h e a s", e=2, s=2))
 
-        def lift_cross_t(h, tile, engine):
-            s = work_tile("s", (h, tile // 2), [P, 256, 4], BF16, 4)
-            first = P * (tile % 2)
-            divide(engine, s[:, first : first + P, :], made["cross_t", h, tile][:].rearrange("p t i -> p i t"))
+        def turn_cross(m):
+            s = made["s", m]
+            words = s[:].rearrange("p h e a s -> p (h e) (a s)").bitcast(F32)
+            bank = new_bank("plane", m)
+            for n in range(4):
+                nc.tensor.transpose(bank[:, n, :], words[:, n, :], ident[:])
 
-        def store_plane(h, c):
-            cols = slice(256 * c, 256 * c + 256)
-            nc.vector.quantize_mx(
-                out=plane_code[h][:, cols].bitcast(FP8X4),
-                scales=plane_scale[4 * h : P, cols],
-                in_=made["s", (h, c)][:].rearrange("p i t -> p (i t)"),
-            )
+        def lift_plane(m, engine):
+            bank = made["bank", ("plane", m)]
+            c, first = m // 2, P * (m % 2)
+            u = work_tile("u", c, [P, 2, 256, 2], F32, 2)
+            copy(engine, u[:, :, first : first + P, :], bank[:].rearrange("p (h e) i -> p h i e", e=2))
+
+        def store_plane(m, n):
+            u = made["u", m // 2]
+            first = P * (m % 2)
+            cols = slice(P * m, P * (m + n))
+            for h in range(2):
+                quantize(
+                    plane_code[:, h, cols],
+                    plane_scale[:, h, cols],
+                    u[:, h, first : first + P * n].rearrange("p i e -> p (i e)").bitcast(BF16),
+                )
             nc.sync.dma_start(
-                out=plane_words[h][:, 1024 * c : 1024 * c + 1024].bitcast(I32),
-                in_=plane_code[h][:, cols].bitcast(I32),
+                out=plane_words[:, :, 4 * P * m : 4 * P * (m + n)].bitcast(I32),
+                in_=plane_code[:, :, cols].bitcast(I32),
             )
+            if m + n in SCALE_STORES:
+                store_scales(SCALE_STORES[m + n], m + n)
 
-        def store_scales(part):
-            cols = slice(512 * part, 512 * part + 512)
+        def store_scales(m, end):
+            cols = slice(P * m, P * end)
             for quad in range(4):
-                nc.sync.dma_start(
-                    out=out_2[:, 4 * quad : 4 * quad + 4, cols].bitcast(I32),
-                    in_=plane_scale[32 * quad : 32 * quad + 8, cols].bitcast(I32),
+                queue = nc.scalar if end == 8 and quad % 2 == 1 else nc.sync
+                queue.dma_start(
+                    out=out_2[:, 4 * quad : 4 * quad + 4, cols].rearrange("h r m -> r h m").bitcast(I32),
+                    in_=plane_scale[32 * quad : 32 * quad + 4, :, cols].bitcast(I32),
                 )
 
 
-        steps = {
-            "turn": turn, "lift": lift, "encode_y": encode_y, "encode_x": encode_x,
-            "spread_bias": spread_bias, "lift_bias": lift_bias, "widen_bias": widen_bias,
-            "turn_bias": turn_bias, "lift_bias_column": lift_bias_column,
-            "dot_y": dot_y, "add_y": add_y, "tanh_y": tanh_y, "weigh_y": weigh_y,
-            "scale_y": scale_y, "weave_y": weave_y, "encode_fy": encode_fy,
-            "dot_x": dot_x, "add_x": add_x, "tanh_x": tanh_x, "weigh_x": weigh_x,
-            "dot_obs": dot_obs, "tanh_obs": tanh_obs, "turn_obs": turn_obs, "weigh_obs": weigh_obs,
-            "encode_fx": encode_fx,
-            "cross": cross, "store_cross": store_cross, "cross_t": cross_t, "lift_cross_t": lift_cross_t,
-            "store_plane": store_plane, "store_scales": store_scales,
-        }
-        for step in SCORE.split():
-            parts = step.split(".")
-            steps[parts[0]](*[int(a) if a in "01234567" else a for a in parts[1:]])
+        tensor, vector, scalar = [], [], []
+
+        def both(step, *args):
+            return [(step,) + args + (k,) for k in range(2)]
+
+        def tiles(step, op, c):
+            return [(step, op, 2 * c), (step, op, 2 * c + 1)]
+
+        def row_pair(step, op, g, i, *engine):
+            return [(step, op, g, 2 * i) + engine, (step, op, g, 2 * i + 1) + engine]
+
+        tensor += row_pair(turn_rows, "y", 0, 0) + [(spread_bias,)] + row_pair(turn_rows, "y", 0, 1)
+        tensor += [(dot_snap, "y", c, i) for i in range(2) for c in range(2)]
+        tensor += row_pair(turn_rows, "y", 1, 0) + row_pair(turn_rows, "y", 1, 1)
+        tensor += both(dot_snap, "y", 2) + [(turn_bias,)] + row_pair(turn_rows, "x", 0, 0)
+        tensor += both(dot_snap, "y", 3) + tiles(dot_obs, "y", 0) + row_pair(turn_rows, "x", 0, 1)
+        tensor += tiles(dot_obs, "y", 1) + tiles(turn_obs, "y", 0) + row_pair(turn_rows, "x", 1, 0)
+        tensor += tiles(dot_obs, "y", 2) + both(dot_snap, "x", 0) + tiles(turn_obs, "y", 1) + row_pair(turn_rows, "x", 1, 1)
+        tensor += tiles(dot_obs, "y", 3) + tiles(turn_obs, "y", 2)
+        tensor += tiles(dot_obs, "x", 0) + tiles(turn_obs, "y", 3) + tiles(turn_obs, "x", 0)
+
+        vector += [(lift_rows, "y", 0, 1, "V"), (encode_rows, "y", 0, 0), (lift_rows, "y", 0, 3, "V"), (encode_rows, "y", 0, 1)]
+        vector += [(add_bias, "y", c, i) for i in range(2) for c in range(2)]
+        vector += row_pair(lift_rows, "y", 1, 0, "V") + [(encode_rows, "y", 1, 0), (weigh_snap, "y", 0), (encode_rows, "y", 1, 1)]
+        vector += both(add_bias, "y", 2) + [(weigh_snap, "y", 1)]
+        vector += both(add_bias, "y", 3) + [(encode_f, "y", 0, 0), (encode_rows, "x", 0, 0), (weigh_snap, "y", 2)]
+        vector += [(encode_rows, "x", 0, 1)] + tiles(weigh_obs, "y", 0) + [(weigh_snap, "y", 3), (encode_rows, "x", 1, 0), (encode_f, "y", 0, 1)]
+        vector += both(add_bias, "x", 0) + tiles(weigh_obs, "y", 1) + [(encode_rows, "x", 1, 1), (encode_f, "y", 1, 0)]
+        vector += tiles(weigh_obs, "y", 2) + [(weigh_snap, "x", 0)] + tiles(weigh_obs, "y", 3)
+        vector += [(weigh_obs, "x", 0), (encode_f, "y", 1, 1), (weigh_obs, "x", 1)]
+
+        scalar += [(lift_rows, "y", 0, 0, "S"), (lift_bias_row,), (lift_rows, "y", 0, 2, "S")]
+        scalar += [(tanh_snap, "y", 0), (tanh_snap, "y", 1)] + row_pair(lift_rows, "y", 1, 1, "S")
+        scalar += [(lift_bias_column,)] + row_pair(lift_rows, "x", 0, 0, "S") + [(tanh_snap, "y", 2)]
+        scalar += tiles(tanh_obs, "y", 0) + row_pair(lift_rows, "x", 0, 1, "S") + [(tanh_snap, "y", 3)]
+        scalar += tiles(tanh_obs, "y", 1) + row_pair(lift_rows, "x", 1, 0, "S")
+        scalar += tiles(tanh_obs, "y", 2) + row_pair(lift_rows, "x", 1, 1, "S") + [(tanh_snap, "x", 0)]
+        scalar += tiles(tanh_obs, "y", 3) + tiles(tanh_obs, "x", 0)
+
+        tensor += tiles(dot_obs, "x", 1) + both(dot_snap, "x", 1) + both(dot_snap, "x", 2) + both(cross, 0) + tiles(turn_obs, "x", 1)
+        vector += [(encode_f, "x", 0)] + both(add_bias, "x", 1) + both(add_bias, "x", 2)
+        vector += tiles(weigh_obs, "x", 1) + [(weigh_snap, "x", 1), (round_cross, 0)]
+        scalar += tiles(tanh_obs, "x", 1) + [(tanh_snap, "x", 1), (store_cross, 0, 0, "S"), (store_cross, 0, 1, "S"), (tanh_snap, "x", 2)]
+
+        tensor += tiles(dot_obs, "x", 2) + both(cross, 1) + both(dot_snap, "x", 3) + both(cross, 2) + tiles(turn_obs, "x", 2)
+        tensor += [(turn_cross, 0), (turn_cross, 1)]
+        vector += [(encode_f, "x", 1), (weigh_snap, "x", 2)] + both(add_bias, "x", 3) + [(round_cross, 1)]
+        vector += tiles(weigh_obs, "x", 2) + [(round_cross, 2), (encode_f, "x", 2)]
+        scalar += tiles(tanh_obs, "x", 2) + [(store_cross, m, h, "S") for m in (1, 2) for h in range(2)] + [(tanh_snap, "x", 3)]
+
+        tensor += tiles(dot_obs, "x", 3) + both(cross, 3) + both(cross, 4) + tiles(turn_obs, "x", 3)
+        tensor += [(turn_cross, 2), (turn_cross, 3)]
+        vector += [(weigh_snap, "x", 3), (store_plane, 0, 2), (store_cross, 3, 1, "V"), (round_cross, 3)]
+        vector += tiles(weigh_obs, "x", 3) + [(round_cross, 4), (encode_f, "x", 3)]
+        scalar += [(lift_plane, 0, "S"), (lift_plane, 1, "S")] + tiles(tanh_obs, "x", 3)
+        scalar += [(store_cross, 3, 0, "S"), (store_cross, 4, 0, "S"), (store_cross, 4, 1, "S")]
+
+        tensor += both(cross, 5) + [(turn_cross, 4)] + both(cross, 6) + both(cross, 7)
+        tensor += [(turn_cross, m) for m in range(5, 8)]
+        vector += [(store_cross, 5, 1, "V"), (store_plane, 2, 2), (round_cross, 5), (store_cross, 6, 1, "V"), (round_cross, 6)]
+        vector += [(store_cross, 7, 1, "V"), (round_cross, 7), (store_plane, 4, 2), (store_plane, 6, 1), (store_plane, 7, 1)]
+        scalar += [(lift_plane, 2, "S"), (lift_plane, 3, "S"), (store_cross, 5, 0, "S"), (lift_plane, 4, "S")]
+        scalar += [(store_cross, 6, 0, "S"), (store_cross, 7, 0, "S")] + [(lift_plane, m, "S") for m in range(5, 8)]
+
+
+        def inputs(step, args):
+            if step is lift_rows:
+                return [(turn_rows,) + args[:3]]
+            if step is encode_rows:
+                return [(lift_rows, args[0], args[1], 2 * args[2] + k) for k in range(2)]
+            if step is lift_bias_row:
+                return [(spread_bias,)]
+            if step is lift_bias_column:
+                return [(turn_bias,)]
+            if step is dot_snap:
+                return [(encode_rows, args[0], 1 - OBS_HALF[args[0]], args[2])]
+            if step is add_bias:
+                return [(dot_snap,) + args, (lift_bias_row,)]
+            if step is tanh_snap:
+                return [(add_bias,) + args + (i,) for i in range(2)]
+            if step is weigh_snap:
+                return [(tanh_snap,) + args]
+            if step is dot_obs:
+                return [(encode_rows, args[0], OBS_HALF[args[0]], i) for i in range(2)]
+            if step is tanh_obs:
+                return [(dot_obs,) + args, (lift_bias_column,)]
+            if step is turn_obs:
+                return [(tanh_obs,) + args]
+            if step is weigh_obs:
+                return [(turn_obs,) + args]
+            if step is encode_f:
+                if args[0] == "x":
+                    return [(weigh_snap,) + args] + [(weigh_obs, "x", 2 * args[1] + k) for k in range(2)]
+                if args[1] == OBS_HALF["y"]:
+                    return [(weigh_obs, "y", 4 * args[2] + k) for k in range(4)]
+                return [(weigh_snap, "y", 2 * args[2] + k) for k in range(2)]
+            if step is cross:
+                return [(encode_f, "x", args[0] // 2)] + [(encode_f, "y", g, args[1]) for g in range(2)]
+            if step is store_cross:
+                return [(cross,) + args[:2]]
+            if step is round_cross:
+                return [(store_cross, args[0], h) for h in range(2)]
+            if step is turn_cross:
+                return [(round_cross,) + args]
+            if step is lift_plane:
+                return [(turn_cross, args[0])]
+            if step is store_plane:
+                return [(lift_plane, args[0] + k) for k in range(args[1])]
+            return []
+
+        written = set()
+        unread_banks = []
+        while tensor or vector or scalar:
+            progress = False
+            for queue in (vector, scalar, tensor):
+                while queue:
+                    step, args = queue[0][0], queue[0][1:]
+                    wanted = inputs(step, args)
+                    if not all(name in written for name in wanted):
+                        break
+                    if queue is tensor:
+                        if len(unread_banks) >= BANKS and unread_banks[-BANKS] not in written:
+                            break
+                        unread_banks.append(("read", step) + args)
+                    step(*args)
+                    key = args[:-1] if args and args[-1] in ("S", "V") else args
+                    written.add((step,) + key)
+                    if queue is not tensor:
+                        for name in wanted:
+                            written.add(("read",) + name)
+                    queue.remove(queue[0])
+                    progress = True
+                    if queue is tensor:
+                        break
+            assert progress

@@ -18,7 +18,8 @@ ACT = mybir.ActivationFunctionType
 ALU = mybir.AluOpType
 
 BANKS = 8
-SCALE_STORES = {4: 0, 8: 4}
+LAST = 7
+FROM_BANK = [0, LAST]
 
 OBS_HALF = {"y": 1, "x": 1}
 
@@ -88,7 +89,6 @@ def tile_extendeddmdkoopmancrossmoment_x2_kernel(
         load_w(1)
         load_rows("y", y, 1, 2, 2)
         nc.sync.dma_start(out=b_tiles[:], in_=b.rearrange("(m n) -> m n", n=P))
-        nc.gpsimd.tensor_copy(out=b_square[0:8, :], in_=b_tiles[:])
         load_weights("x", p)
         for g in range(2):
             for j in range(0, 4, 2):
@@ -167,6 +167,9 @@ def tile_extendeddmdkoopmancrossmoment_x2_kernel(
             bank = made["bank", ("bias_row",)]
             nc.scalar.copy(out=bias_words[:], in_=bank[:].rearrange("p m n -> p n m"))
 
+        def widen_bias():
+            nc.scalar.copy(out=b_square[0:8, :], in_=b_tiles[:])
+
         def turn_bias():
             bank = new_bank("bias_column")
             nc.tensor.transpose(bank[:, 0, :], b_square[:], ident[:])
@@ -195,7 +198,7 @@ def tile_extendeddmdkoopmancrossmoment_x2_kernel(
                 key, first = (op, g, col // 512), col % 512
             else:
                 key, first = (op, col // 256), 256 * g + col % 256
-            f = work_tile("f", key, [P, 512, 4], BF16, 4)
+            f = work_tile("f", key, [P, 512, 4], BF16, 5)
             return f[:, first : first + n, :]
 
         def encode_f(*key):
@@ -237,19 +240,16 @@ def tile_extendeddmdkoopmancrossmoment_x2_kernel(
 
         def tanh_snap(op, c):
             z = made["z", (op, c)]
-            th = work_tile("th", (op, c), [P, 2, 256, 2], F32, 4)
-            nc.scalar.activation(
-                out=th[:].rearrange("p i o k -> p (i o k)"), in_=z[:].rearrange("p i o k -> p (i o k)"), func=ACT.Tanh
-            )
+            th = work_tile("th", (op, c), [P, 256, 2, 2], F32, 4)
+            nc.scalar.activation(out=th[:], in_=z[:].rearrange("p i o k -> p o i k"), func=ACT.Tanh)
 
         def weigh_snap(op, c):
             th = made["th", (op, c)]
             g = 1 - OBS_HALF[op]
-            weights = weight[op][:, g, :].rearrange("p (i k) -> p i k", i=2)
             nc.vector.tensor_tensor(
-                out=f_part(op, g, 256 * c, 256).rearrange("p o (i k) -> p o i k", i=2),
-                in0=th[:].rearrange("p i o k -> p o i k"),
-                in1=weights.unsqueeze(1).to_broadcast([P, 256, 2, 2]),
+                out=f_part(op, g, 256 * c, 256),
+                in0=th[:].rearrange("p o i k -> p o (i k)"),
+                in1=weight[op][:, g, :].unsqueeze(1).to_broadcast([P, 256, 4]),
                 op=ALU.mult,
             )
 
@@ -296,6 +296,12 @@ def tile_extendeddmdkoopmancrossmoment_x2_kernel(
         plane_scale = keep.tile([P, 2, SIZE], U8, name="plane_scale", align_bytes=64)
         plane_words = out_1.rearrange("g p m t -> p g (m t)")
 
+        def divide(engine, out, in_):
+            if engine == "S":
+                nc.scalar.activation(out=out, in_=in_, func=ACT.Copy, scale=INV_DIV)
+            else:
+                nc.vector.tensor_scalar(out=out, in0=in_, scalar1=INV_DIV, scalar2=None, op0=ALU.mult)
+
         def cross(m, h):
             c, first = m // 2, P * (m % 2)
             bank = new_bank("cross", m, h)
@@ -314,16 +320,20 @@ def tile_extendeddmdkoopmancrossmoment_x2_kernel(
         def store_cross(m, h, engine):
             sums = made["bank", ("cross", m, h)][:].rearrange("p t a -> p (t a)")
             r = work_tile("r", m, [P, 2, 512], F32, 5)
-            if engine == "S":
-                nc.scalar.activation(out=r[:, h, :], in_=sums, func=ACT.Copy, scale=INV_DIV)
-            else:
-                nc.vector.tensor_scalar(out=r[:, h, :], in0=sums, scalar1=INV_DIV, scalar2=None, op0=ALU.mult)
-            nc.sync.dma_start(out=out_0[P * m : P * m + P, 512 * h : 512 * h + 512], in_=r[:, h, :])
+            divide(engine, r[:, h, :], sums)
+
+        def send_cross(m, h):
+            nc.sync.dma_start(out=out_0[P * m : P * m + P, 512 * h : 512 * h + 512], in_=made["r", m][:, h, :])
 
         def round_cross(m):
             r = made["r", m]
             s = work_tile("s", m, [P, 2, 2, P, 2], BF16, 5)
             nc.vector.tensor_copy(out=s[:], in_=r[:].rearrange("p h (a e s) -> p h e a s", e=2, s=2))
+
+        def round_bank(m, h, engine):
+            sums = made["bank", ("cross", m, h)][:].rearrange("p t a -> p (t a)")
+            s = work_tile("s", m, [P, 2, 2, P, 2], BF16, 5)
+            divide(engine, s[:, h], sums.rearrange("p (a e s) -> p e a s", e=2, s=2))
 
         def turn_cross(m):
             s = made["s", m]
@@ -331,6 +341,27 @@ def tile_extendeddmdkoopmancrossmoment_x2_kernel(
             bank = new_bank("plane", m)
             for n in range(4):
                 nc.tensor.transpose(bank[:, n, :], words[:, n, :], ident[:])
+
+        def turn_last(h):
+            words = made["s", LAST][:, h].rearrange("p e a s -> p e (a s)").bitcast(F32)
+            bank = new_bank("last", h)
+            for e in range(2):
+                nc.tensor.transpose(bank[:, e, :], words[:, e, :], ident[:])
+
+        def lift_last(h, engine):
+            u = work_tile("u", LAST // 2, [P, 2, 256, 2], F32, 2)
+            copy(engine, u[:, h, P:, :], made["bank", ("last", h)][:, 0:2, :].rearrange("p e i -> p i e"))
+
+        def store_last(h):
+            cols = slice(P * LAST, SIZE)
+            quantize(
+                plane_code[:, h, cols],
+                plane_scale[:, h, cols],
+                made["u", LAST // 2][:, h, P:].rearrange("p i e -> p (i e)").bitcast(BF16),
+            )
+
+        def send_last():
+            send_plane(LAST, 1)
 
         def lift_plane(m, engine):
             bank = made["bank", ("plane", m)]
@@ -348,12 +379,12 @@ def tile_extendeddmdkoopmancrossmoment_x2_kernel(
                     plane_scale[:, h, cols],
                     u[:, h, first : first + P * n].rearrange("p i e -> p (i e)").bitcast(BF16),
                 )
+
+        def send_plane(m, n):
             nc.sync.dma_start(
                 out=plane_words[:, :, 4 * P * m : 4 * P * (m + n)].bitcast(I32),
-                in_=plane_code[:, :, cols].bitcast(I32),
+                in_=plane_code[:, :, P * m : P * (m + n)].bitcast(I32),
             )
-            if m + n in SCALE_STORES:
-                store_scales(SCALE_STORES[m + n], m + n)
 
         def store_scales(m, end):
             cols = slice(P * m, P * end)
@@ -365,7 +396,7 @@ def tile_extendeddmdkoopmancrossmoment_x2_kernel(
                 )
 
 
-        tensor, vector, scalar = [], [], []
+        tensor, vector, scalar, sync = [], [], [], []
 
         def both(step, *args):
             return [(step,) + args + (k,) for k in range(2)]
@@ -376,58 +407,56 @@ def tile_extendeddmdkoopmancrossmoment_x2_kernel(
         def row_pair(step, op, g, i, *engine):
             return [(step, op, g, 2 * i) + engine, (step, op, g, 2 * i + 1) + engine]
 
+        def outs(m, engines):
+            return [(store_cross, m, h, engines[h]) for h in range(2)]
+
         tensor += row_pair(turn_rows, "y", 0, 0) + [(spread_bias,)] + row_pair(turn_rows, "y", 0, 1)
         tensor += [(dot_snap, "y", c, i) for i in range(2) for c in range(2)]
         tensor += row_pair(turn_rows, "y", 1, 0) + row_pair(turn_rows, "y", 1, 1)
         tensor += both(dot_snap, "y", 2) + [(turn_bias,)] + row_pair(turn_rows, "x", 0, 0)
-        tensor += both(dot_snap, "y", 3) + tiles(dot_obs, "y", 0) + row_pair(turn_rows, "x", 0, 1)
-        tensor += tiles(dot_obs, "y", 1) + tiles(turn_obs, "y", 0) + row_pair(turn_rows, "x", 1, 0)
-        tensor += tiles(dot_obs, "y", 2) + both(dot_snap, "x", 0) + tiles(turn_obs, "y", 1) + row_pair(turn_rows, "x", 1, 1)
-        tensor += tiles(dot_obs, "y", 3) + tiles(turn_obs, "y", 2)
-        tensor += tiles(dot_obs, "x", 0) + tiles(turn_obs, "y", 3) + tiles(turn_obs, "x", 0)
+        tensor += both(dot_snap, "y", 3) + tiles(dot_obs, "y", 0) + row_pair(turn_rows, "x", 0, 1) + tiles(turn_obs, "y", 0)
+        tensor += tiles(dot_obs, "y", 1) + both(dot_snap, "x", 0) + row_pair(turn_rows, "x", 1, 0) + tiles(turn_obs, "y", 1)
+        tensor += tiles(dot_obs, "y", 2) + both(dot_snap, "x", 1) + row_pair(turn_rows, "x", 1, 1) + tiles(turn_obs, "y", 2)
+        tensor += tiles(dot_obs, "y", 3) + both(dot_snap, "x", 2) + tiles(turn_obs, "y", 3)
+        tensor += tiles(dot_obs, "x", 0) + tiles(dot_obs, "x", 1) + tiles(turn_obs, "x", 0) + tiles(turn_obs, "x", 1)
+        tensor += tiles(dot_obs, "x", 2) + both(dot_snap, "x", 3) + both(cross, 0) + both(cross, 1) + tiles(turn_obs, "x", 2)
+        tensor += tiles(dot_obs, "x", 3) + both(cross, 2) + both(cross, 3) + tiles(turn_obs, "x", 3) + [(turn_cross, 0), (turn_cross, 1)]
+        tensor += both(cross, 4) + both(cross, 5) + [(turn_cross, 2), (turn_cross, 3)]
+        tensor += both(cross, 6) + both(cross, 7) + [(turn_cross, m) for m in range(4, 7)] + both(turn_last)
 
         vector += [(lift_rows, "y", 0, 1, "V"), (encode_rows, "y", 0, 0), (lift_rows, "y", 0, 3, "V"), (encode_rows, "y", 0, 1)]
         vector += [(add_bias, "y", c, i) for i in range(2) for c in range(2)]
         vector += row_pair(lift_rows, "y", 1, 0, "V") + [(encode_rows, "y", 1, 0), (weigh_snap, "y", 0), (encode_rows, "y", 1, 1)]
         vector += both(add_bias, "y", 2) + [(weigh_snap, "y", 1)]
-        vector += both(add_bias, "y", 3) + [(encode_f, "y", 0, 0), (encode_rows, "x", 0, 0), (weigh_snap, "y", 2)]
-        vector += [(encode_rows, "x", 0, 1)] + tiles(weigh_obs, "y", 0) + [(weigh_snap, "y", 3), (encode_rows, "x", 1, 0), (encode_f, "y", 0, 1)]
-        vector += both(add_bias, "x", 0) + tiles(weigh_obs, "y", 1) + [(encode_rows, "x", 1, 1), (encode_f, "y", 1, 0)]
-        vector += tiles(weigh_obs, "y", 2) + [(weigh_snap, "x", 0)] + tiles(weigh_obs, "y", 3)
-        vector += [(weigh_obs, "x", 0), (encode_f, "y", 1, 1), (weigh_obs, "x", 1)]
+        vector += both(add_bias, "y", 3) + [(encode_rows, "x", 0, 0), (encode_f, "y", 0, 0), (weigh_snap, "y", 2)]
+        vector += [(encode_rows, "x", 0, 1)] + tiles(weigh_obs, "y", 0) + [(weigh_snap, "y", 3)]
+        vector += both(add_bias, "x", 0) + [(encode_rows, "x", 1, 0)] + tiles(weigh_obs, "y", 1) + [(encode_f, "y", 0, 1)]
+        vector += both(add_bias, "x", 1) + [(encode_f, "y", 1, 0), (encode_rows, "x", 1, 1)] + tiles(weigh_obs, "y", 2)
+        vector += both(add_bias, "x", 2) + tiles(weigh_obs, "y", 3) + [(weigh_snap, "x", 0), (encode_f, "y", 1, 1)]
+        vector += tiles(weigh_obs, "x", 0) + [(weigh_obs, "x", 2), (encode_f, "x", 0), (weigh_obs, "x", 3)]
+        vector += [(weigh_snap, "x", 1)] + both(add_bias, "x", 3) + [(encode_f, "x", 1)] + tiles(weigh_obs, "x", 2)
+        vector += [(weigh_snap, "x", 2), (round_cross, 1), (encode_f, "x", 2)] + tiles(weigh_obs, "x", 3)
+        vector += [(weigh_snap, "x", 3), (round_cross, 2), (encode_f, "x", 3), (round_cross, 3), (store_plane, 0, 2)]
+        vector += [(round_cross, 4), (round_cross, 5), (store_cross, 6, 1, "V"), (store_plane, 2, 2), (round_cross, 6)]
+        vector += [(round_bank, 7, 1, "V"), (store_cross, 7, 1, "V"), (store_plane, 4, 2), (lift_last, 0, "V"), (store_plane, 6, 1)]
+        vector += [(store_last, 0), (store_last, 1)]
 
         scalar += [(lift_rows, "y", 0, 0, "S"), (lift_bias_row,), (lift_rows, "y", 0, 2, "S")]
-        scalar += [(tanh_snap, "y", 0), (tanh_snap, "y", 1)] + row_pair(lift_rows, "y", 1, 1, "S")
+        scalar += [(tanh_snap, "y", 0), (tanh_snap, "y", 1), (widen_bias,)] + row_pair(lift_rows, "y", 1, 1, "S")
         scalar += [(lift_bias_column,)] + row_pair(lift_rows, "x", 0, 0, "S") + [(tanh_snap, "y", 2)]
         scalar += tiles(tanh_obs, "y", 0) + row_pair(lift_rows, "x", 0, 1, "S") + [(tanh_snap, "y", 3)]
         scalar += tiles(tanh_obs, "y", 1) + row_pair(lift_rows, "x", 1, 0, "S")
-        scalar += tiles(tanh_obs, "y", 2) + row_pair(lift_rows, "x", 1, 1, "S") + [(tanh_snap, "x", 0)]
-        scalar += tiles(tanh_obs, "y", 3) + tiles(tanh_obs, "x", 0)
+        scalar += tiles(tanh_obs, "y", 2) + [(tanh_snap, "x", 0)] + row_pair(lift_rows, "x", 1, 1, "S")
+        scalar += tiles(tanh_obs, "y", 3) + [(tanh_snap, "x", 1)]
+        scalar += tiles(tanh_obs, "x", 0) + tiles(tanh_obs, "x", 1) + [(tanh_snap, "x", 2)]
+        scalar += tiles(tanh_obs, "x", 2) + [(round_bank, 0, 0, "S"), (store_cross, 0, 0, "S"), (round_bank, 0, 1, "S"), (store_cross, 0, 1, "S")] + outs(1, "SS")
+        scalar += tiles(tanh_obs, "x", 3) + [(tanh_snap, "x", 3)] + outs(2, "SS") + outs(3, "SS") + [(lift_plane, 0, "S"), (lift_plane, 1, "S")]
+        scalar += outs(4, "SS") + outs(5, "SS") + [(lift_plane, 2, "S"), (lift_plane, 3, "S"), (store_cross, 6, 0, "S")]
+        scalar += [(round_bank, 7, 0, "S"), (store_cross, 7, 0, "S")] + [(lift_plane, m, "S") for m in range(4, 7)] + [(lift_last, 1, "S")]
 
-        tensor += tiles(dot_obs, "x", 1) + both(dot_snap, "x", 1) + both(dot_snap, "x", 2) + both(cross, 0) + tiles(turn_obs, "x", 1)
-        vector += [(encode_f, "x", 0)] + both(add_bias, "x", 1) + both(add_bias, "x", 2)
-        vector += tiles(weigh_obs, "x", 1) + [(weigh_snap, "x", 1), (round_cross, 0)]
-        scalar += tiles(tanh_obs, "x", 1) + [(tanh_snap, "x", 1), (store_cross, 0, 0, "S"), (store_cross, 0, 1, "S"), (tanh_snap, "x", 2)]
-
-        tensor += tiles(dot_obs, "x", 2) + both(cross, 1) + both(dot_snap, "x", 3) + both(cross, 2) + tiles(turn_obs, "x", 2)
-        tensor += [(turn_cross, 0), (turn_cross, 1)]
-        vector += [(encode_f, "x", 1), (weigh_snap, "x", 2)] + both(add_bias, "x", 3) + [(round_cross, 1)]
-        vector += tiles(weigh_obs, "x", 2) + [(round_cross, 2), (encode_f, "x", 2)]
-        scalar += tiles(tanh_obs, "x", 2) + [(store_cross, m, h, "S") for m in (1, 2) for h in range(2)] + [(tanh_snap, "x", 3)]
-
-        tensor += tiles(dot_obs, "x", 3) + both(cross, 3) + both(cross, 4) + tiles(turn_obs, "x", 3)
-        tensor += [(turn_cross, 2), (turn_cross, 3)]
-        vector += [(weigh_snap, "x", 3), (store_plane, 0, 2), (store_cross, 3, 1, "V"), (round_cross, 3)]
-        vector += tiles(weigh_obs, "x", 3) + [(round_cross, 4), (encode_f, "x", 3)]
-        scalar += [(lift_plane, 0, "S"), (lift_plane, 1, "S")] + tiles(tanh_obs, "x", 3)
-        scalar += [(store_cross, 3, 0, "S"), (store_cross, 4, 0, "S"), (store_cross, 4, 1, "S")]
-
-        tensor += both(cross, 5) + [(turn_cross, 4)] + both(cross, 6) + both(cross, 7)
-        tensor += [(turn_cross, m) for m in range(5, 8)]
-        vector += [(store_cross, 5, 1, "V"), (store_plane, 2, 2), (round_cross, 5), (store_cross, 6, 1, "V"), (round_cross, 6)]
-        vector += [(store_cross, 7, 1, "V"), (round_cross, 7), (store_plane, 4, 2), (store_plane, 6, 1), (store_plane, 7, 1)]
-        scalar += [(lift_plane, 2, "S"), (lift_plane, 3, "S"), (store_cross, 5, 0, "S"), (lift_plane, 4, "S")]
-        scalar += [(store_cross, 6, 0, "S"), (store_cross, 7, 0, "S")] + [(lift_plane, m, "S") for m in range(5, 8)]
+        sync += [(send_cross, m, h) for m in range(5) for h in range(2)] + [(send_plane, 0, 2)] + both(send_cross, 5)
+        sync += both(send_cross, 6) + [(send_plane, 2, 2), (store_scales, 0, 4)]
+        sync += both(send_cross, 7) + [(send_plane, 4, 3), (send_last,), (store_scales, 4, 8)]
 
 
         def inputs(step, args):
@@ -464,10 +493,30 @@ def tile_extendeddmdkoopmancrossmoment_x2_kernel(
             if step is cross:
                 return [(encode_f, "x", args[0] // 2)] + [(encode_f, "y", g, args[1]) for g in range(2)]
             if step is store_cross:
+                return [(round_bank if args[0] in FROM_BANK else cross,) + args[:2]]
+            if step is send_cross:
+                return [(store_cross,) + args]
+            if step is send_plane:
+                return [(store_plane, 6, 1) if args[1] == 3 else (store_plane,) + args]
+            if step is send_last:
+                return [(store_last, 1)]
+            if step is store_scales:
+                return [(store_last, 1) if args[1] == 8 else (store_plane, args[1] - 2, 2)]
+            if step is turn_bias:
+                return [(widen_bias,)]
+            if step is round_bank:
                 return [(cross,) + args[:2]]
+            if step is turn_last:
+                return [(round_bank, LAST, args[0])]
+            if step is lift_last:
+                return [(turn_last, args[0])]
+            if step is store_last:
+                return [(lift_last, args[0])]
             if step is round_cross:
                 return [(store_cross, args[0], h) for h in range(2)]
             if step is turn_cross:
+                if args[0] in FROM_BANK:
+                    return [(round_bank, args[0], h) for h in range(2)]
                 return [(round_cross,) + args]
             if step is lift_plane:
                 return [(turn_cross, args[0])]
@@ -477,9 +526,9 @@ def tile_extendeddmdkoopmancrossmoment_x2_kernel(
 
         written = set()
         unread_banks = []
-        while tensor or vector or scalar:
+        while tensor or vector or scalar or sync:
             progress = False
-            for queue in (vector, scalar, tensor):
+            for queue in (vector, scalar, sync, tensor):
                 while queue:
                     step, args = queue[0][0], queue[0][1:]
                     wanted = inputs(step, args)
@@ -492,9 +541,11 @@ def tile_extendeddmdkoopmancrossmoment_x2_kernel(
                     step(*args)
                     key = args[:-1] if args and args[-1] in ("S", "V") else args
                     written.add((step,) + key)
-                    if queue is not tensor:
+                    if queue is not tensor and step is not round_bank:
                         for name in wanted:
                             written.add(("read",) + name)
+                    if step is store_cross:
+                        written.add(("read", cross) + key)
                     queue.remove(queue[0])
                     progress = True
                     if queue is tensor:

@@ -18,10 +18,10 @@ ACT = mybir.ActivationFunctionType
 ALU = mybir.AluOpType
 
 BANKS = 8
-LAST = 7
-FROM_BANK = [0, LAST]
+SORTED = [("y", 1, 0), ("y", 1, 1), ("y", 1, 2), ("y", 1, 3)]
+FROM_BANK = [(0, 0), (3, 1)]
 
-OBS_HALF = {"y": 1, "x": 1}
+SNAP = [("y", 0, 0), ("y", 0, 1), ("y", 0, 2), ("y", 0, 3), ("x", 0, 0), ("x", 0, 1), ("x", 0, 3)]
 
 
 def tile_extendeddmdkoopmancrossmoment_x2_kernel(
@@ -86,8 +86,8 @@ def tile_extendeddmdkoopmancrossmoment_x2_kernel(
         load_w(0)
         load_weights("y", q)
         load_rows("y", y, 1, 0, 2)
-        load_w(1)
         load_rows("y", y, 1, 2, 2)
+        load_w(1)
         nc.sync.dma_start(out=b_tiles[:], in_=b.rearrange("(m n) -> m n", n=P))
         load_weights("x", p)
         for g in range(2):
@@ -118,38 +118,39 @@ def tile_extendeddmdkoopmancrossmoment_x2_kernel(
         row_scale = {}
         for op in ("y", "x"):
             for g in range(2):
-                dims = [P, 2, 4, P] if g == OBS_HALF[op] else [P, 4, 2, P]
+                dims = [P, 2, 4, P]
                 row_code[op, g] = keep.tile(dims, U32, name=f"row_code_{op}{g}", align_bytes=64)
                 row_scale[op, g] = keep.tile(dims, U8, name=f"row_scale_{op}{g}", align_bytes=64)
+
+        def deal_rows(op, g, j, engine):
+            dealt = work_tile("dealt", (op, g, j), [P, 2, 2, P], F32, 4)
+            copy(engine, dealt[:], row_words[op, g, j].rearrange("p (c a e) -> p c e a", c=2, e=2))
 
         def turn_rows(op, g, j):
             bank = new_bank("rows", op, g, j)
             words = row_words[op, g, j]
             for c in range(2):
                 for e in range(2):
-                    nc.tensor.transpose(bank[:, 2 * c + e, :], words[:, 256 * c + e : 256 * (c + 1) : 2], ident[:])
+                    if (op, g, j) in SORTED:
+                        columns = made["dealt", (op, g, j)][:, c, e, :]
+                    else:
+                        columns = words[:, 256 * c + e : 256 * (c + 1) : 2]
+                    nc.tensor.transpose(bank[:, 2 * c + e, :], columns, ident[:])
 
         def lift_rows(op, g, j, engine):
             bank = made["bank", ("rows", op, g, j)]
             pair = work_tile("pair", (op, g, j // 2), [P, 2, 2, P, 2], F32, 3)
-            out = pair[:, :, j % 2] if g == OBS_HALF[op] else pair[:, j % 2]
+            out = pair[:, :, j % 2]
             copy(engine, out, bank[:].rearrange("p (c e) r -> p c r e", e=2))
 
         def encode_rows(op, g, i):
             j = 2 * i
             pair = made["pair", (op, g, i)]
-            if g == OBS_HALF[op]:
-                for c in range(2):
-                    quantize(
-                        row_code[op, g][:, c, j : j + 2].rearrange("p j r -> p (j r)"),
-                        row_scale[op, g][:, c, j : j + 2].rearrange("p j r -> p (j r)"),
-                        pair[:, c].rearrange("p j r e -> p (j r e)").bitcast(BF16),
-                    )
-            else:
+            for c in range(2):
                 quantize(
-                    row_code[op, g][:, j : j + 2].rearrange("p j c r -> p (j c r)"),
-                    row_scale[op, g][:, j : j + 2].rearrange("p j c r -> p (j c r)"),
-                    pair[:].rearrange("p j c r e -> p (j c r e)").bitcast(BF16),
+                    row_code[op, g][:, c, j : j + 2].rearrange("p j r -> p (j r)"),
+                    row_scale[op, g][:, c, j : j + 2].rearrange("p j r -> p (j r)"),
+                    pair[:, c].rearrange("p j r e -> p (j r e)").bitcast(BF16),
                 )
 
 
@@ -212,25 +213,24 @@ def tile_extendeddmdkoopmancrossmoment_x2_kernel(
                     values,
                 )
 
-        def dot_snap(op, c, i):
-            g = 1 - OBS_HALF[op]
-            bank = new_bank("snap", op, c, i)
+        def dot_snap(op, g, c, i):
+            bank = new_bank("snap", op, g, c, i)
             sums = bank[:].rearrange("p (k a) r -> p k (a r)", k=2)
             for k in range(2):
                 for n in range(2):
                     nc.tensor.matmul_mx(
                         out=sums[:, k, :],
-                        lhsT=row_code[op, g][:, 2 * i + k, n, :].bitcast(FP8X4),
-                        lhsT_scale=row_scale[op, g][:, 2 * i + k, n, :],
+                        lhsT=row_code[op, g][:, n, 2 * i + k, :].bitcast(FP8X4),
+                        lhsT_scale=row_scale[op, g][:, n, 2 * i + k, :],
                         rhs=w_code[:, n, 256 * c : 256 * c + 256].bitcast(FP8X4),
                         rhs_scale=w_scale[4 * n : P, 256 * c : 256 * c + 256],
                         start=(n == 0),
                         stop=(n == 1),
                     )
 
-        def add_bias(op, c, i):
-            sums = made["bank", ("snap", op, c, i)][:].rearrange("p (k a) r -> p k (a r)", k=2)
-            z = work_tile("z", (op, c), [P, 2, 256, 2], F32, 4)
+        def add_bias(op, g, c, i):
+            sums = made["bank", ("snap", op, g, c, i)][:].rearrange("p (k a) r -> p k (a r)", k=2)
+            z = work_tile("z", (op, g, c), [P, 2, 256, 2], F32, 4)
             nc.vector.tensor_tensor(
                 out=z[:, i],
                 in0=sums.rearrange("p k o -> p o k"),
@@ -238,14 +238,13 @@ def tile_extendeddmdkoopmancrossmoment_x2_kernel(
                 op=ALU.add,
             )
 
-        def tanh_snap(op, c):
-            z = made["z", (op, c)]
-            th = work_tile("th", (op, c), [P, 256, 2, 2], F32, 4)
+        def tanh_snap(op, g, c):
+            z = made["z", (op, g, c)]
+            th = work_tile("th", (op, g, c), [P, 256, 2, 2], F32, 3)
             nc.scalar.activation(out=th[:], in_=z[:].rearrange("p i o k -> p o i k"), func=ACT.Tanh)
 
-        def weigh_snap(op, c):
-            th = made["th", (op, c)]
-            g = 1 - OBS_HALF[op]
+        def weigh_snap(op, g, c, engine):
+            th = made["th", (op, g, c)]
             nc.vector.tensor_tensor(
                 out=f_part(op, g, 256 * c, 256),
                 in0=th[:].rearrange("p o i k -> p o (i k)"),
@@ -253,9 +252,8 @@ def tile_extendeddmdkoopmancrossmoment_x2_kernel(
                 op=ALU.mult,
             )
 
-        def dot_obs(op, m):
-            g = OBS_HALF[op]
-            bank = new_bank("obs", op, m)
+        def dot_obs(op, g, m):
+            bank = new_bank("obs", op, g, m)
             sums = bank[:].rearrange("p j r -> p (j r)")
             for n in range(2):
                 nc.tensor.matmul_mx(
@@ -268,22 +266,21 @@ def tile_extendeddmdkoopmancrossmoment_x2_kernel(
                     stop=(n == 1),
                 )
 
-        def tanh_obs(op, m):
-            sums = made["bank", ("obs", op, m)][:].rearrange("p j r -> p (j r)")
-            t = work_tile("t", (op, m), [P, 4, P], F32, 6)
+        def tanh_obs(op, g, m):
+            sums = made["bank", ("obs", op, g, m)][:].rearrange("p j r -> p (j r)")
+            t = work_tile("t", (op, g, m), [P, 4, P], F32, 10)
             nc.scalar.activation(
                 out=t[:].rearrange("p j r -> p (j r)"), in_=sums, func=ACT.Tanh, bias=bias_column[:, m : m + 1]
             )
 
-        def turn_obs(op, m):
-            t = made["t", (op, m)]
-            bank = new_bank("turned", op, m)
+        def turn_obs(op, g, m):
+            t = made["t", (op, g, m)]
+            bank = new_bank("turned", op, g, m)
             for j in range(4):
                 nc.tensor.transpose(bank[:, j, :], t[:, j, :], ident[:])
 
-        def weigh_obs(op, m):
-            bank = made["bank", ("turned", op, m)]
-            g = OBS_HALF[op]
+        def weigh_obs(op, g, m):
+            bank = made["bank", ("turned", op, g, m)]
             nc.vector.tensor_tensor(
                 out=f_part(op, g, P * m, P),
                 in0=bank[:].rearrange("p j o -> p o j"),
@@ -293,7 +290,7 @@ def tile_extendeddmdkoopmancrossmoment_x2_kernel(
 
 
         plane_code = keep.tile([P, 2, SIZE], U32, name="plane_code", align_bytes=64)
-        plane_scale = keep.tile([P, 2, SIZE], U8, name="plane_scale", align_bytes=64)
+        plane_scale = keep.tile([P, SIZE], U8, name="plane_scale", align_bytes=64)
         plane_words = out_1.rearrange("g p m t -> p g (m t)")
 
         def divide(engine, out, in_):
@@ -302,97 +299,74 @@ def tile_extendeddmdkoopmancrossmoment_x2_kernel(
             else:
                 nc.vector.tensor_scalar(out=out, in0=in_, scalar1=INV_DIV, scalar2=None, op0=ALU.mult)
 
-        def cross(m, h):
-            c, first = m // 2, P * (m % 2)
-            bank = new_bank("cross", m, h)
-            sums = bank[:].rearrange("p t a -> p (t a)")
+        def cross(c, h, k):
+            bank = new_bank("cross", c, h, k)
             for g in range(2):
                 nc.tensor.matmul_mx(
-                    out=sums,
-                    lhsT=fx_code[c][:, g, first : first + P].bitcast(FP8X4),
-                    lhsT_scale=fx_scale[c][:, g, first : first + P],
+                    out=bank[:].rearrange("p t a -> p (t a)"),
+                    lhsT=fx_code[c][:, g, P * k : P * k + P].bitcast(FP8X4),
+                    lhsT_scale=fx_scale[c][:, g, P * k : P * k + P],
                     rhs=fy_code[g, h][:].bitcast(FP8X4),
                     rhs_scale=fy_scale[g, h][:],
                     start=(g == 0),
                     stop=(g == 1),
                 )
 
-        def store_cross(m, h, engine):
-            sums = made["bank", ("cross", m, h)][:].rearrange("p t a -> p (t a)")
-            r = work_tile("r", m, [P, 2, 512], F32, 5)
-            divide(engine, r[:, h, :], sums)
+        def lift_cross(c, h, k, engine):
+            r = work_tile("r", (c, h), [P, 2, 512], F32, 6)
+            divide(engine, r[:, k, :], made["bank", ("cross", c, h, k)][:].rearrange("p t a -> p (t a)"))
 
-        def send_cross(m, h):
-            nc.sync.dma_start(out=out_0[P * m : P * m + P, 512 * h : 512 * h + 512], in_=made["r", m][:, h, :])
+        def send_cross(c, h, k):
+            rows = slice(256 * c + P * k, 256 * c + P * k + P)
+            nc.sync.dma_start(out=out_0[rows, 512 * h : 512 * h + 512], in_=made["r", (c, h)][:, k, :])
 
-        def round_cross(m):
-            r = made["r", m]
-            s = work_tile("s", m, [P, 2, 2, P, 2], BF16, 5)
-            nc.vector.tensor_copy(out=s[:], in_=r[:].rearrange("p h (a e s) -> p h e a s", e=2, s=2))
+        def round_cross(c, h):
+            s = work_tile("s", (c, h), [P, 2, 2, P, 2], BF16, 4)
+            nc.vector.tensor_copy(out=s[:], in_=made["r", (c, h)][:].rearrange("p k (a e s) -> p k e a s", e=2, s=2))
 
-        def round_bank(m, h, engine):
-            sums = made["bank", ("cross", m, h)][:].rearrange("p t a -> p (t a)")
-            s = work_tile("s", m, [P, 2, 2, P, 2], BF16, 5)
-            divide(engine, s[:, h], sums.rearrange("p (a e s) -> p e a s", e=2, s=2))
+        def round_bank(c, h, k, engine):
+            sums = made["bank", ("cross", c, h, k)][:].rearrange("p t a -> p (t a)")
+            s = work_tile("s", (c, h), [P, 2, 2, P, 2], BF16, 4)
+            divide(engine, s[:, k], sums.rearrange("p (a e s) -> p e a s", e=2, s=2))
 
-        def turn_cross(m):
-            s = made["s", m]
-            words = s[:].rearrange("p h e a s -> p (h e) (a s)").bitcast(F32)
-            bank = new_bank("plane", m)
+        def turn_cross(c, h):
+            words = made["s", (c, h)][:].rearrange("p k e a s -> p (k e) (a s)").bitcast(F32)
+            bank = new_bank("plane", c, h)
             for n in range(4):
                 nc.tensor.transpose(bank[:, n, :], words[:, n, :], ident[:])
 
-        def turn_last(h):
-            words = made["s", LAST][:, h].rearrange("p e a s -> p e (a s)").bitcast(F32)
-            bank = new_bank("last", h)
-            for e in range(2):
-                nc.tensor.transpose(bank[:, e, :], words[:, e, :], ident[:])
+        def lift_plane(c, h, engine):
+            u = work_tile("u", (c, h), [P, 2, P, 2], F32, 4)
+            copy(engine, u[:], made["bank", ("plane", c, h)][:].rearrange("p (k e) i -> p k i e", e=2))
 
-        def lift_last(h, engine):
-            u = work_tile("u", LAST // 2, [P, 2, 256, 2], F32, 2)
-            copy(engine, u[:, h, P:, :], made["bank", ("last", h)][:, 0:2, :].rearrange("p e i -> p i e"))
+        def encode_plane(c, h):
+            cols = slice(256 * c, 256 * c + 256)
+            values = made["u", (c, h)][:].rearrange("p k i e -> p (k i e)").bitcast(BF16)
+            quantize(plane_code[:, h, cols], plane_scale[4 * h : P, cols], values)
 
-        def store_last(h):
-            cols = slice(P * LAST, SIZE)
-            quantize(
-                plane_code[:, h, cols],
-                plane_scale[:, h, cols],
-                made["u", LAST // 2][:, h, P:].rearrange("p i e -> p (i e)").bitcast(BF16),
-            )
-
-        def send_last():
-            send_plane(LAST, 1)
-
-        def lift_plane(m, engine):
-            bank = made["bank", ("plane", m)]
-            c, first = m // 2, P * (m % 2)
-            u = work_tile("u", c, [P, 2, 256, 2], F32, 2)
-            copy(engine, u[:, :, first : first + P, :], bank[:].rearrange("p (h e) i -> p h i e", e=2))
-
-        def store_plane(m, n):
-            u = made["u", m // 2]
-            first = P * (m % 2)
-            cols = slice(P * m, P * (m + n))
-            for h in range(2):
-                quantize(
-                    plane_code[:, h, cols],
-                    plane_scale[:, h, cols],
-                    u[:, h, first : first + P * n].rearrange("p i e -> p (i e)").bitcast(BF16),
-                )
-
-        def send_plane(m, n):
+        def send_plane(first, end):
             nc.sync.dma_start(
-                out=plane_words[:, :, 4 * P * m : 4 * P * (m + n)].bitcast(I32),
-                in_=plane_code[:, :, P * m : P * (m + n)].bitcast(I32),
+                out=plane_words[:, :, 1024 * first : 1024 * end].bitcast(I32),
+                in_=plane_code[:, :, 256 * first : 256 * end].bitcast(I32),
             )
 
-        def store_scales(m, end):
-            cols = slice(P * m, P * end)
+        def send_half_plane(c, h):
+            nc.sync.dma_start(
+                out=plane_words[:, h, 1024 * c : 1024 * c + 1024].bitcast(I32),
+                in_=plane_code[:, h, 256 * c : 256 * c + 256].bitcast(I32),
+            )
+
+        def send_unit(c, h):
+            rows = out_0[256 * c : 256 * c + 256, 512 * h : 512 * h + 512]
+            nc.sync.dma_start(out=rows.rearrange("(k p) n -> p k n", k=2), in_=made["r", (c, h)][:])
+
+        def store_scales(first, end):
+            cols = slice(256 * first, 256 * end)
             for quad in range(4):
-                queue = nc.scalar if end == 8 and quad % 2 == 1 else nc.sync
+                queue = nc.scalar if end == 4 and quad % 2 == 1 else nc.sync
                 queue.dma_start(
-                    out=out_2[:, 4 * quad : 4 * quad + 4, cols].rearrange("h r m -> r h m").bitcast(I32),
-                    in_=plane_scale[32 * quad : 32 * quad + 4, :, cols].bitcast(I32),
+                    out=out_2[:, 4 * quad : 4 * quad + 4, cols].bitcast(I32),
+                    in_=plane_scale[32 * quad : 32 * quad + 8, cols].bitcast(I32),
                 )
 
 
@@ -401,65 +375,55 @@ def tile_extendeddmdkoopmancrossmoment_x2_kernel(
         def both(step, *args):
             return [(step,) + args + (k,) for k in range(2)]
 
-        def tiles(step, op, c):
-            return [(step, op, 2 * c), (step, op, 2 * c + 1)]
+        def tiles(step, op, g, c):
+            return [(step, op, g, 2 * c), (step, op, g, 2 * c + 1)]
 
         def row_pair(step, op, g, i, *engine):
             return [(step, op, g, 2 * i) + engine, (step, op, g, 2 * i + 1) + engine]
 
-        def outs(m, engines):
-            return [(store_cross, m, h, engines[h]) for h in range(2)]
-
         tensor += row_pair(turn_rows, "y", 0, 0) + [(spread_bias,)] + row_pair(turn_rows, "y", 0, 1)
-        tensor += [(dot_snap, "y", c, i) for i in range(2) for c in range(2)]
-        tensor += row_pair(turn_rows, "y", 1, 0) + row_pair(turn_rows, "y", 1, 1)
-        tensor += both(dot_snap, "y", 2) + [(turn_bias,)] + row_pair(turn_rows, "x", 0, 0)
-        tensor += both(dot_snap, "y", 3) + tiles(dot_obs, "y", 0) + row_pair(turn_rows, "x", 0, 1) + tiles(turn_obs, "y", 0)
-        tensor += tiles(dot_obs, "y", 1) + both(dot_snap, "x", 0) + row_pair(turn_rows, "x", 1, 0) + tiles(turn_obs, "y", 1)
-        tensor += tiles(dot_obs, "y", 2) + both(dot_snap, "x", 1) + row_pair(turn_rows, "x", 1, 1) + tiles(turn_obs, "y", 2)
-        tensor += tiles(dot_obs, "y", 3) + both(dot_snap, "x", 2) + tiles(turn_obs, "y", 3)
-        tensor += tiles(dot_obs, "x", 0) + tiles(dot_obs, "x", 1) + tiles(turn_obs, "x", 0) + tiles(turn_obs, "x", 1)
-        tensor += tiles(dot_obs, "x", 2) + both(dot_snap, "x", 3) + both(cross, 0) + both(cross, 1) + tiles(turn_obs, "x", 2)
-        tensor += tiles(dot_obs, "x", 3) + both(cross, 2) + both(cross, 3) + tiles(turn_obs, "x", 3) + [(turn_cross, 0), (turn_cross, 1)]
-        tensor += both(cross, 4) + both(cross, 5) + [(turn_cross, 2), (turn_cross, 3)]
-        tensor += both(cross, 6) + both(cross, 7) + [(turn_cross, m) for m in range(4, 7)] + both(turn_last)
+        tensor += [(dot_snap, "y", 0, 0, 0)] + [(dot_snap, "y", 0, 1, 0)] + [(dot_snap, "y", 0, 0, 1)] + [(dot_snap, "y", 0, 1, 1)] + row_pair(turn_rows, "y", 1, 0) + row_pair(turn_rows, "y", 1, 1)
+        tensor += both(dot_snap, "y", 0, 2) + [(turn_bias,)] + row_pair(turn_rows, "x", 0, 0)
+        tensor += both(dot_snap, "y", 0, 3) + tiles(dot_obs, "y", 1, 0) + row_pair(turn_rows, "x", 0, 1) + tiles(turn_obs, "y", 1, 0)
+        tensor += tiles(dot_obs, "y", 1, 1) + both(dot_snap, "x", 0, 0) + row_pair(turn_rows, "x", 1, 0) + tiles(turn_obs, "y", 1, 1)
+        tensor += tiles(dot_obs, "y", 1, 2) + both(dot_snap, "x", 0, 1) + row_pair(turn_rows, "x", 1, 1) + tiles(turn_obs, "y", 1, 2)
+        tensor += tiles(dot_obs, "y", 1, 3) + tiles(dot_obs, "x", 0, 2) + tiles(turn_obs, "y", 1, 3)
+        tensor += tiles(dot_obs, "x", 1, 0) + tiles(dot_obs, "x", 1, 1) + tiles(turn_obs, "x", 1, 0) + tiles(turn_obs, "x", 1, 1)
+        tensor += tiles(dot_obs, "x", 1, 2) + both(dot_snap, "x", 0, 3) + both(cross, 0, 0) + both(cross, 0, 1) + tiles(turn_obs, "x", 1, 2) + tiles(turn_obs, "x", 0, 2)
+        tensor += tiles(dot_obs, "x", 1, 3) + both(cross, 1, 0) + both(cross, 1, 1) + tiles(turn_obs, "x", 1, 3) + [(turn_cross, 0, 0)] + [(turn_cross, 0, 1)]
+        tensor += both(cross, 2, 0) + both(cross, 2, 1) + [(turn_cross, 1, 0)] + [(turn_cross, 1, 1)]
+        tensor += both(cross, 3, 0) + both(cross, 3, 1) + [(turn_cross, 2, 0)] + [(turn_cross, 2, 1)] + [(turn_cross, 3, 0)] + [(turn_cross, 3, 1)]
 
-        vector += [(lift_rows, "y", 0, 1, "V"), (encode_rows, "y", 0, 0), (lift_rows, "y", 0, 3, "V"), (encode_rows, "y", 0, 1)]
-        vector += [(add_bias, "y", c, i) for i in range(2) for c in range(2)]
-        vector += row_pair(lift_rows, "y", 1, 0, "V") + [(encode_rows, "y", 1, 0), (weigh_snap, "y", 0), (encode_rows, "y", 1, 1)]
-        vector += both(add_bias, "y", 2) + [(weigh_snap, "y", 1)]
-        vector += both(add_bias, "y", 3) + [(encode_rows, "x", 0, 0), (encode_f, "y", 0, 0), (weigh_snap, "y", 2)]
-        vector += [(encode_rows, "x", 0, 1)] + tiles(weigh_obs, "y", 0) + [(weigh_snap, "y", 3)]
-        vector += both(add_bias, "x", 0) + [(encode_rows, "x", 1, 0)] + tiles(weigh_obs, "y", 1) + [(encode_f, "y", 0, 1)]
-        vector += both(add_bias, "x", 1) + [(encode_f, "y", 1, 0), (encode_rows, "x", 1, 1)] + tiles(weigh_obs, "y", 2)
-        vector += both(add_bias, "x", 2) + tiles(weigh_obs, "y", 3) + [(weigh_snap, "x", 0), (encode_f, "y", 1, 1)]
-        vector += tiles(weigh_obs, "x", 0) + [(weigh_obs, "x", 2), (encode_f, "x", 0), (weigh_obs, "x", 3)]
-        vector += [(weigh_snap, "x", 1)] + both(add_bias, "x", 3) + [(encode_f, "x", 1)] + tiles(weigh_obs, "x", 2)
-        vector += [(weigh_snap, "x", 2), (round_cross, 1), (encode_f, "x", 2)] + tiles(weigh_obs, "x", 3)
-        vector += [(weigh_snap, "x", 3), (round_cross, 2), (encode_f, "x", 3), (round_cross, 3), (store_plane, 0, 2)]
-        vector += [(round_cross, 4), (round_cross, 5), (store_cross, 6, 1, "V"), (store_plane, 2, 2), (round_cross, 6)]
-        vector += [(round_bank, 7, 1, "V"), (store_cross, 7, 1, "V"), (store_plane, 4, 2), (lift_last, 0, "V"), (store_plane, 6, 1)]
-        vector += [(store_last, 0), (store_last, 1)]
+        vector += [(lift_rows, "y", 0, 1, "V"), (encode_rows, "y", 0, 0), (lift_rows, "y", 0, 3, "V"), (encode_rows, "y", 0, 1), (add_bias, "y", 0, 0, 0), (add_bias, "y", 0, 1, 0), (add_bias, "y", 0, 0, 1), (add_bias, "y", 0, 1, 1), (lift_rows, "y", 1, 1, "V"), (encode_rows, "y", 1, 0)]
+        vector += [(add_bias, "y", 0, 2, 0), (encode_rows, "y", 1, 1), (weigh_snap, "y", 0, 0, "V"), (add_bias, "y", 0, 2, 1)]
+        vector += [(add_bias, "y", 0, 3, 0), (add_bias, "y", 0, 3, 1), (encode_rows, "x", 0, 0), (weigh_snap, "y", 0, 1, "V"), (encode_rows, "x", 0, 1), (weigh_obs, "y", 1, 0), (weigh_obs, "y", 1, 1)]
+        vector += [(add_bias, "x", 0, 0, 0), (add_bias, "x", 0, 0, 1), (weigh_snap, "y", 0, 2, "V"), (weigh_obs, "y", 1, 2), (weigh_obs, "y", 1, 3), (weigh_snap, "y", 0, 3, "V"), (encode_rows, "x", 1, 0)]
+        vector += [(add_bias, "x", 0, 1, 0), (add_bias, "x", 0, 1, 1), (encode_f, "y", 0, 0), (weigh_obs, "y", 1, 4), (weigh_obs, "y", 1, 5), (encode_rows, "x", 1, 1), (encode_f, "y", 0, 1)]
+        vector += [(encode_f, "y", 1, 0), (weigh_obs, "y", 1, 6), (weigh_obs, "y", 1, 7), (weigh_snap, "x", 0, 0, "V")]
+        vector += [(weigh_obs, "x", 1, 0), (weigh_obs, "x", 1, 1), (encode_f, "y", 1, 1), (encode_f, "x", 0), (weigh_obs, "x", 1, 2), (weigh_obs, "x", 1, 3)]
+        vector += [(weigh_snap, "x", 0, 1, "V"), (add_bias, "x", 0, 3, 0), (encode_f, "x", 1), (add_bias, "x", 0, 3, 1), (weigh_obs, "x", 1, 4), (weigh_obs, "x", 1, 5), (weigh_obs, "x", 0, 4), (weigh_obs, "x", 0, 5)]
+        vector += [(weigh_snap, "x", 0, 3, "V"), (round_cross, 0, 1), (encode_f, "x", 2), (weigh_obs, "x", 1, 6), (weigh_obs, "x", 1, 7), (round_cross, 1, 0), (round_cross, 1, 1), (encode_f, "x", 3)]
+        vector += [(encode_plane, 0, 0), (round_cross, 2, 0), (encode_plane, 0, 1), (lift_plane, 1, 1, "V"), (encode_plane, 1, 0), (round_cross, 2, 1), (encode_plane, 1, 1)]
+        vector += [(round_cross, 3, 0), (lift_plane, 2, 0, "V"), (lift_plane, 2, 1, "V"), (encode_plane, 2, 0), (lift_plane, 3, 1, "V"), (encode_plane, 3, 0), (encode_plane, 2, 1), (encode_plane, 3, 1)]
 
-        scalar += [(lift_rows, "y", 0, 0, "S"), (lift_bias_row,), (lift_rows, "y", 0, 2, "S")]
-        scalar += [(tanh_snap, "y", 0), (tanh_snap, "y", 1), (widen_bias,)] + row_pair(lift_rows, "y", 1, 1, "S")
-        scalar += [(lift_bias_column,)] + row_pair(lift_rows, "x", 0, 0, "S") + [(tanh_snap, "y", 2)]
-        scalar += tiles(tanh_obs, "y", 0) + row_pair(lift_rows, "x", 0, 1, "S") + [(tanh_snap, "y", 3)]
-        scalar += tiles(tanh_obs, "y", 1) + row_pair(lift_rows, "x", 1, 0, "S")
-        scalar += tiles(tanh_obs, "y", 2) + [(tanh_snap, "x", 0)] + row_pair(lift_rows, "x", 1, 1, "S")
-        scalar += tiles(tanh_obs, "y", 3) + [(tanh_snap, "x", 1)]
-        scalar += tiles(tanh_obs, "x", 0) + tiles(tanh_obs, "x", 1) + [(tanh_snap, "x", 2)]
-        scalar += tiles(tanh_obs, "x", 2) + [(round_bank, 0, 0, "S"), (store_cross, 0, 0, "S"), (round_bank, 0, 1, "S"), (store_cross, 0, 1, "S")] + outs(1, "SS")
-        scalar += tiles(tanh_obs, "x", 3) + [(tanh_snap, "x", 3)] + outs(2, "SS") + outs(3, "SS") + [(lift_plane, 0, "S"), (lift_plane, 1, "S")]
-        scalar += outs(4, "SS") + outs(5, "SS") + [(lift_plane, 2, "S"), (lift_plane, 3, "S"), (store_cross, 6, 0, "S")]
-        scalar += [(round_bank, 7, 0, "S"), (store_cross, 7, 0, "S")] + [(lift_plane, m, "S") for m in range(4, 7)] + [(lift_last, 1, "S")]
+        scalar += [(lift_rows, "y", 0, 0, "S"), (lift_bias_row,), (lift_rows, "y", 0, 2, "S"), (deal_rows, "y", 1, 0, "S"), (deal_rows, "y", 1, 1, "S"), (deal_rows, "y", 1, 2, "S"), (deal_rows, "y", 1, 3, "S"), (widen_bias,), (lift_rows, "y", 1, 0, "S"), (lift_rows, "y", 1, 2, "S"), (lift_rows, "y", 1, 3, "S")]
+        scalar += [(tanh_snap, "y", 0, 0), (tanh_snap, "y", 0, 1), (lift_bias_column,), (lift_rows, "x", 0, 0, "S"), (lift_rows, "x", 0, 1, "S")]
+        scalar += [(tanh_obs, "y", 1, 0), (tanh_obs, "y", 1, 1), (lift_rows, "x", 0, 2, "S"), (lift_rows, "x", 0, 3, "S"), (tanh_snap, "y", 0, 2)]
+        scalar += [(tanh_obs, "y", 1, 2), (tanh_obs, "y", 1, 3), (tanh_snap, "y", 0, 3), (lift_rows, "x", 1, 0, "S"), (lift_rows, "x", 1, 1, "S")]
+        scalar += [(tanh_obs, "y", 1, 4), (tanh_obs, "y", 1, 5), (tanh_snap, "x", 0, 0), (lift_rows, "x", 1, 2, "S"), (lift_rows, "x", 1, 3, "S")]
+        scalar += [(tanh_obs, "y", 1, 6), (tanh_obs, "y", 1, 7), (tanh_obs, "x", 0, 4), (tanh_obs, "x", 0, 5)]
+        scalar += [(tanh_obs, "x", 1, 0), (tanh_obs, "x", 1, 1), (tanh_obs, "x", 1, 2), (tanh_obs, "x", 1, 3), (tanh_snap, "x", 0, 1)]
+        scalar += [(tanh_obs, "x", 1, 4), (tanh_obs, "x", 1, 5), (round_bank, 0, 0, 0, "S"), (lift_cross, 0, 0, 0, "S"), (round_bank, 0, 0, 1, "S"), (lift_cross, 0, 0, 1, "S"), (lift_cross, 0, 1, 0, "S"), (lift_cross, 0, 1, 1, "S"), (tanh_snap, "x", 0, 3)]
+        scalar += [(tanh_obs, "x", 1, 6), (tanh_obs, "x", 1, 7), (lift_cross, 1, 0, 0, "S"), (lift_cross, 1, 0, 1, "S"), (lift_cross, 1, 1, 0, "S"), (lift_cross, 1, 1, 1, "S"), (lift_plane, 0, 0, "S"), (lift_plane, 0, 1, "S")]
+        scalar += [(lift_cross, 2, 0, 0, "S"), (lift_cross, 2, 0, 1, "S"), (lift_cross, 2, 1, 0, "S"), (lift_cross, 2, 1, 1, "S"), (lift_plane, 1, 0, "S")]
+        scalar += [(lift_cross, 3, 0, 0, "S"), (lift_cross, 3, 0, 1, "S"), (round_bank, 3, 1, 0, "S"), (round_bank, 3, 1, 1, "S"), (lift_cross, 3, 1, 0, "S"), (lift_plane, 3, 0, "S"), (lift_cross, 3, 1, 1, "S")]
 
-        sync += [(send_cross, m, h) for m in range(5) for h in range(2)] + [(send_plane, 0, 2)] + both(send_cross, 5)
-        sync += both(send_cross, 6) + [(send_plane, 2, 2), (store_scales, 0, 4)]
-        sync += both(send_cross, 7) + [(send_plane, 4, 3), (send_last,), (store_scales, 4, 8)]
+        sync += [(send_unit, 0, 0), (send_unit, 0, 1), (send_unit, 1, 0), (send_unit, 1, 1), (send_cross, 2, 0, 0), (send_cross, 2, 0, 1), (send_cross, 2, 1, 0), (send_cross, 2, 1, 1), (send_plane, 0, 1), (send_cross, 3, 0, 0), (send_cross, 3, 0, 1), (send_plane, 1, 2), (send_cross, 3, 1, 0), (send_cross, 3, 1, 1), (send_half_plane, 3, 0), (send_plane, 2, 3), (send_half_plane, 3, 1), (store_scales, 0, 4)]
 
 
         def inputs(step, args):
+            if step is turn_rows and args in SORTED:
+                return [(deal_rows,) + args]
             if step is lift_rows:
                 return [(turn_rows,) + args[:3]]
             if step is encode_rows:
@@ -469,15 +433,15 @@ def tile_extendeddmdkoopmancrossmoment_x2_kernel(
             if step is lift_bias_column:
                 return [(turn_bias,)]
             if step is dot_snap:
-                return [(encode_rows, args[0], 1 - OBS_HALF[args[0]], args[2])]
+                return [(encode_rows, args[0], args[1], args[3])]
             if step is add_bias:
                 return [(dot_snap,) + args, (lift_bias_row,)]
             if step is tanh_snap:
                 return [(add_bias,) + args + (i,) for i in range(2)]
             if step is weigh_snap:
-                return [(tanh_snap,) + args]
+                return [(tanh_snap,) + args[:3]]
             if step is dot_obs:
-                return [(encode_rows, args[0], OBS_HALF[args[0]], i) for i in range(2)]
+                return [(encode_rows, args[0], args[1], i) for i in range(2)]
             if step is tanh_obs:
                 return [(dot_obs,) + args, (lift_bias_column,)]
             if step is turn_obs:
@@ -486,42 +450,42 @@ def tile_extendeddmdkoopmancrossmoment_x2_kernel(
                 return [(turn_obs,) + args]
             if step is encode_f:
                 if args[0] == "x":
-                    return [(weigh_snap,) + args] + [(weigh_obs, "x", 2 * args[1] + k) for k in range(2)]
-                if args[1] == OBS_HALF["y"]:
-                    return [(weigh_obs, "y", 4 * args[2] + k) for k in range(4)]
-                return [(weigh_snap, "y", 2 * args[2] + k) for k in range(2)]
+                    parts = [("x", g, args[1]) for g in range(2)]
+                else:
+                    parts = [("y", args[1], 2 * args[2] + k) for k in range(2)]
+                wanted = []
+                for op, g, c in parts:
+                    if (op, g, c) in SNAP:
+                        wanted += [(weigh_snap, op, g, c)]
+                    else:
+                        wanted += [(weigh_obs, op, g, 2 * c + k) for k in range(2)]
+                return wanted
             if step is cross:
-                return [(encode_f, "x", args[0] // 2)] + [(encode_f, "y", g, args[1]) for g in range(2)]
-            if step is store_cross:
-                return [(round_bank if args[0] in FROM_BANK else cross,) + args[:2]]
-            if step is send_cross:
-                return [(store_cross,) + args]
-            if step is send_plane:
-                return [(store_plane, 6, 1) if args[1] == 3 else (store_plane,) + args]
-            if step is send_last:
-                return [(store_last, 1)]
-            if step is store_scales:
-                return [(store_last, 1) if args[1] == 8 else (store_plane, args[1] - 2, 2)]
-            if step is turn_bias:
-                return [(widen_bias,)]
+                return [(encode_f, "x", args[0])] + [(encode_f, "y", g, args[1]) for g in range(2)]
             if step is round_bank:
-                return [(cross,) + args[:2]]
-            if step is turn_last:
-                return [(round_bank, LAST, args[0])]
-            if step is lift_last:
-                return [(turn_last, args[0])]
-            if step is store_last:
-                return [(lift_last, args[0])]
+                return [(cross,) + args[:3]]
+            if step is lift_cross:
+                return [(round_bank if args[:2] in FROM_BANK else cross,) + args[:3]]
+            if step is send_cross:
+                return [(lift_cross,) + args]
             if step is round_cross:
-                return [(store_cross, args[0], h) for h in range(2)]
+                return [(lift_cross,) + args + (k,) for k in range(2)]
             if step is turn_cross:
-                if args[0] in FROM_BANK:
-                    return [(round_bank, args[0], h) for h in range(2)]
+                if args in FROM_BANK:
+                    return [(round_bank,) + args + (k,) for k in range(2)]
                 return [(round_cross,) + args]
             if step is lift_plane:
-                return [(turn_cross, args[0])]
-            if step is store_plane:
-                return [(lift_plane, args[0] + k) for k in range(args[1])]
+                return [(turn_cross,) + args[:2]]
+            if step is encode_plane:
+                return [(lift_plane,) + args]
+            if step is send_half_plane:
+                return [(encode_plane,) + args]
+            if step is send_unit:
+                return [(lift_cross,) + args + (k,) for k in range(2)]
+            if step is send_plane or step is store_scales:
+                return [(encode_plane, c, h) for c in range(*args) for h in range(2)]
+            if step is turn_bias:
+                return [(widen_bias,)]
             return []
 
         written = set()
@@ -539,12 +503,12 @@ def tile_extendeddmdkoopmancrossmoment_x2_kernel(
                             break
                         unread_banks.append(("read", step) + args)
                     step(*args)
-                    key = args[:-1] if args and args[-1] in ("S", "V") else args
+                    key = args[:-1] if args and args[-1] in ("S", "V", "G") else args
                     written.add((step,) + key)
                     if queue is not tensor and step is not round_bank:
                         for name in wanted:
                             written.add(("read",) + name)
-                    if step is store_cross:
+                    if step is lift_cross:
                         written.add(("read", cross) + key)
                     queue.remove(queue[0])
                     progress = True

@@ -18,10 +18,13 @@ ACT = mybir.ActivationFunctionType
 ALU = mybir.AluOpType
 
 BANKS = 8
-SORTED = [("y", 1, 0), ("y", 1, 1), ("y", 1, 2), ("y", 1, 3)]
+SNAP = [("y", 0, c) for c in range(4)] + [("x", 0, c) for c in (0, 1, 3)]
+SORTED = [("y", 1, j) for j in range(4)]
 FROM_BANK = [(0, 0), (3, 1)]
-
-SNAP = [("y", 0, 0), ("y", 0, 1), ("y", 0, 2), ("y", 0, 3), ("x", 0, 0), ("x", 0, 1), ("x", 0, 3)]
+VECTOR_LIFTS_FROM = 1
+HOP = 2
+WINDOW = 12
+SHARE = 0.25
 
 
 def tile_extendeddmdkoopmancrossmoment_x2_kernel(
@@ -118,39 +121,37 @@ def tile_extendeddmdkoopmancrossmoment_x2_kernel(
         row_scale = {}
         for op in ("y", "x"):
             for g in range(2):
-                dims = [P, 2, 4, P]
-                row_code[op, g] = keep.tile(dims, U32, name=f"row_code_{op}{g}", align_bytes=64)
-                row_scale[op, g] = keep.tile(dims, U8, name=f"row_scale_{op}{g}", align_bytes=64)
+                row_code[op, g] = keep.tile([P, 2, 4, P], U32, name=f"row_code_{op}{g}", align_bytes=64)
+                row_scale[op, g] = keep.tile([P, 2, 4, P], U8, name=f"row_scale_{op}{g}", align_bytes=64)
 
-        def deal_rows(op, g, j, engine):
-            dealt = work_tile("dealt", (op, g, j), [P, 2, 2, P], F32, 4)
-            copy(engine, dealt[:], row_words[op, g, j].rearrange("p (c a e) -> p c e a", c=2, e=2))
+        def sort_rows(op, g, j):
+            words = work_tile("sorted", (op, g, j), [P, 2, 2, P], F32, len(SORTED))
+            nc.scalar.copy(out=words[:], in_=row_words[op, g, j].rearrange("p (n a e) -> p n e a", n=2, e=2))
 
         def turn_rows(op, g, j):
             bank = new_bank("rows", op, g, j)
             words = row_words[op, g, j]
-            for c in range(2):
+            for n in range(2):
                 for e in range(2):
                     if (op, g, j) in SORTED:
-                        columns = made["dealt", (op, g, j)][:, c, e, :]
+                        columns = made["sorted", (op, g, j)][:, n, e, :]
                     else:
-                        columns = words[:, 256 * c + e : 256 * (c + 1) : 2]
-                    nc.tensor.transpose(bank[:, 2 * c + e, :], columns, ident[:])
+                        columns = words[:, 256 * n + e : 256 * (n + 1) : 2]
+                    nc.tensor.transpose(bank[:, 2 * n + e, :], columns, ident[:])
 
         def lift_rows(op, g, j, engine):
             bank = made["bank", ("rows", op, g, j)]
             pair = work_tile("pair", (op, g, j // 2), [P, 2, 2, P, 2], F32, 3)
-            out = pair[:, :, j % 2]
-            copy(engine, out, bank[:].rearrange("p (c e) r -> p c r e", e=2))
+            copy(engine, pair[:, :, j % 2], bank[:].rearrange("p (n e) r -> p n r e", e=2))
 
         def encode_rows(op, g, i):
             j = 2 * i
             pair = made["pair", (op, g, i)]
-            for c in range(2):
+            for n in range(2):
                 quantize(
-                    row_code[op, g][:, c, j : j + 2].rearrange("p j r -> p (j r)"),
-                    row_scale[op, g][:, c, j : j + 2].rearrange("p j r -> p (j r)"),
-                    pair[:, c].rearrange("p j r e -> p (j r e)").bitcast(BF16),
+                    row_code[op, g][:, n, j : j + 2].rearrange("p j r -> p (j r)"),
+                    row_scale[op, g][:, n, j : j + 2].rearrange("p j r -> p (j r)"),
+                    pair[:, n].rearrange("p j r e -> p (j r e)").bitcast(BF16),
                 )
 
 
@@ -240,10 +241,10 @@ def tile_extendeddmdkoopmancrossmoment_x2_kernel(
 
         def tanh_snap(op, g, c):
             z = made["z", (op, g, c)]
-            th = work_tile("th", (op, g, c), [P, 256, 2, 2], F32, 3)
+            th = work_tile("th", (op, g, c), [P, 256, 2, 2], F32, 4)
             nc.scalar.activation(out=th[:], in_=z[:].rearrange("p i o k -> p o i k"), func=ACT.Tanh)
 
-        def weigh_snap(op, g, c, engine):
+        def weigh_snap(op, g, c):
             th = made["th", (op, g, c)]
             nc.vector.tensor_tensor(
                 out=f_part(op, g, 256 * c, 256),
@@ -268,7 +269,7 @@ def tile_extendeddmdkoopmancrossmoment_x2_kernel(
 
         def tanh_obs(op, g, m):
             sums = made["bank", ("obs", op, g, m)][:].rearrange("p j r -> p (j r)")
-            t = work_tile("t", (op, g, m), [P, 4, P], F32, 10)
+            t = work_tile("t", (op, g, m), [P, 4, P], F32, 8)
             nc.scalar.activation(
                 out=t[:].rearrange("p j r -> p (j r)"), in_=sums, func=ACT.Tanh, bias=bias_column[:, m : m + 1]
             )
@@ -293,11 +294,8 @@ def tile_extendeddmdkoopmancrossmoment_x2_kernel(
         plane_scale = keep.tile([P, SIZE], U8, name="plane_scale", align_bytes=64)
         plane_words = out_1.rearrange("g p m t -> p g (m t)")
 
-        def divide(engine, out, in_):
-            if engine == "S":
-                nc.scalar.activation(out=out, in_=in_, func=ACT.Copy, scale=INV_DIV)
-            else:
-                nc.vector.tensor_scalar(out=out, in0=in_, scalar1=INV_DIV, scalar2=None, op0=ALU.mult)
+        def divide(out, in_):
+            nc.scalar.activation(out=out, in_=in_, func=ACT.Copy, scale=INV_DIV)
 
         def cross(c, h, k):
             bank = new_bank("cross", c, h, k)
@@ -312,9 +310,9 @@ def tile_extendeddmdkoopmancrossmoment_x2_kernel(
                     stop=(g == 1),
                 )
 
-        def lift_cross(c, h, k, engine):
+        def lift_cross(c, h, k):
             r = work_tile("r", (c, h), [P, 2, 512], F32, 6)
-            divide(engine, r[:, k, :], made["bank", ("cross", c, h, k)][:].rearrange("p t a -> p (t a)"))
+            divide(r[:, k, :], made["bank", ("cross", c, h, k)][:].rearrange("p t a -> p (t a)"))
 
         def send_cross(c, h, k):
             rows = slice(256 * c + P * k, 256 * c + P * k + P)
@@ -324,10 +322,10 @@ def tile_extendeddmdkoopmancrossmoment_x2_kernel(
             s = work_tile("s", (c, h), [P, 2, 2, P, 2], BF16, 4)
             nc.vector.tensor_copy(out=s[:], in_=made["r", (c, h)][:].rearrange("p k (a e s) -> p k e a s", e=2, s=2))
 
-        def round_bank(c, h, k, engine):
+        def round_bank(c, h, k):
             sums = made["bank", ("cross", c, h, k)][:].rearrange("p t a -> p (t a)")
             s = work_tile("s", (c, h), [P, 2, 2, P, 2], BF16, 4)
-            divide(engine, s[:, k], sums.rearrange("p (a e s) -> p e a s", e=2, s=2))
+            divide(s[:, k], sums.rearrange("p (a e s) -> p e a s", e=2, s=2))
 
         def turn_cross(c, h):
             words = made["s", (c, h)][:].rearrange("p k e a s -> p (k e) (a s)").bitcast(F32)
@@ -344,10 +342,10 @@ def tile_extendeddmdkoopmancrossmoment_x2_kernel(
             values = made["u", (c, h)][:].rearrange("p k i e -> p (k i e)").bitcast(BF16)
             quantize(plane_code[:, h, cols], plane_scale[4 * h : P, cols], values)
 
-        def send_plane(first, end):
+        def send_plane(c):
             nc.sync.dma_start(
-                out=plane_words[:, :, 1024 * first : 1024 * end].bitcast(I32),
-                in_=plane_code[:, :, 256 * first : 256 * end].bitcast(I32),
+                out=plane_words[:, :, 1024 * c : 1024 * c + 1024].bitcast(I32),
+                in_=plane_code[:, :, 256 * c : 256 * c + 256].bitcast(I32),
             )
 
         def send_half_plane(c, h):
@@ -360,17 +358,14 @@ def tile_extendeddmdkoopmancrossmoment_x2_kernel(
             rows = out_0[256 * c : 256 * c + 256, 512 * h : 512 * h + 512]
             nc.sync.dma_start(out=rows.rearrange("(k p) n -> p k n", k=2), in_=made["r", (c, h)][:])
 
-        def store_scales(first, end):
-            cols = slice(256 * first, 256 * end)
+        def send_scales():
             for quad in range(4):
-                queue = nc.scalar if end == 4 and quad % 2 == 1 else nc.sync
+                queue = nc.scalar if quad % 2 == 1 else nc.sync
                 queue.dma_start(
-                    out=out_2[:, 4 * quad : 4 * quad + 4, cols].bitcast(I32),
-                    in_=plane_scale[32 * quad : 32 * quad + 8, cols].bitcast(I32),
+                    out=out_2[:, 4 * quad : 4 * quad + 4, :].bitcast(I32),
+                    in_=plane_scale[32 * quad : 32 * quad + 8, :].bitcast(I32),
                 )
 
-
-        tensor, vector, scalar, sync = [], [], [], []
 
         def both(step, *args):
             return [(step,) + args + (k,) for k in range(2)]
@@ -378,52 +373,71 @@ def tile_extendeddmdkoopmancrossmoment_x2_kernel(
         def tiles(step, op, g, c):
             return [(step, op, g, 2 * c), (step, op, g, 2 * c + 1)]
 
-        def row_pair(step, op, g, i, *engine):
-            return [(step, op, g, 2 * i) + engine, (step, op, g, 2 * i + 1) + engine]
+        def row_pair(op, g, i):
+            return [(turn_rows, op, g, 2 * i), (turn_rows, op, g, 2 * i + 1)]
 
-        tensor += row_pair(turn_rows, "y", 0, 0) + [(spread_bias,)] + row_pair(turn_rows, "y", 0, 1)
-        tensor += [(dot_snap, "y", 0, 0, 0)] + [(dot_snap, "y", 0, 1, 0)] + [(dot_snap, "y", 0, 0, 1)] + [(dot_snap, "y", 0, 1, 1)] + row_pair(turn_rows, "y", 1, 0) + row_pair(turn_rows, "y", 1, 1)
-        tensor += both(dot_snap, "y", 0, 2) + [(turn_bias,)] + row_pair(turn_rows, "x", 0, 0)
-        tensor += both(dot_snap, "y", 0, 3) + tiles(dot_obs, "y", 1, 0) + row_pair(turn_rows, "x", 0, 1) + tiles(turn_obs, "y", 1, 0)
-        tensor += tiles(dot_obs, "y", 1, 1) + both(dot_snap, "x", 0, 0) + row_pair(turn_rows, "x", 1, 0) + tiles(turn_obs, "y", 1, 1)
-        tensor += tiles(dot_obs, "y", 1, 2) + both(dot_snap, "x", 0, 1) + row_pair(turn_rows, "x", 1, 1) + tiles(turn_obs, "y", 1, 2)
+        def crosses(c):
+            return both(cross, c, 0) + both(cross, c, 1)
+
+        tensor = row_pair("y", 0, 0) + [(spread_bias,)] + row_pair("y", 0, 1)
+        tensor += [(dot_snap, "y", 0, c, i) for i in range(2) for c in range(2)]
+        tensor += row_pair("y", 1, 0) + row_pair("y", 1, 1)
+        tensor += both(dot_snap, "y", 0, 2) + [(turn_bias,)] + row_pair("x", 0, 0)
+        tensor += both(dot_snap, "y", 0, 3) + tiles(dot_obs, "y", 1, 0)
+        tensor += row_pair("x", 0, 1) + tiles(turn_obs, "y", 1, 0)
+        for i in range(2):
+            tensor += tiles(dot_obs, "y", 1, i + 1) + both(dot_snap, "x", 0, i)
+            tensor += row_pair("x", 1, i) + tiles(turn_obs, "y", 1, i + 1)
         tensor += tiles(dot_obs, "y", 1, 3) + tiles(dot_obs, "x", 0, 2) + tiles(turn_obs, "y", 1, 3)
-        tensor += tiles(dot_obs, "x", 1, 0) + tiles(dot_obs, "x", 1, 1) + tiles(turn_obs, "x", 1, 0) + tiles(turn_obs, "x", 1, 1)
-        tensor += tiles(dot_obs, "x", 1, 2) + both(dot_snap, "x", 0, 3) + both(cross, 0, 0) + both(cross, 0, 1) + tiles(turn_obs, "x", 1, 2) + tiles(turn_obs, "x", 0, 2)
-        tensor += tiles(dot_obs, "x", 1, 3) + both(cross, 1, 0) + both(cross, 1, 1) + tiles(turn_obs, "x", 1, 3) + [(turn_cross, 0, 0)] + [(turn_cross, 0, 1)]
-        tensor += both(cross, 2, 0) + both(cross, 2, 1) + [(turn_cross, 1, 0)] + [(turn_cross, 1, 1)]
-        tensor += both(cross, 3, 0) + both(cross, 3, 1) + [(turn_cross, 2, 0)] + [(turn_cross, 2, 1)] + [(turn_cross, 3, 0)] + [(turn_cross, 3, 1)]
+        tensor += tiles(dot_obs, "x", 1, 0) + tiles(dot_obs, "x", 1, 1)
+        tensor += tiles(turn_obs, "x", 1, 0) + tiles(turn_obs, "x", 1, 1)
+        tensor += tiles(dot_obs, "x", 1, 2) + both(dot_snap, "x", 0, 3) + crosses(0)
+        tensor += tiles(turn_obs, "x", 1, 2) + tiles(turn_obs, "x", 0, 2)
+        tensor += tiles(dot_obs, "x", 1, 3) + crosses(1) + tiles(turn_obs, "x", 1, 3) + both(turn_cross, 0)
+        tensor += crosses(2) + both(turn_cross, 1)
+        tensor += crosses(3) + both(turn_cross, 2) + both(turn_cross, 3)
 
-        vector += [(lift_rows, "y", 0, 1, "V"), (encode_rows, "y", 0, 0), (lift_rows, "y", 0, 3, "V"), (encode_rows, "y", 0, 1), (add_bias, "y", 0, 0, 0), (add_bias, "y", 0, 1, 0), (add_bias, "y", 0, 0, 1), (add_bias, "y", 0, 1, 1), (lift_rows, "y", 1, 1, "V"), (encode_rows, "y", 1, 0)]
-        vector += [(add_bias, "y", 0, 2, 0), (encode_rows, "y", 1, 1), (weigh_snap, "y", 0, 0, "V"), (add_bias, "y", 0, 2, 1)]
-        vector += [(add_bias, "y", 0, 3, 0), (add_bias, "y", 0, 3, 1), (encode_rows, "x", 0, 0), (weigh_snap, "y", 0, 1, "V"), (encode_rows, "x", 0, 1), (weigh_obs, "y", 1, 0), (weigh_obs, "y", 1, 1)]
-        vector += [(add_bias, "x", 0, 0, 0), (add_bias, "x", 0, 0, 1), (weigh_snap, "y", 0, 2, "V"), (weigh_obs, "y", 1, 2), (weigh_obs, "y", 1, 3), (weigh_snap, "y", 0, 3, "V"), (encode_rows, "x", 1, 0)]
-        vector += [(add_bias, "x", 0, 1, 0), (add_bias, "x", 0, 1, 1), (encode_f, "y", 0, 0), (weigh_obs, "y", 1, 4), (weigh_obs, "y", 1, 5), (encode_rows, "x", 1, 1), (encode_f, "y", 0, 1)]
-        vector += [(encode_f, "y", 1, 0), (weigh_obs, "y", 1, 6), (weigh_obs, "y", 1, 7), (weigh_snap, "x", 0, 0, "V")]
-        vector += [(weigh_obs, "x", 1, 0), (weigh_obs, "x", 1, 1), (encode_f, "y", 1, 1), (encode_f, "x", 0), (weigh_obs, "x", 1, 2), (weigh_obs, "x", 1, 3)]
-        vector += [(weigh_snap, "x", 0, 1, "V"), (add_bias, "x", 0, 3, 0), (encode_f, "x", 1), (add_bias, "x", 0, 3, 1), (weigh_obs, "x", 1, 4), (weigh_obs, "x", 1, 5), (weigh_obs, "x", 0, 4), (weigh_obs, "x", 0, 5)]
-        vector += [(weigh_snap, "x", 0, 3, "V"), (round_cross, 0, 1), (encode_f, "x", 2), (weigh_obs, "x", 1, 6), (weigh_obs, "x", 1, 7), (round_cross, 1, 0), (round_cross, 1, 1), (encode_f, "x", 3)]
-        vector += [(encode_plane, 0, 0), (round_cross, 2, 0), (encode_plane, 0, 1), (lift_plane, 1, 1, "V"), (encode_plane, 1, 0), (round_cross, 2, 1), (encode_plane, 1, 1)]
-        vector += [(round_cross, 3, 0), (lift_plane, 2, 0, "V"), (lift_plane, 2, 1, "V"), (encode_plane, 2, 0), (lift_plane, 3, 1, "V"), (encode_plane, 3, 0), (encode_plane, 2, 1), (encode_plane, 3, 1)]
 
-        scalar += [(lift_rows, "y", 0, 0, "S"), (lift_bias_row,), (lift_rows, "y", 0, 2, "S"), (deal_rows, "y", 1, 0, "S"), (deal_rows, "y", 1, 1, "S"), (deal_rows, "y", 1, 2, "S"), (deal_rows, "y", 1, 3, "S"), (widen_bias,), (lift_rows, "y", 1, 0, "S"), (lift_rows, "y", 1, 2, "S"), (lift_rows, "y", 1, 3, "S")]
-        scalar += [(tanh_snap, "y", 0, 0), (tanh_snap, "y", 0, 1), (lift_bias_column,), (lift_rows, "x", 0, 0, "S"), (lift_rows, "x", 0, 1, "S")]
-        scalar += [(tanh_obs, "y", 1, 0), (tanh_obs, "y", 1, 1), (lift_rows, "x", 0, 2, "S"), (lift_rows, "x", 0, 3, "S"), (tanh_snap, "y", 0, 2)]
-        scalar += [(tanh_obs, "y", 1, 2), (tanh_obs, "y", 1, 3), (tanh_snap, "y", 0, 3), (lift_rows, "x", 1, 0, "S"), (lift_rows, "x", 1, 1, "S")]
-        scalar += [(tanh_obs, "y", 1, 4), (tanh_obs, "y", 1, 5), (tanh_snap, "x", 0, 0), (lift_rows, "x", 1, 2, "S"), (lift_rows, "x", 1, 3, "S")]
-        scalar += [(tanh_obs, "y", 1, 6), (tanh_obs, "y", 1, 7), (tanh_obs, "x", 0, 4), (tanh_obs, "x", 0, 5)]
-        scalar += [(tanh_obs, "x", 1, 0), (tanh_obs, "x", 1, 1), (tanh_obs, "x", 1, 2), (tanh_obs, "x", 1, 3), (tanh_snap, "x", 0, 1)]
-        scalar += [(tanh_obs, "x", 1, 4), (tanh_obs, "x", 1, 5), (round_bank, 0, 0, 0, "S"), (lift_cross, 0, 0, 0, "S"), (round_bank, 0, 0, 1, "S"), (lift_cross, 0, 0, 1, "S"), (lift_cross, 0, 1, 0, "S"), (lift_cross, 0, 1, 1, "S"), (tanh_snap, "x", 0, 3)]
-        scalar += [(tanh_obs, "x", 1, 6), (tanh_obs, "x", 1, 7), (lift_cross, 1, 0, 0, "S"), (lift_cross, 1, 0, 1, "S"), (lift_cross, 1, 1, 0, "S"), (lift_cross, 1, 1, 1, "S"), (lift_plane, 0, 0, "S"), (lift_plane, 0, 1, "S")]
-        scalar += [(lift_cross, 2, 0, 0, "S"), (lift_cross, 2, 0, 1, "S"), (lift_cross, 2, 1, 0, "S"), (lift_cross, 2, 1, 1, "S"), (lift_plane, 1, 0, "S")]
-        scalar += [(lift_cross, 3, 0, 0, "S"), (lift_cross, 3, 0, 1, "S"), (round_bank, 3, 1, 0, "S"), (round_bank, 3, 1, 1, "S"), (lift_cross, 3, 1, 0, "S"), (lift_plane, 3, 0, "S"), (lift_cross, 3, 1, 1, "S")]
-
-        sync += [(send_unit, 0, 0), (send_unit, 0, 1), (send_unit, 1, 0), (send_unit, 1, 1), (send_cross, 2, 0, 0), (send_cross, 2, 0, 1), (send_cross, 2, 1, 0), (send_cross, 2, 1, 1), (send_plane, 0, 1), (send_cross, 3, 0, 0), (send_cross, 3, 0, 1), (send_plane, 1, 2), (send_cross, 3, 1, 0), (send_cross, 3, 1, 1), (send_half_plane, 3, 0), (send_plane, 2, 3), (send_half_plane, 3, 1), (store_scales, 0, 4)]
+        vector, scalar, sync = [], [], []
+        for op in ("y", "x"):
+            for g in range(2):
+                vector += both(encode_rows, op, g)
+                for j in range(4):
+                    if (op, g, j) in SORTED:
+                        scalar += [(sort_rows, op, g, j)]
+                    if op == "y" and j % 2 == 1:
+                        vector += [(lift_rows, op, g, j, "V")]
+                    else:
+                        scalar += [(lift_rows, op, g, j, "S")]
+                for c in range(4):
+                    if (op, g, c) in SNAP:
+                        vector += both(add_bias, op, g, c) + [(weigh_snap, op, g, c)]
+                        scalar += [(tanh_snap, op, g, c)]
+                    else:
+                        scalar += tiles(tanh_obs, op, g, c)
+                        vector += tiles(weigh_obs, op, g, c)
+        scalar += [(lift_bias_row,), (widen_bias,), (lift_bias_column,)]
+        vector += [(encode_f, "y", g, h) for g in range(2) for h in range(2)] + [(encode_f, "x", c) for c in range(4)]
+        for c in range(4):
+            for h in range(2):
+                scalar += both(lift_cross, c, h)
+                if (c, h) in FROM_BANK:
+                    scalar += both(round_bank, c, h)
+                else:
+                    vector += [(round_cross, c, h)]
+                if c >= VECTOR_LIFTS_FROM and h == 0:
+                    vector += [(lift_plane, c, h, "V")]
+                else:
+                    scalar += [(lift_plane, c, h, "S")]
+                vector += [(encode_plane, c, h)]
+                sync += [(send_unit, c, h)] if c < 2 else both(send_cross, c, h)
+            sync += [(send_plane, c)] if c < 3 else both(send_half_plane, c)
+        sync += [(send_scales,)]
 
 
         def inputs(step, args):
             if step is turn_rows and args in SORTED:
-                return [(deal_rows,) + args]
+                return [(sort_rows,) + args]
             if step is lift_rows:
                 return [(turn_rows,) + args[:3]]
             if step is encode_rows:
@@ -439,7 +453,7 @@ def tile_extendeddmdkoopmancrossmoment_x2_kernel(
             if step is tanh_snap:
                 return [(add_bias,) + args + (i,) for i in range(2)]
             if step is weigh_snap:
-                return [(tanh_snap,) + args[:3]]
+                return [(tanh_snap,) + args]
             if step is dot_obs:
                 return [(encode_rows, args[0], args[1], i) for i in range(2)]
             if step is tanh_obs:
@@ -463,9 +477,9 @@ def tile_extendeddmdkoopmancrossmoment_x2_kernel(
             if step is cross:
                 return [(encode_f, "x", args[0])] + [(encode_f, "y", g, args[1]) for g in range(2)]
             if step is round_bank:
-                return [(cross,) + args[:3]]
+                return [(cross,) + args]
             if step is lift_cross:
-                return [(round_bank if args[:2] in FROM_BANK else cross,) + args[:3]]
+                return [(round_bank if args[:2] in FROM_BANK else cross,) + args]
             if step is send_cross:
                 return [(lift_cross,) + args]
             if step is round_cross:
@@ -482,14 +496,60 @@ def tile_extendeddmdkoopmancrossmoment_x2_kernel(
                 return [(encode_plane,) + args]
             if step is send_unit:
                 return [(lift_cross,) + args + (k,) for k in range(2)]
-            if step is send_plane or step is store_scales:
-                return [(encode_plane, c, h) for c in range(*args) for h in range(2)]
+            if step is send_plane:
+                return [(encode_plane,) + args + (h,) for h in range(2)]
+            if step is send_scales:
+                return [(encode_plane, c, h) for c in range(4) for h in range(2)]
             if step is turn_bias:
                 return [(widen_bias,)]
             return []
 
+
+        def name_of(entry):
+            return entry[:-1] if entry[-1] in ("S", "V") else entry
+
+        place = {entry: n for n, entry in enumerate(tensor)}
+        reads = {name_of(entry): inputs(entry[0], entry[1:]) for entry in tensor + vector + scalar + sync}
+        users = {}
+        for name, wanted in reads.items():
+            for source in wanted:
+                users.setdefault(source, []).append(name)
+        after_loads = place[dot_snap, "y", 0, 1, 0]
+
+        def earliest(name):
+            if name in place:
+                return place[name]
+            return max([earliest(source) + HOP for source in reads[name]] or [after_loads])
+
+        def latest(name):
+            if name in place:
+                return place[name]
+            banks = [(cross,) + name[1:]] if name[0] is lift_cross else [s for s in reads[name] if s in place]
+            limits = [latest(user) - HOP for user in users.get(name, [])]
+            limits += [place[bank] + BANKS - HOP for bank in banks]
+            return min(limits + [earliest(name) + (HOP if name[0] is encode_plane else WINDOW)])
+
+        def position(name):
+            if name in place:
+                return place[name]
+            if name in sync:
+                return max(position(source) for source in reads[name])
+            if name[0] in (encode_rows, add_bias, weigh_snap, weigh_obs, encode_f, round_cross):
+                share = 1
+            elif name[0] is tanh_snap:
+                share = 0
+            else:
+                share = SHARE
+            first = max([position(source) + HOP for source in reads[name]] + [earliest(name)])
+            return first + share * max(0, latest(name) - first)
+
+        vector = sorted(vector, key=lambda entry: position(name_of(entry)))
+        scalar = sorted(scalar, key=lambda entry: position(name_of(entry)))
+        sync = sorted(sync, key=position)
+
+
         written = set()
-        unread_banks = []
+        bank_reads = []
         while tensor or vector or scalar or sync:
             progress = False
             for queue in (vector, scalar, sync, tensor):
@@ -499,17 +559,16 @@ def tile_extendeddmdkoopmancrossmoment_x2_kernel(
                     if not all(name in written for name in wanted):
                         break
                     if queue is tensor:
-                        if len(unread_banks) >= BANKS and unread_banks[-BANKS] not in written:
+                        if len(bank_reads) >= BANKS and bank_reads[-BANKS] not in written:
                             break
-                        unread_banks.append(("read", step) + args)
+                        bank_reads.append(("read", step) + args)
                     step(*args)
-                    key = args[:-1] if args and args[-1] in ("S", "V", "G") else args
-                    written.add((step,) + key)
+                    written.add(name_of(queue[0]))
                     if queue is not tensor and step is not round_bank:
                         for name in wanted:
                             written.add(("read",) + name)
                     if step is lift_cross:
-                        written.add(("read", cross) + key)
+                        written.add(("read", cross) + args)
                     queue.remove(queue[0])
                     progress = True
                     if queue is tensor:

@@ -24,7 +24,7 @@ FROM_BANK = [(0, 0), (3, 1)]
 VECTOR_LIFTS_FROM = 1
 HOP = 2
 WINDOW = 12
-SHARE = 0.25
+SHARE = 0.5
 
 
 def tile_extendeddmdkoopmancrossmoment_x2_kernel(
@@ -88,10 +88,10 @@ def tile_extendeddmdkoopmancrossmoment_x2_kernel(
         load_rows("y", y, 0, 2, 2)
         load_w(0)
         load_weights("y", q)
+        nc.sync.dma_start(out=b_tiles[:], in_=b.rearrange("(m n) -> m n", n=P))
         load_rows("y", y, 1, 0, 2)
         load_rows("y", y, 1, 2, 2)
         load_w(1)
-        nc.sync.dma_start(out=b_tiles[:], in_=b.rearrange("(m n) -> m n", n=P))
         load_weights("x", p)
         for g in range(2):
             for j in range(0, 4, 2):
@@ -381,8 +381,8 @@ def tile_extendeddmdkoopmancrossmoment_x2_kernel(
 
         tensor = row_pair("y", 0, 0) + [(spread_bias,)] + row_pair("y", 0, 1)
         tensor += [(dot_snap, "y", 0, c, i) for i in range(2) for c in range(2)]
-        tensor += row_pair("y", 1, 0) + row_pair("y", 1, 1)
-        tensor += both(dot_snap, "y", 0, 2) + [(turn_bias,)] + row_pair("x", 0, 0)
+        tensor += row_pair("y", 1, 0) + row_pair("y", 1, 1) + [(turn_bias,)]
+        tensor += both(dot_snap, "y", 0, 2) + row_pair("x", 0, 0)
         tensor += both(dot_snap, "y", 0, 3) + tiles(dot_obs, "y", 1, 0)
         tensor += row_pair("x", 0, 1) + tiles(turn_obs, "y", 1, 0)
         for i in range(2):
@@ -395,7 +395,7 @@ def tile_extendeddmdkoopmancrossmoment_x2_kernel(
         tensor += tiles(turn_obs, "x", 1, 2) + tiles(turn_obs, "x", 0, 2)
         tensor += tiles(dot_obs, "x", 1, 3) + crosses(1) + tiles(turn_obs, "x", 1, 3) + both(turn_cross, 0)
         tensor += crosses(2) + both(turn_cross, 1)
-        tensor += crosses(3) + both(turn_cross, 2) + both(turn_cross, 3)
+        tensor += crosses(3) + [(turn_cross, c, h) for h in range(2) for c in (2, 3)]
 
 
         vector, scalar, sync = [], [], []
@@ -529,17 +529,14 @@ def tile_extendeddmdkoopmancrossmoment_x2_kernel(
             limits += [place[bank] + BANKS - HOP for bank in banks]
             return min(limits + [earliest(name) + (HOP if name[0] is encode_plane else WINDOW)])
 
+        on_vector = [name_of(entry) for entry in vector]
+
         def position(name):
             if name in place:
                 return place[name]
             if name in sync:
                 return max(position(source) for source in reads[name])
-            if name[0] in (encode_rows, add_bias, weigh_snap, weigh_obs, encode_f, round_cross):
-                share = 1
-            elif name[0] is tanh_snap:
-                share = 0
-            else:
-                share = SHARE
+            share = 1 if name in on_vector else SHARE
             first = max([position(source) + HOP for source in reads[name]] + [earliest(name)])
             return first + share * max(0, latest(name) - first)
 

@@ -50,11 +50,6 @@ def tile_extendeddmdkoopmancrossmoment_x2_kernel(
 
         b_rows = keep.tile([P, 8], BF16, name="b_rows", align_bytes=64)
         nc.scalar.dma_start(out=b_rows[:], in_=b.rearrange("(n w) -> n w", w=8))
-        for quad in range(4):
-            nc.scalar.dma_start(
-                out=w_scale[32 * quad : 32 * quad + 8, :].bitcast(I32),
-                in_=w_scales[:, 4 * quad : 4 * quad + 4, :].bitcast(I32),
-            )
 
         row_words = {}
 
@@ -86,6 +81,11 @@ def tile_extendeddmdkoopmancrossmoment_x2_kernel(
         load_rows("y", y, 0, 0, 1)
         load_rows("y", y, 0, 1, 1)
         load_rows("y", y, 0, 2, 2)
+        for quad in range(4):
+            nc.sync.dma_start(
+                out=w_scale[32 * quad : 32 * quad + 8, :].bitcast(I32),
+                in_=w_scales[:, 4 * quad : 4 * quad + 4, :].bitcast(I32),
+            )
         load_w(0)
         load_weights("y", q)
         nc.sync.dma_start(out=b_tiles[:], in_=b.rearrange("(m n) -> m n", n=P))

@@ -43,7 +43,7 @@ def tile_extendeddmdkoopmancrossmoment_x2_kernel(
         ident = keep.tile([P, P], F32, name="ident", align_bytes=64)
         make_identity(nc, ident[:])
 
-        w_scale = keep.tile([P, SIZE], U8, name="w_scale", align_bytes=64)
+        w_scale = keep.tile([P, SIZE], U8, name="w_scale", align_bytes=256)
         nc.vector.memset(w_scale[:].bitcast(I32), 0)
         b_square = keep.tile([P, P], F32, name="b_square", align_bytes=64)
         nc.gpsimd.memset(b_square[:], 0.0)
@@ -61,7 +61,7 @@ def tile_extendeddmdkoopmancrossmoment_x2_kernel(
             for k in range(n):
                 row_words[op, g, j + k] = rows[:, k, :].bitcast(F32)
 
-        w_code = keep.tile([P, 2, SIZE], U32, name="w_code", align_bytes=64)
+        w_code = keep.tile([P, 2, SIZE], U32, name="w_code", align_bytes=256)
         w_source = w_words.rearrange("c p n t -> p c (n t)")
 
         def load_w(h):
@@ -121,8 +121,8 @@ def tile_extendeddmdkoopmancrossmoment_x2_kernel(
         row_scale = {}
         for op in ("y", "x"):
             for g in range(2):
-                row_code[op, g] = keep.tile([P, 2, 4, P], U32, name=f"row_code_{op}{g}", align_bytes=64)
-                row_scale[op, g] = keep.tile([P, 2, 4, P], U8, name=f"row_scale_{op}{g}", align_bytes=64)
+                row_code[op, g] = keep.tile([P, 2, 4, P], U32, name=f"row_code_{op}{g}", align_bytes=256)
+                row_scale[op, g] = keep.tile([P, 2, 4, P], U8, name=f"row_scale_{op}{g}", align_bytes=256)
 
         def sort_rows(op, g, j):
             words = work_tile("sorted", (op, g, j), [P, 2, 2, P], F32, len(SORTED))
@@ -185,13 +185,13 @@ def tile_extendeddmdkoopmancrossmoment_x2_kernel(
         fy_scale = {}
         for g in range(2):
             for h in range(2):
-                fy_code[g, h] = keep.tile([P, 512], U32, name=f"fy_code{g}{h}", align_bytes=64)
-                fy_scale[g, h] = keep.tile([P, 512], U8, name=f"fy_scale{g}{h}", align_bytes=64)
+                fy_code[g, h] = keep.tile([P, 512], U32, name=f"fy_code{g}{h}", align_bytes=256)
+                fy_scale[g, h] = keep.tile([P, 512], U8, name=f"fy_scale{g}{h}", align_bytes=256)
         fx_code = []
         fx_scale = []
         for c in range(4):
-            code = keep.tile([P, 2, 256], U32, name=f"fx_code{c}", align_bytes=64)
-            scale = keep.tile([P, 2, 256], U8, name=f"fx_scale{c}", align_bytes=64)
+            code = keep.tile([P, 2, 256], U32, name=f"fx_code{c}", align_bytes=256)
+            scale = keep.tile([P, 2, 256], U8, name=f"fx_scale{c}", align_bytes=256)
             fx_code.append(code)
             fx_scale.append(scale)
 

@@ -18,13 +18,13 @@ ACT = mybir.ActivationFunctionType
 ALU = mybir.AluOpType
 
 BANKS = 8
-SNAP = [("y", 0, c) for c in range(4)] + [("x", 0, c) for c in (0, 1, 3)]
+ALIGN = 64
+SNAP = [("y", 0, c) for c in range(4)] + [("x", 0, 2), ("x", 0, 3)]
+WORD = [("x", 0, 0), ("x", 0, 1)] + [("x", 1, c) for c in range(3)]
 SORTED = [("y", 1, j) for j in range(4)]
-FROM_BANK = [(0, 0), (3, 1)]
-VECTOR_LIFTS_FROM = 1
-HOP = 2
-WINDOW = 12
-SHARE = 0.5
+PAIRWISE = [("y", 0), ("y", 1), ("x", 0), ("x", 1)]
+FROM_BANK = []
+DEPTH = {"sorted": 4, "half": 2, "z": 3, "th": 3, "t": 4, "tw": 3, "v": 3, "f": 5, "r": 6, "s": 4, "u": 4}
 
 
 def tile_extendeddmdkoopmancrossmoment_x2_kernel(
@@ -43,7 +43,7 @@ def tile_extendeddmdkoopmancrossmoment_x2_kernel(
         ident = keep.tile([P, P], F32, name="ident", align_bytes=64)
         make_identity(nc, ident[:])
 
-        w_scale = keep.tile([P, SIZE], U8, name="w_scale", align_bytes=256)
+        w_scale = keep.tile([P, SIZE], U8, name="w_scale", align_bytes=ALIGN)
         nc.vector.memset(w_scale[:].bitcast(I32), 0)
         b_square = keep.tile([P, P], F32, name="b_square", align_bytes=64)
         nc.gpsimd.memset(b_square[:], 0.0)
@@ -61,14 +61,21 @@ def tile_extendeddmdkoopmancrossmoment_x2_kernel(
             for k in range(n):
                 row_words[op, g, j + k] = rows[:, k, :].bitcast(F32)
 
-        w_code = keep.tile([P, 2, SIZE], U32, name="w_code", align_bytes=256)
+        w_code = keep.tile([P, 2, SIZE], U32, name="w_code", align_bytes=ALIGN)
         w_source = w_words.rearrange("c p n t -> p c (n t)")
 
-        def load_w(h):
+        def load_w(first, n):
             nc.sync.dma_start(
-                out=w_code[:, :, 512 * h : 512 * h + 512].bitcast(I32),
-                in_=w_source[:, :, 2048 * h : 2048 * h + 2048].bitcast(I32),
+                out=w_code[:, :, first : first + n].bitcast(I32),
+                in_=w_source[:, :, 4 * first : 4 * (first + n)].bitcast(I32),
             )
+
+        def load_w_scales():
+            for quad in range(4):
+                nc.sync.dma_start(
+                    out=w_scale[32 * quad : 32 * quad + 8, :].bitcast(I32),
+                    in_=w_scales[:, 4 * quad : 4 * quad + 4, :].bitcast(I32),
+                )
 
         weight = {}
 
@@ -81,17 +88,14 @@ def tile_extendeddmdkoopmancrossmoment_x2_kernel(
         load_rows("y", y, 0, 0, 1)
         load_rows("y", y, 0, 1, 1)
         load_rows("y", y, 0, 2, 2)
-        for quad in range(4):
-            nc.sync.dma_start(
-                out=w_scale[32 * quad : 32 * quad + 8, :].bitcast(I32),
-                in_=w_scales[:, 4 * quad : 4 * quad + 4, :].bitcast(I32),
-            )
-        load_w(0)
+        load_w_scales()
+        load_w(0, 256)
+        load_w(256, 256)
         load_weights("y", q)
         nc.sync.dma_start(out=b_tiles[:], in_=b.rearrange("(m n) -> m n", n=P))
         load_rows("y", y, 1, 0, 2)
         load_rows("y", y, 1, 2, 2)
-        load_w(1)
+        load_w(512, 512)
         load_weights("x", p)
         for g in range(2):
             for j in range(0, 4, 2):
@@ -102,9 +106,9 @@ def tile_extendeddmdkoopmancrossmoment_x2_kernel(
             made["bank", key] = bank
             return bank
 
-        def work_tile(name, key, dims, dtype, bufs):
+        def work_tile(name, key, dims, dtype):
             if (name, key) not in made:
-                made[name, key] = work.tile(dims, dtype, name=name, tag=name, bufs=bufs, align_bytes=64)
+                made[name, key] = work.tile(dims, dtype, name=name, tag=name, bufs=DEPTH[name], align_bytes=64)
             return made[name, key]
 
         def copy(engine, out, in_):
@@ -121,14 +125,14 @@ def tile_extendeddmdkoopmancrossmoment_x2_kernel(
         row_scale = {}
         for op in ("y", "x"):
             for g in range(2):
-                row_code[op, g] = keep.tile([P, 2, 4, P], U32, name=f"row_code_{op}{g}", align_bytes=256)
-                row_scale[op, g] = keep.tile([P, 2, 4, P], U8, name=f"row_scale_{op}{g}", align_bytes=256)
+                row_code[op, g] = keep.tile([P, 2, 4, P], U32, name=f"row_code_{op}{g}", align_bytes=ALIGN)
+                row_scale[op, g] = keep.tile([P, 2, 4, P], U8, name=f"row_scale_{op}{g}", align_bytes=ALIGN)
 
-        def sort_rows(op, g, j):
-            words = work_tile("sorted", (op, g, j), [P, 2, 2, P], F32, len(SORTED))
-            nc.scalar.copy(out=words[:], in_=row_words[op, g, j].rearrange("p (n a e) -> p n e a", n=2, e=2))
+        def sort_rows(engine, op, g, j):
+            words = work_tile("sorted", (op, g, j), [P, 2, 2, P], F32)
+            copy(engine, words[:], row_words[op, g, j].rearrange("p (n a e) -> p n e a", n=2, e=2))
 
-        def turn_rows(op, g, j):
+        def turn_rows(engine, op, g, j):
             bank = new_bank("rows", op, g, j)
             words = row_words[op, g, j]
             for n in range(2):
@@ -139,59 +143,66 @@ def tile_extendeddmdkoopmancrossmoment_x2_kernel(
                         columns = words[:, 256 * n + e : 256 * (n + 1) : 2]
                     nc.tensor.transpose(bank[:, 2 * n + e, :], columns, ident[:])
 
-        def lift_rows(op, g, j, engine):
+        def lift_rows(engine, op, g, j):
             bank = made["bank", ("rows", op, g, j)]
-            pair = work_tile("pair", (op, g, j // 2), [P, 2, 2, P, 2], F32, 3)
-            copy(engine, pair[:, :, j % 2], bank[:].rearrange("p (n e) r -> p n r e", e=2))
+            half = work_tile("half", (op, g), [P, 2, 4, P, 2], F32)
+            copy(engine, half[:, :, j], bank[:].rearrange("p (n e) r -> p n r e", e=2))
 
-        def encode_rows(op, g, i):
+        def encode_pair(engine, op, g, i):
             j = 2 * i
-            pair = made["pair", (op, g, i)]
+            half = made["half", (op, g)]
             for n in range(2):
                 quantize(
                     row_code[op, g][:, n, j : j + 2].rearrange("p j r -> p (j r)"),
                     row_scale[op, g][:, n, j : j + 2].rearrange("p j r -> p (j r)"),
-                    pair[:, n].rearrange("p j r e -> p (j r e)").bitcast(BF16),
+                    half[:, n, j : j + 2].rearrange("p j r e -> p (j r e)").bitcast(BF16),
                 )
+
+        def encode_half(engine, op, g):
+            quantize(
+                row_code[op, g][:].rearrange("p n j r -> p (n j r)"),
+                row_scale[op, g][:].rearrange("p n j r -> p (n j r)"),
+                made["half", (op, g)][:].rearrange("p n j r e -> p (n j r e)").bitcast(BF16),
+            )
 
 
         bias_words = keep.tile([P, P, 4], F32, name="bias_words", align_bytes=64)
         bias_row = bias_words[:].rearrange("p n m -> p (n m)").bitcast(BF16)
         bias_column = keep.tile([P, 8], F32, name="bias_column", align_bytes=64)
 
-        def spread_bias():
+        def spread_bias(engine):
             bank = new_bank("bias_row")
             words = b_rows[:].bitcast(F32)
             for m in range(4):
                 nc.tensor.transpose(bank[:, m, :], words[:, m : m + 1].to_broadcast([P, P]), ident[:])
 
-        def lift_bias_row():
+        def lift_bias_row(engine):
             bank = made["bank", ("bias_row",)]
-            nc.scalar.copy(out=bias_words[:], in_=bank[:].rearrange("p m n -> p n m"))
+            copy(engine, bias_words[:], bank[:].rearrange("p m n -> p n m"))
 
-        def widen_bias():
-            nc.scalar.copy(out=b_square[0:8, :], in_=b_tiles[:])
+        def widen_bias(engine):
+            copy(engine, b_square[0:8, :], b_tiles[:])
 
-        def turn_bias():
+        def turn_bias(engine):
             bank = new_bank("bias_column")
             nc.tensor.transpose(bank[:, 0, :], b_square[:], ident[:])
 
-        def lift_bias_column():
+        def lift_bias_column(engine):
             bank = made["bank", ("bias_column",)]
-            nc.scalar.copy(out=bias_column[:], in_=bank[:, 0, 0:8])
+            copy(engine, bias_column[:], bank[:, 0, 0:8])
 
 
         fy_code = {}
         fy_scale = {}
         for g in range(2):
             for h in range(2):
-                fy_code[g, h] = keep.tile([P, 512], U32, name=f"fy_code{g}{h}", align_bytes=256)
-                fy_scale[g, h] = keep.tile([P, 512], U8, name=f"fy_scale{g}{h}", align_bytes=256)
+                fy_code[g, h] = keep.tile([P, 512], U32, name=f"fy_code{g}{h}", align_bytes=ALIGN)
+                fy_scale[g, h] = keep.tile([P, 512], U8, name=f"fy_scale{g}{h}", align_bytes=ALIGN)
         fx_code = []
         fx_scale = []
         for c in range(4):
-            code = keep.tile([P, 2, 256], U32, name=f"fx_code{c}", align_bytes=256)
-            scale = keep.tile([P, 2, 256], U8, name=f"fx_scale{c}", align_bytes=256)
+            code = keep.tile([P, 2, 256], U32, name=f"fx_code{c}", align_bytes=ALIGN)
+            scale = keep.tile([P, 2, 256], U8, name=f"fx_scale{c}", align_bytes=ALIGN)
             fx_code.append(code)
             fx_scale.append(scale)
 
@@ -200,21 +211,20 @@ def tile_extendeddmdkoopmancrossmoment_x2_kernel(
                 key, first = (op, g, col // 512), col % 512
             else:
                 key, first = (op, col // 256), 256 * g + col % 256
-            f = work_tile("f", key, [P, 512, 4], BF16, 5)
-            return f[:, first : first + n, :]
+            f = work_tile("f", key, [P, 2048], BF16)
+            return f[:, 4 * first : 4 * (first + n)]
 
-        def encode_f(*key):
-            values = made["f", key][:].rearrange("p o j -> p (o j)")
-            if key[0] == "y":
-                quantize(fy_code[key[1], key[2]][:], fy_scale[key[1], key[2]][:], values)
-            else:
-                quantize(
-                    fx_code[key[1]][:].rearrange("p g o -> p (g o)"),
-                    fx_scale[key[1]][:].rearrange("p g o -> p (g o)"),
-                    values,
-                )
+        def encode_fy(engine, g, h):
+            quantize(fy_code[g, h][:], fy_scale[g, h][:], made["f", ("y", g, h)][:])
 
-        def dot_snap(op, g, c, i):
+        def encode_fx(engine, c):
+            quantize(
+                fx_code[c][:].rearrange("p g o -> p (g o)"),
+                fx_scale[c][:].rearrange("p g o -> p (g o)"),
+                made["f", ("x", c)][:],
+            )
+
+        def dot_snap(engine, op, g, c, i):
             bank = new_bank("snap", op, g, c, i)
             sums = bank[:].rearrange("p (k a) r -> p k (a r)", k=2)
             for k in range(2):
@@ -229,9 +239,9 @@ def tile_extendeddmdkoopmancrossmoment_x2_kernel(
                         stop=(n == 1),
                     )
 
-        def add_bias(op, g, c, i):
+        def add_bias(engine, op, g, c, i):
             sums = made["bank", ("snap", op, g, c, i)][:].rearrange("p (k a) r -> p k (a r)", k=2)
-            z = work_tile("z", (op, g, c), [P, 2, 256, 2], F32, 4)
+            z = work_tile("z", (op, g, c), [P, 2, 256, 2], F32)
             nc.vector.tensor_tensor(
                 out=z[:, i],
                 in0=sums.rearrange("p k o -> p o k"),
@@ -239,21 +249,21 @@ def tile_extendeddmdkoopmancrossmoment_x2_kernel(
                 op=ALU.add,
             )
 
-        def tanh_snap(op, g, c):
+        def tanh_snap(engine, op, g, c):
             z = made["z", (op, g, c)]
-            th = work_tile("th", (op, g, c), [P, 256, 2, 2], F32, 4)
+            th = work_tile("th", (op, g, c), [P, 256, 2, 2], F32)
             nc.scalar.activation(out=th[:], in_=z[:].rearrange("p i o k -> p o i k"), func=ACT.Tanh)
 
-        def weigh_snap(op, g, c):
+        def weigh_snap(engine, op, g, c):
             th = made["th", (op, g, c)]
             nc.vector.tensor_tensor(
-                out=f_part(op, g, 256 * c, 256),
+                out=f_part(op, g, 256 * c, 256).rearrange("p (o j) -> p o j", j=4),
                 in0=th[:].rearrange("p o i k -> p o (i k)"),
                 in1=weight[op][:, g, :].unsqueeze(1).to_broadcast([P, 256, 4]),
                 op=ALU.mult,
             )
 
-        def dot_obs(op, g, m):
+        def dot_obs(engine, op, g, m):
             bank = new_bank("obs", op, g, m)
             sums = bank[:].rearrange("p j r -> p (j r)")
             for n in range(2):
@@ -267,37 +277,89 @@ def tile_extendeddmdkoopmancrossmoment_x2_kernel(
                     stop=(n == 1),
                 )
 
-        def tanh_obs(op, g, m):
+        def tanh_obs(engine, op, g, m):
             sums = made["bank", ("obs", op, g, m)][:].rearrange("p j r -> p (j r)")
-            t = work_tile("t", (op, g, m), [P, 4, P], F32, 8)
+            t = work_tile("t", (op, g, m), [P, 4, P], F32)
             nc.scalar.activation(
                 out=t[:].rearrange("p j r -> p (j r)"), in_=sums, func=ACT.Tanh, bias=bias_column[:, m : m + 1]
             )
 
-        def turn_obs(op, g, m):
+        def turn_obs(engine, op, g, m):
             t = made["t", (op, g, m)]
             bank = new_bank("turned", op, g, m)
             for j in range(4):
                 nc.tensor.transpose(bank[:, j, :], t[:, j, :], ident[:])
 
-        def weigh_obs(op, g, m):
+        def weigh_obs(engine, op, g, m):
             bank = made["bank", ("turned", op, g, m)]
             nc.vector.tensor_tensor(
-                out=f_part(op, g, P * m, P),
+                out=f_part(op, g, P * m, P).rearrange("p (o j) -> p o j", j=4),
                 in0=bank[:].rearrange("p j o -> p o j"),
                 in1=weight[op][:, g, :].unsqueeze(1).to_broadcast([P, P, 4]),
                 op=ALU.mult,
             )
+
+        weight_row = keep.tile([P, 512], F32, name="weight_row", align_bytes=64)
+
+        def spread_weights(engine):
+            bank = new_bank("weight_row")
+            words = weight["x"][:].rearrange("p g j -> p (g j)").bitcast(F32)
+            for m in range(4):
+                nc.tensor.transpose(bank[:, m, :], words[:, m : m + 1].to_broadcast([P, P]), ident[:])
+
+        def lift_weights(engine):
+            copy(engine, weight_row[:], made["bank", ("weight_row",)][:].rearrange("p m r -> p (m r)"))
+
+        def tanh_word(engine, op, g, m):
+            sums = made["bank", ("obs", op, g, m)][:]
+            t = work_tile("tw", (op, g, m // 2), [P, 1024], F32)
+            nc.scalar.activation(
+                out=t[:, 512 * (m % 2) : 512 * (m % 2) + 512].rearrange("p (e r s) -> p e r s", e=2, s=2),
+                in_=sums.rearrange("p (e s) r -> p e r s", e=2),
+                func=ACT.Tanh,
+                bias=bias_column[:, m : m + 1],
+            )
+
+        def weigh_word(engine, op, g, m):
+            v = work_tile("v", (op, g, m // 2), [P, 1024], BF16)
+            nc.vector.tensor_tensor(
+                out=v[:, 512 * (m % 2) : 512 * (m % 2) + 512],
+                in0=made["tw", (op, g, m // 2)][:, 512 * (m % 2) : 512 * (m % 2) + 512],
+                in1=weight_row[:, 256 * g : 256 * g + 256].bitcast(BF16),
+                op=ALU.mult,
+            )
+
+        def weigh_words(engine, op, g, c):
+            v = work_tile("v", (op, g, c), [P, 1024], BF16)
+            nc.vector.tensor_tensor(
+                out=v[:].rearrange("p (k n) -> p k n", k=2),
+                in0=made["tw", (op, g, c)][:].rearrange("p (k n) -> p k n", k=2),
+                in1=weight_row[:, 256 * g : 256 * g + 256].bitcast(BF16).unsqueeze(1).to_broadcast([P, 2, 512]),
+                op=ALU.mult,
+            )
+
+        def turn_word(engine, op, g, c):
+            words = made["v", (op, g, c)][:].bitcast(F32)
+            bank = new_bank("word", op, g, c)
+            for n in range(4):
+                nc.tensor.transpose(bank[:, n, :], words[:, P * n : P * n + P], ident[:])
+
+        def lift_word(engine, op, g, c):
+            out = f_part(op, g, 256 * c, 256).bitcast(F32).rearrange("p (k o e) -> p k o e", k=2, e=2)
+            copy(engine, out, made["bank", ("word", op, g, c)][:].rearrange("p (k e) o -> p k o e", e=2))
 
 
         plane_code = keep.tile([P, 2, SIZE], U32, name="plane_code", align_bytes=64)
         plane_scale = keep.tile([P, SIZE], U8, name="plane_scale", align_bytes=64)
         plane_words = out_1.rearrange("g p m t -> p g (m t)")
 
-        def divide(out, in_):
-            nc.scalar.activation(out=out, in_=in_, func=ACT.Copy, scale=INV_DIV)
+        def divide(engine, out, in_):
+            if engine == "S":
+                nc.scalar.activation(out=out, in_=in_, func=ACT.Copy, scale=INV_DIV)
+            else:
+                nc.vector.tensor_scalar(out=out, in0=in_, scalar1=INV_DIV, scalar2=None, op0=ALU.mult)
 
-        def cross(c, h, k):
+        def cross(engine, c, h, k):
             bank = new_bank("cross", c, h, k)
             for g in range(2):
                 nc.tensor.matmul_mx(
@@ -310,55 +372,55 @@ def tile_extendeddmdkoopmancrossmoment_x2_kernel(
                     stop=(g == 1),
                 )
 
-        def lift_cross(c, h, k):
-            r = work_tile("r", (c, h), [P, 2, 512], F32, 6)
-            divide(r[:, k, :], made["bank", ("cross", c, h, k)][:].rearrange("p t a -> p (t a)"))
+        def lift_cross(engine, c, h, k):
+            r = work_tile("r", (c, h), [P, 2, 512], F32)
+            divide(engine, r[:, k, :], made["bank", ("cross", c, h, k)][:].rearrange("p t a -> p (t a)"))
 
-        def send_cross(c, h, k):
+        def send_cross(engine, c, h, k):
             rows = slice(256 * c + P * k, 256 * c + P * k + P)
             nc.sync.dma_start(out=out_0[rows, 512 * h : 512 * h + 512], in_=made["r", (c, h)][:, k, :])
 
-        def round_cross(c, h):
-            s = work_tile("s", (c, h), [P, 2, 2, P, 2], BF16, 4)
-            nc.vector.tensor_copy(out=s[:], in_=made["r", (c, h)][:].rearrange("p k (a e s) -> p k e a s", e=2, s=2))
+        def round_cross(engine, c, h):
+            s = work_tile("s", (c, h), [P, 2, 2, P, 2], BF16)
+            copy(engine, s[:], made["r", (c, h)][:].rearrange("p k (a e s) -> p k e a s", e=2, s=2))
 
-        def round_bank(c, h, k):
+        def round_bank(engine, c, h, k):
             sums = made["bank", ("cross", c, h, k)][:].rearrange("p t a -> p (t a)")
-            s = work_tile("s", (c, h), [P, 2, 2, P, 2], BF16, 4)
-            divide(s[:, k], sums.rearrange("p (a e s) -> p e a s", e=2, s=2))
+            s = work_tile("s", (c, h), [P, 2, 2, P, 2], BF16)
+            divide(engine, s[:, k], sums.rearrange("p (a e s) -> p e a s", e=2, s=2))
 
-        def turn_cross(c, h):
+        def turn_cross(engine, c, h):
             words = made["s", (c, h)][:].rearrange("p k e a s -> p (k e) (a s)").bitcast(F32)
             bank = new_bank("plane", c, h)
             for n in range(4):
                 nc.tensor.transpose(bank[:, n, :], words[:, n, :], ident[:])
 
-        def lift_plane(c, h, engine):
-            u = work_tile("u", (c, h), [P, 2, P, 2], F32, 4)
+        def lift_plane(engine, c, h):
+            u = work_tile("u", (c, h), [P, 2, P, 2], F32)
             copy(engine, u[:], made["bank", ("plane", c, h)][:].rearrange("p (k e) i -> p k i e", e=2))
 
-        def encode_plane(c, h):
+        def encode_plane(engine, c, h):
             cols = slice(256 * c, 256 * c + 256)
             values = made["u", (c, h)][:].rearrange("p k i e -> p (k i e)").bitcast(BF16)
             quantize(plane_code[:, h, cols], plane_scale[4 * h : P, cols], values)
 
-        def send_plane(c):
+        def send_plane(engine, c):
             nc.sync.dma_start(
                 out=plane_words[:, :, 1024 * c : 1024 * c + 1024].bitcast(I32),
                 in_=plane_code[:, :, 256 * c : 256 * c + 256].bitcast(I32),
             )
 
-        def send_half_plane(c, h):
+        def send_half_plane(engine, c, h):
             nc.sync.dma_start(
                 out=plane_words[:, h, 1024 * c : 1024 * c + 1024].bitcast(I32),
                 in_=plane_code[:, h, 256 * c : 256 * c + 256].bitcast(I32),
             )
 
-        def send_unit(c, h):
+        def send_unit(engine, c, h):
             rows = out_0[256 * c : 256 * c + 256, 512 * h : 512 * h + 512]
             nc.sync.dma_start(out=rows.rearrange("(k p) n -> p k n", k=2), in_=made["r", (c, h)][:])
 
-        def send_scales():
+        def send_scales(engine):
             for quad in range(4):
                 queue = nc.scalar if quad % 2 == 1 else nc.sync
                 queue.dma_start(
@@ -370,204 +432,177 @@ def tile_extendeddmdkoopmancrossmoment_x2_kernel(
         def both(step, *args):
             return [(step,) + args + (k,) for k in range(2)]
 
+        def four(step, *args):
+            return [(step,) + args + (k,) for k in range(4)]
+
         def tiles(step, op, g, c):
             return [(step, op, g, 2 * c), (step, op, g, 2 * c + 1)]
-
-        def row_pair(op, g, i):
-            return [(turn_rows, op, g, 2 * i), (turn_rows, op, g, 2 * i + 1)]
 
         def crosses(c):
             return both(cross, c, 0) + both(cross, c, 1)
 
-        tensor = row_pair("y", 0, 0) + [(spread_bias,)] + row_pair("y", 0, 1)
+        def weave(a, b):
+            out = []
+            for k in range(max(len(a), len(b))):
+                out += a[k : k + 1] + b[k : k + 1]
+            return out
+
+        def pair(step, op, g, i):
+            return [(step, op, g, 2 * i), (step, op, g, 2 * i + 1)]
+
+        def units(step, *panels):
+            return [(step, c, h) for c in panels for h in range(2)]
+
+        def lifts(c):
+            return both(lift_cross, c, 0) + both(lift_cross, c, 1)
+
+        tensor = pair(turn_rows, "y", 0, 0) + [(spread_bias,)] + pair(turn_rows, "y", 0, 1)
         tensor += [(dot_snap, "y", 0, c, i) for i in range(2) for c in range(2)]
-        tensor += row_pair("y", 1, 0) + row_pair("y", 1, 1) + [(turn_bias,)]
-        tensor += both(dot_snap, "y", 0, 2) + row_pair("x", 0, 0)
+        tensor += four(turn_rows, "y", 1) + [(turn_bias,)]
+        tensor += both(dot_snap, "y", 0, 2)
+        tensor += pair(turn_rows, "x", 0, 0) + [(spread_weights,)]
         tensor += both(dot_snap, "y", 0, 3) + tiles(dot_obs, "y", 1, 0)
-        tensor += row_pair("x", 0, 1) + tiles(turn_obs, "y", 1, 0)
-        for i in range(2):
-            tensor += tiles(dot_obs, "y", 1, i + 1) + both(dot_snap, "x", 0, i)
-            tensor += row_pair("x", 1, i) + tiles(turn_obs, "y", 1, i + 1)
-        tensor += tiles(dot_obs, "y", 1, 3) + tiles(dot_obs, "x", 0, 2) + tiles(turn_obs, "y", 1, 3)
-        tensor += tiles(dot_obs, "x", 1, 0) + tiles(dot_obs, "x", 1, 1)
-        tensor += tiles(turn_obs, "x", 1, 0) + tiles(turn_obs, "x", 1, 1)
-        tensor += tiles(dot_obs, "x", 1, 2) + both(dot_snap, "x", 0, 3) + crosses(0)
-        tensor += tiles(turn_obs, "x", 1, 2) + tiles(turn_obs, "x", 0, 2)
-        tensor += tiles(dot_obs, "x", 1, 3) + crosses(1) + tiles(turn_obs, "x", 1, 3) + both(turn_cross, 0)
-        tensor += crosses(2) + both(turn_cross, 1)
-        tensor += crosses(3) + [(turn_cross, c, h) for h in range(2) for c in (2, 3)]
+        tensor += pair(turn_rows, "x", 0, 1) + tiles(turn_obs, "y", 1, 0)
+        tensor += tiles(dot_obs, "y", 1, 1) + tiles(dot_obs, "x", 0, 0)
+        tensor += pair(turn_rows, "x", 1, 0) + tiles(turn_obs, "y", 1, 1)
+        tensor += tiles(dot_obs, "y", 1, 2) + tiles(dot_obs, "x", 0, 1)
+        tensor += pair(turn_rows, "x", 1, 1) + tiles(turn_obs, "y", 1, 2) + [(turn_word, "x", 0, 0)]
+        tensor += tiles(dot_obs, "y", 1, 3) + tiles(dot_obs, "x", 1, 0) + both(dot_snap, "x", 0, 2)
+        tensor += tiles(turn_obs, "y", 1, 3) + [(turn_word, "x", 0, 1), (turn_word, "x", 1, 0)]
+        tensor += tiles(dot_obs, "x", 1, 1) + tiles(dot_obs, "x", 1, 2) + crosses(0)
+        tensor += [(turn_word, "x", 1, 1), (turn_word, "x", 1, 2)]
+        tensor += both(dot_snap, "x", 0, 3) + tiles(dot_obs, "x", 1, 3) + crosses(1)
+        tensor += tiles(turn_obs, "x", 1, 3) + units(turn_cross, 0)
+        tensor += crosses(2) + units(turn_cross, 1)
+        tensor += crosses(3) + units(turn_cross, 2, 3)
+
+        scalar = [(lift_rows, "y", 0, 0), (lift_rows, "y", 0, 2), (lift_bias_row,)] + four(sort_rows, "y", 1)
+        scalar += [(widen_bias,), (lift_rows, "y", 1, 0), (lift_rows, "y", 1, 2), (lift_bias_column,)]
+        scalar += [(tanh_snap, "y", 0, 0), (tanh_snap, "y", 0, 1)] + pair(lift_rows, "x", 0, 0) + [(lift_weights,)]
+        scalar += tiles(tanh_obs, "y", 1, 0) + pair(lift_rows, "x", 0, 1) + [(tanh_snap, "y", 0, 2)]
+        scalar += tiles(tanh_obs, "y", 1, 1) + tiles(tanh_word, "x", 0, 0) + pair(lift_rows, "x", 1, 0)
+        scalar += [(tanh_snap, "y", 0, 3)] + tiles(tanh_obs, "y", 1, 2) + tiles(tanh_word, "x", 0, 1)
+        scalar += pair(lift_rows, "x", 1, 1) + [(lift_word, "x", 0, 0)]
+        scalar += tiles(tanh_obs, "y", 1, 3) + tiles(tanh_word, "x", 1, 0)
+        scalar += [(lift_word, "x", 0, 1), (lift_word, "x", 1, 0)]
+        scalar += tiles(tanh_word, "x", 1, 1) + tiles(tanh_word, "x", 1, 2) + [(tanh_snap, "x", 0, 2)] + both(lift_cross, 0, 0)
+        scalar += [(lift_word, "x", 1, 1), (lift_word, "x", 1, 2), (lift_cross, 0, 1, 1)]
+        scalar += tiles(tanh_obs, "x", 1, 3) + [(tanh_snap, "x", 0, 3)] + lifts(1)
+        scalar += units(lift_plane, 0) + lifts(2) + units(lift_plane, 1) + both(lift_cross, 3, 0) + [(lift_cross, 3, 1, 1)]
+        scalar += [(lift_plane, 2, 0), (lift_plane, 2, 1), (lift_plane, 3, 1)]
+
+        vector = [(lift_rows, "y", 0, 1), (encode_pair, "y", 0, 0), (lift_rows, "y", 0, 3), (encode_pair, "y", 0, 1)]
+        vector += [(add_bias, "y", 0, c, i) for i in range(2) for c in range(2)]
+        vector += [(lift_rows, "y", 1, 1), (lift_rows, "y", 1, 3)] + both(encode_pair, "y", 1)
+        vector += both(add_bias, "y", 0, 2) + [(weigh_snap, "y", 0, 0)] + both(add_bias, "y", 0, 3)
+        vector += [(encode_pair, "x", 0, 0), (weigh_snap, "y", 0, 1), (encode_pair, "x", 0, 1)]
+        vector += tiles(weigh_obs, "y", 1, 0) + [(encode_fy, 0, 0), (weigh_snap, "y", 0, 2)]
+        vector += [(weigh_words, "x", 0, 0)] + tiles(weigh_obs, "y", 1, 1)
+        vector += [(encode_pair, "x", 1, 0), (encode_fy, 1, 0), (weigh_snap, "y", 0, 3)]
+        vector += [(weigh_words, "x", 0, 1)] + [(encode_pair, "x", 1, 1)] + tiles(weigh_obs, "y", 1, 2)
+        vector += [(encode_fy, 0, 1)] + tiles(weigh_word, "x", 1, 0) + both(add_bias, "x", 0, 2)
+        vector += tiles(weigh_obs, "y", 1, 3) + [(encode_fx, 0), (encode_fy, 1, 1)]
+        vector += [(weigh_words, "x", 1, 1), (weigh_words, "x", 1, 2), (weigh_snap, "x", 0, 2)]
+        vector += [(lift_cross, 0, 1, 0), (encode_fx, 1)] + both(add_bias, "x", 0, 3) + units(round_cross, 0)
+        vector += [(encode_fx, 2), (weigh_snap, "x", 0, 3)] + tiles(weigh_obs, "x", 1, 3)
+        vector += units(round_cross, 1) + [(encode_fx, 3), (encode_plane, 0, 0), (round_cross, 2, 0), (encode_plane, 0, 1)]
+        vector += [(round_cross, 2, 1), (encode_plane, 1, 0), (lift_cross, 3, 1, 0), (encode_plane, 1, 1)]
+        vector += units(round_cross, 3) + [(encode_plane, 2, 0), (lift_plane, 3, 0), (encode_plane, 2, 1)]
+        vector += units(encode_plane, 3)
+
+        sync = units(send_unit, 0, 1) + [(send_unit, 2, 0), (send_plane, 0), (send_unit, 2, 1)]
+        sync += both(send_cross, 3, 0) + [(send_plane, 1)] + both(send_cross, 3, 1) + [(send_plane, 2)]
+        sync += units(send_half_plane, 3) + [(send_scales,)]
 
 
-        vector, scalar, sync = [], [], []
+        reads = {}
+
+        def weighed(op, g, c):
+            if (op, g, c) in SNAP:
+                return [(weigh_snap, op, g, c)]
+            if (op, g, c) in WORD:
+                return [(lift_word, op, g, c)]
+            return tiles(weigh_obs, op, g, c)
+
+        reads[spread_bias,] = []
+        reads[lift_bias_row,] = [(spread_bias,)]
+        reads[widen_bias,] = []
+        reads[turn_bias,] = [(widen_bias,)]
+        reads[lift_bias_column,] = [(turn_bias,)]
+        reads[spread_weights,] = []
+        reads[lift_weights,] = [(spread_weights,)]
         for op in ("y", "x"):
             for g in range(2):
-                vector += both(encode_rows, op, g)
                 for j in range(4):
                     if (op, g, j) in SORTED:
-                        scalar += [(sort_rows, op, g, j)]
-                    if op == "y" and j % 2 == 1:
-                        vector += [(lift_rows, op, g, j, "V")]
-                    else:
-                        scalar += [(lift_rows, op, g, j, "S")]
+                        reads[sort_rows, op, g, j] = []
+                    reads[turn_rows, op, g, j] = [(sort_rows, op, g, j)] if (op, g, j) in SORTED else []
+                    reads[lift_rows, op, g, j] = [(turn_rows, op, g, j)]
+                if (op, g) in PAIRWISE:
+                    coded = both(encode_pair, op, g)
+                    for i in range(2):
+                        reads[coded[i]] = [(lift_rows, op, g, 2 * i + k) for k in range(2)]
+                else:
+                    coded = [(encode_half, op, g)] * 2
+                    reads[coded[0]] = four(lift_rows, op, g)
                 for c in range(4):
                     if (op, g, c) in SNAP:
-                        vector += both(add_bias, op, g, c) + [(weigh_snap, op, g, c)]
-                        scalar += [(tanh_snap, op, g, c)]
-                    else:
-                        scalar += tiles(tanh_obs, op, g, c)
-                        vector += tiles(weigh_obs, op, g, c)
-        scalar += [(lift_bias_row,), (widen_bias,), (lift_bias_column,)]
-        vector += [(encode_f, "y", g, h) for g in range(2) for h in range(2)] + [(encode_f, "x", c) for c in range(4)]
-        for c in range(4):
+                        for i in range(2):
+                            reads[dot_snap, op, g, c, i] = [coded[i]]
+                            reads[add_bias, op, g, c, i] = [(dot_snap, op, g, c, i), (lift_bias_row,)]
+                        reads[tanh_snap, op, g, c] = both(add_bias, op, g, c)
+                        reads[weigh_snap, op, g, c] = [(tanh_snap, op, g, c)]
+                        continue
+                    for m in (2 * c, 2 * c + 1):
+                        reads[dot_obs, op, g, m] = coded
+                        if (op, g, c) in WORD:
+                            reads[tanh_word, op, g, m] = [(dot_obs, op, g, m), (lift_bias_column,)]
+                            reads[weigh_word, op, g, m] = [(tanh_word, op, g, m), (lift_weights,)]
+                        else:
+                            reads[tanh_obs, op, g, m] = [(dot_obs, op, g, m), (lift_bias_column,)]
+                            reads[turn_obs, op, g, m] = [(tanh_obs, op, g, m)]
+                            reads[weigh_obs, op, g, m] = [(turn_obs, op, g, m)]
+                    if (op, g, c) in WORD:
+                        reads[weigh_words, op, g, c] = tiles(tanh_word, op, g, c) + [(lift_weights,)]
+                        whole = (weigh_words, op, g, c) in vector
+                        reads[turn_word, op, g, c] = [(weigh_words, op, g, c)] if whole else tiles(weigh_word, op, g, c)
+                        reads[lift_word, op, g, c] = [(turn_word, op, g, c)]
+        for g in range(2):
             for h in range(2):
-                scalar += both(lift_cross, c, h)
-                if (c, h) in FROM_BANK:
-                    scalar += both(round_bank, c, h)
-                else:
-                    vector += [(round_cross, c, h)]
-                if c >= VECTOR_LIFTS_FROM and h == 0:
-                    vector += [(lift_plane, c, h, "V")]
-                else:
-                    scalar += [(lift_plane, c, h, "S")]
-                vector += [(encode_plane, c, h)]
-                sync += [(send_unit, c, h)] if c < 2 else both(send_cross, c, h)
-            sync += [(send_plane, c)] if c < 3 else both(send_half_plane, c)
-        sync += [(send_scales,)]
+                reads[encode_fy, g, h] = weighed("y", g, 2 * h) + weighed("y", g, 2 * h + 1)
+        for c in range(4):
+            reads[encode_fx, c] = weighed("x", 0, c) + weighed("x", 1, c)
+            for h in range(2):
+                for k in range(2):
+                    reads[cross, c, h, k] = [(encode_fx, c), (encode_fy, 0, h), (encode_fy, 1, h)]
+                    reads[lift_cross, c, h, k] = [(cross, c, h, k)]
+                    reads[send_cross, c, h, k] = [(lift_cross, c, h, k)]
+                    reads[round_bank, c, h, k] = [(cross, c, h, k)]
+                reads[round_cross, c, h] = both(lift_cross, c, h)
+                reads[turn_cross, c, h] = both(round_bank, c, h) if (c, h) in FROM_BANK else [(round_cross, c, h)]
+                reads[lift_plane, c, h] = [(turn_cross, c, h)]
+                reads[encode_plane, c, h] = [(lift_plane, c, h)]
+                reads[send_unit, c, h] = both(lift_cross, c, h)
+                reads[send_half_plane, c, h] = [(encode_plane, c, h)]
+            reads[send_plane, c] = both(encode_plane, c)
+        reads[send_scales,] = [(encode_plane, c, h) for c in range(4) for h in range(2)]
 
-
-        def inputs(step, args):
-            if step is turn_rows and args in SORTED:
-                return [(sort_rows,) + args]
-            if step is lift_rows:
-                return [(turn_rows,) + args[:3]]
-            if step is encode_rows:
-                return [(lift_rows, args[0], args[1], 2 * args[2] + k) for k in range(2)]
-            if step is lift_bias_row:
-                return [(spread_bias,)]
-            if step is lift_bias_column:
-                return [(turn_bias,)]
-            if step is dot_snap:
-                return [(encode_rows, args[0], args[1], args[3])]
-            if step is add_bias:
-                return [(dot_snap,) + args, (lift_bias_row,)]
-            if step is tanh_snap:
-                return [(add_bias,) + args + (i,) for i in range(2)]
-            if step is weigh_snap:
-                return [(tanh_snap,) + args]
-            if step is dot_obs:
-                return [(encode_rows, args[0], args[1], i) for i in range(2)]
-            if step is tanh_obs:
-                return [(dot_obs,) + args, (lift_bias_column,)]
-            if step is turn_obs:
-                return [(tanh_obs,) + args]
-            if step is weigh_obs:
-                return [(turn_obs,) + args]
-            if step is encode_f:
-                if args[0] == "x":
-                    parts = [("x", g, args[1]) for g in range(2)]
-                else:
-                    parts = [("y", args[1], 2 * args[2] + k) for k in range(2)]
-                wanted = []
-                for op, g, c in parts:
-                    if (op, g, c) in SNAP:
-                        wanted += [(weigh_snap, op, g, c)]
-                    else:
-                        wanted += [(weigh_obs, op, g, 2 * c + k) for k in range(2)]
-                return wanted
-            if step is cross:
-                return [(encode_f, "x", args[0])] + [(encode_f, "y", g, args[1]) for g in range(2)]
-            if step is round_bank:
-                return [(cross,) + args]
-            if step is lift_cross:
-                return [(round_bank if args[:2] in FROM_BANK else cross,) + args]
-            if step is send_cross:
-                return [(lift_cross,) + args]
-            if step is round_cross:
-                return [(lift_cross,) + args + (k,) for k in range(2)]
-            if step is turn_cross:
-                if args in FROM_BANK:
-                    return [(round_bank,) + args + (k,) for k in range(2)]
-                return [(round_cross,) + args]
-            if step is lift_plane:
-                return [(turn_cross,) + args[:2]]
-            if step is encode_plane:
-                return [(lift_plane,) + args]
-            if step is send_half_plane:
-                return [(encode_plane,) + args]
-            if step is send_unit:
-                return [(lift_cross,) + args + (k,) for k in range(2)]
-            if step is send_plane:
-                return [(encode_plane,) + args + (h,) for h in range(2)]
-            if step is send_scales:
-                return [(encode_plane, c, h) for c in range(4) for h in range(2)]
-            if step is turn_bias:
-                return [(widen_bias,)]
-            return []
-
-
-        def name_of(entry):
-            return entry[:-1] if entry[-1] in ("S", "V") else entry
-
-        place = {entry: n for n, entry in enumerate(tensor)}
-        reads = {name_of(entry): inputs(entry[0], entry[1:]) for entry in tensor + vector + scalar + sync}
-        users = {}
-        for name, wanted in reads.items():
-            for source in wanted:
-                users.setdefault(source, []).append(name)
-        after_loads = place[dot_snap, "y", 0, 1, 0]
-
-        def earliest(name):
-            if name in place:
-                return place[name]
-            return max([earliest(source) + HOP for source in reads[name]] or [after_loads])
-
-        def latest(name):
-            if name in place:
-                return place[name]
-            banks = [(cross,) + name[1:]] if name[0] is lift_cross else [s for s in reads[name] if s in place]
-            limits = [latest(user) - HOP for user in users.get(name, [])]
-            limits += [place[bank] + BANKS - HOP for bank in banks]
-            return min(limits + [earliest(name) + (HOP if name[0] is encode_plane else WINDOW)])
-
-        on_vector = [name_of(entry) for entry in vector]
-
-        def position(name):
-            if name in place:
-                return place[name]
-            if name in sync:
-                return max(position(source) for source in reads[name])
-            share = 1 if name in on_vector else SHARE
-            first = max([position(source) + HOP for source in reads[name]] + [earliest(name)])
-            return first + share * max(0, latest(name) - first)
-
-        vector = sorted(vector, key=lambda entry: position(name_of(entry)))
-        scalar = sorted(scalar, key=lambda entry: position(name_of(entry)))
-        sync = sorted(sync, key=position)
-
-
+        queues = {"V": vector, "S": scalar, "Q": sync, "T": list(tensor)}
+        users = {name: [user for user in vector + scalar if name in reads[user]] for name in tensor}
         written = set()
-        bank_reads = []
-        while tensor or vector or scalar or sync:
+        while any(queues.values()):
             progress = False
-            for queue in (vector, scalar, sync, tensor):
-                while queue:
-                    step, args = queue[0][0], queue[0][1:]
-                    wanted = inputs(step, args)
-                    if not all(name in written for name in wanted):
-                        break
-                    if queue is tensor:
-                        if len(bank_reads) >= BANKS and bank_reads[-BANKS] not in written:
+            for engine, queue in queues.items():
+                while queue and all(source in written for source in reads[queue[0]]):
+                    name = queue[0]
+                    if engine == "T":
+                        n = tensor.index(name)
+                        if n >= BANKS and not all(user in written for user in users[tensor[n - BANKS]]):
                             break
-                        bank_reads.append(("read", step) + args)
-                    step(*args)
-                    written.add(name_of(queue[0]))
-                    if queue is not tensor and step is not round_bank:
-                        for name in wanted:
-                            written.add(("read",) + name)
-                    if step is lift_cross:
-                        written.add(("read", cross) + args)
-                    queue.remove(queue[0])
+                    name[0](engine, *name[1:])
+                    written.add(name)
+                    queue.remove(name)
                     progress = True
-                    if queue is tensor:
+                    if engine == "T":
                         break
             assert progress

@@ -19,12 +19,13 @@ ALU = mybir.AluOpType
 
 BANKS = 8
 ALIGN = 64
-SNAP = [("y", 0, c) for c in range(4)] + [("x", 0, 2), ("x", 0, 3)]
-WORD = [("x", 0, 0), ("x", 0, 1)] + [("x", 1, c) for c in range(3)]
+SNAP = [("y", 0, c) for c in range(4)] + [("x", 0, c) for c in (0, 3)]
+WORD = [("x", 0, 1), ("x", 0, 2), ("x", 1, 1), ("x", 1, 2)]
 SORTED = [("y", 1, j) for j in range(4)]
 PAIRWISE = [("y", 0), ("y", 1), ("x", 0), ("x", 1)]
-FROM_BANK = []
-DEPTH = {"sorted": 4, "half": 2, "z": 3, "th": 3, "t": 4, "tw": 3, "v": 3, "f": 5, "r": 6, "s": 4, "u": 4}
+FROM_BANK = [(3, 1)]
+DEPTH = {"sorted": 4, "pair": 3, "z": 3, "th": 3, "t": 4, "tw": 3, "v": 3, "f": 5, "r": 6, "s": 4, "u": 4, "u_tile": 2}
+FIRST = [("y", 0, 0, 0), ("y", 0, 1, 0)]
 
 
 def tile_extendeddmdkoopmancrossmoment_x2_kernel(
@@ -64,10 +65,10 @@ def tile_extendeddmdkoopmancrossmoment_x2_kernel(
         w_code = keep.tile([P, 2, SIZE], U32, name="w_code", align_bytes=ALIGN)
         w_source = w_words.rearrange("c p n t -> p c (n t)")
 
-        def load_w(first, n):
+        def load_w(passes, h):
             nc.sync.dma_start(
-                out=w_code[:, :, first : first + n].bitcast(I32),
-                in_=w_source[:, :, 4 * first : 4 * (first + n)].bitcast(I32),
+                out=w_code[:, passes, 512 * h : 512 * h + 512].bitcast(I32),
+                in_=w_source[:, passes, 2048 * h : 2048 * h + 2048].bitcast(I32),
             )
 
         def load_w_scales():
@@ -89,13 +90,13 @@ def tile_extendeddmdkoopmancrossmoment_x2_kernel(
         load_rows("y", y, 0, 1, 1)
         load_rows("y", y, 0, 2, 2)
         load_w_scales()
-        load_w(0, 256)
-        load_w(256, 256)
-        load_weights("y", q)
-        nc.sync.dma_start(out=b_tiles[:], in_=b.rearrange("(m n) -> m n", n=P))
+        load_w(slice(0, 1), 0)
+        load_w(slice(1, 2), 0)
         load_rows("y", y, 1, 0, 2)
         load_rows("y", y, 1, 2, 2)
-        load_w(512, 512)
+        nc.sync.dma_start(out=b_tiles[:], in_=b.rearrange("(m n) -> m n", n=P))
+        load_w(slice(0, 2), 1)
+        load_weights("y", q)
         load_weights("x", p)
         for g in range(2):
             for j in range(0, 4, 2):
@@ -145,17 +146,17 @@ def tile_extendeddmdkoopmancrossmoment_x2_kernel(
 
         def lift_rows(engine, op, g, j):
             bank = made["bank", ("rows", op, g, j)]
-            half = work_tile("half", (op, g), [P, 2, 4, P, 2], F32)
-            copy(engine, half[:, :, j], bank[:].rearrange("p (n e) r -> p n r e", e=2))
+            pair = work_tile("pair", (op, g, j // 2), [P, 2, 2, P, 2], F32)
+            copy(engine, pair[:, :, j % 2], bank[:].rearrange("p (n e) r -> p n r e", e=2))
 
         def encode_pair(engine, op, g, i):
             j = 2 * i
-            half = made["half", (op, g)]
+            pair = made["pair", (op, g, i)]
             for n in range(2):
                 quantize(
                     row_code[op, g][:, n, j : j + 2].rearrange("p j r -> p (j r)"),
                     row_scale[op, g][:, n, j : j + 2].rearrange("p j r -> p (j r)"),
-                    half[:, n, j : j + 2].rearrange("p j r e -> p (j r e)").bitcast(BF16),
+                    pair[:, n].rearrange("p j r e -> p (j r e)").bitcast(BF16),
                 )
 
         def encode_half(engine, op, g):
@@ -224,20 +225,26 @@ def tile_extendeddmdkoopmancrossmoment_x2_kernel(
                 made["f", ("x", c)][:],
             )
 
-        def dot_snap(engine, op, g, c, i):
-            bank = new_bank("snap", op, g, c, i)
-            sums = bank[:].rearrange("p (k a) r -> p k (a r)", k=2)
+        def snap_pass(op, g, c, i, n):
+            sums = made["bank", ("snap", op, g, c, i)][:].rearrange("p (k a) r -> p k (a r)", k=2)
             for k in range(2):
-                for n in range(2):
-                    nc.tensor.matmul_mx(
-                        out=sums[:, k, :],
-                        lhsT=row_code[op, g][:, n, 2 * i + k, :].bitcast(FP8X4),
-                        lhsT_scale=row_scale[op, g][:, n, 2 * i + k, :],
-                        rhs=w_code[:, n, 256 * c : 256 * c + 256].bitcast(FP8X4),
-                        rhs_scale=w_scale[4 * n : P, 256 * c : 256 * c + 256],
-                        start=(n == 0),
-                        stop=(n == 1),
-                    )
+                nc.tensor.matmul_mx(
+                    out=sums[:, k, :],
+                    lhsT=row_code[op, g][:, n, 2 * i + k, :].bitcast(FP8X4),
+                    lhsT_scale=row_scale[op, g][:, n, 2 * i + k, :],
+                    rhs=w_code[:, n, 256 * c : 256 * c + 256].bitcast(FP8X4),
+                    rhs_scale=w_scale[4 * n : P, 256 * c : 256 * c + 256],
+                    start=(n == 0 and k == 0),
+                    stop=(n == 1 and k == 1),
+                )
+
+        def dot_snap(engine, op, g, c, i):
+            new_bank("snap", op, g, c, i)
+            snap_pass(op, g, c, i, 0)
+            if (op, g, c, i) == FIRST[1]:
+                snap_pass(*FIRST[0], 1)
+            if (op, g, c, i) != FIRST[0]:
+                snap_pass(op, g, c, i, 1)
 
         def add_bias(engine, op, g, c, i):
             sums = made["bank", ("snap", op, g, c, i)][:].rearrange("p (k a) r -> p k (a r)", k=2)
@@ -404,6 +411,21 @@ def tile_extendeddmdkoopmancrossmoment_x2_kernel(
             values = made["u", (c, h)][:].rearrange("p k i e -> p (k i e)").bitcast(BF16)
             quantize(plane_code[:, h, cols], plane_scale[4 * h : P, cols], values)
 
+        def turn_tile(engine, c, h, k):
+            words = made["s", (c, h)][:, k].rearrange("p e a s -> p e (a s)").bitcast(F32)
+            bank = new_bank("plane", c, h, k)
+            for e in range(2):
+                nc.tensor.transpose(bank[:, e, :], words[:, e, :], ident[:])
+
+        def lift_tile(engine, c, h, k):
+            u = work_tile("u_tile", (c, h, k), [P, P, 2], F32)
+            copy(engine, u[:], made["bank", ("plane", c, h, k)][:, 0:2].rearrange("p e i -> p i e"))
+
+        def encode_tile(engine, c, h, k):
+            cols = slice(256 * c + P * k, 256 * c + P * k + P)
+            values = made["u_tile", (c, h, k)][:].rearrange("p i e -> p (i e)").bitcast(BF16)
+            quantize(plane_code[:, h, cols], plane_scale[4 * h : P, cols], values)
+
         def send_plane(engine, c):
             nc.sync.dma_start(
                 out=plane_words[:, :, 1024 * c : 1024 * c + 1024].bitcast(I32),
@@ -414,6 +436,11 @@ def tile_extendeddmdkoopmancrossmoment_x2_kernel(
             nc.sync.dma_start(
                 out=plane_words[:, h, 1024 * c : 1024 * c + 1024].bitcast(I32),
                 in_=plane_code[:, h, 256 * c : 256 * c + 256].bitcast(I32),
+            )
+
+        def send_last_planes(engine, h):
+            nc.sync.dma_start(
+                out=plane_words[:, h, 2048:4096].bitcast(I32), in_=plane_code[:, h, 512:1024].bitcast(I32)
             )
 
         def send_unit(engine, c, h):
@@ -458,61 +485,59 @@ def tile_extendeddmdkoopmancrossmoment_x2_kernel(
 
         tensor = pair(turn_rows, "y", 0, 0) + [(spread_bias,)] + pair(turn_rows, "y", 0, 1)
         tensor += [(dot_snap, "y", 0, c, i) for i in range(2) for c in range(2)]
-        tensor += four(turn_rows, "y", 1) + [(turn_bias,)]
-        tensor += both(dot_snap, "y", 0, 2)
-        tensor += pair(turn_rows, "x", 0, 0) + [(spread_weights,)]
+        tensor += pair(turn_rows, "y", 1, 0) + pair(turn_rows, "y", 1, 1) + [(turn_bias,)]
+        tensor += both(dot_snap, "y", 0, 2) + pair(turn_rows, "x", 0, 0) + [(spread_weights,)]
         tensor += both(dot_snap, "y", 0, 3) + tiles(dot_obs, "y", 1, 0)
         tensor += pair(turn_rows, "x", 0, 1) + tiles(turn_obs, "y", 1, 0)
-        tensor += tiles(dot_obs, "y", 1, 1) + tiles(dot_obs, "x", 0, 0)
+        tensor += tiles(dot_obs, "y", 1, 1) + both(dot_snap, "x", 0, 0)
         tensor += pair(turn_rows, "x", 1, 0) + tiles(turn_obs, "y", 1, 1)
         tensor += tiles(dot_obs, "y", 1, 2) + tiles(dot_obs, "x", 0, 1)
-        tensor += pair(turn_rows, "x", 1, 1) + tiles(turn_obs, "y", 1, 2) + [(turn_word, "x", 0, 0)]
-        tensor += tiles(dot_obs, "y", 1, 3) + tiles(dot_obs, "x", 1, 0) + both(dot_snap, "x", 0, 2)
-        tensor += tiles(turn_obs, "y", 1, 3) + [(turn_word, "x", 0, 1), (turn_word, "x", 1, 0)]
-        tensor += tiles(dot_obs, "x", 1, 1) + tiles(dot_obs, "x", 1, 2) + crosses(0)
+        tensor += pair(turn_rows, "x", 1, 1) + tiles(turn_obs, "y", 1, 2)
+        tensor += tiles(dot_obs, "y", 1, 3) + tiles(dot_obs, "x", 0, 2)
+        tensor += tiles(turn_obs, "y", 1, 3) + [(turn_word, "x", 0, 1)]
+        tensor += tiles(dot_obs, "x", 1, 0) + tiles(dot_obs, "x", 1, 1)
+        tensor += tiles(turn_obs, "x", 1, 0) + [(turn_word, "x", 0, 2)]
+        tensor += tiles(dot_obs, "x", 1, 2) + both(dot_snap, "x", 0, 3) + crosses(0)
         tensor += [(turn_word, "x", 1, 1), (turn_word, "x", 1, 2)]
-        tensor += both(dot_snap, "x", 0, 3) + tiles(dot_obs, "x", 1, 3) + crosses(1)
-        tensor += tiles(turn_obs, "x", 1, 3) + units(turn_cross, 0)
-        tensor += crosses(2) + units(turn_cross, 1)
-        tensor += crosses(3) + units(turn_cross, 2, 3)
+        tensor += tiles(dot_obs, "x", 1, 3) + crosses(1) + tiles(turn_obs, "x", 1, 3) + both(turn_cross, 0)
+        tensor += crosses(2) + both(turn_cross, 1)
+        tensor += crosses(3) + [(turn_cross, c, h) for h in range(2) for c in (2, 3)]
 
         scalar = [(lift_rows, "y", 0, 0), (lift_rows, "y", 0, 2), (lift_bias_row,)] + four(sort_rows, "y", 1)
-        scalar += [(widen_bias,), (lift_rows, "y", 1, 0), (lift_rows, "y", 1, 2), (lift_bias_column,)]
-        scalar += [(tanh_snap, "y", 0, 0), (tanh_snap, "y", 0, 1)] + pair(lift_rows, "x", 0, 0) + [(lift_weights,)]
+        scalar += [(widen_bias,), (tanh_snap, "y", 0, 0)] + [(lift_rows, "y", 1, j) for j in (0, 2, 3)]
+        scalar += [(lift_bias_column,), (tanh_snap, "y", 0, 1)] + pair(lift_rows, "x", 0, 0) + [(lift_weights,)]
         scalar += tiles(tanh_obs, "y", 1, 0) + pair(lift_rows, "x", 0, 1) + [(tanh_snap, "y", 0, 2)]
-        scalar += tiles(tanh_obs, "y", 1, 1) + tiles(tanh_word, "x", 0, 0) + pair(lift_rows, "x", 1, 0)
-        scalar += [(tanh_snap, "y", 0, 3)] + tiles(tanh_obs, "y", 1, 2) + tiles(tanh_word, "x", 0, 1)
-        scalar += pair(lift_rows, "x", 1, 1) + [(lift_word, "x", 0, 0)]
-        scalar += tiles(tanh_obs, "y", 1, 3) + tiles(tanh_word, "x", 1, 0)
-        scalar += [(lift_word, "x", 0, 1), (lift_word, "x", 1, 0)]
-        scalar += tiles(tanh_word, "x", 1, 1) + tiles(tanh_word, "x", 1, 2) + [(tanh_snap, "x", 0, 2)] + both(lift_cross, 0, 0)
-        scalar += [(lift_word, "x", 1, 1), (lift_word, "x", 1, 2), (lift_cross, 0, 1, 1)]
-        scalar += tiles(tanh_obs, "x", 1, 3) + [(tanh_snap, "x", 0, 3)] + lifts(1)
-        scalar += units(lift_plane, 0) + lifts(2) + units(lift_plane, 1) + both(lift_cross, 3, 0) + [(lift_cross, 3, 1, 1)]
-        scalar += [(lift_plane, 2, 0), (lift_plane, 2, 1), (lift_plane, 3, 1)]
+        scalar += tiles(tanh_obs, "y", 1, 1) + [(tanh_snap, "y", 0, 3)] + pair(lift_rows, "x", 1, 0)
+        scalar += tiles(tanh_obs, "y", 1, 2) + tiles(tanh_word, "x", 0, 1) + pair(lift_rows, "x", 1, 1)
+        scalar += tiles(tanh_obs, "y", 1, 3) + tiles(tanh_word, "x", 0, 2) + [(tanh_snap, "x", 0, 0)]
+        scalar += tiles(tanh_obs, "x", 1, 0) + [(lift_word, "x", 0, 1)]
+        scalar += tiles(tanh_word, "x", 1, 1) + tiles(tanh_word, "x", 1, 2) + [(lift_word, "x", 0, 2)]
+        scalar += both(lift_cross, 0, 0) + [(lift_cross, 0, 1, 0), (lift_word, "x", 1, 1), (lift_cross, 0, 1, 1)]
+        scalar += [(tanh_snap, "x", 0, 3)] + tiles(tanh_obs, "x", 1, 3) + lifts(1) + units(lift_plane, 0)
+        scalar += lifts(2) + [(lift_plane, 1, 1)] + both(lift_cross, 3, 0) + both(round_bank, 3, 1) + both(lift_cross, 3, 1)
+        scalar += [(lift_plane, 2, 1), (lift_plane, 3, 1)]
 
         vector = [(lift_rows, "y", 0, 1), (encode_pair, "y", 0, 0), (lift_rows, "y", 0, 3), (encode_pair, "y", 0, 1)]
         vector += [(add_bias, "y", 0, c, i) for i in range(2) for c in range(2)]
-        vector += [(lift_rows, "y", 1, 1), (lift_rows, "y", 1, 3)] + both(encode_pair, "y", 1)
-        vector += both(add_bias, "y", 0, 2) + [(weigh_snap, "y", 0, 0)] + both(add_bias, "y", 0, 3)
-        vector += [(encode_pair, "x", 0, 0), (weigh_snap, "y", 0, 1), (encode_pair, "x", 0, 1)]
-        vector += tiles(weigh_obs, "y", 1, 0) + [(encode_fy, 0, 0), (weigh_snap, "y", 0, 2)]
-        vector += [(weigh_words, "x", 0, 0)] + tiles(weigh_obs, "y", 1, 1)
-        vector += [(encode_pair, "x", 1, 0), (encode_fy, 1, 0), (weigh_snap, "y", 0, 3)]
-        vector += [(weigh_words, "x", 0, 1)] + [(encode_pair, "x", 1, 1)] + tiles(weigh_obs, "y", 1, 2)
-        vector += [(encode_fy, 0, 1)] + tiles(weigh_word, "x", 1, 0) + both(add_bias, "x", 0, 2)
-        vector += tiles(weigh_obs, "y", 1, 3) + [(encode_fx, 0), (encode_fy, 1, 1)]
-        vector += [(weigh_words, "x", 1, 1), (weigh_words, "x", 1, 2), (weigh_snap, "x", 0, 2)]
-        vector += [(lift_cross, 0, 1, 0), (encode_fx, 1)] + both(add_bias, "x", 0, 3) + units(round_cross, 0)
-        vector += [(encode_fx, 2), (weigh_snap, "x", 0, 3)] + tiles(weigh_obs, "x", 1, 3)
-        vector += units(round_cross, 1) + [(encode_fx, 3), (encode_plane, 0, 0), (round_cross, 2, 0), (encode_plane, 0, 1)]
-        vector += [(round_cross, 2, 1), (encode_plane, 1, 0), (lift_cross, 3, 1, 0), (encode_plane, 1, 1)]
-        vector += units(round_cross, 3) + [(encode_plane, 2, 0), (lift_plane, 3, 0), (encode_plane, 2, 1)]
-        vector += units(encode_plane, 3)
+        vector += [(lift_rows, "y", 1, 1), (weigh_snap, "y", 0, 0)] + both(encode_pair, "y", 1)
+        vector += both(add_bias, "y", 0, 2) + [(weigh_snap, "y", 0, 1)] + both(add_bias, "y", 0, 3)
+        vector += [(encode_pair, "x", 0, 0), (encode_fy, 0, 0), (encode_pair, "x", 0, 1)]
+        vector += tiles(weigh_obs, "y", 1, 0) + [(weigh_snap, "y", 0, 2)] + both(add_bias, "x", 0, 0)
+        vector += [(weigh_snap, "y", 0, 3)] + tiles(weigh_obs, "y", 1, 1) + [(encode_fy, 0, 1)]
+        vector += [(encode_pair, "x", 1, 0), (encode_fy, 1, 0), (weigh_words, "x", 0, 1)]
+        vector += [(weigh_obs, "y", 1, 4), (encode_pair, "x", 1, 1), (weigh_obs, "y", 1, 5)]
+        vector += tiles(weigh_obs, "y", 1, 3) + [(weigh_words, "x", 0, 2), (weigh_snap, "x", 0, 0)] + tiles(weigh_obs, "x", 1, 0)
+        vector += [(encode_fx, 0), (encode_fy, 1, 1), (weigh_words, "x", 1, 1), (weigh_words, "x", 1, 2)]
+        vector += both(add_bias, "x", 0, 3) + [(encode_fx, 1), (round_cross, 0, 0), (lift_word, "x", 1, 2)]
+        vector += [(round_cross, 0, 1), (encode_fx, 2), (weigh_snap, "x", 0, 3)] + tiles(weigh_obs, "x", 1, 3)
+        vector += units(round_cross, 1) + [(encode_fx, 3)]
+        vector += units(encode_plane, 0) + [(lift_plane, 1, 0), (round_cross, 2, 0), (encode_plane, 1, 0), (round_cross, 2, 1)]
+        vector += [(encode_plane, 1, 1), (round_cross, 3, 0), (lift_plane, 2, 0), (lift_plane, 3, 0)]
+        vector += [(encode_plane, c, h) for h in range(2) for c in (2, 3)]
 
-        sync = units(send_unit, 0, 1) + [(send_unit, 2, 0), (send_plane, 0), (send_unit, 2, 1)]
-        sync += both(send_cross, 3, 0) + [(send_plane, 1)] + both(send_cross, 3, 1) + [(send_plane, 2)]
-        sync += units(send_half_plane, 3) + [(send_scales,)]
+        sync = units(send_unit, 0, 1)
+        sync += both(send_cross, 2, 0) + [(send_plane, 0)] + both(send_cross, 2, 1) + both(send_cross, 3, 0) + [(send_plane, 1)]
+        sync += both(send_cross, 3, 1) + both(send_last_planes) + [(send_scales,)]
 
 
         reads = {}
@@ -523,6 +548,9 @@ def tile_extendeddmdkoopmancrossmoment_x2_kernel(
             if (op, g, c) in WORD:
                 return [(lift_word, op, g, c)]
             return tiles(weigh_obs, op, g, c)
+
+        def planes(c, h):
+            return [(encode_plane, c, h)] if (encode_plane, c, h) in vector else both(encode_tile, c, h)
 
         reads[spread_bias,] = []
         reads[lift_bias_row,] = [(spread_bias,)]
@@ -576,17 +604,25 @@ def tile_extendeddmdkoopmancrossmoment_x2_kernel(
                 for k in range(2):
                     reads[cross, c, h, k] = [(encode_fx, c), (encode_fy, 0, h), (encode_fy, 1, h)]
                     reads[lift_cross, c, h, k] = [(cross, c, h, k)]
+                    if (c, h) in FROM_BANK:
+                        reads[lift_cross, c, h, k].append((round_bank, c, h, k))
                     reads[send_cross, c, h, k] = [(lift_cross, c, h, k)]
                     reads[round_bank, c, h, k] = [(cross, c, h, k)]
+                    reads[turn_tile, c, h, k] = [(round_bank, c, h, k)]
+                    reads[lift_tile, c, h, k] = [(turn_tile, c, h, k)]
+                    reads[encode_tile, c, h, k] = [(lift_tile, c, h, k)]
                 reads[round_cross, c, h] = both(lift_cross, c, h)
                 reads[turn_cross, c, h] = both(round_bank, c, h) if (c, h) in FROM_BANK else [(round_cross, c, h)]
                 reads[lift_plane, c, h] = [(turn_cross, c, h)]
                 reads[encode_plane, c, h] = [(lift_plane, c, h)]
                 reads[send_unit, c, h] = both(lift_cross, c, h)
-                reads[send_half_plane, c, h] = [(encode_plane, c, h)]
-            reads[send_plane, c] = both(encode_plane, c)
-        reads[send_scales,] = [(encode_plane, c, h) for c in range(4) for h in range(2)]
+                reads[send_half_plane, c, h] = planes(c, h)
+            reads[send_plane, c] = planes(c, 0) + planes(c, 1)
+        for h in range(2):
+            reads[send_last_planes, h] = planes(2, h) + planes(3, h)
+        reads[send_scales,] = [name for c in range(4) for h in range(2) for name in planes(c, h)]
 
+        reads[(add_bias,) + FIRST[0]].append((dot_snap,) + FIRST[1])
         queues = {"V": vector, "S": scalar, "Q": sync, "T": list(tensor)}
         users = {name: [user for user in vector + scalar if name in reads[user]] for name in tensor}
         written = set()

@@ -21,10 +21,10 @@ BANKS = 8
 ALIGN = 64
 SNAP = [("y", 0, c) for c in range(4)] + [("x", 0, c) for c in (0, 3)]
 WORD = [("x", 0, 1), ("x", 0, 2), ("x", 1, 1), ("x", 1, 2)]
-SORTED = [("y", 1, j) for j in range(4)]
-PAIRWISE = [("y", 0), ("y", 1), ("x", 0), ("x", 1)]
+SORTED = [("y", 1, 0), ("y", 1, 1)]
+PAIRWISE = [("y", 0), ("x", 0)]
 FROM_BANK = [(3, 1)]
-DEPTH = {"sorted": 4, "pair": 3, "z": 3, "th": 3, "t": 4, "tw": 3, "v": 3, "f": 5, "r": 6, "s": 4, "u": 4, "u_tile": 2}
+DEPTH = {"sorted": 2, "pair": 2, "half": 1, "z": 3, "th": 3, "t": 4, "tw": 3, "v": 3, "f": 5, "r": 6, "s": 4, "u": 4, "u_tile": 2}
 FIRST = [("y", 0, 0, 0), ("y", 0, 1, 0)]
 
 
@@ -80,9 +80,9 @@ def tile_extendeddmdkoopmancrossmoment_x2_kernel(
 
         weight = {}
 
-        def load_weights(op, source):
+        def load_weights(op, source, queue):
             weight[op] = keep.tile([P, 2, 4], BF16, name=f"weight_{op}", align_bytes=64)
-            nc.sync.dma_start(out=weight[op][:], in_=source.rearrange("(g p j) -> p g j", g=2, j=4))
+            queue.dma_start(out=weight[op][:], in_=source.rearrange("(g p j) -> p g j", g=2, j=4))
 
         b_tiles = keep.tile([8, P], BF16, name="b_tiles", align_bytes=64)
 
@@ -96,8 +96,8 @@ def tile_extendeddmdkoopmancrossmoment_x2_kernel(
         load_rows("y", y, 1, 2, 2)
         nc.sync.dma_start(out=b_tiles[:], in_=b.rearrange("(m n) -> m n", n=P))
         load_w(slice(0, 2), 1)
-        load_weights("y", q)
-        load_weights("x", p)
+        load_weights("y", q, nc.sync)
+        load_weights("x", p, nc.sync)
         for g in range(2):
             for j in range(0, 4, 2):
                 load_rows("x", x, g, j, 2)
@@ -146,8 +146,11 @@ def tile_extendeddmdkoopmancrossmoment_x2_kernel(
 
         def lift_rows(engine, op, g, j):
             bank = made["bank", ("rows", op, g, j)]
-            pair = work_tile("pair", (op, g, j // 2), [P, 2, 2, P, 2], F32)
-            copy(engine, pair[:, :, j % 2], bank[:].rearrange("p (n e) r -> p n r e", e=2))
+            if (op, g) in PAIRWISE:
+                out = work_tile("pair", (op, g, j // 2), [P, 2, 2, P, 2], F32)[:, :, j % 2]
+            else:
+                out = work_tile("half", (op, g), [P, 2, 4, P, 2], F32)[:, :, j]
+            copy(engine, out, bank[:].rearrange("p (n e) r -> p n r e", e=2))
 
         def encode_pair(engine, op, g, i):
             j = 2 * i
@@ -501,9 +504,9 @@ def tile_extendeddmdkoopmancrossmoment_x2_kernel(
         tensor += [(turn_word, "x", 1, 1), (turn_word, "x", 1, 2)]
         tensor += tiles(dot_obs, "x", 1, 3) + crosses(1) + tiles(turn_obs, "x", 1, 3) + both(turn_cross, 0)
         tensor += crosses(2) + both(turn_cross, 1)
-        tensor += crosses(3) + [(turn_cross, c, h) for h in range(2) for c in (2, 3)]
+        tensor += crosses(3) + units(turn_cross, 2, 3)
 
-        scalar = [(lift_rows, "y", 0, 0), (lift_rows, "y", 0, 2), (lift_bias_row,)] + four(sort_rows, "y", 1)
+        scalar = [(lift_rows, "y", 0, 0), (lift_rows, "y", 0, 2), (lift_bias_row,)] + pair(sort_rows, "y", 1, 0)
         scalar += [(widen_bias,), (tanh_snap, "y", 0, 0)] + [(lift_rows, "y", 1, j) for j in (0, 2, 3)]
         scalar += [(lift_bias_column,), (tanh_snap, "y", 0, 1)] + pair(lift_rows, "x", 0, 0) + [(lift_weights,)]
         scalar += tiles(tanh_obs, "y", 1, 0) + pair(lift_rows, "x", 0, 1) + [(tanh_snap, "y", 0, 2)]
@@ -514,25 +517,25 @@ def tile_extendeddmdkoopmancrossmoment_x2_kernel(
         scalar += tiles(tanh_word, "x", 1, 1) + tiles(tanh_word, "x", 1, 2) + [(lift_word, "x", 0, 2)]
         scalar += both(lift_cross, 0, 0) + [(lift_cross, 0, 1, 0), (lift_word, "x", 1, 1), (lift_cross, 0, 1, 1)]
         scalar += [(tanh_snap, "x", 0, 3)] + tiles(tanh_obs, "x", 1, 3) + lifts(1) + units(lift_plane, 0)
-        scalar += lifts(2) + [(lift_plane, 1, 1)] + both(lift_cross, 3, 0) + both(round_bank, 3, 1) + both(lift_cross, 3, 1)
-        scalar += [(lift_plane, 2, 1), (lift_plane, 3, 1)]
+        scalar += lifts(2) + [(lift_plane, 1, 1)] + both(lift_cross, 3, 0) + both(round_bank, 3, 1)
+        scalar += units(lift_plane, 2) + [(lift_plane, 3, 1)]
 
         vector = [(lift_rows, "y", 0, 1), (encode_pair, "y", 0, 0), (lift_rows, "y", 0, 3), (encode_pair, "y", 0, 1)]
         vector += [(add_bias, "y", 0, c, i) for i in range(2) for c in range(2)]
-        vector += [(lift_rows, "y", 1, 1), (weigh_snap, "y", 0, 0)] + both(encode_pair, "y", 1)
-        vector += both(add_bias, "y", 0, 2) + [(weigh_snap, "y", 0, 1)] + both(add_bias, "y", 0, 3)
+        vector += [(lift_rows, "y", 1, 1), (weigh_snap, "y", 0, 0)] + [(add_bias, "y", 0, 2, 0), (encode_half, "y", 1)]
+        vector += [(add_bias, "y", 0, 2, 1)] + [(weigh_snap, "y", 0, 1)] + both(add_bias, "y", 0, 3)
         vector += [(encode_pair, "x", 0, 0), (encode_fy, 0, 0), (encode_pair, "x", 0, 1)]
         vector += tiles(weigh_obs, "y", 1, 0) + [(weigh_snap, "y", 0, 2)] + both(add_bias, "x", 0, 0)
         vector += [(weigh_snap, "y", 0, 3)] + tiles(weigh_obs, "y", 1, 1) + [(encode_fy, 0, 1)]
-        vector += [(encode_pair, "x", 1, 0), (encode_fy, 1, 0), (weigh_words, "x", 0, 1)]
-        vector += [(weigh_obs, "y", 1, 4), (encode_pair, "x", 1, 1), (weigh_obs, "y", 1, 5)]
+        vector += [(encode_fy, 1, 0), (weigh_words, "x", 0, 1)]
+        vector += [(weigh_obs, "y", 1, 4), (encode_half, "x", 1), (weigh_obs, "y", 1, 5)]
         vector += tiles(weigh_obs, "y", 1, 3) + [(weigh_words, "x", 0, 2), (weigh_snap, "x", 0, 0)] + tiles(weigh_obs, "x", 1, 0)
         vector += [(encode_fx, 0), (encode_fy, 1, 1), (weigh_words, "x", 1, 1), (weigh_words, "x", 1, 2)]
         vector += both(add_bias, "x", 0, 3) + [(encode_fx, 1), (round_cross, 0, 0), (lift_word, "x", 1, 2)]
         vector += [(round_cross, 0, 1), (encode_fx, 2), (weigh_snap, "x", 0, 3)] + tiles(weigh_obs, "x", 1, 3)
         vector += units(round_cross, 1) + [(encode_fx, 3)]
-        vector += units(encode_plane, 0) + [(lift_plane, 1, 0), (round_cross, 2, 0), (encode_plane, 1, 0), (round_cross, 2, 1)]
-        vector += [(encode_plane, 1, 1), (round_cross, 3, 0), (lift_plane, 2, 0), (lift_plane, 3, 0)]
+        vector += [(encode_plane, 0, 0), (round_cross, 2, 0), (encode_plane, 0, 1), (lift_plane, 1, 0), (round_cross, 2, 1)]
+        vector += units(encode_plane, 1) + [(round_cross, 3, 0)] + both(lift_cross, 3, 1) + [(lift_plane, 3, 0)]
         vector += [(encode_plane, c, h) for h in range(2) for c in (2, 3)]
 
         sync = units(send_unit, 0, 1)

@@ -21,10 +21,10 @@ BANKS = 8
 ALIGN = 64
 SNAP = [("y", 0, c) for c in range(4)] + [("x", 0, c) for c in (0, 3)]
 WORD = [("x", 0, 1), ("x", 0, 2), ("x", 1, 1), ("x", 1, 2)]
-SORTED = [("y", 1, 0), ("y", 1, 1)]
+SORTED = [("y", 1, j) for j in range(4)]
 PAIRWISE = [("y", 0), ("x", 0)]
 FROM_BANK = [(3, 1)]
-DEPTH = {"sorted": 2, "pair": 2, "half": 1, "z": 3, "th": 3, "t": 4, "tw": 3, "v": 3, "f": 5, "r": 6, "s": 4, "u": 4, "u_tile": 2}
+DEPTH = {"sorted": 4, "pair": 2, "half": 1, "z": 3, "th": 3, "t": 4, "tw": 3, "v": 3, "f": 5, "r": 6, "s": 4, "u": 4, "u_tile": 2}
 FIRST = [("y", 0, 0, 0), ("y", 0, 1, 0)]
 
 
@@ -506,7 +506,7 @@ def tile_extendeddmdkoopmancrossmoment_x2_kernel(
         tensor += crosses(2) + both(turn_cross, 1)
         tensor += crosses(3) + units(turn_cross, 2, 3)
 
-        scalar = [(lift_rows, "y", 0, 0), (lift_rows, "y", 0, 2), (lift_bias_row,)] + pair(sort_rows, "y", 1, 0)
+        scalar = [(lift_rows, "y", 0, 0), (lift_rows, "y", 0, 2), (lift_bias_row,)] + four(sort_rows, "y", 1)
         scalar += [(widen_bias,), (tanh_snap, "y", 0, 0)] + [(lift_rows, "y", 1, j) for j in (0, 2, 3)]
         scalar += [(lift_bias_column,), (tanh_snap, "y", 0, 1)] + pair(lift_rows, "x", 0, 0) + [(lift_weights,)]
         scalar += tiles(tanh_obs, "y", 1, 0) + pair(lift_rows, "x", 0, 1) + [(tanh_snap, "y", 0, 2)]
@@ -534,8 +534,8 @@ def tile_extendeddmdkoopmancrossmoment_x2_kernel(
         vector += both(add_bias, "x", 0, 3) + [(encode_fx, 1), (round_cross, 0, 0), (lift_word, "x", 1, 2)]
         vector += [(round_cross, 0, 1), (encode_fx, 2), (weigh_snap, "x", 0, 3)] + tiles(weigh_obs, "x", 1, 3)
         vector += units(round_cross, 1) + [(encode_fx, 3)]
-        vector += [(encode_plane, 0, 0), (round_cross, 2, 0), (encode_plane, 0, 1), (lift_plane, 1, 0), (round_cross, 2, 1)]
-        vector += units(encode_plane, 1) + [(round_cross, 3, 0)] + both(lift_cross, 3, 1) + [(lift_plane, 3, 0)]
+        vector += units(encode_plane, 0) + [(lift_plane, 1, 0), (round_cross, 2, 0), (encode_plane, 1, 0), (round_cross, 2, 1)]
+        vector += [(encode_plane, 1, 1), (round_cross, 3, 0)] + both(lift_cross, 3, 1) + [(lift_plane, 3, 0)]
         vector += [(encode_plane, c, h) for h in range(2) for c in (2, 3)]
 
         sync = units(send_unit, 0, 1)

@@ -19,13 +19,12 @@ ALU = mybir.AluOpType
 
 BANKS = 8
 ALIGN = 64
-SNAP = [("y", 0, c) for c in range(4)] + [("x", 0, c) for c in (0, 3)]
-WORD = [("x", 0, 1), ("x", 0, 2), ("x", 1, 1), ("x", 1, 2)]
+POOL = [("y", 0, 0), ("y", 0, 2), ("y", 1, 0), ("y", 1, 2), ("x", 0, 0), ("x", 0, 1), ("x", 0, 2)]
+SNAP = POOL + [("y", 0, 1), ("x", 0, 3)]
 SORTED = [("y", 1, j) for j in range(4)]
-PAIRWISE = [("y", 0), ("x", 0)]
-FROM_BANK = [(3, 1)]
-DEPTH = {"sorted": 4, "pair": 2, "half": 1, "z": 3, "th": 3, "t": 4, "tw": 3, "v": 3, "f": 5, "r": 6, "s": 4, "u": 4, "u_tile": 2}
-FIRST = [("y", 0, 0, 0), ("y", 0, 1, 0)]
+PAIRWISE = [("y", 0)]
+TWICE = []
+DEPTH = {"bank": BANKS, "sorted": 4, "pair": 2, "half": 2, "z": 3, "th": 4, "t": 6, "f": 4, "run": 2, "r": 6, "s": 6, "u": 6}
 
 
 def tile_extendeddmdkoopmancrossmoment_x2_kernel(
@@ -41,21 +40,21 @@ def tile_extendeddmdkoopmancrossmoment_x2_kernel(
         made = {}
 
 
-        ident = keep.tile([P, P], F32, name="ident", align_bytes=64)
+        ident = keep.tile([P, P], F32, name="ident", align_bytes=ALIGN)
         make_identity(nc, ident[:])
 
         w_scale = keep.tile([P, SIZE], U8, name="w_scale", align_bytes=ALIGN)
         nc.vector.memset(w_scale[:].bitcast(I32), 0)
-        b_square = keep.tile([P, P], F32, name="b_square", align_bytes=64)
+        b_square = keep.tile([P, P], F32, name="b_square", align_bytes=ALIGN)
         nc.gpsimd.memset(b_square[:], 0.0)
 
-        b_rows = keep.tile([P, 8], BF16, name="b_rows", align_bytes=64)
+        b_rows = keep.tile([P, 8], BF16, name="b_rows", align_bytes=ALIGN)
         nc.scalar.dma_start(out=b_rows[:], in_=b.rearrange("(n w) -> n w", w=8))
 
         row_words = {}
 
         def load_rows(op, source, g, j, n):
-            rows = keep.tile([P, n, SIZE], BF16, name=f"rows_{op}{g}{j}", align_bytes=64)
+            rows = keep.tile([P, n, SIZE], BF16, name=f"rows_{op}{g}{j}", align_bytes=ALIGN)
             nc.sync.dma_start(
                 out=rows[:], in_=source.rearrange("(g p j) d -> g p j d", g=2, j=4)[g, :, j : j + n, :]
             )
@@ -80,11 +79,11 @@ def tile_extendeddmdkoopmancrossmoment_x2_kernel(
 
         weight = {}
 
-        def load_weights(op, source, queue):
-            weight[op] = keep.tile([P, 2, 4], BF16, name=f"weight_{op}", align_bytes=64)
-            queue.dma_start(out=weight[op][:], in_=source.rearrange("(g p j) -> p g j", g=2, j=4))
+        def load_weights(op, source):
+            weight[op] = keep.tile([P, 2, 4], BF16, name=f"weight_{op}", align_bytes=ALIGN)
+            nc.sync.dma_start(out=weight[op][:], in_=source.rearrange("(g p j) -> p g j", g=2, j=4))
 
-        b_tiles = keep.tile([8, P], BF16, name="b_tiles", align_bytes=64)
+        b_tiles = keep.tile([8, P], BF16, name="b_tiles", align_bytes=ALIGN)
 
         load_rows("y", y, 0, 0, 1)
         load_rows("y", y, 0, 1, 1)
@@ -95,28 +94,35 @@ def tile_extendeddmdkoopmancrossmoment_x2_kernel(
         load_rows("y", y, 1, 0, 2)
         load_rows("y", y, 1, 2, 2)
         nc.sync.dma_start(out=b_tiles[:], in_=b.rearrange("(m n) -> m n", n=P))
+        load_weights("y", q)
         load_w(slice(0, 2), 1)
-        load_weights("y", q, nc.sync)
-        load_weights("x", p, nc.sync)
+        load_weights("x", p)
         for g in range(2):
             for j in range(0, 4, 2):
                 load_rows("x", x, g, j, 2)
 
-        def new_bank(*key):
-            bank = psum.tile([P, 4, P], F32, name="bank", tag="bank", bufs=BANKS)
-            made["bank", key] = bank
-            return bank
+        def ring(tag, key, dims, dtype):
+            if (tag, key) not in made:
+                if tag == "bank":
+                    made[tag, key] = psum.tile(dims, dtype, name=tag, tag=tag, bufs=DEPTH[tag])
+                else:
+                    made[tag, key] = work.tile(dims, dtype, name=tag, tag=tag, bufs=DEPTH[tag], align_bytes=ALIGN)
+            return made[tag, key]
 
-        def work_tile(name, key, dims, dtype):
-            if (name, key) not in made:
-                made[name, key] = work.tile(dims, dtype, name=name, tag=name, bufs=DEPTH[name], align_bytes=64)
-            return made[name, key]
+        def bank_of(*key):
+            return ring("bank", key, [P, 4, P], F32)
 
         def copy(engine, out, in_):
             if engine == "S":
                 nc.scalar.copy(out=out, in_=in_)
             else:
                 nc.vector.tensor_copy(out=out, in_=in_)
+
+        def divide(engine, out, in_):
+            if engine == "S":
+                nc.scalar.activation(out=out, in_=in_, func=ACT.Copy, scale=INV_DIV)
+            else:
+                nc.vector.tensor_scalar(out=out, in0=in_, scalar1=INV_DIV, scalar2=None, op0=ALU.mult)
 
         def quantize(code, scale, in_):
             nc.vector.quantize_mx(out=code.bitcast(FP8X4), scales=scale, in_=in_)
@@ -129,12 +135,15 @@ def tile_extendeddmdkoopmancrossmoment_x2_kernel(
                 row_code[op, g] = keep.tile([P, 2, 4, P], U32, name=f"row_code_{op}{g}", align_bytes=ALIGN)
                 row_scale[op, g] = keep.tile([P, 2, 4, P], U8, name=f"row_scale_{op}{g}", align_bytes=ALIGN)
 
+        def half_key(op, g):
+            return ("half", (op, g))
+
         def sort_rows(engine, op, g, j):
-            words = work_tile("sorted", (op, g, j), [P, 2, 2, P], F32)
+            words = ring("sorted", (op, g, j), [P, 2, 2, P], F32)
             copy(engine, words[:], row_words[op, g, j].rearrange("p (n a e) -> p n e a", n=2, e=2))
 
         def turn_rows(engine, op, g, j):
-            bank = new_bank("rows", op, g, j)
+            bank = bank_of("rows", op, g, j)
             words = row_words[op, g, j]
             for n in range(2):
                 for e in range(2):
@@ -145,11 +154,11 @@ def tile_extendeddmdkoopmancrossmoment_x2_kernel(
                     nc.tensor.transpose(bank[:, 2 * n + e, :], columns, ident[:])
 
         def lift_rows(engine, op, g, j):
-            bank = made["bank", ("rows", op, g, j)]
+            bank = bank_of("rows", op, g, j)
             if (op, g) in PAIRWISE:
-                out = work_tile("pair", (op, g, j // 2), [P, 2, 2, P, 2], F32)[:, :, j % 2]
+                out = ring("pair", (op, g, j // 2), [P, 2, 2, P, 2], F32)[:, :, j % 2]
             else:
-                out = work_tile("half", (op, g), [P, 2, 4, P, 2], F32)[:, :, j]
+                out = ring(*half_key(op, g), [P, 2, 4, P, 2], F32)[:, :, j]
             copy(engine, out, bank[:].rearrange("p (n e) r -> p n r e", e=2))
 
         def encode_pair(engine, op, g, i):
@@ -166,34 +175,34 @@ def tile_extendeddmdkoopmancrossmoment_x2_kernel(
             quantize(
                 row_code[op, g][:].rearrange("p n j r -> p (n j r)"),
                 row_scale[op, g][:].rearrange("p n j r -> p (n j r)"),
-                made["half", (op, g)][:].rearrange("p n j r e -> p (n j r e)").bitcast(BF16),
+                made[half_key(op, g)][:].rearrange("p n j r e -> p (n j r e)").bitcast(BF16),
             )
 
 
-        bias_words = keep.tile([P, P, 4], F32, name="bias_words", align_bytes=64)
+        bias_words = keep.tile([P, P, 4], F32, name="bias_words", align_bytes=ALIGN)
         bias_row = bias_words[:].rearrange("p n m -> p (n m)").bitcast(BF16)
-        bias_column = keep.tile([P, 8], F32, name="bias_column", align_bytes=64)
+        bias_column = keep.tile([P, 8], F32, name="bias_column", align_bytes=ALIGN)
 
         def spread_bias(engine):
-            bank = new_bank("bias_row")
             words = b_rows[:].bitcast(F32)
             for m in range(4):
-                nc.tensor.transpose(bank[:, m, :], words[:, m : m + 1].to_broadcast([P, P]), ident[:])
+                nc.tensor.transpose(bank_of("bias_row")[:, m, :], words[:, m : m + 1].to_broadcast([P, P]), ident[:])
 
         def lift_bias_row(engine):
-            bank = made["bank", ("bias_row",)]
-            copy(engine, bias_words[:], bank[:].rearrange("p m n -> p n m"))
+            copy(engine, bias_words[:], bank_of("bias_row")[:].rearrange("p m n -> p n m"))
 
         def widen_bias(engine):
             copy(engine, b_square[0:8, :], b_tiles[:])
 
         def turn_bias(engine):
-            bank = new_bank("bias_column")
-            nc.tensor.transpose(bank[:, 0, :], b_square[:], ident[:])
+            nc.tensor.transpose(bank_of("bias_column")[:, 0, :], b_square[:], ident[:])
 
         def lift_bias_column(engine):
-            bank = made["bank", ("bias_column",)]
-            copy(engine, bias_column[:], bank[:, 0, 0:8])
+            copy(engine, bias_column[:], bank_of("bias_column")[:, 0, 0:8])
+
+        def repeat_weights(engine, op, g, c):
+            run = ring("run", (op, g, c), [P, 16, 4], BF16)
+            copy(engine, run[:], weight[op][:, g].unsqueeze(1).to_broadcast([P, 16, 4]))
 
 
         fy_code = {}
@@ -210,29 +219,38 @@ def tile_extendeddmdkoopmancrossmoment_x2_kernel(
             fx_code.append(code)
             fx_scale.append(scale)
 
-        def f_part(op, g, col, n):
+        def f_key(op, g, c):
+            return ("f", (op, g, c // 2) if op == "y" else (op, c))
+
+        def f_part(op, g, first, n):
+            tag, key = f_key(op, g, first // 256)
+            f = ring(tag, key, [P, 2048], BF16)
             if op == "y":
-                key, first = (op, g, col // 512), col % 512
-            else:
-                key, first = (op, col // 256), 256 * g + col % 256
-            f = work_tile("f", key, [P, 2048], BF16)
-            return f[:, 4 * first : 4 * (first + n)]
+                a = (first % 512) // 4
+                return f[:].rearrange("p (t a j) -> p t a j", t=4, j=4)[:, :, a : a + n // 4, :]
+            o = 256 * g + first % 256
+            return f[:, 4 * o : 4 * (o + n)].rearrange("p (t a j) -> p t a j", t=4, j=4)
+
+        def dealt(op):
+            return "(a t)" if op == "y" else "(t a)"
 
         def encode_fy(engine, g, h):
-            quantize(fy_code[g, h][:], fy_scale[g, h][:], made["f", ("y", g, h)][:])
+            quantize(fy_code[g, h][:], fy_scale[g, h][:], made[f_key("y", g, 2 * h)][:])
 
         def encode_fx(engine, c):
             quantize(
                 fx_code[c][:].rearrange("p g o -> p (g o)"),
                 fx_scale[c][:].rearrange("p g o -> p (g o)"),
-                made["f", ("x", c)][:],
+                made[f_key("x", 0, c)][:],
             )
 
+        def snap_sums(op, g, c, i):
+            return bank_of("snap", op, g, c, i)[:].rearrange("p (k a) r -> p k (a r)", k=2)
+
         def snap_pass(op, g, c, i, n):
-            sums = made["bank", ("snap", op, g, c, i)][:].rearrange("p (k a) r -> p k (a r)", k=2)
             for k in range(2):
                 nc.tensor.matmul_mx(
-                    out=sums[:, k, :],
+                    out=snap_sums(op, g, c, i)[:, k, :],
                     lhsT=row_code[op, g][:, n, 2 * i + k, :].bitcast(FP8X4),
                     lhsT_scale=row_scale[op, g][:, n, 2 * i + k, :],
                     rhs=w_code[:, n, 256 * c : 256 * c + 256].bitcast(FP8X4),
@@ -242,40 +260,50 @@ def tile_extendeddmdkoopmancrossmoment_x2_kernel(
                 )
 
         def dot_snap(engine, op, g, c, i):
-            new_bank("snap", op, g, c, i)
-            snap_pass(op, g, c, i, 0)
-            if (op, g, c, i) == FIRST[1]:
-                snap_pass(*FIRST[0], 1)
-            if (op, g, c, i) != FIRST[0]:
-                snap_pass(op, g, c, i, 1)
+            for n in range(2):
+                snap_pass(op, g, c, i, n)
+
+        def dot_first(engine):
+            for n in range(2):
+                for c in range(2):
+                    snap_pass("y", 0, c, 0, n)
 
         def add_bias(engine, op, g, c, i):
-            sums = made["bank", ("snap", op, g, c, i)][:].rearrange("p (k a) r -> p k (a r)", k=2)
-            z = work_tile("z", (op, g, c), [P, 2, 256, 2], F32)
+            z = ring("z", (op, g, c), [P, 2, 4, 64, 2], F32)
+            bias = bias_row[:, 256 * c : 256 * c + 256].rearrange(f"p {dealt(op)} -> p t a", t=4)
             nc.vector.tensor_tensor(
                 out=z[:, i],
-                in0=sums.rearrange("p k o -> p o k"),
-                in1=bias_row[:, 256 * c : 256 * c + 256].unsqueeze(2).to_broadcast([P, 256, 2]),
+                in0=snap_sums(op, g, c, i).rearrange(f"p k {dealt(op)} -> p t a k", t=4),
+                in1=bias.unsqueeze(3).to_broadcast([P, 4, 64, 2]),
                 op=ALU.add,
             )
 
         def tanh_snap(engine, op, g, c):
             z = made["z", (op, g, c)]
-            th = work_tile("th", (op, g, c), [P, 256, 2, 2], F32)
-            nc.scalar.activation(out=th[:], in_=z[:].rearrange("p i o k -> p o i k"), func=ACT.Tanh)
+            th = ring("th", (op, g, c), [P, 256, 2, 2], F32)
+            nc.scalar.activation(out=th[:], in_=z[:].rearrange("p i t a k -> p (t a) i k"), func=ACT.Tanh)
 
         def weigh_snap(engine, op, g, c):
-            th = made["th", (op, g, c)]
-            nc.vector.tensor_tensor(
-                out=f_part(op, g, 256 * c, 256).rearrange("p (o j) -> p o j", j=4),
-                in0=th[:].rearrange("p o i k -> p o (i k)"),
-                in1=weight[op][:, g, :].unsqueeze(1).to_broadcast([P, 256, 4]),
-                op=ALU.mult,
-            )
+            th = made["th", (op, g, c)][:].rearrange("p (t a) i k -> p t a (i k)", t=4)
+            out = f_part(op, g, 256 * c, 256)
+            if engine == "G":
+                run = made["run", (op, g, c)][:].rearrange("p r j -> p (r j)").unsqueeze(1).unsqueeze(1)
+                nc.gpsimd.tensor_tensor(
+                    out=out.rearrange("p t (a r) j -> p t a (r j)", r=16),
+                    in0=th.rearrange("p t (a r) j -> p t a (r j)", r=16),
+                    in1=run.to_broadcast([P, 4, 4, 64]),
+                    op=ALU.mult,
+                )
+            else:
+                nc.vector.tensor_tensor(
+                    out=out,
+                    in0=th,
+                    in1=weight[op][:, g, :].unsqueeze(1).unsqueeze(1).to_broadcast([P, 4, 64, 4]),
+                    op=ALU.mult,
+                )
 
         def dot_obs(engine, op, g, m):
-            bank = new_bank("obs", op, g, m)
-            sums = bank[:].rearrange("p j r -> p (j r)")
+            sums = bank_of("obs", op, g, m)[:].rearrange("p j r -> p (j r)")
             for n in range(2):
                 nc.tensor.matmul_mx(
                     out=sums,
@@ -288,92 +316,34 @@ def tile_extendeddmdkoopmancrossmoment_x2_kernel(
                 )
 
         def tanh_obs(engine, op, g, m):
-            sums = made["bank", ("obs", op, g, m)][:].rearrange("p j r -> p (j r)")
-            t = work_tile("t", (op, g, m), [P, 4, P], F32)
+            sums = bank_of("obs", op, g, m)[:].rearrange("p j r -> p (j r)")
+            t = ring("t", (op, g, m), [P, 4, P], F32)
             nc.scalar.activation(
                 out=t[:].rearrange("p j r -> p (j r)"), in_=sums, func=ACT.Tanh, bias=bias_column[:, m : m + 1]
             )
 
         def turn_obs(engine, op, g, m):
             t = made["t", (op, g, m)]
-            bank = new_bank("turned", op, g, m)
             for j in range(4):
-                nc.tensor.transpose(bank[:, j, :], t[:, j, :], ident[:])
+                nc.tensor.transpose(bank_of("turned", op, g, m)[:, j, :], t[:, j, :], ident[:])
 
         def weigh_obs(engine, op, g, m):
-            bank = made["bank", ("turned", op, g, m)]
             nc.vector.tensor_tensor(
-                out=f_part(op, g, P * m, P).rearrange("p (o j) -> p o j", j=4),
-                in0=bank[:].rearrange("p j o -> p o j"),
-                in1=weight[op][:, g, :].unsqueeze(1).to_broadcast([P, P, 4]),
+                out=f_part(op, g, P * m, P),
+                in0=bank_of("turned", op, g, m)[:].rearrange(f"p j {dealt(op)} -> p t a j", t=4),
+                in1=weight[op][:, g, :].unsqueeze(1).unsqueeze(1).to_broadcast([P, 4, 32, 4]),
                 op=ALU.mult,
             )
 
-        weight_row = keep.tile([P, 512], F32, name="weight_row", align_bytes=64)
 
-        def spread_weights(engine):
-            bank = new_bank("weight_row")
-            words = weight["x"][:].rearrange("p g j -> p (g j)").bitcast(F32)
-            for m in range(4):
-                nc.tensor.transpose(bank[:, m, :], words[:, m : m + 1].to_broadcast([P, P]), ident[:])
-
-        def lift_weights(engine):
-            copy(engine, weight_row[:], made["bank", ("weight_row",)][:].rearrange("p m r -> p (m r)"))
-
-        def tanh_word(engine, op, g, m):
-            sums = made["bank", ("obs", op, g, m)][:]
-            t = work_tile("tw", (op, g, m // 2), [P, 1024], F32)
-            nc.scalar.activation(
-                out=t[:, 512 * (m % 2) : 512 * (m % 2) + 512].rearrange("p (e r s) -> p e r s", e=2, s=2),
-                in_=sums.rearrange("p (e s) r -> p e r s", e=2),
-                func=ACT.Tanh,
-                bias=bias_column[:, m : m + 1],
-            )
-
-        def weigh_word(engine, op, g, m):
-            v = work_tile("v", (op, g, m // 2), [P, 1024], BF16)
-            nc.vector.tensor_tensor(
-                out=v[:, 512 * (m % 2) : 512 * (m % 2) + 512],
-                in0=made["tw", (op, g, m // 2)][:, 512 * (m % 2) : 512 * (m % 2) + 512],
-                in1=weight_row[:, 256 * g : 256 * g + 256].bitcast(BF16),
-                op=ALU.mult,
-            )
-
-        def weigh_words(engine, op, g, c):
-            v = work_tile("v", (op, g, c), [P, 1024], BF16)
-            nc.vector.tensor_tensor(
-                out=v[:].rearrange("p (k n) -> p k n", k=2),
-                in0=made["tw", (op, g, c)][:].rearrange("p (k n) -> p k n", k=2),
-                in1=weight_row[:, 256 * g : 256 * g + 256].bitcast(BF16).unsqueeze(1).to_broadcast([P, 2, 512]),
-                op=ALU.mult,
-            )
-
-        def turn_word(engine, op, g, c):
-            words = made["v", (op, g, c)][:].bitcast(F32)
-            bank = new_bank("word", op, g, c)
-            for n in range(4):
-                nc.tensor.transpose(bank[:, n, :], words[:, P * n : P * n + P], ident[:])
-
-        def lift_word(engine, op, g, c):
-            out = f_part(op, g, 256 * c, 256).bitcast(F32).rearrange("p (k o e) -> p k o e", k=2, e=2)
-            copy(engine, out, made["bank", ("word", op, g, c)][:].rearrange("p (k e) o -> p k o e", e=2))
-
-
-        plane_code = keep.tile([P, 2, SIZE], U32, name="plane_code", align_bytes=64)
-        plane_scale = keep.tile([P, SIZE], U8, name="plane_scale", align_bytes=64)
+        plane_code = keep.tile([P, 2, SIZE], U32, name="plane_code", align_bytes=ALIGN)
+        plane_scale = keep.tile([P, SIZE], U8, name="plane_scale", align_bytes=ALIGN)
         plane_words = out_1.rearrange("g p m t -> p g (m t)")
 
-        def divide(engine, out, in_):
-            if engine == "S":
-                nc.scalar.activation(out=out, in_=in_, func=ACT.Copy, scale=INV_DIV)
-            else:
-                nc.vector.tensor_scalar(out=out, in0=in_, scalar1=INV_DIV, scalar2=None, op0=ALU.mult)
-
         def cross(engine, c, h, k):
-            bank = new_bank("cross", c, h, k)
             for g in range(2):
                 nc.tensor.matmul_mx(
-                    out=bank[:].rearrange("p t a -> p (t a)"),
+                    out=bank_of("cross", c, h, k)[:].rearrange("p t a -> p (t a)"),
                     lhsT=fx_code[c][:, g, P * k : P * k + P].bitcast(FP8X4),
                     lhsT_scale=fx_scale[c][:, g, P * k : P * k + P],
                     rhs=fy_code[g, h][:].bitcast(FP8X4),
@@ -383,51 +353,54 @@ def tile_extendeddmdkoopmancrossmoment_x2_kernel(
                 )
 
         def lift_cross(engine, c, h, k):
-            r = work_tile("r", (c, h), [P, 2, 512], F32)
-            divide(engine, r[:, k, :], made["bank", ("cross", c, h, k)][:].rearrange("p t a -> p (t a)"))
-
-        def send_cross(engine, c, h, k):
-            rows = slice(256 * c + P * k, 256 * c + P * k + P)
-            nc.sync.dma_start(out=out_0[rows, 512 * h : 512 * h + 512], in_=made["r", (c, h)][:, k, :])
+            r = ring("r", (c, h), [P, 2, P, 4], F32)
+            divide(engine, r[:, k], bank_of("cross", c, h, k)[:].rearrange("p t a -> p a t"))
 
         def round_cross(engine, c, h):
-            s = work_tile("s", (c, h), [P, 2, 2, P, 2], BF16)
-            copy(engine, s[:], made["r", (c, h)][:].rearrange("p k (a e s) -> p k e a s", e=2, s=2))
-
-        def round_bank(engine, c, h, k):
-            sums = made["bank", ("cross", c, h, k)][:].rearrange("p t a -> p (t a)")
-            s = work_tile("s", (c, h), [P, 2, 2, P, 2], BF16)
-            divide(engine, s[:, k], sums.rearrange("p (a e s) -> p e a s", e=2, s=2))
+            s = ring("s", (c, h), [P, 2, 2, P, 2], BF16)
+            copy(engine, s[:], made["r", (c, h)][:].rearrange("p k a (e s) -> p k e a s", e=2))
 
         def turn_cross(engine, c, h):
             words = made["s", (c, h)][:].rearrange("p k e a s -> p (k e) (a s)").bitcast(F32)
-            bank = new_bank("plane", c, h)
             for n in range(4):
-                nc.tensor.transpose(bank[:, n, :], words[:, n, :], ident[:])
+                nc.tensor.transpose(bank_of("plane", c, h)[:, n, :], words[:, n, :], ident[:])
 
         def lift_plane(engine, c, h):
-            u = work_tile("u", (c, h), [P, 2, P, 2], F32)
-            copy(engine, u[:], made["bank", ("plane", c, h)][:].rearrange("p (k e) i -> p k i e", e=2))
+            u = ring("u", (c, h), [P, 2, P, 4], BF16)
+            words = u[:].rearrange("p k i t -> p (k i t)").bitcast(F32).rearrange("p (k i e) -> p k i e", k=2, e=2)
+            copy(engine, words, bank_of("plane", c, h)[:].rearrange("p (k e) i -> p k i e", e=2))
+
+        def cross_back(engine, c, h, k):
+            for t in range(4):
+                for g in range(2):
+                    nc.tensor.matmul_mx(
+                        out=bank_of("back", c, h, k)[:, t, :],
+                        lhsT=fy_code[g, h][:, P * t : P * t + P].bitcast(FP8X4),
+                        lhsT_scale=fy_scale[g, h][:, P * t : P * t + P],
+                        rhs=fx_code[c][:, g, P * k : P * k + P].bitcast(FP8X4),
+                        rhs_scale=fx_scale[c][:, g, P * k : P * k + P],
+                        start=(g == 0),
+                        stop=(g == 1),
+                    )
+
+        def lift_back(engine, c, h, k):
+            u = ring("u", (c, h), [P, 2, P, 4], BF16)
+            divide(engine, u[:, k], bank_of("back", c, h, k)[:].rearrange("p t i -> p i t"))
 
         def encode_plane(engine, c, h):
             cols = slice(256 * c, 256 * c + 256)
-            values = made["u", (c, h)][:].rearrange("p k i e -> p (k i e)").bitcast(BF16)
+            values = made["u", (c, h)][:].rearrange("p k i t -> p (k i t)")
             quantize(plane_code[:, h, cols], plane_scale[4 * h : P, cols], values)
 
-        def turn_tile(engine, c, h, k):
-            words = made["s", (c, h)][:, k].rearrange("p e a s -> p e (a s)").bitcast(F32)
-            bank = new_bank("plane", c, h, k)
-            for e in range(2):
-                nc.tensor.transpose(bank[:, e, :], words[:, e, :], ident[:])
+        def send_cross(engine, c, h, k):
+            rows = slice(256 * c + P * k, 256 * c + P * k + P)
+            values = made["r", (c, h)][:, k].rearrange("p a t -> p (a t)")
+            nc.sync.dma_start(out=out_0[rows, 512 * h : 512 * h + 512], in_=values)
 
-        def lift_tile(engine, c, h, k):
-            u = work_tile("u_tile", (c, h, k), [P, P, 2], F32)
-            copy(engine, u[:], made["bank", ("plane", c, h, k)][:, 0:2].rearrange("p e i -> p i e"))
-
-        def encode_tile(engine, c, h, k):
-            cols = slice(256 * c + P * k, 256 * c + P * k + P)
-            values = made["u_tile", (c, h, k)][:].rearrange("p i e -> p (i e)").bitcast(BF16)
-            quantize(plane_code[:, h, cols], plane_scale[4 * h : P, cols], values)
+        def send_unit(engine, c, h):
+            rows = out_0[256 * c : 256 * c + 256, 512 * h : 512 * h + 512]
+            values = made["r", (c, h)][:].rearrange("p k a t -> p k (a t)")
+            nc.sync.dma_start(out=rows.rearrange("(k p) n -> p k n", k=2), in_=values)
 
         def send_plane(engine, c):
             nc.sync.dma_start(
@@ -435,20 +408,10 @@ def tile_extendeddmdkoopmancrossmoment_x2_kernel(
                 in_=plane_code[:, :, 256 * c : 256 * c + 256].bitcast(I32),
             )
 
-        def send_half_plane(engine, c, h):
-            nc.sync.dma_start(
-                out=plane_words[:, h, 1024 * c : 1024 * c + 1024].bitcast(I32),
-                in_=plane_code[:, h, 256 * c : 256 * c + 256].bitcast(I32),
-            )
-
         def send_last_planes(engine, h):
             nc.sync.dma_start(
                 out=plane_words[:, h, 2048:4096].bitcast(I32), in_=plane_code[:, h, 512:1024].bitcast(I32)
             )
-
-        def send_unit(engine, c, h):
-            rows = out_0[256 * c : 256 * c + 256, 512 * h : 512 * h + 512]
-            nc.sync.dma_start(out=rows.rearrange("(k p) n -> p k n", k=2), in_=made["r", (c, h)][:])
 
         def send_scales(engine):
             for quad in range(4):
@@ -468,180 +431,184 @@ def tile_extendeddmdkoopmancrossmoment_x2_kernel(
         def tiles(step, op, g, c):
             return [(step, op, g, 2 * c), (step, op, g, 2 * c + 1)]
 
-        def crosses(c):
-            return both(cross, c, 0) + both(cross, c, 1)
-
-        def weave(a, b):
-            out = []
-            for k in range(max(len(a), len(b))):
-                out += a[k : k + 1] + b[k : k + 1]
-            return out
+        def banks(step, c):
+            return both(step, c, 0) + both(step, c, 1)
 
         def pair(step, op, g, i):
             return [(step, op, g, 2 * i), (step, op, g, 2 * i + 1)]
 
-        def units(step, *panels):
-            return [(step, c, h) for c in panels for h in range(2)]
-
-        def lifts(c):
-            return both(lift_cross, c, 0) + both(lift_cross, c, 1)
-
         tensor = pair(turn_rows, "y", 0, 0) + [(spread_bias,)] + pair(turn_rows, "y", 0, 1)
-        tensor += [(dot_snap, "y", 0, c, i) for i in range(2) for c in range(2)]
-        tensor += pair(turn_rows, "y", 1, 0) + pair(turn_rows, "y", 1, 1) + [(turn_bias,)]
-        tensor += both(dot_snap, "y", 0, 2) + pair(turn_rows, "x", 0, 0) + [(spread_weights,)]
-        tensor += both(dot_snap, "y", 0, 3) + tiles(dot_obs, "y", 1, 0)
-        tensor += pair(turn_rows, "x", 0, 1) + tiles(turn_obs, "y", 1, 0)
-        tensor += tiles(dot_obs, "y", 1, 1) + both(dot_snap, "x", 0, 0)
+        tensor += [(dot_first,), (dot_snap, "y", 0, 0, 1), (dot_snap, "y", 0, 1, 1)]
+        tensor += four(turn_rows, "y", 1)
+        tensor += both(dot_snap, "y", 0, 2) + pair(turn_rows, "x", 0, 0) + [(turn_bias,)]
+        tensor += tiles(dot_obs, "y", 0, 3) + both(dot_snap, "y", 1, 0)
+        tensor += pair(turn_rows, "x", 0, 1) + tiles(turn_obs, "y", 0, 3)
+        tensor += tiles(dot_obs, "y", 1, 1) + both(dot_snap, "y", 1, 2)
         tensor += pair(turn_rows, "x", 1, 0) + tiles(turn_obs, "y", 1, 1)
-        tensor += tiles(dot_obs, "y", 1, 2) + tiles(dot_obs, "x", 0, 1)
-        tensor += pair(turn_rows, "x", 1, 1) + tiles(turn_obs, "y", 1, 2)
-        tensor += tiles(dot_obs, "y", 1, 3) + tiles(dot_obs, "x", 0, 2)
-        tensor += tiles(turn_obs, "y", 1, 3) + [(turn_word, "x", 0, 1)]
-        tensor += tiles(dot_obs, "x", 1, 0) + tiles(dot_obs, "x", 1, 1)
-        tensor += tiles(turn_obs, "x", 1, 0) + [(turn_word, "x", 0, 2)]
-        tensor += tiles(dot_obs, "x", 1, 2) + both(dot_snap, "x", 0, 3) + crosses(0)
-        tensor += [(turn_word, "x", 1, 1), (turn_word, "x", 1, 2)]
-        tensor += tiles(dot_obs, "x", 1, 3) + crosses(1) + tiles(turn_obs, "x", 1, 3) + both(turn_cross, 0)
-        tensor += crosses(2) + both(turn_cross, 1)
-        tensor += crosses(3) + units(turn_cross, 2, 3)
+        tensor += tiles(dot_obs, "y", 1, 3) + both(dot_snap, "x", 0, 0)
+        tensor += pair(turn_rows, "x", 1, 1) + tiles(turn_obs, "y", 1, 3)
+        tensor += both(dot_snap, "x", 0, 1) + both(dot_snap, "x", 0, 2) + tiles(dot_obs, "x", 1, 0) + tiles(dot_obs, "x", 1, 1)
+        tensor += tiles(turn_obs, "x", 1, 0)
+        tensor += tiles(dot_obs, "x", 1, 2) + both(dot_snap, "x", 0, 3) + tiles(dot_obs, "x", 1, 3)
+        tensor += tiles(turn_obs, "x", 1, 1)
+        tensor += banks(cross, 0) + tiles(turn_obs, "x", 1, 2)
+        tensor += banks(cross, 1) + tiles(turn_obs, "x", 1, 3)
+        tensor += banks(cross, 2) + both(turn_cross, 0)
+        tensor += banks(cross, 3) + both(turn_cross, 1) + both(turn_cross, 2) + both(turn_cross, 3)
 
         scalar = [(lift_rows, "y", 0, 0), (lift_rows, "y", 0, 2), (lift_bias_row,)] + four(sort_rows, "y", 1)
-        scalar += [(widen_bias,), (tanh_snap, "y", 0, 0)] + [(lift_rows, "y", 1, j) for j in (0, 2, 3)]
-        scalar += [(lift_bias_column,), (tanh_snap, "y", 0, 1)] + pair(lift_rows, "x", 0, 0) + [(lift_weights,)]
-        scalar += tiles(tanh_obs, "y", 1, 0) + pair(lift_rows, "x", 0, 1) + [(tanh_snap, "y", 0, 2)]
-        scalar += tiles(tanh_obs, "y", 1, 1) + [(tanh_snap, "y", 0, 3)] + pair(lift_rows, "x", 1, 0)
-        scalar += tiles(tanh_obs, "y", 1, 2) + tiles(tanh_word, "x", 0, 1) + pair(lift_rows, "x", 1, 1)
-        scalar += tiles(tanh_obs, "y", 1, 3) + tiles(tanh_word, "x", 0, 2) + [(tanh_snap, "x", 0, 0)]
-        scalar += tiles(tanh_obs, "x", 1, 0) + [(lift_word, "x", 0, 1)]
-        scalar += tiles(tanh_word, "x", 1, 1) + tiles(tanh_word, "x", 1, 2) + [(lift_word, "x", 0, 2)]
-        scalar += both(lift_cross, 0, 0) + [(lift_cross, 0, 1, 0), (lift_word, "x", 1, 1), (lift_cross, 0, 1, 1)]
-        scalar += [(tanh_snap, "x", 0, 3)] + tiles(tanh_obs, "x", 1, 3) + lifts(1) + units(lift_plane, 0)
-        scalar += lifts(2) + [(lift_plane, 1, 1)] + both(lift_cross, 3, 0) + both(round_bank, 3, 1)
-        scalar += units(lift_plane, 2) + [(lift_plane, 3, 1)]
+        scalar += [(lift_rows, "y", 1, 0), (widen_bias,), (lift_rows, "y", 1, 3), (tanh_snap, "y", 0, 0)]
+        scalar += [(tanh_snap, "y", 0, 1), (lift_bias_column,)] + tiles(tanh_obs, "y", 0, 3) + [(tanh_snap, "y", 0, 2)]
+        scalar += pair(lift_rows, "x", 0, 1) + tiles(tanh_obs, "y", 1, 1) + [(tanh_snap, "y", 1, 0)]
+        scalar += pair(lift_rows, "x", 1, 0) + tiles(tanh_obs, "y", 1, 3) + [(tanh_snap, "y", 1, 2)] + pair(lift_rows, "x", 1, 1)
+        scalar += [(tanh_snap, "x", 0, 0)]
+        scalar += tiles(tanh_obs, "x", 1, 0) + tiles(tanh_obs, "x", 1, 1) + [(tanh_snap, "x", 0, 1)]
+        scalar += tiles(tanh_obs, "x", 1, 2) + [(tanh_snap, "x", 0, 2)] + tiles(tanh_obs, "x", 1, 3)
+        scalar += [(lift_cross, 0, 0, 0), (tanh_snap, "x", 0, 3), (round_cross, 0, 0), (lift_cross, 1, 0, 0), (round_cross, 0, 1)]
+        scalar += both(lift_cross, 1, 1) + banks(lift_cross, 2) + both(lift_plane, 0) + banks(lift_cross, 3) + both(lift_plane, 1)
+        scalar += [(lift_plane, 2, 0), (lift_plane, 2, 1), (lift_plane, 3, 1)]
 
         vector = [(lift_rows, "y", 0, 1), (encode_pair, "y", 0, 0), (lift_rows, "y", 0, 3), (encode_pair, "y", 0, 1)]
         vector += [(add_bias, "y", 0, c, i) for i in range(2) for c in range(2)]
-        vector += [(lift_rows, "y", 1, 1), (weigh_snap, "y", 0, 0)] + [(add_bias, "y", 0, 2, 0), (encode_half, "y", 1)]
-        vector += [(add_bias, "y", 0, 2, 1)] + [(weigh_snap, "y", 0, 1)] + both(add_bias, "y", 0, 3)
-        vector += [(encode_pair, "x", 0, 0), (encode_fy, 0, 0), (encode_pair, "x", 0, 1)]
-        vector += tiles(weigh_obs, "y", 1, 0) + [(weigh_snap, "y", 0, 2)] + both(add_bias, "x", 0, 0)
-        vector += [(weigh_snap, "y", 0, 3)] + tiles(weigh_obs, "y", 1, 1) + [(encode_fy, 0, 1)]
-        vector += [(encode_fy, 1, 0), (weigh_words, "x", 0, 1)]
-        vector += [(weigh_obs, "y", 1, 4), (encode_half, "x", 1), (weigh_obs, "y", 1, 5)]
-        vector += tiles(weigh_obs, "y", 1, 3) + [(weigh_words, "x", 0, 2), (weigh_snap, "x", 0, 0)] + tiles(weigh_obs, "x", 1, 0)
-        vector += [(encode_fx, 0), (encode_fy, 1, 1), (weigh_words, "x", 1, 1), (weigh_words, "x", 1, 2)]
-        vector += both(add_bias, "x", 0, 3) + [(encode_fx, 1), (round_cross, 0, 0), (lift_word, "x", 1, 2)]
-        vector += [(round_cross, 0, 1), (encode_fx, 2), (weigh_snap, "x", 0, 3)] + tiles(weigh_obs, "x", 1, 3)
-        vector += units(round_cross, 1) + [(encode_fx, 3)]
-        vector += units(encode_plane, 0) + [(lift_plane, 1, 0), (round_cross, 2, 0), (encode_plane, 1, 0), (round_cross, 2, 1)]
-        vector += [(encode_plane, 1, 1), (round_cross, 3, 0)] + both(lift_cross, 3, 1) + [(lift_plane, 3, 0)]
-        vector += [(encode_plane, c, h) for h in range(2) for c in (2, 3)]
+        vector += [(lift_rows, "y", 1, 1), (lift_rows, "y", 1, 2), (add_bias, "y", 0, 2, 0), (encode_half, "y", 1), (repeat_weights, "y", 0, 0)]
+        vector += [(add_bias, "y", 0, 2, 1)] + pair(lift_rows, "x", 0, 0) + both(add_bias, "y", 1, 0)
+        vector += [(weigh_snap, "y", 0, 1), (repeat_weights, "y", 0, 2)] + tiles(weigh_obs, "y", 0, 3) + both(add_bias, "y", 1, 2)
+        vector += [(encode_half, "x", 0), (encode_fy, 0, 0), (repeat_weights, "y", 1, 0)]
+        vector += tiles(weigh_obs, "y", 1, 1) + both(add_bias, "x", 0, 0)
+        vector += [(encode_fy, 0, 1), (encode_fy, 1, 0), (encode_half, "x", 1), (repeat_weights, "y", 1, 2), (repeat_weights, "x", 0, 0)]
+        vector += tiles(weigh_obs, "y", 1, 3) + both(add_bias, "x", 0, 1) + both(add_bias, "x", 0, 2)
+        vector += tiles(weigh_obs, "x", 1, 0) + [(encode_fx, 0), (encode_fy, 1, 1), (repeat_weights, "x", 0, 1)]
+        vector += both(add_bias, "x", 0, 3) + tiles(weigh_obs, "x", 1, 1) + [(lift_cross, 0, 0, 1), (encode_fx, 1), (repeat_weights, "x", 0, 2)]
+        vector += both(lift_cross, 0, 1) + tiles(weigh_obs, "x", 1, 2) + [(lift_cross, 1, 0, 1), (encode_fx, 2)]
+        vector += tiles(weigh_obs, "x", 1, 3) + [(weigh_snap, "x", 0, 3), (round_cross, 1, 0), (encode_fx, 3), (round_cross, 1, 1)]
+        vector += both(round_cross, 2) + [(encode_plane, 0, 0), (round_cross, 3, 0), (encode_plane, 0, 1), (round_cross, 3, 1)]
+        vector += [(encode_plane, 1, 0), (lift_plane, 3, 0), (encode_plane, 1, 1)] + [(encode_plane, c, h) for h in range(2) for c in (2, 3)]
 
-        sync = units(send_unit, 0, 1)
-        sync += both(send_cross, 2, 0) + [(send_plane, 0)] + both(send_cross, 2, 1) + both(send_cross, 3, 0) + [(send_plane, 1)]
-        sync += both(send_cross, 3, 1) + both(send_last_planes) + [(send_scales,)]
+        pool = [(weigh_snap,) + key for key in POOL]
+
+        sync = both(send_unit, 0) + both(send_unit, 1) + banks(send_cross, 2) + both(send_cross, 3, 0) + both(send_cross, 3, 1)
+        sync += both(send_plane) + both(send_last_planes) + [(send_scales,)]
 
 
         reads = {}
+        touches = {}
+
+        def wire(step, sources, *tiles_touched):
+            reads[step] = list(sources)
+            touches[step] = list(tiles_touched)
 
         def weighed(op, g, c):
-            if (op, g, c) in SNAP:
-                return [(weigh_snap, op, g, c)]
-            if (op, g, c) in WORD:
-                return [(lift_word, op, g, c)]
-            return tiles(weigh_obs, op, g, c)
+            return [(weigh_snap, op, g, c)] if (op, g, c) in SNAP else tiles(weigh_obs, op, g, c)
 
-        def planes(c, h):
-            return [(encode_plane, c, h)] if (encode_plane, c, h) in vector else both(encode_tile, c, h)
-
-        reads[spread_bias,] = []
-        reads[lift_bias_row,] = [(spread_bias,)]
-        reads[widen_bias,] = []
-        reads[turn_bias,] = [(widen_bias,)]
-        reads[lift_bias_column,] = [(turn_bias,)]
-        reads[spread_weights,] = []
-        reads[lift_weights,] = [(spread_weights,)]
+        wire((spread_bias,), [], ("bank", ("bias_row",)))
+        wire((lift_bias_row,), [(spread_bias,)], ("bank", ("bias_row",)))
+        wire((widen_bias,), [])
+        wire((turn_bias,), [(widen_bias,)], ("bank", ("bias_column",)))
+        wire((lift_bias_column,), [(turn_bias,)], ("bank", ("bias_column",)))
+        first_banks = [("bank", ("snap", "y", 0, c, 0)) for c in range(2)]
+        wire((dot_first,), [(encode_pair, "y", 0, 0)], *first_banks)
         for op in ("y", "x"):
             for g in range(2):
                 for j in range(4):
-                    if (op, g, j) in SORTED:
-                        reads[sort_rows, op, g, j] = []
-                    reads[turn_rows, op, g, j] = [(sort_rows, op, g, j)] if (op, g, j) in SORTED else []
-                    reads[lift_rows, op, g, j] = [(turn_rows, op, g, j)]
+                    key = (op, g, j)
+                    bank = ("bank", ("rows",) + key)
+                    lifted = ("pair", (op, g, j // 2)) if (op, g) in PAIRWISE else half_key(op, g)
+                    if key in SORTED:
+                        wire((sort_rows,) + key, [], ("sorted", key))
+                        wire((turn_rows,) + key, [(sort_rows,) + key], bank, ("sorted", key))
+                    else:
+                        wire((turn_rows,) + key, [], bank)
+                    wire((lift_rows,) + key, [(turn_rows,) + key], bank, lifted)
                 if (op, g) in PAIRWISE:
                     coded = both(encode_pair, op, g)
                     for i in range(2):
-                        reads[coded[i]] = [(lift_rows, op, g, 2 * i + k) for k in range(2)]
+                        wire(coded[i], pair(lift_rows, op, g, i), ("pair", (op, g, i)))
                 else:
                     coded = [(encode_half, op, g)] * 2
-                    reads[coded[0]] = four(lift_rows, op, g)
+                    wire(coded[0], four(lift_rows, op, g), half_key(op, g))
                 for c in range(4):
-                    if (op, g, c) in SNAP:
+                    key = (op, g, c)
+                    if key in SNAP:
                         for i in range(2):
-                            reads[dot_snap, op, g, c, i] = [coded[i]]
-                            reads[add_bias, op, g, c, i] = [(dot_snap, op, g, c, i), (lift_bias_row,)]
-                        reads[tanh_snap, op, g, c] = both(add_bias, op, g, c)
-                        reads[weigh_snap, op, g, c] = [(tanh_snap, op, g, c)]
+                            bank = ("bank", ("snap",) + key + (i,))
+                            dot = (dot_first,) if bank in first_banks else (dot_snap,) + key + (i,)
+                            if bank not in first_banks:
+                                wire(dot, [coded[i]], bank)
+                            wire((add_bias,) + key + (i,), [dot, (lift_bias_row,)], bank, ("z", key))
+                        wire((tanh_snap,) + key, both(add_bias, *key), ("z", key), ("th", key))
+                        if key in POOL:
+                            wire((repeat_weights,) + key, [], ("run", key))
+                            sources = [(tanh_snap,) + key, (repeat_weights,) + key]
+                            wire((weigh_snap,) + key, sources, ("th", key), f_key(*key), ("run", key))
+                        else:
+                            wire((weigh_snap,) + key, [(tanh_snap,) + key], ("th", key), f_key(*key))
                         continue
                     for m in (2 * c, 2 * c + 1):
-                        reads[dot_obs, op, g, m] = coded
-                        if (op, g, c) in WORD:
-                            reads[tanh_word, op, g, m] = [(dot_obs, op, g, m), (lift_bias_column,)]
-                            reads[weigh_word, op, g, m] = [(tanh_word, op, g, m), (lift_weights,)]
-                        else:
-                            reads[tanh_obs, op, g, m] = [(dot_obs, op, g, m), (lift_bias_column,)]
-                            reads[turn_obs, op, g, m] = [(tanh_obs, op, g, m)]
-                            reads[weigh_obs, op, g, m] = [(turn_obs, op, g, m)]
-                    if (op, g, c) in WORD:
-                        reads[weigh_words, op, g, c] = tiles(tanh_word, op, g, c) + [(lift_weights,)]
-                        whole = (weigh_words, op, g, c) in vector
-                        reads[turn_word, op, g, c] = [(weigh_words, op, g, c)] if whole else tiles(weigh_word, op, g, c)
-                        reads[lift_word, op, g, c] = [(turn_word, op, g, c)]
+                        tile = (op, g, m)
+                        sums, turned = ("bank", ("obs",) + tile), ("bank", ("turned",) + tile)
+                        wire((dot_obs,) + tile, coded, sums)
+                        wire((tanh_obs,) + tile, [(dot_obs,) + tile, (lift_bias_column,)], sums, ("t", tile))
+                        wire((turn_obs,) + tile, [(tanh_obs,) + tile], turned, ("t", tile))
+                        wire((weigh_obs,) + tile, [(turn_obs,) + tile], turned, f_key(*key))
         for g in range(2):
             for h in range(2):
-                reads[encode_fy, g, h] = weighed("y", g, 2 * h) + weighed("y", g, 2 * h + 1)
+                wire((encode_fy, g, h), weighed("y", g, 2 * h) + weighed("y", g, 2 * h + 1), f_key("y", g, 2 * h))
         for c in range(4):
-            reads[encode_fx, c] = weighed("x", 0, c) + weighed("x", 1, c)
+            wire((encode_fx, c), weighed("x", 0, c) + weighed("x", 1, c), f_key("x", 0, c))
             for h in range(2):
+                unit = (c, h)
+                coded = [(encode_fx, c), (encode_fy, 0, h), (encode_fy, 1, h)]
                 for k in range(2):
-                    reads[cross, c, h, k] = [(encode_fx, c), (encode_fy, 0, h), (encode_fy, 1, h)]
-                    reads[lift_cross, c, h, k] = [(cross, c, h, k)]
-                    if (c, h) in FROM_BANK:
-                        reads[lift_cross, c, h, k].append((round_bank, c, h, k))
-                    reads[send_cross, c, h, k] = [(lift_cross, c, h, k)]
-                    reads[round_bank, c, h, k] = [(cross, c, h, k)]
-                    reads[turn_tile, c, h, k] = [(round_bank, c, h, k)]
-                    reads[lift_tile, c, h, k] = [(turn_tile, c, h, k)]
-                    reads[encode_tile, c, h, k] = [(lift_tile, c, h, k)]
-                reads[round_cross, c, h] = both(lift_cross, c, h)
-                reads[turn_cross, c, h] = both(round_bank, c, h) if (c, h) in FROM_BANK else [(round_cross, c, h)]
-                reads[lift_plane, c, h] = [(turn_cross, c, h)]
-                reads[encode_plane, c, h] = [(lift_plane, c, h)]
-                reads[send_unit, c, h] = both(lift_cross, c, h)
-                reads[send_half_plane, c, h] = planes(c, h)
-            reads[send_plane, c] = planes(c, 0) + planes(c, 1)
-        for h in range(2):
-            reads[send_last_planes, h] = planes(2, h) + planes(3, h)
-        reads[send_scales,] = [name for c in range(4) for h in range(2) for name in planes(c, h)]
+                    bank = ("bank", ("cross", c, h, k))
+                    wire((cross, c, h, k), coded, bank)
+                    wire((lift_cross, c, h, k), [(cross, c, h, k)], bank, ("r", unit))
+                    if (send_cross, c, h, k) in sync:
+                        wire((send_cross, c, h, k), [(lift_cross, c, h, k)], ("r", unit))
+                if (send_unit, c, h) in sync:
+                    wire((send_unit, c, h), both(lift_cross, c, h), ("r", unit))
+                if unit in TWICE:
+                    for k in range(2):
+                        bank = ("bank", ("back", c, h, k))
+                        wire((cross_back, c, h, k), coded, bank)
+                        wire((lift_back, c, h, k), [(cross_back, c, h, k)], bank, ("u", unit))
+                    wire((encode_plane, c, h), both(lift_back, c, h), ("u", unit))
+                else:
+                    bank = ("bank", ("plane", c, h))
+                    wire((round_cross, c, h), both(lift_cross, c, h), ("r", unit), ("s", unit))
+                    wire((turn_cross, c, h), [(round_cross, c, h)], bank, ("s", unit))
+                    wire((lift_plane, c, h), [(turn_cross, c, h)], bank, ("u", unit))
+                    wire((encode_plane, c, h), [(lift_plane, c, h)], ("u", unit))
+        for n in range(2):
+            wire((send_plane, n), both(encode_plane, n))
+            wire((send_last_planes, n), [(encode_plane, 2, n), (encode_plane, 3, n)])
+        wire((send_scales,), [(encode_plane, c, h) for c in range(4) for h in range(2)])
 
-        reads[(add_bias,) + FIRST[0]].append((dot_snap,) + FIRST[1])
-        queues = {"V": vector, "S": scalar, "Q": sync, "T": list(tensor)}
-        users = {name: [user for user in vector + scalar if name in reads[user]] for name in tensor}
+
+        queues = {"V": vector, "S": scalar, "G": pool, "Q": sync, "T": tensor}
+        assert sorted(map(str, reads)) == sorted(str(step) for queue in queues.values() for step in queue)
+        given = {tag: [] for tag in DEPTH}
         written = set()
+
+        def place_free(step):
+            for tag in DEPTH:
+                new = [tile for tile in touches[step] if tile[0] == tag and tile not in given[tag]]
+                count = len(given[tag]) + len(new) - DEPTH[tag]
+                for old in given[tag][: max(count, 0)]:
+                    if not all(user in written for user in touches if old in touches[user]):
+                        return False
+            return True
+
         while any(queues.values()):
             progress = False
             for engine, queue in queues.items():
-                while queue and all(source in written for source in reads[queue[0]]):
-                    name = queue[0]
-                    if engine == "T":
-                        n = tensor.index(name)
-                        if n >= BANKS and not all(user in written for user in users[tensor[n - BANKS]]):
-                            break
-                    name[0](engine, *name[1:])
-                    written.add(name)
-                    queue.remove(name)
+                while queue and all(source in written for source in reads[queue[0]]) and place_free(queue[0]):
+                    step = queue.pop(0)
+                    for tile in touches[step]:
+                        if tile not in given[tile[0]]:
+                            given[tile[0]].append(tile)
+                    step[0](engine, *step[1:])
+                    written.add(step)
                     progress = True
                     if engine == "T":
                         break
-            assert progress
+            assert progress, [(queue[0][0], queue[0][1:]) for queue in queues.values() if queue]

@@ -21,10 +21,12 @@ BANKS = 8
 ALIGN = 64
 POOL = [("y", 0, 0), ("y", 0, 2), ("y", 1, 0), ("y", 1, 2), ("x", 0, 0), ("x", 0, 1), ("x", 0, 2)]
 SNAP = POOL + [("y", 0, 1), ("x", 0, 3)]
-SORTED = [("y", 1, j) for j in range(4)]
+SORTED = [(op, 1, j) for op in ("y", "x") for j in range(4)]
 PAIRWISE = [("y", 0)]
-TWICE = []
-DEPTH = {"bank": BANKS, "sorted": 4, "pair": 2, "half": 2, "z": 3, "th": 4, "t": 6, "f": 4, "run": 2, "r": 6, "s": 6, "u": 6}
+TWICE = [(3, 1)]
+FROM_BANK = []
+SCALAR_QUADS = (1, 3)
+DEPTH = {"bank": BANKS, "sorted": 4, "pair": 2, "half": 2, "z": 3, "th": 4, "t": 6, "f": 6, "run": 3, "r": 6, "s": 5, "u": 5}
 
 
 def tile_extendeddmdkoopmancrossmoment_x2_kernel(
@@ -360,6 +362,10 @@ def tile_extendeddmdkoopmancrossmoment_x2_kernel(
             s = ring("s", (c, h), [P, 2, 2, P, 2], BF16)
             copy(engine, s[:], made["r", (c, h)][:].rearrange("p k a (e s) -> p k e a s", e=2))
 
+        def round_bank(engine, c, h, k):
+            s = ring("s", (c, h), [P, 2, 2, P, 2], BF16)
+            divide(engine, s[:, k], bank_of("cross", c, h, k)[:].rearrange("p (e s) a -> p e a s", e=2))
+
         def turn_cross(engine, c, h):
             words = made["s", (c, h)][:].rearrange("p k e a s -> p (k e) (a s)").bitcast(F32)
             for n in range(4):
@@ -408,14 +414,15 @@ def tile_extendeddmdkoopmancrossmoment_x2_kernel(
                 in_=plane_code[:, :, 256 * c : 256 * c + 256].bitcast(I32),
             )
 
-        def send_last_planes(engine, h):
+        def send_pass(engine, h, c, n):
             nc.sync.dma_start(
-                out=plane_words[:, h, 2048:4096].bitcast(I32), in_=plane_code[:, h, 512:1024].bitcast(I32)
+                out=plane_words[:, h, 1024 * c : 1024 * (c + n)].bitcast(I32),
+                in_=plane_code[:, h, 256 * c : 256 * (c + n)].bitcast(I32),
             )
 
         def send_scales(engine):
             for quad in range(4):
-                queue = nc.scalar if quad % 2 == 1 else nc.sync
+                queue = nc.scalar if quad in SCALAR_QUADS else nc.sync
                 queue.dma_start(
                     out=out_2[:, 4 * quad : 4 * quad + 4, :].bitcast(I32),
                     in_=plane_scale[32 * quad : 32 * quad + 8, :].bitcast(I32),
@@ -448,46 +455,46 @@ def tile_extendeddmdkoopmancrossmoment_x2_kernel(
         tensor += tiles(dot_obs, "y", 1, 3) + both(dot_snap, "x", 0, 0)
         tensor += pair(turn_rows, "x", 1, 1) + tiles(turn_obs, "y", 1, 3)
         tensor += both(dot_snap, "x", 0, 1) + both(dot_snap, "x", 0, 2) + tiles(dot_obs, "x", 1, 0) + tiles(dot_obs, "x", 1, 1)
-        tensor += tiles(turn_obs, "x", 1, 0)
+        tensor += tiles(turn_obs, "x", 1, 0) + tiles(turn_obs, "x", 1, 1)
         tensor += tiles(dot_obs, "x", 1, 2) + both(dot_snap, "x", 0, 3) + tiles(dot_obs, "x", 1, 3)
-        tensor += tiles(turn_obs, "x", 1, 1)
-        tensor += banks(cross, 0) + tiles(turn_obs, "x", 1, 2)
-        tensor += banks(cross, 1) + tiles(turn_obs, "x", 1, 3)
-        tensor += banks(cross, 2) + both(turn_cross, 0)
-        tensor += banks(cross, 3) + both(turn_cross, 1) + both(turn_cross, 2) + both(turn_cross, 3)
+        tensor += tiles(turn_obs, "x", 1, 2) + tiles(turn_obs, "x", 1, 3)
+        tensor += [(cross, c, h, k) for h in range(2) for c in range(2) for k in range(2)] + banks(cross, 2)
+        tensor += [(turn_cross, c, h) for h in range(2) for c in range(2)]
+        tensor += both(cross, 3, 0) + both(cross_back, 3, 1) + both(cross, 3, 1) + [(turn_cross, 2, 0), (turn_cross, 3, 0), (turn_cross, 2, 1)]
 
         scalar = [(lift_rows, "y", 0, 0), (lift_rows, "y", 0, 2), (lift_bias_row,)] + four(sort_rows, "y", 1)
         scalar += [(lift_rows, "y", 1, 0), (widen_bias,), (lift_rows, "y", 1, 3), (tanh_snap, "y", 0, 0)]
         scalar += [(tanh_snap, "y", 0, 1), (lift_bias_column,)] + tiles(tanh_obs, "y", 0, 3) + [(tanh_snap, "y", 0, 2)]
-        scalar += pair(lift_rows, "x", 0, 1) + tiles(tanh_obs, "y", 1, 1) + [(tanh_snap, "y", 1, 0)]
-        scalar += pair(lift_rows, "x", 1, 0) + tiles(tanh_obs, "y", 1, 3) + [(tanh_snap, "y", 1, 2)] + pair(lift_rows, "x", 1, 1)
-        scalar += [(tanh_snap, "x", 0, 0)]
+        scalar += [(lift_rows, "x", 0, 2)] + pair(sort_rows, "x", 1, 0) + tiles(tanh_obs, "y", 1, 1) + [(tanh_snap, "y", 1, 0)]
+        scalar += pair(lift_rows, "x", 1, 0) + pair(sort_rows, "x", 1, 1) + tiles(tanh_obs, "y", 1, 3) + pair(lift_rows, "x", 1, 1)
+        scalar += [(tanh_snap, "y", 1, 2), (tanh_snap, "x", 0, 0)]
         scalar += tiles(tanh_obs, "x", 1, 0) + tiles(tanh_obs, "x", 1, 1) + [(tanh_snap, "x", 0, 1)]
-        scalar += tiles(tanh_obs, "x", 1, 2) + [(tanh_snap, "x", 0, 2)] + tiles(tanh_obs, "x", 1, 3)
-        scalar += [(lift_cross, 0, 0, 0), (tanh_snap, "x", 0, 3), (round_cross, 0, 0), (lift_cross, 1, 0, 0), (round_cross, 0, 1)]
-        scalar += both(lift_cross, 1, 1) + banks(lift_cross, 2) + both(lift_plane, 0) + banks(lift_cross, 3) + both(lift_plane, 1)
-        scalar += [(lift_plane, 2, 0), (lift_plane, 2, 1), (lift_plane, 3, 1)]
+        scalar += tiles(tanh_obs, "x", 1, 2) + [(tanh_snap, "x", 0, 2)] + tiles(tanh_obs, "x", 1, 3) + [(tanh_snap, "x", 0, 3)]
+        scalar += both(lift_cross, 0, 0) + both(lift_cross, 1, 0) + [(lift_cross, 0, 1, 1)] + both(lift_cross, 1, 1)
+        scalar += both(lift_cross, 2, 0) + [(round_cross, 1, 1)] + both(lift_cross, 2, 1) + [(lift_plane, 1, 0), (lift_plane, 0, 1)]
+        scalar += [(lift_cross, 3, 0, 0), (lift_plane, 1, 1)] + both(lift_back, 3, 1)
+        scalar += [(lift_cross, 3, 1, 1)] + both(lift_plane, 2)
 
         vector = [(lift_rows, "y", 0, 1), (encode_pair, "y", 0, 0), (lift_rows, "y", 0, 3), (encode_pair, "y", 0, 1)]
         vector += [(add_bias, "y", 0, c, i) for i in range(2) for c in range(2)]
-        vector += [(lift_rows, "y", 1, 1), (lift_rows, "y", 1, 2), (add_bias, "y", 0, 2, 0), (encode_half, "y", 1), (repeat_weights, "y", 0, 0)]
-        vector += [(add_bias, "y", 0, 2, 1)] + pair(lift_rows, "x", 0, 0) + both(add_bias, "y", 1, 0)
-        vector += [(weigh_snap, "y", 0, 1), (repeat_weights, "y", 0, 2)] + tiles(weigh_obs, "y", 0, 3) + both(add_bias, "y", 1, 2)
+        vector += [(lift_rows, "y", 1, 1), (lift_rows, "y", 1, 2), (encode_half, "y", 1), (repeat_weights, "y", 0, 0)]
+        vector += both(add_bias, "y", 0, 2) + pair(lift_rows, "x", 0, 0) + [(add_bias, "y", 1, 0, 0)]
+        vector += [(weigh_snap, "y", 0, 1), (repeat_weights, "y", 0, 2), (add_bias, "y", 1, 0, 1)] + [(lift_rows, "x", 0, 3)] + tiles(weigh_obs, "y", 0, 3) + [(add_bias, "y", 1, 2, 0)]
         vector += [(encode_half, "x", 0), (encode_fy, 0, 0), (repeat_weights, "y", 1, 0)]
-        vector += tiles(weigh_obs, "y", 1, 1) + both(add_bias, "x", 0, 0)
-        vector += [(encode_fy, 0, 1), (encode_fy, 1, 0), (encode_half, "x", 1), (repeat_weights, "y", 1, 2), (repeat_weights, "x", 0, 0)]
+        vector += [(add_bias, "y", 1, 2, 1)] + tiles(weigh_obs, "y", 1, 1) + both(add_bias, "x", 0, 0)
+        vector += [(encode_fy, 1, 0), (encode_half, "x", 1)] + [(repeat_weights,) + key for key in POOL[3:6]]
         vector += tiles(weigh_obs, "y", 1, 3) + both(add_bias, "x", 0, 1) + both(add_bias, "x", 0, 2)
-        vector += tiles(weigh_obs, "x", 1, 0) + [(encode_fx, 0), (encode_fy, 1, 1), (repeat_weights, "x", 0, 1)]
-        vector += both(add_bias, "x", 0, 3) + tiles(weigh_obs, "x", 1, 1) + [(lift_cross, 0, 0, 1), (encode_fx, 1), (repeat_weights, "x", 0, 2)]
-        vector += both(lift_cross, 0, 1) + tiles(weigh_obs, "x", 1, 2) + [(lift_cross, 1, 0, 1), (encode_fx, 2)]
-        vector += tiles(weigh_obs, "x", 1, 3) + [(weigh_snap, "x", 0, 3), (round_cross, 1, 0), (encode_fx, 3), (round_cross, 1, 1)]
-        vector += both(round_cross, 2) + [(encode_plane, 0, 0), (round_cross, 3, 0), (encode_plane, 0, 1), (round_cross, 3, 1)]
-        vector += [(encode_plane, 1, 0), (lift_plane, 3, 0), (encode_plane, 1, 1)] + [(encode_plane, c, h) for h in range(2) for c in (2, 3)]
+        vector += tiles(weigh_obs, "x", 1, 0) + tiles(weigh_obs, "x", 1, 1) + both(add_bias, "x", 0, 3)
+        vector += [(encode_fx, 0), (encode_fx, 1), (encode_fy, 0, 1), (encode_fy, 1, 1), (repeat_weights, "x", 0, 2)]
+        vector += tiles(weigh_obs, "x", 1, 2) + tiles(weigh_obs, "x", 1, 3) + [(lift_cross, 0, 1, 0), (encode_fx, 2)]
+        vector += [(round_cross, 0, 0), (round_cross, 1, 0), (weigh_snap, "x", 0, 3), (round_cross, 0, 1), (encode_fx, 3)]
+        vector += [(lift_plane, 0, 0), (round_cross, 2, 0), (encode_plane, 0, 0), (round_cross, 2, 1), (encode_plane, 1, 0), (lift_cross, 3, 0, 1), (encode_plane, 0, 1), (round_cross, 3, 0)]
+        vector += [(encode_plane, 1, 1), (lift_cross, 3, 1, 0), (encode_plane, 3, 1), (lift_plane, 3, 0), (encode_plane, 2, 0), (encode_plane, 3, 0), (encode_plane, 2, 1)]
 
         pool = [(weigh_snap,) + key for key in POOL]
 
-        sync = both(send_unit, 0) + both(send_unit, 1) + banks(send_cross, 2) + both(send_cross, 3, 0) + both(send_cross, 3, 1)
-        sync += both(send_plane) + both(send_last_planes) + [(send_scales,)]
+        sync = [(send_unit, c, h) for h in range(2) for c in range(2)] + banks(send_cross, 2) + [(send_pass, 0, 0, 2)] + both(send_cross, 3, 0)
+        sync += [(send_pass, 1, 0, 2), (send_cross, 3, 1, 0), (send_pass, 1, 3, 1), (send_cross, 3, 1, 1), (send_pass, 0, 2, 2), (send_pass, 1, 2, 1), (send_scales,)]
 
 
         reads = {}
@@ -561,7 +568,10 @@ def tile_extendeddmdkoopmancrossmoment_x2_kernel(
                 for k in range(2):
                     bank = ("bank", ("cross", c, h, k))
                     wire((cross, c, h, k), coded, bank)
-                    wire((lift_cross, c, h, k), [(cross, c, h, k)], bank, ("r", unit))
+                    if unit in FROM_BANK:
+                        wire((round_bank, c, h, k), [(cross, c, h, k)], bank, ("s", unit))
+                    first = round_bank if unit in FROM_BANK else cross
+                    wire((lift_cross, c, h, k), [(first, c, h, k)], bank, ("r", unit))
                     if (send_cross, c, h, k) in sync:
                         wire((send_cross, c, h, k), [(lift_cross, c, h, k)], ("r", unit))
                 if (send_unit, c, h) in sync:
@@ -574,13 +584,20 @@ def tile_extendeddmdkoopmancrossmoment_x2_kernel(
                     wire((encode_plane, c, h), both(lift_back, c, h), ("u", unit))
                 else:
                     bank = ("bank", ("plane", c, h))
-                    wire((round_cross, c, h), both(lift_cross, c, h), ("r", unit), ("s", unit))
-                    wire((turn_cross, c, h), [(round_cross, c, h)], bank, ("s", unit))
+                    if unit in FROM_BANK:
+                        rounded = both(round_bank, c, h)
+                    else:
+                        rounded = [(round_cross, c, h)]
+                        wire(rounded[0], both(lift_cross, c, h), ("r", unit), ("s", unit))
+                    wire((turn_cross, c, h), rounded, bank, ("s", unit))
                     wire((lift_plane, c, h), [(turn_cross, c, h)], bank, ("u", unit))
                     wire((encode_plane, c, h), [(lift_plane, c, h)], ("u", unit))
-        for n in range(2):
-            wire((send_plane, n), both(encode_plane, n))
-            wire((send_last_planes, n), [(encode_plane, 2, n), (encode_plane, 3, n)])
+        for step in sync:
+            if step[0] == send_plane:
+                wire(step, both(encode_plane, step[1]))
+            if step[0] == send_pass:
+                h, c, n = step[1:]
+                wire(step, [(encode_plane, c + k, h) for k in range(n)])
         wire((send_scales,), [(encode_plane, c, h) for c in range(4) for h in range(2)])
 
 

@@ -19,14 +19,15 @@ ALU = mybir.AluOpType
 
 BANKS = 8
 ALIGN = 64
-POOL = [("y", 0, 0), ("y", 0, 2), ("y", 1, 0), ("y", 1, 2), ("x", 0, 0), ("x", 0, 1), ("x", 0, 2)]
-SNAP = POOL + [("y", 0, 1), ("x", 0, 3)]
-SORTED = [(op, 1, j) for op in ("y", "x") for j in range(4)]
+POOL = [("y", 0, 0), ("y", 0, 1), ("y", 0, 2), ("y", 1, 0), ("y", 1, 2), ("x", 0, 0), ("x", 0, 1), ("x", 0, 2)]
+SNAP = POOL + [("x", 0, 3)]
+SORTED = [("y", 1, j) for j in range(4)] + [("x", 0, 3)] + [("x", 1, j) for j in range(3)]
 PAIRWISE = [("y", 0)]
 TWICE = [(3, 1)]
 FROM_BANK = []
 SCALAR_QUADS = (1, 3)
-DEPTH = {"bank": BANKS, "sorted": 4, "pair": 2, "half": 2, "z": 3, "th": 4, "t": 6, "f": 6, "run": 3, "r": 6, "s": 5, "u": 5}
+SHARED = {("y", 0, 2): ("y", 0, 1), ("x", 0, 1): ("x", 0, 0)}
+DEPTH = {"bank": BANKS, "sorted": 4, "pair": 2, "half": 2, "z": 3, "th": 4, "t": 6, "f": 6, "run": 3, "r": 6, "s": 5, "u": 3}
 
 
 def tile_extendeddmdkoopmancrossmoment_x2_kernel(
@@ -289,7 +290,7 @@ def tile_extendeddmdkoopmancrossmoment_x2_kernel(
             th = made["th", (op, g, c)][:].rearrange("p (t a) i k -> p t a (i k)", t=4)
             out = f_part(op, g, 256 * c, 256)
             if engine == "G":
-                run = made["run", (op, g, c)][:].rearrange("p r j -> p (r j)").unsqueeze(1).unsqueeze(1)
+                run = made["run", SHARED.get((op, g, c), (op, g, c))][:].rearrange("p r j -> p (r j)").unsqueeze(1).unsqueeze(1)
                 nc.gpsimd.tensor_tensor(
                     out=out.rearrange("p t (a r) j -> p t a (r j)", r=16),
                     in0=th.rearrange("p t (a r) j -> p t a (r j)", r=16),
@@ -372,8 +373,8 @@ def tile_extendeddmdkoopmancrossmoment_x2_kernel(
                 nc.tensor.transpose(bank_of("plane", c, h)[:, n, :], words[:, n, :], ident[:])
 
         def lift_plane(engine, c, h):
-            u = ring("u", (c, h), [P, 2, P, 4], BF16)
-            words = u[:].rearrange("p k i t -> p (k i t)").bitcast(F32).rearrange("p (k i e) -> p k i e", k=2, e=2)
+            u = ring("u", (c // 2, h), [P, 2, 2, P, 4], BF16)
+            words = u[:, c % 2].rearrange("p k i t -> p (k i t)").bitcast(F32).rearrange("p (k i e) -> p k i e", k=2, e=2)
             copy(engine, words, bank_of("plane", c, h)[:].rearrange("p (k e) i -> p k i e", e=2))
 
         def cross_back(engine, c, h, k):
@@ -390,12 +391,12 @@ def tile_extendeddmdkoopmancrossmoment_x2_kernel(
                     )
 
         def lift_back(engine, c, h, k):
-            u = ring("u", (c, h), [P, 2, P, 4], BF16)
-            divide(engine, u[:, k], bank_of("back", c, h, k)[:].rearrange("p t i -> p i t"))
+            u = ring("u", (c // 2, h), [P, 2, 2, P, 4], BF16)
+            divide(engine, u[:, c % 2, k], bank_of("back", c, h, k)[:].rearrange("p t i -> p i t"))
 
-        def encode_plane(engine, c, h):
-            cols = slice(256 * c, 256 * c + 256)
-            values = made["u", (c, h)][:].rearrange("p k i t -> p (k i t)")
+        def encode_plane(engine, c, h, n):
+            cols = slice(256 * c, 256 * (c + n))
+            values = made["u", (c // 2, h)][:, c % 2 : c % 2 + n].rearrange("p c k i t -> p (c k i t)")
             quantize(plane_code[:, h, cols], plane_scale[4 * h : P, cols], values)
 
         def send_cross(engine, c, h, k):
@@ -407,12 +408,6 @@ def tile_extendeddmdkoopmancrossmoment_x2_kernel(
             rows = out_0[256 * c : 256 * c + 256, 512 * h : 512 * h + 512]
             values = made["r", (c, h)][:].rearrange("p k a t -> p k (a t)")
             nc.sync.dma_start(out=rows.rearrange("(k p) n -> p k n", k=2), in_=values)
-
-        def send_plane(engine, c):
-            nc.sync.dma_start(
-                out=plane_words[:, :, 1024 * c : 1024 * c + 1024].bitcast(I32),
-                in_=plane_code[:, :, 256 * c : 256 * c + 256].bitcast(I32),
-            )
 
         def send_pass(engine, h, c, n):
             nc.sync.dma_start(
@@ -448,9 +443,9 @@ def tile_extendeddmdkoopmancrossmoment_x2_kernel(
         tensor += [(dot_first,), (dot_snap, "y", 0, 0, 1), (dot_snap, "y", 0, 1, 1)]
         tensor += four(turn_rows, "y", 1)
         tensor += both(dot_snap, "y", 0, 2) + pair(turn_rows, "x", 0, 0) + [(turn_bias,)]
-        tensor += tiles(dot_obs, "y", 0, 3) + both(dot_snap, "y", 1, 0)
+        tensor += tiles(dot_obs, "y", 0, 3)
         tensor += pair(turn_rows, "x", 0, 1) + tiles(turn_obs, "y", 0, 3)
-        tensor += tiles(dot_obs, "y", 1, 1) + both(dot_snap, "y", 1, 2)
+        tensor += both(dot_snap, "y", 1, 0) + tiles(dot_obs, "y", 1, 1) + both(dot_snap, "y", 1, 2)
         tensor += pair(turn_rows, "x", 1, 0) + tiles(turn_obs, "y", 1, 1)
         tensor += tiles(dot_obs, "y", 1, 3) + both(dot_snap, "x", 0, 0)
         tensor += pair(turn_rows, "x", 1, 1) + tiles(turn_obs, "y", 1, 3)
@@ -463,10 +458,10 @@ def tile_extendeddmdkoopmancrossmoment_x2_kernel(
         tensor += both(cross, 3, 0) + both(cross_back, 3, 1) + both(cross, 3, 1) + [(turn_cross, 2, 0), (turn_cross, 3, 0), (turn_cross, 2, 1)]
 
         scalar = [(lift_rows, "y", 0, 0), (lift_rows, "y", 0, 2), (lift_bias_row,)] + four(sort_rows, "y", 1)
-        scalar += [(lift_rows, "y", 1, 0), (widen_bias,), (lift_rows, "y", 1, 3), (tanh_snap, "y", 0, 0)]
-        scalar += [(tanh_snap, "y", 0, 1), (lift_bias_column,)] + tiles(tanh_obs, "y", 0, 3) + [(tanh_snap, "y", 0, 2)]
-        scalar += [(lift_rows, "x", 0, 2)] + pair(sort_rows, "x", 1, 0) + tiles(tanh_obs, "y", 1, 1) + [(tanh_snap, "y", 1, 0)]
-        scalar += pair(lift_rows, "x", 1, 0) + pair(sort_rows, "x", 1, 1) + tiles(tanh_obs, "y", 1, 3) + pair(lift_rows, "x", 1, 1)
+        scalar += [(tanh_snap, "y", 0, 0), (lift_rows, "y", 1, 3), (widen_bias,), (tanh_snap, "y", 0, 1), (sort_rows, "x", 0, 3), (lift_bias_column,)]
+        scalar += tiles(tanh_obs, "y", 0, 3) + [(tanh_snap, "y", 0, 2), (lift_rows, "x", 0, 2)]
+        scalar += pair(sort_rows, "x", 1, 0) + tiles(tanh_obs, "y", 1, 1) + [(tanh_snap, "y", 1, 0)]
+        scalar += pair(lift_rows, "x", 1, 0) + [(sort_rows, "x", 1, 2)] + tiles(tanh_obs, "y", 1, 3) + pair(lift_rows, "x", 1, 1)
         scalar += [(tanh_snap, "y", 1, 2), (tanh_snap, "x", 0, 0)]
         scalar += tiles(tanh_obs, "x", 1, 0) + tiles(tanh_obs, "x", 1, 1) + [(tanh_snap, "x", 0, 1)]
         scalar += tiles(tanh_obs, "x", 1, 2) + [(tanh_snap, "x", 0, 2)] + tiles(tanh_obs, "x", 1, 3) + [(tanh_snap, "x", 0, 3)]
@@ -477,24 +472,24 @@ def tile_extendeddmdkoopmancrossmoment_x2_kernel(
 
         vector = [(lift_rows, "y", 0, 1), (encode_pair, "y", 0, 0), (lift_rows, "y", 0, 3), (encode_pair, "y", 0, 1)]
         vector += [(add_bias, "y", 0, c, i) for i in range(2) for c in range(2)]
-        vector += [(lift_rows, "y", 1, 1), (lift_rows, "y", 1, 2), (encode_half, "y", 1), (repeat_weights, "y", 0, 0)]
-        vector += both(add_bias, "y", 0, 2) + pair(lift_rows, "x", 0, 0) + [(add_bias, "y", 1, 0, 0)]
-        vector += [(weigh_snap, "y", 0, 1), (repeat_weights, "y", 0, 2), (add_bias, "y", 1, 0, 1)] + [(lift_rows, "x", 0, 3)] + tiles(weigh_obs, "y", 0, 3) + [(add_bias, "y", 1, 2, 0)]
-        vector += [(encode_half, "x", 0), (encode_fy, 0, 0), (repeat_weights, "y", 1, 0)]
-        vector += [(add_bias, "y", 1, 2, 1)] + tiles(weigh_obs, "y", 1, 1) + both(add_bias, "x", 0, 0)
-        vector += [(encode_fy, 1, 0), (encode_half, "x", 1)] + [(repeat_weights,) + key for key in POOL[3:6]]
+        vector += [(repeat_weights, "y", 0, 0)] + [(lift_rows, "y", 1, j) for j in range(3)] + both(add_bias, "y", 0, 2) + [(lift_rows, "x", 0, 0)]
+        vector += [(repeat_weights, "y", 0, 1), (encode_half, "y", 1)] + [(lift_rows, "x", 0, j) for j in (1, 3)]
+        vector += tiles(weigh_obs, "y", 0, 3) + both(add_bias, "y", 1, 0) + both(add_bias, "y", 1, 2)
+        vector += [(repeat_weights, "x", 0, 0), (encode_half, "x", 0), (repeat_weights, "y", 1, 0), (encode_fy, 0, 0)]
+        vector += tiles(weigh_obs, "y", 1, 1) + both(add_bias, "x", 0, 0)
+        vector += [(encode_fy, 1, 0), (repeat_weights, "y", 1, 2), (encode_half, "x", 1)]
         vector += tiles(weigh_obs, "y", 1, 3) + both(add_bias, "x", 0, 1) + both(add_bias, "x", 0, 2)
         vector += tiles(weigh_obs, "x", 1, 0) + tiles(weigh_obs, "x", 1, 1) + both(add_bias, "x", 0, 3)
-        vector += [(encode_fx, 0), (encode_fx, 1), (encode_fy, 0, 1), (encode_fy, 1, 1), (repeat_weights, "x", 0, 2)]
+        vector += [(encode_fx, 0), (encode_fx, 1), (encode_fy, 0, 1), (repeat_weights, "x", 0, 2), (encode_fy, 1, 1)]
         vector += tiles(weigh_obs, "x", 1, 2) + tiles(weigh_obs, "x", 1, 3) + [(lift_cross, 0, 1, 0), (encode_fx, 2)]
         vector += [(round_cross, 0, 0), (round_cross, 1, 0), (weigh_snap, "x", 0, 3), (round_cross, 0, 1), (encode_fx, 3)]
-        vector += [(lift_plane, 0, 0), (round_cross, 2, 0), (encode_plane, 0, 0), (round_cross, 2, 1), (encode_plane, 1, 0), (lift_cross, 3, 0, 1), (encode_plane, 0, 1), (round_cross, 3, 0)]
-        vector += [(encode_plane, 1, 1), (lift_cross, 3, 1, 0), (encode_plane, 3, 1), (lift_plane, 3, 0), (encode_plane, 2, 0), (encode_plane, 3, 0), (encode_plane, 2, 1)]
+        vector += [(lift_plane, 0, 0), (round_cross, 2, 0), (encode_plane, 0, 0, 1), (round_cross, 2, 1), (encode_plane, 1, 0, 1), (lift_cross, 3, 0, 1), (encode_plane, 0, 1, 1), (round_cross, 3, 0)]
+        vector += [(encode_plane, 1, 1, 1), (lift_cross, 3, 1, 0), (encode_plane, 3, 1, 1), (lift_plane, 3, 0), (encode_plane, 2, 0, 1), (encode_plane, 3, 0, 1), (encode_plane, 2, 1, 1)]
 
         pool = [(weigh_snap,) + key for key in POOL]
 
-        sync = [(send_unit, c, h) for h in range(2) for c in range(2)] + banks(send_cross, 2) + [(send_pass, 0, 0, 2)] + both(send_cross, 3, 0)
-        sync += [(send_pass, 1, 0, 2), (send_cross, 3, 1, 0), (send_pass, 1, 3, 1), (send_cross, 3, 1, 1), (send_pass, 0, 2, 2), (send_pass, 1, 2, 1), (send_scales,)]
+        sync = both(send_cross, 0, 0) + [(send_unit, 1, 0), (send_unit, 0, 1), (send_unit, 1, 1), (send_unit, 2, 0)] + both(send_cross, 2, 1) + [(send_pass, 0, 0, 2)] + both(send_cross, 3, 0)
+        sync += [(send_pass, 1, 0, 2)] + both(send_cross, 3, 1) + [(send_pass, 0, 2, 2), (send_pass, 1, 2, 2), (send_scales,)]
 
 
         reads = {}
@@ -544,9 +539,10 @@ def tile_extendeddmdkoopmancrossmoment_x2_kernel(
                             wire((add_bias,) + key + (i,), [dot, (lift_bias_row,)], bank, ("z", key))
                         wire((tanh_snap,) + key, both(add_bias, *key), ("z", key), ("th", key))
                         if key in POOL:
-                            wire((repeat_weights,) + key, [], ("run", key))
-                            sources = [(tanh_snap,) + key, (repeat_weights,) + key]
-                            wire((weigh_snap,) + key, sources, ("th", key), f_key(*key), ("run", key))
+                            run = SHARED.get(key, key)
+                            wire((repeat_weights,) + run, [], ("run", run))
+                            sources = [(tanh_snap,) + key, (repeat_weights,) + run]
+                            wire((weigh_snap,) + key, sources, ("th", key), f_key(*key), ("run", run))
                         else:
                             wire((weigh_snap,) + key, [(tanh_snap,) + key], ("th", key), f_key(*key))
                         continue
@@ -560,6 +556,7 @@ def tile_extendeddmdkoopmancrossmoment_x2_kernel(
         for g in range(2):
             for h in range(2):
                 wire((encode_fy, g, h), weighed("y", g, 2 * h) + weighed("y", g, 2 * h + 1), f_key("y", g, 2 * h))
+        laid = {}
         for c in range(4):
             wire((encode_fx, c), weighed("x", 0, c) + weighed("x", 1, c), f_key("x", 0, c))
             for h in range(2):
@@ -580,8 +577,8 @@ def tile_extendeddmdkoopmancrossmoment_x2_kernel(
                     for k in range(2):
                         bank = ("bank", ("back", c, h, k))
                         wire((cross_back, c, h, k), coded, bank)
-                        wire((lift_back, c, h, k), [(cross_back, c, h, k)], bank, ("u", unit))
-                    wire((encode_plane, c, h), both(lift_back, c, h), ("u", unit))
+                        wire((lift_back, c, h, k), [(cross_back, c, h, k)], bank, ("u", (c // 2, h)))
+                    laid[unit] = both(lift_back, c, h)
                 else:
                     bank = ("bank", ("plane", c, h))
                     if unit in FROM_BANK:
@@ -590,15 +587,20 @@ def tile_extendeddmdkoopmancrossmoment_x2_kernel(
                         rounded = [(round_cross, c, h)]
                         wire(rounded[0], both(lift_cross, c, h), ("r", unit), ("s", unit))
                     wire((turn_cross, c, h), rounded, bank, ("s", unit))
-                    wire((lift_plane, c, h), [(turn_cross, c, h)], bank, ("u", unit))
-                    wire((encode_plane, c, h), [(lift_plane, c, h)], ("u", unit))
+                    wire((lift_plane, c, h), [(turn_cross, c, h)], bank, ("u", (c // 2, h)))
+                    laid[unit] = [(lift_plane, c, h)]
+        encoded = {}
+        for step in vector:
+            if step[0] == encode_plane:
+                c, h, n = step[1:]
+                wire(step, [source for k in range(n) for source in laid[c + k, h]], ("u", (c // 2, h)))
+                for k in range(n):
+                    encoded[c + k, h] = step
         for step in sync:
-            if step[0] == send_plane:
-                wire(step, both(encode_plane, step[1]))
             if step[0] == send_pass:
                 h, c, n = step[1:]
-                wire(step, [(encode_plane, c + k, h) for k in range(n)])
-        wire((send_scales,), [(encode_plane, c, h) for c in range(4) for h in range(2)])
+                wire(step, [encoded[c + k, h] for k in range(n)])
+        wire((send_scales,), encoded.values())
 
 
         queues = {"V": vector, "S": scalar, "G": pool, "Q": sync, "T": tensor}

@@ -21,13 +21,13 @@ BANKS = 8
 ALIGN = 64
 POOL = [("y", 0, 0), ("y", 0, 1), ("y", 0, 2), ("y", 1, 0), ("y", 1, 2), ("x", 0, 0), ("x", 0, 1), ("x", 0, 2)]
 SNAP = POOL + [("x", 0, 3)]
-SORTED = [("y", 1, j) for j in range(4)] + [("x", 0, 3)] + [("x", 1, j) for j in range(3)]
+SORTED = [(op, 1, j) for op in ("y", "x") for j in range(4)] + [("x", 0, 3)]
 PAIRWISE = [("y", 0)]
-TWICE = [(3, 1)]
-FROM_BANK = []
+TWICE = []
+FROM_BANK = [(3, 1)]
 SCALAR_QUADS = (1, 3)
 SHARED = {("y", 0, 2): ("y", 0, 1), ("x", 0, 1): ("x", 0, 0)}
-DEPTH = {"bank": BANKS, "sorted": 4, "pair": 2, "half": 2, "z": 3, "th": 4, "t": 6, "f": 6, "run": 3, "r": 6, "s": 5, "u": 3}
+DEPTH = {"bank": BANKS, "sorted": 4, "pair": 2, "half": 2, "z": 3, "th": 4, "t": 5, "f": 5, "run": 3, "r": 6, "s": 5, "u": 4}
 
 
 def tile_extendeddmdkoopmancrossmoment_x2_kernel(
@@ -441,55 +441,50 @@ def tile_extendeddmdkoopmancrossmoment_x2_kernel(
 
         tensor = pair(turn_rows, "y", 0, 0) + [(spread_bias,)] + pair(turn_rows, "y", 0, 1)
         tensor += [(dot_first,), (dot_snap, "y", 0, 0, 1), (dot_snap, "y", 0, 1, 1)]
-        tensor += four(turn_rows, "y", 1)
-        tensor += both(dot_snap, "y", 0, 2) + pair(turn_rows, "x", 0, 0) + [(turn_bias,)]
-        tensor += tiles(dot_obs, "y", 0, 3)
-        tensor += pair(turn_rows, "x", 0, 1) + tiles(turn_obs, "y", 0, 3)
+        tensor += four(turn_rows, "y", 1) + [(turn_bias,)]
+        tensor += both(dot_snap, "y", 0, 2) + tiles(dot_obs, "y", 0, 3)
+        tensor += four(turn_rows, "x", 0) + tiles(turn_obs, "y", 0, 3)
         tensor += both(dot_snap, "y", 1, 0) + tiles(dot_obs, "y", 1, 1) + both(dot_snap, "y", 1, 2)
-        tensor += pair(turn_rows, "x", 1, 0) + tiles(turn_obs, "y", 1, 1)
-        tensor += tiles(dot_obs, "y", 1, 3) + both(dot_snap, "x", 0, 0)
-        tensor += pair(turn_rows, "x", 1, 1) + tiles(turn_obs, "y", 1, 3)
-        tensor += both(dot_snap, "x", 0, 1) + both(dot_snap, "x", 0, 2) + tiles(dot_obs, "x", 1, 0) + tiles(dot_obs, "x", 1, 1)
-        tensor += tiles(turn_obs, "x", 1, 0) + tiles(turn_obs, "x", 1, 1)
+        tensor += four(turn_rows, "x", 1) + tiles(turn_obs, "y", 1, 1)
+        tensor += both(dot_snap, "x", 0, 0) + tiles(dot_obs, "y", 1, 3) + both(dot_snap, "x", 0, 1) + both(dot_snap, "x", 0, 2)
+        tensor += tiles(dot_obs, "x", 1, 0) + tiles(dot_obs, "x", 1, 1)
+        tensor += tiles(turn_obs, "y", 1, 3) + tiles(turn_obs, "x", 1, 0) + tiles(turn_obs, "x", 1, 1)
         tensor += tiles(dot_obs, "x", 1, 2) + both(dot_snap, "x", 0, 3) + tiles(dot_obs, "x", 1, 3)
         tensor += tiles(turn_obs, "x", 1, 2) + tiles(turn_obs, "x", 1, 3)
-        tensor += [(cross, c, h, k) for h in range(2) for c in range(2) for k in range(2)] + banks(cross, 2)
-        tensor += [(turn_cross, c, h) for h in range(2) for c in range(2)]
-        tensor += both(cross, 3, 0) + both(cross_back, 3, 1) + both(cross, 3, 1) + [(turn_cross, 2, 0), (turn_cross, 3, 0), (turn_cross, 2, 1)]
+        tensor += banks(cross, 0) + banks(cross, 1) + banks(cross, 2) + both(turn_cross, 0) + both(turn_cross, 1)
+        tensor += banks(cross, 3) + [(turn_cross, c, h) for h in range(2) for c in (2, 3)]
 
         scalar = [(lift_rows, "y", 0, 0), (lift_rows, "y", 0, 2), (lift_bias_row,)] + four(sort_rows, "y", 1)
-        scalar += [(tanh_snap, "y", 0, 0), (lift_rows, "y", 1, 3), (widen_bias,), (tanh_snap, "y", 0, 1), (sort_rows, "x", 0, 3), (lift_bias_column,)]
-        scalar += tiles(tanh_obs, "y", 0, 3) + [(tanh_snap, "y", 0, 2), (lift_rows, "x", 0, 2)]
-        scalar += pair(sort_rows, "x", 1, 0) + tiles(tanh_obs, "y", 1, 1) + [(tanh_snap, "y", 1, 0)]
-        scalar += pair(lift_rows, "x", 1, 0) + [(sort_rows, "x", 1, 2)] + tiles(tanh_obs, "y", 1, 3) + pair(lift_rows, "x", 1, 1)
-        scalar += [(tanh_snap, "y", 1, 2), (tanh_snap, "x", 0, 0)]
+        scalar += [(widen_bias,), (tanh_snap, "y", 0, 0), (lift_rows, "y", 1, 3), (lift_bias_column,), (tanh_snap, "y", 0, 1)]
+        scalar += [(sort_rows, "x", 0, 3)] + tiles(tanh_obs, "y", 0, 3) + [(tanh_snap, "y", 0, 2), (lift_rows, "x", 0, 2)]
+        scalar += four(sort_rows, "x", 1) + tiles(tanh_obs, "y", 1, 1) + [(tanh_snap, "y", 1, 0)]
+        scalar += four(lift_rows, "x", 1) + tiles(tanh_obs, "y", 1, 3) + [(tanh_snap, "y", 1, 2), (tanh_snap, "x", 0, 0)]
         scalar += tiles(tanh_obs, "x", 1, 0) + tiles(tanh_obs, "x", 1, 1) + [(tanh_snap, "x", 0, 1)]
         scalar += tiles(tanh_obs, "x", 1, 2) + [(tanh_snap, "x", 0, 2)] + tiles(tanh_obs, "x", 1, 3) + [(tanh_snap, "x", 0, 3)]
-        scalar += both(lift_cross, 0, 0) + both(lift_cross, 1, 0) + [(lift_cross, 0, 1, 1)] + both(lift_cross, 1, 1)
-        scalar += both(lift_cross, 2, 0) + [(round_cross, 1, 1)] + both(lift_cross, 2, 1) + [(lift_plane, 1, 0), (lift_plane, 0, 1)]
-        scalar += [(lift_cross, 3, 0, 0), (lift_plane, 1, 1)] + both(lift_back, 3, 1)
-        scalar += [(lift_cross, 3, 1, 1)] + both(lift_plane, 2)
+        scalar += banks(lift_cross, 0)[:3] + banks(lift_cross, 1) + banks(lift_cross, 2) + both(lift_plane, 0) + both(lift_plane, 1)
+        scalar += [(lift_cross, 3, 0, 1)] + both(round_bank, 3, 1) + [(lift_plane, c, h) for h in range(2) for c in (2, 3)]
 
         vector = [(lift_rows, "y", 0, 1), (encode_pair, "y", 0, 0), (lift_rows, "y", 0, 3), (encode_pair, "y", 0, 1)]
         vector += [(add_bias, "y", 0, c, i) for i in range(2) for c in range(2)]
-        vector += [(repeat_weights, "y", 0, 0)] + [(lift_rows, "y", 1, j) for j in range(3)] + both(add_bias, "y", 0, 2) + [(lift_rows, "x", 0, 0)]
-        vector += [(repeat_weights, "y", 0, 1), (encode_half, "y", 1)] + [(lift_rows, "x", 0, j) for j in (1, 3)]
+        vector += [(repeat_weights, "y", 0, 0)] + [(lift_rows, "y", 1, j) for j in range(3)] + both(add_bias, "y", 0, 2)
+        vector += [(repeat_weights, "y", 0, 1), (encode_half, "y", 1)] + [(lift_rows, "x", 0, j) for j in (0, 1, 3)]
         vector += tiles(weigh_obs, "y", 0, 3) + both(add_bias, "y", 1, 0) + both(add_bias, "y", 1, 2)
         vector += [(repeat_weights, "x", 0, 0), (encode_half, "x", 0), (repeat_weights, "y", 1, 0), (encode_fy, 0, 0)]
         vector += tiles(weigh_obs, "y", 1, 1) + both(add_bias, "x", 0, 0)
-        vector += [(encode_fy, 1, 0), (repeat_weights, "y", 1, 2), (encode_half, "x", 1)]
-        vector += tiles(weigh_obs, "y", 1, 3) + both(add_bias, "x", 0, 1) + both(add_bias, "x", 0, 2)
+        vector += [(encode_half, "x", 1), (repeat_weights, "y", 1, 2), (encode_fy, 1, 0)]
+        vector += both(add_bias, "x", 0, 1) + both(add_bias, "x", 0, 2) + tiles(weigh_obs, "y", 1, 3)
         vector += tiles(weigh_obs, "x", 1, 0) + tiles(weigh_obs, "x", 1, 1) + both(add_bias, "x", 0, 3)
-        vector += [(encode_fx, 0), (encode_fx, 1), (encode_fy, 0, 1), (repeat_weights, "x", 0, 2), (encode_fy, 1, 1)]
-        vector += tiles(weigh_obs, "x", 1, 2) + tiles(weigh_obs, "x", 1, 3) + [(lift_cross, 0, 1, 0), (encode_fx, 2)]
-        vector += [(round_cross, 0, 0), (round_cross, 1, 0), (weigh_snap, "x", 0, 3), (round_cross, 0, 1), (encode_fx, 3)]
-        vector += [(lift_plane, 0, 0), (round_cross, 2, 0), (encode_plane, 0, 0, 1), (round_cross, 2, 1), (encode_plane, 1, 0, 1), (lift_cross, 3, 0, 1), (encode_plane, 0, 1, 1), (round_cross, 3, 0)]
-        vector += [(encode_plane, 1, 1, 1), (lift_cross, 3, 1, 0), (encode_plane, 3, 1, 1), (lift_plane, 3, 0), (encode_plane, 2, 0, 1), (encode_plane, 3, 0, 1), (encode_plane, 2, 1, 1)]
+        vector += [(encode_fx, 0), (encode_fy, 0, 1), (encode_fy, 1, 1), (repeat_weights, "x", 0, 2), (encode_fx, 1)]
+        vector += tiles(weigh_obs, "x", 1, 2) + tiles(weigh_obs, "x", 1, 3) + [(lift_cross, 0, 1, 1), (encode_fx, 2)]
+        vector += both(round_cross, 0) + [(weigh_snap, "x", 0, 3)] + both(round_cross, 1) + [(encode_fx, 3)]
+        vector += both(round_cross, 2) + [(lift_cross, 3, 0, 0), (encode_plane, 0, 0, 2), (round_cross, 3, 0), (encode_plane, 0, 1, 2)]
+        vector += both(lift_cross, 3, 1) + [(encode_plane, c, h, 1) for h in range(2) for c in (2, 3)]
 
         pool = [(weigh_snap,) + key for key in POOL]
 
-        sync = both(send_cross, 0, 0) + [(send_unit, 1, 0), (send_unit, 0, 1), (send_unit, 1, 1), (send_unit, 2, 0)] + both(send_cross, 2, 1) + [(send_pass, 0, 0, 2)] + both(send_cross, 3, 0)
-        sync += [(send_pass, 1, 0, 2)] + both(send_cross, 3, 1) + [(send_pass, 0, 2, 2), (send_pass, 1, 2, 2), (send_scales,)]
+        sync = both(send_cross, 0, 0) + [(send_unit, 0, 1)] + both(send_unit, 1) + both(send_unit, 2)
+        sync += both(send_cross, 3, 0) + [(send_pass, 0, 0, 2), (send_pass, 1, 0, 2)] + both(send_cross, 3, 1)
+        sync += [(send_pass, 0, 2, 2), (send_pass, 1, 2, 2), (send_scales,)]
 
 
         reads = {}

@@ -21,13 +21,12 @@ BANKS = 8
 ALIGN = 64
 POOL = [("y", 0, 0), ("y", 0, 1), ("y", 0, 2), ("y", 1, 0), ("y", 1, 2), ("x", 0, 0), ("x", 0, 1), ("x", 0, 2)]
 SNAP = POOL + [("x", 0, 3)]
-SORTED = [(op, 1, j) for op in ("y", "x") for j in range(4)] + [("x", 0, 3)]
+SORTED = [(op, 1, i) for op in ("y", "x") for i in range(2)] + [("x", 0, 1)]
 PAIRWISE = [("y", 0)]
-TWICE = []
 FROM_BANK = [(3, 1)]
 SCALAR_QUADS = (1, 3)
 SHARED = {("y", 0, 2): ("y", 0, 1), ("x", 0, 1): ("x", 0, 0)}
-DEPTH = {"bank": BANKS, "sorted": 4, "pair": 2, "half": 2, "z": 3, "th": 4, "t": 5, "f": 5, "run": 3, "r": 6, "s": 5, "u": 4}
+DEPTH = {"bank": BANKS, "sorted": 2, "pair": 2, "half": 3, "z": 3, "th": 4, "t": 5, "f": 4, "run": 3, "s": 3, "u": 4}
 
 
 def tile_extendeddmdkoopmancrossmoment_x2_kernel(
@@ -55,12 +54,14 @@ def tile_extendeddmdkoopmancrossmoment_x2_kernel(
         nc.scalar.dma_start(out=b_rows[:], in_=b.rearrange("(n w) -> n w", w=8))
 
         row_words = {}
+        row_pairs = {}
 
         def load_rows(op, source, g, j, n):
             rows = keep.tile([P, n, SIZE], BF16, name=f"rows_{op}{g}{j}", align_bytes=ALIGN)
             nc.sync.dma_start(
                 out=rows[:], in_=source.rearrange("(g p j) d -> g p j d", g=2, j=4)[g, :, j : j + n, :]
             )
+            row_pairs[op, g, j // 2] = rows[:].bitcast(F32)
             for k in range(n):
                 row_words[op, g, j + k] = rows[:, k, :].bitcast(F32)
 
@@ -87,6 +88,7 @@ def tile_extendeddmdkoopmancrossmoment_x2_kernel(
             nc.sync.dma_start(out=weight[op][:], in_=source.rearrange("(g p j) -> p g j", g=2, j=4))
 
         b_tiles = keep.tile([8, P], BF16, name="b_tiles", align_bytes=ALIGN)
+        nc.scalar.dma_start(out=b_tiles[:], in_=b.rearrange("(m n) -> m n", n=P))
 
         load_rows("y", y, 0, 0, 1)
         load_rows("y", y, 0, 1, 1)
@@ -96,7 +98,6 @@ def tile_extendeddmdkoopmancrossmoment_x2_kernel(
         load_w(slice(1, 2), 0)
         load_rows("y", y, 1, 0, 2)
         load_rows("y", y, 1, 2, 2)
-        nc.sync.dma_start(out=b_tiles[:], in_=b.rearrange("(m n) -> m n", n=P))
         load_weights("y", q)
         load_w(slice(0, 2), 1)
         load_weights("x", p)
@@ -141,17 +142,17 @@ def tile_extendeddmdkoopmancrossmoment_x2_kernel(
         def half_key(op, g):
             return ("half", (op, g))
 
-        def sort_rows(engine, op, g, j):
-            words = ring("sorted", (op, g, j), [P, 2, 2, P], F32)
-            copy(engine, words[:], row_words[op, g, j].rearrange("p (n a e) -> p n e a", n=2, e=2))
+        def sort_pair(engine, op, g, i):
+            words = ring("sorted", (op, g, i), [P, 4, 2, P], F32)
+            copy(engine, words[:], row_pairs[op, g, i].rearrange("p j (n a e) -> p (j n) e a", n=2, e=2))
 
         def turn_rows(engine, op, g, j):
             bank = bank_of("rows", op, g, j)
             words = row_words[op, g, j]
             for n in range(2):
                 for e in range(2):
-                    if (op, g, j) in SORTED:
-                        columns = made["sorted", (op, g, j)][:, n, e, :]
+                    if (op, g, j // 2) in SORTED:
+                        columns = made["sorted", (op, g, j // 2)][:, 2 * (j % 2) + n, e, :]
                     else:
                         columns = words[:, 256 * n + e : 256 * (n + 1) : 2]
                     nc.tensor.transpose(bank[:, 2 * n + e, :], columns, ident[:])
@@ -208,43 +209,30 @@ def tile_extendeddmdkoopmancrossmoment_x2_kernel(
             copy(engine, run[:], weight[op][:, g].unsqueeze(1).to_broadcast([P, 16, 4]))
 
 
-        fy_code = {}
-        fy_scale = {}
-        for g in range(2):
-            for h in range(2):
-                fy_code[g, h] = keep.tile([P, 512], U32, name=f"fy_code{g}{h}", align_bytes=ALIGN)
-                fy_scale[g, h] = keep.tile([P, 512], U8, name=f"fy_scale{g}{h}", align_bytes=ALIGN)
-        fx_code = []
-        fx_scale = []
-        for c in range(4):
-            code = keep.tile([P, 2, 256], U32, name=f"fx_code{c}", align_bytes=ALIGN)
-            scale = keep.tile([P, 2, 256], U8, name=f"fx_scale{c}", align_bytes=ALIGN)
-            fx_code.append(code)
-            fx_scale.append(scale)
+        f_code = {}
+        f_scale = {}
+        for op in ("y", "x"):
+            for n in range(2):
+                f_code[op, n] = keep.tile([P, 2, 512], U32, name=f"f_code_{op}{n}", align_bytes=ALIGN)
+                f_scale[op, n] = keep.tile([P, 2, 512], U8, name=f"f_scale_{op}{n}", align_bytes=ALIGN)
 
         def f_key(op, g, c):
-            return ("f", (op, g, c // 2) if op == "y" else (op, c))
+            return ("f", (op, c // 2))
 
         def f_part(op, g, first, n):
             tag, key = f_key(op, g, first // 256)
-            f = ring(tag, key, [P, 2048], BF16)
+            f = ring(tag, key, [P, 2, 512, 4], BF16)
             if op == "y":
-                a = (first % 512) // 4
-                return f[:].rearrange("p (t a j) -> p t a j", t=4, j=4)[:, :, a : a + n // 4, :]
+                return f[:, g, first % 512 : first % 512 + n]
             o = 256 * g + first % 256
-            return f[:, 4 * o : 4 * (o + n)].rearrange("p (t a j) -> p t a j", t=4, j=4)
+            return f[:, first // 256 % 2, o : o + n]
 
-        def dealt(op):
-            return "(a t)" if op == "y" else "(t a)"
-
-        def encode_fy(engine, g, h):
-            quantize(fy_code[g, h][:], fy_scale[g, h][:], made[f_key("y", g, 2 * h)][:])
-
-        def encode_fx(engine, c):
+        def encode_f(engine, op, n, first, count):
+            part = slice(first, first + count)
             quantize(
-                fx_code[c][:].rearrange("p g o -> p (g o)"),
-                fx_scale[c][:].rearrange("p g o -> p (g o)"),
-                made[f_key("x", 0, c)][:],
+                f_code[op, n][:, part].rearrange("p a o -> p (a o)"),
+                f_scale[op, n][:, part].rearrange("p a o -> p (a o)"),
+                made["f", (op, n)][:, part].rearrange("p a o j -> p (a o j)"),
             )
 
         def snap_sums(op, g, c, i):
@@ -272,37 +260,33 @@ def tile_extendeddmdkoopmancrossmoment_x2_kernel(
                     snap_pass("y", 0, c, 0, n)
 
         def add_bias(engine, op, g, c, i):
-            z = ring("z", (op, g, c), [P, 2, 4, 64, 2], F32)
-            bias = bias_row[:, 256 * c : 256 * c + 256].rearrange(f"p {dealt(op)} -> p t a", t=4)
+            z = ring("z", (op, g, c), [P, 2, 256, 2], F32)
             nc.vector.tensor_tensor(
                 out=z[:, i],
-                in0=snap_sums(op, g, c, i).rearrange(f"p k {dealt(op)} -> p t a k", t=4),
-                in1=bias.unsqueeze(3).to_broadcast([P, 4, 64, 2]),
+                in0=snap_sums(op, g, c, i).rearrange("p k o -> p o k"),
+                in1=bias_row[:, 256 * c : 256 * c + 256].unsqueeze(2).to_broadcast([P, 256, 2]),
                 op=ALU.add,
             )
 
         def tanh_snap(engine, op, g, c):
             z = made["z", (op, g, c)]
             th = ring("th", (op, g, c), [P, 256, 2, 2], F32)
-            nc.scalar.activation(out=th[:], in_=z[:].rearrange("p i t a k -> p (t a) i k"), func=ACT.Tanh)
+            nc.scalar.activation(out=th[:], in_=z[:].rearrange("p i o k -> p o i k"), func=ACT.Tanh)
 
         def weigh_snap(engine, op, g, c):
-            th = made["th", (op, g, c)][:].rearrange("p (t a) i k -> p t a (i k)", t=4)
+            th = made["th", (op, g, c)][:].rearrange("p o i k -> p o (i k)")
             out = f_part(op, g, 256 * c, 256)
             if engine == "G":
-                run = made["run", SHARED.get((op, g, c), (op, g, c))][:].rearrange("p r j -> p (r j)").unsqueeze(1).unsqueeze(1)
+                run = made["run", SHARED.get((op, g, c), (op, g, c))][:].rearrange("p r j -> p (r j)")
                 nc.gpsimd.tensor_tensor(
-                    out=out.rearrange("p t (a r) j -> p t a (r j)", r=16),
-                    in0=th.rearrange("p t (a r) j -> p t a (r j)", r=16),
-                    in1=run.to_broadcast([P, 4, 4, 64]),
+                    out=out.rearrange("p (a r) j -> p a (r j)", r=16),
+                    in0=th.rearrange("p (a r) j -> p a (r j)", r=16),
+                    in1=run.unsqueeze(1).to_broadcast([P, 16, 64]),
                     op=ALU.mult,
                 )
             else:
                 nc.vector.tensor_tensor(
-                    out=out,
-                    in0=th,
-                    in1=weight[op][:, g, :].unsqueeze(1).unsqueeze(1).to_broadcast([P, 4, 64, 4]),
-                    op=ALU.mult,
+                    out=out, in0=th, in1=weight[op][:, g, :].unsqueeze(1).to_broadcast([P, 256, 4]), op=ALU.mult
                 )
 
         def dot_obs(engine, op, g, m):
@@ -333,8 +317,8 @@ def tile_extendeddmdkoopmancrossmoment_x2_kernel(
         def weigh_obs(engine, op, g, m):
             nc.vector.tensor_tensor(
                 out=f_part(op, g, P * m, P),
-                in0=bank_of("turned", op, g, m)[:].rearrange(f"p j {dealt(op)} -> p t a j", t=4),
-                in1=weight[op][:, g, :].unsqueeze(1).unsqueeze(1).to_broadcast([P, 4, 32, 4]),
+                in0=bank_of("turned", op, g, m)[:].rearrange("p j o -> p o j"),
+                in1=weight[op][:, g, :].unsqueeze(1).to_broadcast([P, P, 4]),
                 op=ALU.mult,
             )
 
@@ -345,54 +329,41 @@ def tile_extendeddmdkoopmancrossmoment_x2_kernel(
 
         def cross(engine, c, h, k):
             for g in range(2):
+                columns = slice(256 * g + P * k, 256 * g + P * k + P)
                 nc.tensor.matmul_mx(
-                    out=bank_of("cross", c, h, k)[:].rearrange("p t a -> p (t a)"),
-                    lhsT=fx_code[c][:, g, P * k : P * k + P].bitcast(FP8X4),
-                    lhsT_scale=fx_scale[c][:, g, P * k : P * k + P],
-                    rhs=fy_code[g, h][:].bitcast(FP8X4),
-                    rhs_scale=fy_scale[g, h][:],
+                    out=bank_of("cross", c, h, k)[:].rearrange("p a b -> p (a b)"),
+                    lhsT=f_code["x", c // 2][:, c % 2, columns].bitcast(FP8X4),
+                    lhsT_scale=f_scale["x", c // 2][:, c % 2, columns],
+                    rhs=f_code["y", h][:, g].bitcast(FP8X4),
+                    rhs_scale=f_scale["y", h][:, g],
                     start=(g == 0),
                     stop=(g == 1),
                 )
 
         def lift_cross(engine, c, h, k):
-            r = ring("r", (c, h), [P, 2, P, 4], F32)
-            divide(engine, r[:, k], bank_of("cross", c, h, k)[:].rearrange("p t a -> p a t"))
+            r = ring("half", (c,), [P, 2, 2, 512], F32)
+            divide(engine, r[:, k, h], bank_of("cross", c, h, k)[:].rearrange("p a b -> p (a b)"))
 
-        def round_cross(engine, c, h):
-            s = ring("s", (c, h), [P, 2, 2, P, 2], BF16)
-            copy(engine, s[:], made["r", (c, h)][:].rearrange("p k a (e s) -> p k e a s", e=2))
+        def round_cross(engine, c, h, n):
+            s = ring("s", (c,), [P, 2, 2, 2, P, 2], BF16)
+            values = made["half", (c,)][:, :, h : h + n].rearrange("p k h (a e s) -> p (k h) e a s", e=2, s=2)
+            copy(engine, s[:, :, h : h + n].rearrange("p k h e a s -> p (k h) e a s"), values)
 
         def round_bank(engine, c, h, k):
-            s = ring("s", (c, h), [P, 2, 2, P, 2], BF16)
-            divide(engine, s[:, k], bank_of("cross", c, h, k)[:].rearrange("p (e s) a -> p e a s", e=2))
+            s = ring("s", (c,), [P, 2, 2, 2, P, 2], BF16)
+            values = bank_of("cross", c, h, k)[:].rearrange("p a (b e s) -> p e (a b) s", e=2, s=2)
+            divide(engine, s[:, k, h], values)
 
         def turn_cross(engine, c, h):
-            words = made["s", (c, h)][:].rearrange("p k e a s -> p (k e) (a s)").bitcast(F32)
-            for n in range(4):
-                nc.tensor.transpose(bank_of("plane", c, h)[:, n, :], words[:, n, :], ident[:])
+            for k in range(2):
+                for e in range(2):
+                    words = made["s", (c,)][:, k, h, e].rearrange("p a s -> p (a s)").bitcast(F32)
+                    nc.tensor.transpose(bank_of("plane", c, h)[:, 2 * k + e, :], words, ident[:])
 
         def lift_plane(engine, c, h):
             u = ring("u", (c // 2, h), [P, 2, 2, P, 4], BF16)
             words = u[:, c % 2].rearrange("p k i t -> p (k i t)").bitcast(F32).rearrange("p (k i e) -> p k i e", k=2, e=2)
             copy(engine, words, bank_of("plane", c, h)[:].rearrange("p (k e) i -> p k i e", e=2))
-
-        def cross_back(engine, c, h, k):
-            for t in range(4):
-                for g in range(2):
-                    nc.tensor.matmul_mx(
-                        out=bank_of("back", c, h, k)[:, t, :],
-                        lhsT=fy_code[g, h][:, P * t : P * t + P].bitcast(FP8X4),
-                        lhsT_scale=fy_scale[g, h][:, P * t : P * t + P],
-                        rhs=fx_code[c][:, g, P * k : P * k + P].bitcast(FP8X4),
-                        rhs_scale=fx_scale[c][:, g, P * k : P * k + P],
-                        start=(g == 0),
-                        stop=(g == 1),
-                    )
-
-        def lift_back(engine, c, h, k):
-            u = ring("u", (c // 2, h), [P, 2, 2, P, 4], BF16)
-            divide(engine, u[:, c % 2, k], bank_of("back", c, h, k)[:].rearrange("p t i -> p i t"))
 
         def encode_plane(engine, c, h, n):
             cols = slice(256 * c, 256 * (c + n))
@@ -401,13 +372,17 @@ def tile_extendeddmdkoopmancrossmoment_x2_kernel(
 
         def send_cross(engine, c, h, k):
             rows = slice(256 * c + P * k, 256 * c + P * k + P)
-            values = made["r", (c, h)][:, k].rearrange("p a t -> p (a t)")
+            values = made["half", (c,)][:, k, h]
             nc.sync.dma_start(out=out_0[rows, 512 * h : 512 * h + 512], in_=values)
 
         def send_unit(engine, c, h):
             rows = out_0[256 * c : 256 * c + 256, 512 * h : 512 * h + 512]
-            values = made["r", (c, h)][:].rearrange("p k a t -> p k (a t)")
+            values = made["half", (c,)][:, :, h]
             nc.sync.dma_start(out=rows.rearrange("(k p) n -> p k n", k=2), in_=values)
+
+        def send_rows(engine, c, k):
+            values = made["half", (c,)][:, k].rearrange("p h n -> p (h n)")
+            nc.sync.dma_start(out=out_0[256 * c + P * k : 256 * c + P * k + P, :], in_=values)
 
         def send_pass(engine, h, c, n):
             nc.sync.dma_start(
@@ -436,6 +411,9 @@ def tile_extendeddmdkoopmancrossmoment_x2_kernel(
         def banks(step, c):
             return both(step, c, 0) + both(step, c, 1)
 
+        def rows(step, c):
+            return [(step, c, h, k) for k in range(2) for h in range(2)]
+
         def pair(step, op, g, i):
             return [(step, op, g, 2 * i), (step, op, g, 2 * i + 1)]
 
@@ -446,7 +424,7 @@ def tile_extendeddmdkoopmancrossmoment_x2_kernel(
         tensor += four(turn_rows, "x", 0) + tiles(turn_obs, "y", 0, 3)
         tensor += both(dot_snap, "y", 1, 0) + tiles(dot_obs, "y", 1, 1) + both(dot_snap, "y", 1, 2)
         tensor += four(turn_rows, "x", 1) + tiles(turn_obs, "y", 1, 1)
-        tensor += both(dot_snap, "x", 0, 0) + tiles(dot_obs, "y", 1, 3) + both(dot_snap, "x", 0, 1) + both(dot_snap, "x", 0, 2)
+        tensor += tiles(dot_obs, "y", 1, 3) + both(dot_snap, "x", 0, 0) + both(dot_snap, "x", 0, 1) + both(dot_snap, "x", 0, 2)
         tensor += tiles(dot_obs, "x", 1, 0) + tiles(dot_obs, "x", 1, 1)
         tensor += tiles(turn_obs, "y", 1, 3) + tiles(turn_obs, "x", 1, 0) + tiles(turn_obs, "x", 1, 1)
         tensor += tiles(dot_obs, "x", 1, 2) + both(dot_snap, "x", 0, 3) + tiles(dot_obs, "x", 1, 3)
@@ -454,30 +432,29 @@ def tile_extendeddmdkoopmancrossmoment_x2_kernel(
         tensor += banks(cross, 0) + banks(cross, 1) + banks(cross, 2) + both(turn_cross, 0) + both(turn_cross, 1)
         tensor += banks(cross, 3) + [(turn_cross, c, h) for h in range(2) for c in (2, 3)]
 
-        scalar = [(lift_rows, "y", 0, 0), (lift_rows, "y", 0, 2), (lift_bias_row,)] + four(sort_rows, "y", 1)
-        scalar += [(widen_bias,), (tanh_snap, "y", 0, 0), (lift_rows, "y", 1, 3), (lift_bias_column,), (tanh_snap, "y", 0, 1)]
-        scalar += [(sort_rows, "x", 0, 3)] + tiles(tanh_obs, "y", 0, 3) + [(tanh_snap, "y", 0, 2), (lift_rows, "x", 0, 2)]
-        scalar += four(sort_rows, "x", 1) + tiles(tanh_obs, "y", 1, 1) + [(tanh_snap, "y", 1, 0)]
+        scalar = [(lift_rows, "y", 0, 0), (widen_bias,), (lift_rows, "y", 0, 2), (lift_bias_row,)] + both(sort_pair, "y", 1)
+        scalar += [(tanh_snap, "y", 0, 0), (lift_bias_column,), (tanh_snap, "y", 0, 1), (sort_pair, "x", 0, 1)] + tiles(tanh_obs, "y", 0, 3) + [(tanh_snap, "y", 0, 2), (lift_rows, "x", 0, 3)]
+        scalar += both(sort_pair, "x", 1) + tiles(tanh_obs, "y", 1, 1) + [(tanh_snap, "y", 1, 0)]
         scalar += four(lift_rows, "x", 1) + tiles(tanh_obs, "y", 1, 3) + [(tanh_snap, "y", 1, 2), (tanh_snap, "x", 0, 0)]
         scalar += tiles(tanh_obs, "x", 1, 0) + tiles(tanh_obs, "x", 1, 1) + [(tanh_snap, "x", 0, 1)]
         scalar += tiles(tanh_obs, "x", 1, 2) + [(tanh_snap, "x", 0, 2)] + tiles(tanh_obs, "x", 1, 3) + [(tanh_snap, "x", 0, 3)]
-        scalar += banks(lift_cross, 0)[:3] + banks(lift_cross, 1) + banks(lift_cross, 2) + both(lift_plane, 0) + both(lift_plane, 1)
+        scalar += banks(lift_cross, 0)[:3] + banks(lift_cross, 1) + banks(lift_cross, 2) + [(lift_plane, 0, 0)] + both(lift_plane, 1)
         scalar += [(lift_cross, 3, 0, 1)] + both(round_bank, 3, 1) + [(lift_plane, c, h) for h in range(2) for c in (2, 3)]
 
         vector = [(lift_rows, "y", 0, 1), (encode_pair, "y", 0, 0), (lift_rows, "y", 0, 3), (encode_pair, "y", 0, 1)]
         vector += [(add_bias, "y", 0, c, i) for i in range(2) for c in range(2)]
-        vector += [(repeat_weights, "y", 0, 0)] + [(lift_rows, "y", 1, j) for j in range(3)] + both(add_bias, "y", 0, 2)
-        vector += [(repeat_weights, "y", 0, 1), (encode_half, "y", 1)] + [(lift_rows, "x", 0, j) for j in (0, 1, 3)]
+        vector += [(repeat_weights, "y", 0, 0)] + four(lift_rows, "y", 1) + both(add_bias, "y", 0, 2)
+        vector += [(repeat_weights, "y", 0, 1), (encode_half, "y", 1)] + [(lift_rows, "x", 0, j) for j in range(3)]
         vector += tiles(weigh_obs, "y", 0, 3) + both(add_bias, "y", 1, 0) + both(add_bias, "y", 1, 2)
-        vector += [(repeat_weights, "x", 0, 0), (encode_half, "x", 0), (repeat_weights, "y", 1, 0), (encode_fy, 0, 0)]
+        vector += [(repeat_weights, "x", 0, 0), (encode_half, "x", 0), (repeat_weights, "y", 1, 0), (encode_f, "y", 0, 0, 1)]
         vector += tiles(weigh_obs, "y", 1, 1) + both(add_bias, "x", 0, 0)
-        vector += [(encode_half, "x", 1), (repeat_weights, "y", 1, 2), (encode_fy, 1, 0)]
+        vector += [(encode_half, "x", 1), (repeat_weights, "y", 1, 2), (encode_f, "y", 0, 1, 1)]
         vector += both(add_bias, "x", 0, 1) + both(add_bias, "x", 0, 2) + tiles(weigh_obs, "y", 1, 3)
         vector += tiles(weigh_obs, "x", 1, 0) + tiles(weigh_obs, "x", 1, 1) + both(add_bias, "x", 0, 3)
-        vector += [(encode_fx, 0), (encode_fy, 0, 1), (encode_fy, 1, 1), (repeat_weights, "x", 0, 2), (encode_fx, 1)]
-        vector += tiles(weigh_obs, "x", 1, 2) + tiles(weigh_obs, "x", 1, 3) + [(lift_cross, 0, 1, 1), (encode_fx, 2)]
-        vector += both(round_cross, 0) + [(weigh_snap, "x", 0, 3)] + both(round_cross, 1) + [(encode_fx, 3)]
-        vector += both(round_cross, 2) + [(lift_cross, 3, 0, 0), (encode_plane, 0, 0, 2), (round_cross, 3, 0), (encode_plane, 0, 1, 2)]
+        vector += [(encode_f, "x", 0, 0, 1), (encode_f, "y", 1, 0, 2), (repeat_weights, "x", 0, 2), (encode_f, "x", 0, 1, 1)]
+        vector += tiles(weigh_obs, "x", 1, 2) + tiles(weigh_obs, "x", 1, 3) + [(lift_cross, 0, 1, 1), (encode_f, "x", 1, 0, 1)]
+        vector += [(round_cross, 0, 0, 2), (weigh_snap, "x", 0, 3), (round_cross, 1, 0, 2), (encode_f, "x", 1, 1, 1)]
+        vector += [(round_cross, 2, 0, 2), (lift_plane, 0, 1), (lift_cross, 3, 0, 0), (encode_plane, 0, 0, 2), (round_cross, 3, 0, 1), (encode_plane, 0, 1, 2)]
         vector += both(lift_cross, 3, 1) + [(encode_plane, c, h, 1) for h in range(2) for c in (2, 3)]
 
         pool = [(weigh_snap,) + key for key in POOL]
@@ -510,9 +487,10 @@ def tile_extendeddmdkoopmancrossmoment_x2_kernel(
                     key = (op, g, j)
                     bank = ("bank", ("rows",) + key)
                     lifted = ("pair", (op, g, j // 2)) if (op, g) in PAIRWISE else half_key(op, g)
-                    if key in SORTED:
-                        wire((sort_rows,) + key, [], ("sorted", key))
-                        wire((turn_rows,) + key, [(sort_rows,) + key], bank, ("sorted", key))
+                    slots = (op, g, j // 2)
+                    if slots in SORTED:
+                        wire((sort_pair,) + slots, [], ("sorted", slots))
+                        wire((turn_rows,) + key, [(sort_pair,) + slots], bank, ("sorted", slots))
                     else:
                         wire((turn_rows,) + key, [], bank)
                     wire((lift_rows,) + key, [(turn_rows,) + key], bank, lifted)
@@ -548,42 +526,47 @@ def tile_extendeddmdkoopmancrossmoment_x2_kernel(
                         wire((tanh_obs,) + tile, [(dot_obs,) + tile, (lift_bias_column,)], sums, ("t", tile))
                         wire((turn_obs,) + tile, [(tanh_obs,) + tile], turned, ("t", tile))
                         wire((weigh_obs,) + tile, [(turn_obs,) + tile], turned, f_key(*key))
-        for g in range(2):
-            for h in range(2):
-                wire((encode_fy, g, h), weighed("y", g, 2 * h) + weighed("y", g, 2 * h + 1), f_key("y", g, 2 * h))
+        coded_f = {}
+        rounded = {}
+        for step in vector + scalar:
+            if step[0] == encode_f:
+                op, n, first, count = step[1:]
+                parts = range(first, first + count)
+                if op == "y":
+                    keys = [(op, g, 2 * n + c) for g in parts for c in range(2)]
+                else:
+                    keys = [(op, g, 2 * n + c) for c in parts for g in range(2)]
+                wire(step, [source for key in keys for source in weighed(*key)], ("f", (op, n)))
+                for part in parts:
+                    coded_f[op, n, part] = step
+            if step[0] == round_cross:
+                c, h, n = step[1:]
+                wire(step, banks(lift_cross, c)[2 * h : 2 * (h + n)], ("half", (c,)), ("s", (c,)))
+                for k in range(n):
+                    rounded[c, h + k] = [step]
         laid = {}
         for c in range(4):
-            wire((encode_fx, c), weighed("x", 0, c) + weighed("x", 1, c), f_key("x", 0, c))
             for h in range(2):
                 unit = (c, h)
-                coded = [(encode_fx, c), (encode_fy, 0, h), (encode_fy, 1, h)]
+                coded = [coded_f["x", c // 2, c % 2], coded_f["y", h, 0], coded_f["y", h, 1]]
                 for k in range(2):
                     bank = ("bank", ("cross", c, h, k))
                     wire((cross, c, h, k), coded, bank)
                     if unit in FROM_BANK:
-                        wire((round_bank, c, h, k), [(cross, c, h, k)], bank, ("s", unit))
+                        wire((round_bank, c, h, k), [(cross, c, h, k)], bank, ("s", (c,)))
+                        rounded[unit] = both(round_bank, c, h)
                     first = round_bank if unit in FROM_BANK else cross
-                    wire((lift_cross, c, h, k), [(first, c, h, k)], bank, ("r", unit))
+                    wire((lift_cross, c, h, k), [(first, c, h, k)], bank, ("half", (c,)))
                     if (send_cross, c, h, k) in sync:
-                        wire((send_cross, c, h, k), [(lift_cross, c, h, k)], ("r", unit))
+                        wire((send_cross, c, h, k), [(lift_cross, c, h, k)], ("half", (c,)))
+                if (send_rows, c, h) in sync:
+                    wire((send_rows, c, h), [(lift_cross, c, n, h) for n in range(2)], ("half", (c,)))
                 if (send_unit, c, h) in sync:
-                    wire((send_unit, c, h), both(lift_cross, c, h), ("r", unit))
-                if unit in TWICE:
-                    for k in range(2):
-                        bank = ("bank", ("back", c, h, k))
-                        wire((cross_back, c, h, k), coded, bank)
-                        wire((lift_back, c, h, k), [(cross_back, c, h, k)], bank, ("u", (c // 2, h)))
-                    laid[unit] = both(lift_back, c, h)
-                else:
-                    bank = ("bank", ("plane", c, h))
-                    if unit in FROM_BANK:
-                        rounded = both(round_bank, c, h)
-                    else:
-                        rounded = [(round_cross, c, h)]
-                        wire(rounded[0], both(lift_cross, c, h), ("r", unit), ("s", unit))
-                    wire((turn_cross, c, h), rounded, bank, ("s", unit))
-                    wire((lift_plane, c, h), [(turn_cross, c, h)], bank, ("u", (c // 2, h)))
-                    laid[unit] = [(lift_plane, c, h)]
+                    wire((send_unit, c, h), both(lift_cross, c, h), ("half", (c,)))
+                bank = ("bank", ("plane", c, h))
+                wire((turn_cross, c, h), rounded[unit], bank, ("s", (c,)))
+                wire((lift_plane, c, h), [(turn_cross, c, h)], bank, ("u", (c // 2, h)))
+                laid[unit] = [(lift_plane, c, h)]
         encoded = {}
         for step in vector:
             if step[0] == encode_plane:

@@ -24,9 +24,9 @@ SNAP = POOL + [("x", 0, 3)]
 SORTED = [(op, 1, i) for op in ("y", "x") for i in range(2)] + [("x", 0, 1)]
 PAIRWISE = [("y", 0)]
 FROM_BANK = [(3, 1)]
-SCALAR_QUADS = (1, 3)
+SCALAR_QUADS = (0, 1, 2, 3)
 SHARED = {("y", 0, 2): ("y", 0, 1), ("x", 0, 1): ("x", 0, 0)}
-DEPTH = {"bank": BANKS, "sorted": 2, "pair": 2, "half": 3, "z": 3, "th": 4, "t": 5, "f": 4, "run": 3, "s": 3, "u": 4}
+DEPTH = {"bank": BANKS, "sorted": 3, "pair": 2, "half": 3, "z": 3, "th": 4, "t": 5, "f": 4, "run": 3, "s": 3, "u": 4}
 
 
 def tile_extendeddmdkoopmancrossmoment_x2_kernel(
@@ -238,26 +238,18 @@ def tile_extendeddmdkoopmancrossmoment_x2_kernel(
         def snap_sums(op, g, c, i):
             return bank_of("snap", op, g, c, i)[:].rearrange("p (k a) r -> p k (a r)", k=2)
 
-        def snap_pass(op, g, c, i, n):
-            for k in range(2):
-                nc.tensor.matmul_mx(
-                    out=snap_sums(op, g, c, i)[:, k, :],
-                    lhsT=row_code[op, g][:, n, 2 * i + k, :].bitcast(FP8X4),
-                    lhsT_scale=row_scale[op, g][:, n, 2 * i + k, :],
-                    rhs=w_code[:, n, 256 * c : 256 * c + 256].bitcast(FP8X4),
-                    rhs_scale=w_scale[4 * n : P, 256 * c : 256 * c + 256],
-                    start=(n == 0 and k == 0),
-                    stop=(n == 1 and k == 1),
-                )
-
         def dot_snap(engine, op, g, c, i):
             for n in range(2):
-                snap_pass(op, g, c, i, n)
-
-        def dot_first(engine):
-            for n in range(2):
-                for c in range(2):
-                    snap_pass("y", 0, c, 0, n)
+                for k in range(2):
+                    nc.tensor.matmul_mx(
+                        out=snap_sums(op, g, c, i)[:, k, :],
+                        lhsT=row_code[op, g][:, n, 2 * i + k, :].bitcast(FP8X4),
+                        lhsT_scale=row_scale[op, g][:, n, 2 * i + k, :],
+                        rhs=w_code[:, n, 256 * c : 256 * c + 256].bitcast(FP8X4),
+                        rhs_scale=w_scale[4 * n : P, 256 * c : 256 * c + 256],
+                        start=(n == 0 and k == 0),
+                        stop=(n == 1 and k == 1),
+                    )
 
         def add_bias(engine, op, g, c, i):
             z = ring("z", (op, g, c), [P, 2, 256, 2], F32)
@@ -347,7 +339,14 @@ def tile_extendeddmdkoopmancrossmoment_x2_kernel(
         def round_cross(engine, c, h, n):
             s = ring("s", (c,), [P, 2, 2, 2, P, 2], BF16)
             values = made["half", (c,)][:, :, h : h + n].rearrange("p k h (a e s) -> p (k h) e a s", e=2, s=2)
-            copy(engine, s[:, :, h : h + n].rearrange("p k h e a s -> p (k h) e a s"), values)
+            out = s[:, :, h : h + n].rearrange("p k h e a s -> p (k h) e a s")
+            if engine == "G":
+                for e in range(2):
+                    nc.gpsimd.tensor_scalar(
+                        out=out[:, :, e], in0=values[:, :, e], scalar1=1.0, scalar2=0.0, op0=ALU.mult, op1=ALU.add
+                    )
+            else:
+                copy(engine, out, values)
 
         def round_bank(engine, c, h, k):
             s = ring("s", (c,), [P, 2, 2, 2, P, 2], BF16)
@@ -418,7 +417,7 @@ def tile_extendeddmdkoopmancrossmoment_x2_kernel(
             return [(step, op, g, 2 * i), (step, op, g, 2 * i + 1)]
 
         tensor = pair(turn_rows, "y", 0, 0) + [(spread_bias,)] + pair(turn_rows, "y", 0, 1)
-        tensor += [(dot_first,), (dot_snap, "y", 0, 0, 1), (dot_snap, "y", 0, 1, 1)]
+        tensor += [(dot_snap, "y", 0, c, i) for i in range(2) for c in range(2)]
         tensor += four(turn_rows, "y", 1) + [(turn_bias,)]
         tensor += both(dot_snap, "y", 0, 2) + tiles(dot_obs, "y", 0, 3)
         tensor += four(turn_rows, "x", 0) + tiles(turn_obs, "y", 0, 3)
@@ -430,21 +429,21 @@ def tile_extendeddmdkoopmancrossmoment_x2_kernel(
         tensor += tiles(dot_obs, "x", 1, 2) + both(dot_snap, "x", 0, 3) + tiles(dot_obs, "x", 1, 3)
         tensor += tiles(turn_obs, "x", 1, 2) + tiles(turn_obs, "x", 1, 3)
         tensor += banks(cross, 0) + banks(cross, 1) + banks(cross, 2) + both(turn_cross, 0) + both(turn_cross, 1)
-        tensor += banks(cross, 3) + [(turn_cross, c, h) for h in range(2) for c in (2, 3)]
+        tensor += banks(cross, 3) + both(turn_cross, 2) + both(turn_cross, 3)
 
         scalar = [(lift_rows, "y", 0, 0), (widen_bias,), (lift_rows, "y", 0, 2), (lift_bias_row,)] + both(sort_pair, "y", 1)
-        scalar += [(tanh_snap, "y", 0, 0), (lift_bias_column,), (tanh_snap, "y", 0, 1), (sort_pair, "x", 0, 1)] + tiles(tanh_obs, "y", 0, 3) + [(tanh_snap, "y", 0, 2), (lift_rows, "x", 0, 3)]
-        scalar += both(sort_pair, "x", 1) + tiles(tanh_obs, "y", 1, 1) + [(tanh_snap, "y", 1, 0)]
+        scalar += [(tanh_snap, "y", 0, 0), (lift_bias_column,), (tanh_snap, "y", 0, 1), (sort_pair, "x", 0, 1)] + tiles(tanh_obs, "y", 0, 3)
+        scalar += [(tanh_snap, "y", 0, 2)] + pair(lift_rows, "x", 0, 1) + [(sort_pair, "x", 1, 1)] + tiles(tanh_obs, "y", 1, 1) + [(tanh_snap, "y", 1, 0)]
         scalar += four(lift_rows, "x", 1) + tiles(tanh_obs, "y", 1, 3) + [(tanh_snap, "y", 1, 2), (tanh_snap, "x", 0, 0)]
         scalar += tiles(tanh_obs, "x", 1, 0) + tiles(tanh_obs, "x", 1, 1) + [(tanh_snap, "x", 0, 1)]
         scalar += tiles(tanh_obs, "x", 1, 2) + [(tanh_snap, "x", 0, 2)] + tiles(tanh_obs, "x", 1, 3) + [(tanh_snap, "x", 0, 3)]
         scalar += banks(lift_cross, 0)[:3] + banks(lift_cross, 1) + banks(lift_cross, 2) + [(lift_plane, 0, 0)] + both(lift_plane, 1)
-        scalar += [(lift_cross, 3, 0, 1)] + both(round_bank, 3, 1) + [(lift_plane, c, h) for h in range(2) for c in (2, 3)]
+        scalar += [(lift_cross, 3, 0, 1)] + both(round_bank, 3, 1) + [(lift_plane, 2, 0), (lift_plane, 3, 0), (lift_plane, 2, 1), (lift_plane, 3, 1)]
 
         vector = [(lift_rows, "y", 0, 1), (encode_pair, "y", 0, 0), (lift_rows, "y", 0, 3), (encode_pair, "y", 0, 1)]
         vector += [(add_bias, "y", 0, c, i) for i in range(2) for c in range(2)]
         vector += [(repeat_weights, "y", 0, 0)] + four(lift_rows, "y", 1) + both(add_bias, "y", 0, 2)
-        vector += [(repeat_weights, "y", 0, 1), (encode_half, "y", 1)] + [(lift_rows, "x", 0, j) for j in range(3)]
+        vector += [(encode_half, "y", 1), (repeat_weights, "y", 0, 1), (sort_pair, "x", 1, 0)] + pair(lift_rows, "x", 0, 0)
         vector += tiles(weigh_obs, "y", 0, 3) + both(add_bias, "y", 1, 0) + both(add_bias, "y", 1, 2)
         vector += [(repeat_weights, "x", 0, 0), (encode_half, "x", 0), (repeat_weights, "y", 1, 0), (encode_f, "y", 0, 0, 1)]
         vector += tiles(weigh_obs, "y", 1, 1) + both(add_bias, "x", 0, 0)
@@ -454,14 +453,14 @@ def tile_extendeddmdkoopmancrossmoment_x2_kernel(
         vector += [(encode_f, "x", 0, 0, 1), (encode_f, "y", 1, 0, 2), (repeat_weights, "x", 0, 2), (encode_f, "x", 0, 1, 1)]
         vector += tiles(weigh_obs, "x", 1, 2) + tiles(weigh_obs, "x", 1, 3) + [(lift_cross, 0, 1, 1), (encode_f, "x", 1, 0, 1)]
         vector += [(round_cross, 0, 0, 2), (weigh_snap, "x", 0, 3), (round_cross, 1, 0, 2), (encode_f, "x", 1, 1, 1)]
-        vector += [(round_cross, 2, 0, 2), (lift_plane, 0, 1), (lift_cross, 3, 0, 0), (encode_plane, 0, 0, 2), (round_cross, 3, 0, 1), (encode_plane, 0, 1, 2)]
+        vector += [(lift_plane, 0, 1), (round_cross, 2, 0, 2), (lift_cross, 3, 0, 0), (encode_plane, 0, 0, 2), (round_cross, 3, 0, 1), (encode_plane, 0, 1, 2)]
         vector += both(lift_cross, 3, 1) + [(encode_plane, c, h, 1) for h in range(2) for c in (2, 3)]
 
         pool = [(weigh_snap,) + key for key in POOL]
 
         sync = both(send_cross, 0, 0) + [(send_unit, 0, 1)] + both(send_unit, 1) + both(send_unit, 2)
         sync += both(send_cross, 3, 0) + [(send_pass, 0, 0, 2), (send_pass, 1, 0, 2)] + both(send_cross, 3, 1)
-        sync += [(send_pass, 0, 2, 2), (send_pass, 1, 2, 2), (send_scales,)]
+        sync += [(send_pass, 0, 2, 2), (send_pass, 1, 2, 1), (send_pass, 1, 3, 1), (send_scales,)]
 
 
         reads = {}
@@ -479,8 +478,6 @@ def tile_extendeddmdkoopmancrossmoment_x2_kernel(
         wire((widen_bias,), [])
         wire((turn_bias,), [(widen_bias,)], ("bank", ("bias_column",)))
         wire((lift_bias_column,), [(turn_bias,)], ("bank", ("bias_column",)))
-        first_banks = [("bank", ("snap", "y", 0, c, 0)) for c in range(2)]
-        wire((dot_first,), [(encode_pair, "y", 0, 0)], *first_banks)
         for op in ("y", "x"):
             for g in range(2):
                 for j in range(4):
@@ -506,9 +503,8 @@ def tile_extendeddmdkoopmancrossmoment_x2_kernel(
                     if key in SNAP:
                         for i in range(2):
                             bank = ("bank", ("snap",) + key + (i,))
-                            dot = (dot_first,) if bank in first_banks else (dot_snap,) + key + (i,)
-                            if bank not in first_banks:
-                                wire(dot, [coded[i]], bank)
+                            dot = (dot_snap,) + key + (i,)
+                            wire(dot, [coded[i]], bank)
                             wire((add_bias,) + key + (i,), [dot, (lift_bias_row,)], bank, ("z", key))
                         wire((tanh_snap,) + key, both(add_bias, *key), ("z", key), ("th", key))
                         if key in POOL:
@@ -528,7 +524,7 @@ def tile_extendeddmdkoopmancrossmoment_x2_kernel(
                         wire((weigh_obs,) + tile, [(turn_obs,) + tile], turned, f_key(*key))
         coded_f = {}
         rounded = {}
-        for step in vector + scalar:
+        for step in vector + scalar + pool:
             if step[0] == encode_f:
                 op, n, first, count = step[1:]
                 parts = range(first, first + count)

@@ -26,7 +26,7 @@ PAIRWISE = [("y", 0)]
 FROM_BANK = [(3, 1)]
 SCALAR_QUADS = (0, 1, 2, 3)
 SHARED = {("y", 0, 2): ("y", 0, 1), ("x", 0, 1): ("x", 0, 0)}
-DEPTH = {"bank": BANKS, "sorted": 3, "pair": 2, "half": 3, "z": 3, "th": 4, "t": 5, "f": 4, "run": 3, "s": 3, "u": 4}
+DEPTH = {"bank": BANKS, "sorted": 3, "pair": 2, "half": 3, "z": 3, "th": 4, "t": 5, "f": 4, "run": 4, "s": 3, "u": 4}
 
 
 def tile_extendeddmdkoopmancrossmoment_x2_kernel(
@@ -119,6 +119,8 @@ def tile_extendeddmdkoopmancrossmoment_x2_kernel(
         def copy(engine, out, in_):
             if engine == "S":
                 nc.scalar.copy(out=out, in_=in_)
+            elif engine == "G":
+                nc.gpsimd.tensor_copy(out=out, in_=in_)
             else:
                 nc.vector.tensor_copy(out=out, in_=in_)
 
@@ -437,26 +439,26 @@ def tile_extendeddmdkoopmancrossmoment_x2_kernel(
         scalar += four(lift_rows, "x", 1) + tiles(tanh_obs, "y", 1, 3) + [(tanh_snap, "y", 1, 2), (tanh_snap, "x", 0, 0)]
         scalar += tiles(tanh_obs, "x", 1, 0) + tiles(tanh_obs, "x", 1, 1) + [(tanh_snap, "x", 0, 1)]
         scalar += tiles(tanh_obs, "x", 1, 2) + [(tanh_snap, "x", 0, 2)] + tiles(tanh_obs, "x", 1, 3) + [(tanh_snap, "x", 0, 3)]
-        scalar += banks(lift_cross, 0)[:3] + banks(lift_cross, 1) + banks(lift_cross, 2) + [(lift_plane, 0, 0)] + both(lift_plane, 1)
+        scalar += banks(lift_cross, 0) + banks(lift_cross, 1) + banks(lift_cross, 2) + [(lift_plane, 0, 0)] + both(lift_plane, 1)
         scalar += [(lift_cross, 3, 0, 1)] + both(round_bank, 3, 1) + [(lift_plane, 2, 0), (lift_plane, 3, 0), (lift_plane, 2, 1), (lift_plane, 3, 1)]
 
         vector = [(lift_rows, "y", 0, 1), (encode_pair, "y", 0, 0), (lift_rows, "y", 0, 3), (encode_pair, "y", 0, 1)]
         vector += [(add_bias, "y", 0, c, i) for i in range(2) for c in range(2)]
-        vector += [(repeat_weights, "y", 0, 0)] + four(lift_rows, "y", 1) + both(add_bias, "y", 0, 2)
+        vector += four(lift_rows, "y", 1) + both(add_bias, "y", 0, 2)
         vector += [(encode_half, "y", 1), (repeat_weights, "y", 0, 1), (sort_pair, "x", 1, 0)] + pair(lift_rows, "x", 0, 0)
         vector += tiles(weigh_obs, "y", 0, 3) + both(add_bias, "y", 1, 0) + both(add_bias, "y", 1, 2)
-        vector += [(repeat_weights, "x", 0, 0), (encode_half, "x", 0), (repeat_weights, "y", 1, 0), (encode_f, "y", 0, 0, 1)]
+        vector += [(encode_half, "x", 0), (repeat_weights, "y", 1, 0), (encode_f, "y", 0, 0, 1)]
         vector += tiles(weigh_obs, "y", 1, 1) + both(add_bias, "x", 0, 0)
         vector += [(encode_half, "x", 1), (repeat_weights, "y", 1, 2), (encode_f, "y", 0, 1, 1)]
         vector += both(add_bias, "x", 0, 1) + both(add_bias, "x", 0, 2) + tiles(weigh_obs, "y", 1, 3)
         vector += tiles(weigh_obs, "x", 1, 0) + tiles(weigh_obs, "x", 1, 1) + both(add_bias, "x", 0, 3)
         vector += [(encode_f, "x", 0, 0, 1), (encode_f, "y", 1, 0, 2), (repeat_weights, "x", 0, 2), (encode_f, "x", 0, 1, 1)]
-        vector += tiles(weigh_obs, "x", 1, 2) + tiles(weigh_obs, "x", 1, 3) + [(lift_cross, 0, 1, 1), (encode_f, "x", 1, 0, 1)]
+        vector += tiles(weigh_obs, "x", 1, 2) + tiles(weigh_obs, "x", 1, 3) + [(encode_f, "x", 1, 0, 1)]
         vector += [(round_cross, 0, 0, 2), (weigh_snap, "x", 0, 3), (round_cross, 1, 0, 2), (encode_f, "x", 1, 1, 1)]
         vector += [(lift_plane, 0, 1), (round_cross, 2, 0, 2), (lift_cross, 3, 0, 0), (encode_plane, 0, 0, 2), (round_cross, 3, 0, 1), (encode_plane, 0, 1, 2)]
         vector += both(lift_cross, 3, 1) + [(encode_plane, c, h, 1) for h in range(2) for c in (2, 3)]
 
-        pool = [(weigh_snap,) + key for key in POOL]
+        pool = [(repeat_weights, op, 0, 0) for op in ("y", "x")] + [(weigh_snap,) + key for key in POOL]
 
         sync = both(send_cross, 0, 0) + [(send_unit, 0, 1)] + both(send_unit, 1) + both(send_unit, 2)
         sync += both(send_cross, 3, 0) + [(send_pass, 0, 0, 2), (send_pass, 1, 0, 2)] + both(send_cross, 3, 1)

@@ -437,8 +437,8 @@ def tile_extendeddmdkoopmancrossmoment_x2_kernel(
         scalar += [(tanh_snap, "y", 0, 0), (lift_bias_column,), (tanh_snap, "y", 0, 1), (sort_pair, "x", 0, 1)] + tiles(tanh_obs, "y", 0, 3)
         scalar += [(tanh_snap, "y", 0, 2)] + pair(lift_rows, "x", 0, 1) + [(sort_pair, "x", 1, 1)] + tiles(tanh_obs, "y", 1, 1) + [(tanh_snap, "y", 1, 0)]
         scalar += four(lift_rows, "x", 1) + tiles(tanh_obs, "y", 1, 3) + [(tanh_snap, "y", 1, 2), (tanh_snap, "x", 0, 0)]
-        scalar += tiles(tanh_obs, "x", 1, 0) + tiles(tanh_obs, "x", 1, 1) + [(tanh_snap, "x", 0, 1)]
-        scalar += tiles(tanh_obs, "x", 1, 2) + [(tanh_snap, "x", 0, 2)] + tiles(tanh_obs, "x", 1, 3) + [(tanh_snap, "x", 0, 3)]
+        scalar += tiles(tanh_obs, "x", 1, 0) + tiles(tanh_obs, "x", 1, 1) + [(tanh_snap, "x", 0, 1), (tanh_snap, "x", 0, 2)]
+        scalar += tiles(tanh_obs, "x", 1, 2) + tiles(tanh_obs, "x", 1, 3) + [(tanh_snap, "x", 0, 3)]
         scalar += banks(lift_cross, 0) + banks(lift_cross, 1) + banks(lift_cross, 2) + [(lift_plane, 0, 0)] + both(lift_plane, 1)
         scalar += [(lift_cross, 3, 0, 1)] + both(round_bank, 3, 1) + [(lift_plane, 2, 0), (lift_plane, 3, 0), (lift_plane, 2, 1), (lift_plane, 3, 1)]
 

from contextlib import ExitStack

import concourse.mybir as mybir
from concourse.masks import make_identity

SIZE = 1024
P = 128
FLOPS = 3 * 2 * SIZE * SIZE * SIZE
INV_DIV = 1.0 / 32.0

F32 = mybir.dt.float32
BF16 = mybir.dt.bfloat16
U32 = mybir.dt.uint32
I32 = mybir.dt.int32
U8 = mybir.dt.uint8
FP8X4 = mybir.dt.float8_e4m3fn_x4
ACT = mybir.ActivationFunctionType
ALU = mybir.AluOpType

BANKS = 8
ALIGN = 64
POOL = [("y", 0, 0), ("y", 0, 1), ("y", 0, 2), ("y", 1, 0), ("y", 1, 2), ("x", 0, 0), ("x", 0, 1), ("x", 0, 2)]
SNAP = POOL + [("x", 0, 3)]
SORTED = [(op, 1, i) for op in ("y", "x") for i in range(2)] + [("x", 0, 1)]
PAIRWISE = [("y", 0)]
FROM_BANK = [(3, 1)]
SCALAR_QUADS = (0, 1, 2, 3)
SHARED = {("y", 0, 2): ("y", 0, 1), ("x", 0, 1): ("x", 0, 0)}
DEPTH = {"bank": BANKS, "sorted": 3, "pair": 2, "half": 3, "z": 3, "th": 4, "t": 5, "f": 4, "run": 4, "s": 3, "u": 4}


def tile_extendeddmdkoopmancrossmoment_x2_kernel(
    tc, x, y, w_words, w_scales, b, p, q, out_0, out_1, out_2
):
    nc = tc.nc
    with ExitStack() as ctx:
        keep = ctx.enter_context(tc.tile_pool(name="keep", bufs=1))
        work = ctx.enter_context(tc.tile_pool(name="work", bufs=3))
        psum = ctx.enter_context(tc.psum_pool(name="psum", bufs=1))
        ctx.enter_context(tc.manual_schedule())

        made = {}


        ident = keep.tile([P, P], F32, name="ident", align_bytes=ALIGN)
        make_identity(nc, ident[:])

        w_scale = keep.tile([P, SIZE], U8, name="w_scale", align_bytes=ALIGN)
        nc.vector.memset(w_scale[:].bitcast(I32), 0)
        b_square = keep.tile([P, P], F32, name="b_square", align_bytes=ALIGN)
        nc.gpsimd.memset(b_square[:], 0.0)

        b_rows = keep.tile([P, 8], BF16, name="b_rows", align_bytes=ALIGN)
        nc.scalar.dma_start(out=b_rows[:], in_=b.rearrange("(n w) -> n w", w=8))

        row_words = {}
        row_pairs = {}

        def load_rows(op, source, g, j, n):
            rows = keep.tile([P, n, SIZE], BF16, name=f"rows_{op}{g}{j}", align_bytes=ALIGN)
            nc.sync.dma_start(
                out=rows[:], in_=source.rearrange("(g p j) d -> g p j d", g=2, j=4)[g, :, j : j + n, :]
            )
            row_pairs[op, g, j // 2] = rows[:].bitcast(F32)
            for k in range(n):
                row_words[op, g, j + k] = rows[:, k, :].bitcast(F32)

        w_code = keep.tile([P, 2, SIZE], U32, name="w_code", align_bytes=ALIGN)
        w_source = w_words.rearrange("c p n t -> p c (n t)")

        def load_w(passes, h):
            nc.sync.dma_start(
                out=w_code[:, passes, 512 * h : 512 * h + 512].bitcast(I32),
                in_=w_source[:, passes, 2048 * h : 2048 * h + 2048].bitcast(I32),
            )

        def load_w_scales():
            for quad in range(4):
                nc.sync.dma_start(
                    out=w_scale[32 * quad : 32 * quad + 8, :].bitcast(I32),
                    in_=w_scales[:, 4 * quad : 4 * quad + 4, :].bitcast(I32),
                )

        weight = {}

        def load_weights(op, source):
            weight[op] = keep.tile([P, 2, 4], BF16, name=f"weight_{op}", align_bytes=ALIGN)
            nc.sync.dma_start(out=weight[op][:], in_=source.rearrange("(g p j) -> p g j", g=2, j=4))

        b_tiles = keep.tile([8, P], BF16, name="b_tiles", align_bytes=ALIGN)
        nc.scalar.dma_start(out=b_tiles[:], in_=b.rearrange("(m n) -> m n", n=P))

        load_rows("y", y, 0, 0, 1)
        load_rows("y", y, 0, 1, 1)
        load_rows("y", y, 0, 2, 2)
        load_w_scales()
        load_w(slice(0, 1), 0)
        load_w(slice(1, 2), 0)
        load_rows("y", y, 1, 0, 2)
        load_rows("y", y, 1, 2, 2)
        load_weights("y", q)
        load_w(slice(0, 2), 1)
        load_weights("x", p)
        for g in range(2):
            for j in range(0, 4, 2):
                load_rows("x", x, g, j, 2)

        def ring(tag, key, dims, dtype):
            if (tag, key) not in made:
                if tag == "bank":
                    made[tag, key] = psum.tile(dims, dtype, name=tag, tag=tag, bufs=DEPTH[tag])
                else:
                    made[tag, key] = work.tile(dims, dtype, name=tag, tag=tag, bufs=DEPTH[tag], align_bytes=ALIGN)
            return made[tag, key]

        def bank_of(*key):
            return ring("bank", key, [P, 4, P], F32)

        def copy(engine, out, in_):
            if engine == "S":
                nc.scalar.copy(out=out, in_=in_)
            elif engine == "G":
                nc.gpsimd.tensor_copy(out=out, in_=in_)
            else:
                nc.vector.tensor_copy(out=out, in_=in_)

        def divide(engine, out, in_):
            if engine == "S":
                nc.scalar.activation(out=out, in_=in_, func=ACT.Copy, scale=INV_DIV)
            else:
                nc.vector.tensor_scalar(out=out, in0=in_, scalar1=INV_DIV, scalar2=None, op0=ALU.mult)

        def quantize(code, scale, in_):
            nc.vector.quantize_mx(out=code.bitcast(FP8X4), scales=scale, in_=in_)


        row_code = {}
        row_scale = {}
        for op in ("y", "x"):
            for g in range(2):
                row_code[op, g] = keep.tile([P, 2, 4, P], U32, name=f"row_code_{op}{g}", align_bytes=ALIGN)
                row_scale[op, g] = keep.tile([P, 2, 4, P], U8, name=f"row_scale_{op}{g}", align_bytes=ALIGN)

        def half_key(op, g):
            return ("half", (op, g))

        def sort_pair(engine, op, g, i):
            words = ring("sorted", (op, g, i), [P, 4, 2, P], F32)
            copy(engine, words[:], row_pairs[op, g, i].rearrange("p j (n a e) -> p (j n) e a", n=2, e=2))

        def turn_rows(engine, op, g, j):
            bank = bank_of("rows", op, g, j)
            words = row_words[op, g, j]
            for n in range(2):
                for e in range(2):
                    if (op, g, j // 2) in SORTED:
                        columns = made["sorted", (op, g, j // 2)][:, 2 * (j % 2) + n, e, :]
                    else:
                        columns = words[:, 256 * n + e : 256 * (n + 1) : 2]
                    nc.tensor.transpose(bank[:, 2 * n + e, :], columns, ident[:])

        def lift_rows(engine, op, g, j):
            bank = bank_of("rows", op, g, j)
            if (op, g) in PAIRWISE:
                out = ring("pair", (op, g, j // 2), [P, 2, 2, P, 2], F32)[:, :, j % 2]
            else:
                out = ring(*half_key(op, g), [P, 2, 4, P, 2], F32)[:, :, j]
            copy(engine, out, bank[:].rearrange("p (n e) r -> p n r e", e=2))

        def encode_pair(engine, op, g, i):
            j = 2 * i
            pair = made["pair", (op, g, i)]
            for n in range(2):
                quantize(
                    row_code[op, g][:, n, j : j + 2].rearrange("p j r -> p (j r)"),
                    row_scale[op, g][:, n, j : j + 2].rearrange("p j r -> p (j r)"),
                    pair[:, n].rearrange("p j r e -> p (j r e)").bitcast(BF16),
                )

        def encode_half(engine, op, g):
            quantize(
                row_code[op, g][:].rearrange("p n j r -> p (n j r)"),
                row_scale[op, g][:].rearrange("p n j r -> p (n j r)"),
                made[half_key(op, g)][:].rearrange("p n j r e -> p (n j r e)").bitcast(BF16),
            )


        bias_words = keep.tile([P, P, 4], F32, name="bias_words", align_bytes=ALIGN)
        bias_row = bias_words[:].rearrange("p n m -> p (n m)").bitcast(BF16)
        bias_column = keep.tile([P, 8], F32, name="bias_column", align_bytes=ALIGN)

        def spread_bias(engine):
            words = b_rows[:].bitcast(F32)
            for m in range(4):
                nc.tensor.transpose(bank_of("bias_row")[:, m, :], words[:, m : m + 1].to_broadcast([P, P]), ident[:])

        def lift_bias_row(engine):
            copy(engine, bias_words[:], bank_of("bias_row")[:].rearrange("p m n -> p n m"))

        def widen_bias(engine):
            copy(engine, b_square[0:8, :], b_tiles[:])

        def turn_bias(engine):
            nc.tensor.transpose(bank_of("bias_column")[:, 0, :], b_square[:], ident[:])

        def lift_bias_column(engine):
            copy(engine, bias_column[:], bank_of("bias_column")[:, 0, 0:8])

        def repeat_weights(engine, op, g, c):
            run = ring("run", (op, g, c), [P, 16, 4], BF16)
            copy(engine, run[:], weight[op][:, g].unsqueeze(1).to_broadcast([P, 16, 4]))


        f_code = {}
        f_scale = {}
        for op in ("y", "x"):
            for n in range(2):
                f_code[op, n] = keep.tile([P, 2, 512], U32, name=f"f_code_{op}{n}", align_bytes=ALIGN)
                f_scale[op, n] = keep.tile([P, 2, 512], U8, name=f"f_scale_{op}{n}", align_bytes=ALIGN)

        def f_key(op, g, c):
            return ("f", (op, c // 2))

        def f_part(op, g, first, n):
            tag, key = f_key(op, g, first // 256)
            f = ring(tag, key, [P, 2, 512, 4], BF16)
            if op == "y":
                return f[:, g, first % 512 : first % 512 + n]
            o = 256 * g + first % 256
            return f[:, first // 256 % 2, o : o + n]

        def encode_f(engine, op, n, first, count):
            part = slice(first, first + count)
            quantize(
                f_code[op, n][:, part].rearrange("p a o -> p (a o)"),
                f_scale[op, n][:, part].rearrange("p a o -> p (a o)"),
                made["f", (op, n)][:, part].rearrange("p a o j -> p (a o j)"),
            )

        def snap_sums(op, g, c, i):
            return bank_of("snap", op, g, c, i)[:].rearrange("p (k a) r -> p k (a r)", k=2)

        def dot_snap(engine, op, g, c, i):
            for n in range(2):
                for k in range(2):
                    nc.tensor.matmul_mx(
                        out=snap_sums(op, g, c, i)[:, k, :],
                        lhsT=row_code[op, g][:, n, 2 * i + k, :].bitcast(FP8X4),
                        lhsT_scale=row_scale[op, g][:, n, 2 * i + k, :],
                        rhs=w_code[:, n, 256 * c : 256 * c + 256].bitcast(FP8X4),
                        rhs_scale=w_scale[4 * n : P, 256 * c : 256 * c + 256],
                        start=(n == 0 and k == 0),
                        stop=(n == 1 and k == 1),
                    )

        def add_bias(engine, op, g, c, i):
            z = ring("z", (op, g, c), [P, 2, 256, 2], F32)
            nc.vector.tensor_tensor(
                out=z[:, i],
                in0=snap_sums(op, g, c, i).rearrange("p k o -> p o k"),
                in1=bias_row[:, 256 * c : 256 * c + 256].unsqueeze(2).to_broadcast([P, 256, 2]),
                op=ALU.add,
            )

        def tanh_snap(engine, op, g, c):
            z = made["z", (op, g, c)]
            th = ring("th", (op, g, c), [P, 256, 2, 2], F32)
            nc.scalar.activation(out=th[:], in_=z[:].rearrange("p i o k -> p o i k"), func=ACT.Tanh)

        def weigh_snap(engine, op, g, c):
            th = made["th", (op, g, c)][:].rearrange("p o i k -> p o (i k)")
            out = f_part(op, g, 256 * c, 256)
            if engine == "G":
                run = made["run", SHARED.get((op, g, c), (op, g, c))][:].rearrange("p r j -> p (r j)")
                nc.gpsimd.tensor_tensor(
                    out=out.rearrange("p (a r) j -> p a (r j)", r=16),
                    in0=th.rearrange("p (a r) j -> p a (r j)", r=16),
                    in1=run.unsqueeze(1).to_broadcast([P, 16, 64]),
                    op=ALU.mult,
                )
            else:
                nc.vector.tensor_tensor(
                    out=out, in0=th, in1=weight[op][:, g, :].unsqueeze(1).to_broadcast([P, 256, 4]), op=ALU.mult
                )

        def dot_obs(engine, op, g, m):
            sums = bank_of("obs", op, g, m)[:].rearrange("p j r -> p (j r)")
            for n in range(2):
                nc.tensor.matmul_mx(
                    out=sums,
                    lhsT=w_code[:, n, P * m : P * m + P].bitcast(FP8X4),
                    lhsT_scale=w_scale[4 * n : P, P * m : P * m + P],
                    rhs=row_code[op, g][:, n].rearrange("p j r -> p (j r)").bitcast(FP8X4),
                    rhs_scale=row_scale[op, g][:, n].rearrange("p j r -> p (j r)"),
                    start=(n == 0),
                    stop=(n == 1),
                )

        def tanh_obs(engine, op, g, m):
            sums = bank_of("obs", op, g, m)[:].rearrange("p j r -> p (j r)")
            t = ring("t", (op, g, m), [P, 4, P], F32)
            nc.scalar.activation(
                out=t[:].rearrange("p j r -> p (j r)"), in_=sums, func=ACT.Tanh, bias=bias_column[:, m : m + 1]
            )

        def turn_obs(engine, op, g, m):
            t = made["t", (op, g, m)]
            for j in range(4):
                nc.tensor.transpose(bank_of("turned", op, g, m)[:, j, :], t[:, j, :], ident[:])

        def weigh_obs(engine, op, g, m):
            nc.vector.tensor_tensor(
                out=f_part(op, g, P * m, P),
                in0=bank_of("turned", op, g, m)[:].rearrange("p j o -> p o j"),
                in1=weight[op][:, g, :].unsqueeze(1).to_broadcast([P, P, 4]),
                op=ALU.mult,
            )


        plane_code = keep.tile([P, 2, SIZE], U32, name="plane_code", align_bytes=ALIGN)
        plane_scale = keep.tile([P, SIZE], U8, name="plane_scale", align_bytes=ALIGN)
        plane_words = out_1.rearrange("g p m t -> p g (m t)")

        def cross(engine, c, h, k):
            for g in range(2):
                columns = slice(256 * g + P * k, 256 * g + P * k + P)
                nc.tensor.matmul_mx(
                    out=bank_of("cross", c, h, k)[:].rearrange("p a b -> p (a b)"),
                    lhsT=f_code["x", c // 2][:, c % 2, columns].bitcast(FP8X4),
                    lhsT_scale=f_scale["x", c // 2][:, c % 2, columns],
                    rhs=f_code["y", h][:, g].bitcast(FP8X4),
                    rhs_scale=f_scale["y", h][:, g],
                    start=(g == 0),
                    stop=(g == 1),
                )

        def lift_cross(engine, c, h, k):
            r = ring("half", (c,), [P, 2, 2, 512], F32)
            divide(engine, r[:, k, h], bank_of("cross", c, h, k)[:].rearrange("p a b -> p (a b)"))

        def round_cross(engine, c, h, n):
            s = ring("s", (c,), [P, 2, 2, 2, P, 2], BF16)
            values = made["half", (c,)][:, :, h : h + n].rearrange("p k h (a e s) -> p (k h) e a s", e=2, s=2)
            out = s[:, :, h : h + n].rearrange("p k h e a s -> p (k h) e a s")
            if engine == "G":
                for e in range(2):
                    nc.gpsimd.tensor_scalar(
                        out=out[:, :, e], in0=values[:, :, e], scalar1=1.0, scalar2=0.0, op0=ALU.mult, op1=ALU.add
                    )
            else:
                copy(engine, out, values)

        def round_bank(engine, c, h, k):
            s = ring("s", (c,), [P, 2, 2, 2, P, 2], BF16)
            values = bank_of("cross", c, h, k)[:].rearrange("p a (b e s) -> p e (a b) s", e=2, s=2)
            divide(engine, s[:, k, h], values)

        def turn_cross(engine, c, h):
            for k in range(2):
                for e in range(2):
                    words = made["s", (c,)][:, k, h, e].rearrange("p a s -> p (a s)").bitcast(F32)
                    nc.tensor.transpose(bank_of("plane", c, h)[:, 2 * k + e, :], words, ident[:])

        def lift_plane(engine, c, h):
            u = ring("u", (c // 2, h), [P, 2, 2, P, 4], BF16)
            words = u[:, c % 2].rearrange("p k i t -> p (k i t)").bitcast(F32).rearrange("p (k i e) -> p k i e", k=2, e=2)
            copy(engine, words, bank_of("plane", c, h)[:].rearrange("p (k e) i -> p k i e", e=2))

        def encode_plane(engine, c, h, n):
            cols = slice(256 * c, 256 * (c + n))
            values = made["u", (c // 2, h)][:, c % 2 : c % 2 + n].rearrange("p c k i t -> p (c k i t)")
            quantize(plane_code[:, h, cols], plane_scale[4 * h : P, cols], values)

        def send_cross(engine, c, h, k):
            rows = slice(256 * c + P * k, 256 * c + P * k + P)
            values = made["half", (c,)][:, k, h]
            nc.sync.dma_start(out=out_0[rows, 512 * h : 512 * h + 512], in_=values)

        def send_unit(engine, c, h):
            rows = out_0[256 * c : 256 * c + 256, 512 * h : 512 * h + 512]
            values = made["half", (c,)][:, :, h]
            nc.sync.dma_start(out=rows.rearrange("(k p) n -> p k n", k=2), in_=values)

        def send_rows(engine, c, k):
            values = made["half", (c,)][:, k].rearrange("p h n -> p (h n)")
            nc.sync.dma_start(out=out_0[256 * c + P * k : 256 * c + P * k + P, :], in_=values)

        def send_pass(engine, h, c, n):
            nc.sync.dma_start(
                out=plane_words[:, h, 1024 * c : 1024 * (c + n)].bitcast(I32),
                in_=plane_code[:, h, 256 * c : 256 * (c + n)].bitcast(I32),
            )

        def send_scales(engine):
            for quad in range(4):
                queue = nc.scalar if quad in SCALAR_QUADS else nc.sync
                queue.dma_start(
                    out=out_2[:, 4 * quad : 4 * quad + 4, :].bitcast(I32),
                    in_=plane_scale[32 * quad : 32 * quad + 8, :].bitcast(I32),
                )


        def both(step, *args):
            return [(step,) + args + (k,) for k in range(2)]

        def four(step, *args):
            return [(step,) + args + (k,) for k in range(4)]

        def tiles(step, op, g, c):
            return [(step, op, g, 2 * c), (step, op, g, 2 * c + 1)]

        def banks(step, c):
            return both(step, c, 0) + both(step, c, 1)

        def rows(step, c):
            return [(step, c, h, k) for k in range(2) for h in range(2)]

        def pair(step, op, g, i):
            return [(step, op, g, 2 * i), (step, op, g, 2 * i + 1)]

        tensor = pair(turn_rows, "y", 0, 0) + [(spread_bias,)] + pair(turn_rows, "y", 0, 1)
        tensor += [(dot_snap, "y", 0, c, i) for i in range(2) for c in range(2)]
        tensor += four(turn_rows, "y", 1) + [(turn_bias,)]
        tensor += both(dot_snap, "y", 0, 2) + tiles(dot_obs, "y", 0, 3)
        tensor += four(turn_rows, "x", 0) + tiles(turn_obs, "y", 0, 3)
        tensor += both(dot_snap, "y", 1, 0) + tiles(dot_obs, "y", 1, 1) + both(dot_snap, "y", 1, 2)
        tensor += four(turn_rows, "x", 1) + tiles(turn_obs, "y", 1, 1)
        tensor += tiles(dot_obs, "y", 1, 3) + both(dot_snap, "x", 0, 0) + both(dot_snap, "x", 0, 1) + both(dot_snap, "x", 0, 2)
        tensor += tiles(dot_obs, "x", 1, 0) + tiles(dot_obs, "x", 1, 1)
        tensor += tiles(turn_obs, "y", 1, 3) + tiles(turn_obs, "x", 1, 0) + tiles(turn_obs, "x", 1, 1)
        tensor += tiles(dot_obs, "x", 1, 2) + both(dot_snap, "x", 0, 3) + tiles(dot_obs, "x", 1, 3)
        tensor += tiles(turn_obs, "x", 1, 2) + tiles(turn_obs, "x", 1, 3)
        tensor += banks(cross, 0) + banks(cross, 1) + banks(cross, 2) + both(turn_cross, 0) + both(turn_cross, 1)
        tensor += banks(cross, 3) + both(turn_cross, 2) + both(turn_cross, 3)

        scalar = [(lift_rows, "y", 0, 0), (widen_bias,), (lift_rows, "y", 0, 2), (lift_bias_row,)] + both(sort_pair, "y", 1)
        scalar += [(tanh_snap, "y", 0, 0), (lift_bias_column,), (tanh_snap, "y", 0, 1), (sort_pair, "x", 0, 1)] + tiles(tanh_obs, "y", 0, 3)
        scalar += [(tanh_snap, "y", 0, 2)] + pair(lift_rows, "x", 0, 1) + [(sort_pair, "x", 1, 1)] + tiles(tanh_obs, "y", 1, 1) + [(tanh_snap, "y", 1, 0)]
        scalar += four(lift_rows, "x", 1) + tiles(tanh_obs, "y", 1, 3) + [(tanh_snap, "y", 1, 2), (tanh_snap, "x", 0, 0)]
        scalar += tiles(tanh_obs, "x", 1, 0) + tiles(tanh_obs, "x", 1, 1) + [(tanh_snap, "x", 0, 1), (tanh_snap, "x", 0, 2)]
        scalar += tiles(tanh_obs, "x", 1, 2) + tiles(tanh_obs, "x", 1, 3) + [(tanh_snap, "x", 0, 3)]
        scalar += banks(lift_cross, 0) + banks(lift_cross, 1) + banks(lift_cross, 2) + [(lift_plane, 0, 0)] + both(lift_plane, 1)
        scalar += [(lift_cross, 3, 0, 1)] + both(round_bank, 3, 1) + [(lift_plane, 2, 0), (lift_plane, 3, 0), (lift_plane, 2, 1), (lift_plane, 3, 1)]

        vector = [(lift_rows, "y", 0, 1), (encode_pair, "y", 0, 0), (lift_rows, "y", 0, 3), (encode_pair, "y", 0, 1)]
        vector += [(add_bias, "y", 0, c, i) for i in range(2) for c in range(2)]
        vector += four(lift_rows, "y", 1) + both(add_bias, "y", 0, 2)
        vector += [(encode_half, "y", 1), (repeat_weights, "y", 0, 1), (sort_pair, "x", 1, 0)] + pair(lift_rows, "x", 0, 0)
        vector += tiles(weigh_obs, "y", 0, 3) + both(add_bias, "y", 1, 0) + both(add_bias, "y", 1, 2)
        vector += [(encode_half, "x", 0), (repeat_weights, "y", 1, 0), (encode_f, "y", 0, 0, 1)]
        vector += tiles(weigh_obs, "y", 1, 1) + both(add_bias, "x", 0, 0)
        vector += [(encode_half, "x", 1), (repeat_weights, "y", 1, 2), (encode_f, "y", 0, 1, 1)]
        vector += both(add_bias, "x", 0, 1) + both(add_bias, "x", 0, 2) + tiles(weigh_obs, "y", 1, 3)
        vector += tiles(weigh_obs, "x", 1, 0) + tiles(weigh_obs, "x", 1, 1) + both(add_bias, "x", 0, 3)
        vector += [(encode_f, "x", 0, 0, 1), (encode_f, "y", 1, 0, 2), (repeat_weights, "x", 0, 2), (encode_f, "x", 0, 1, 1)]
        vector += tiles(weigh_obs, "x", 1, 2) + tiles(weigh_obs, "x", 1, 3) + [(encode_f, "x", 1, 0, 1)]
        vector += [(round_cross, 0, 0, 2), (weigh_snap, "x", 0, 3), (round_cross, 1, 0, 2), (encode_f, "x", 1, 1, 1)]
        vector += [(lift_plane, 0, 1), (round_cross, 2, 0, 2), (lift_cross, 3, 0, 0), (encode_plane, 0, 0, 2), (round_cross, 3, 0, 1), (encode_plane, 0, 1, 2)]
        vector += both(lift_cross, 3, 1) + [(encode_plane, c, h, 1) for h in range(2) for c in (2, 3)]

        pool = [(repeat_weights, op, 0, 0) for op in ("y", "x")] + [(weigh_snap,) + key for key in POOL]

        sync = both(send_cross, 0, 0) + [(send_unit, 0, 1)] + both(send_unit, 1) + both(send_unit, 2)
        sync += both(send_cross, 3, 0) + [(send_pass, 0, 0, 2), (send_pass, 1, 0, 2)] + both(send_cross, 3, 1)
        sync += [(send_pass, 0, 2, 2), (send_pass, 1, 2, 1), (send_pass, 1, 3, 1), (send_scales,)]


        reads = {}
        touches = {}

        def wire(step, sources, *tiles_touched):
            reads[step] = list(sources)
            touches[step] = list(tiles_touched)

        def weighed(op, g, c):
            return [(weigh_snap, op, g, c)] if (op, g, c) in SNAP else tiles(weigh_obs, op, g, c)

        wire((spread_bias,), [], ("bank", ("bias_row",)))
        wire((lift_bias_row,), [(spread_bias,)], ("bank", ("bias_row",)))
        wire((widen_bias,), [])
        wire((turn_bias,), [(widen_bias,)], ("bank", ("bias_column",)))
        wire((lift_bias_column,), [(turn_bias,)], ("bank", ("bias_column",)))
        for op in ("y", "x"):
            for g in range(2):
                for j in range(4):
                    key = (op, g, j)
                    bank = ("bank", ("rows",) + key)
                    lifted = ("pair", (op, g, j // 2)) if (op, g) in PAIRWISE else half_key(op, g)
                    slots = (op, g, j // 2)
                    if slots in SORTED:
                        wire((sort_pair,) + slots, [], ("sorted", slots))
                        wire((turn_rows,) + key, [(sort_pair,) + slots], bank, ("sorted", slots))
                    else:
                        wire((turn_rows,) + key, [], bank)
                    wire((lift_rows,) + key, [(turn_rows,) + key], bank, lifted)
                if (op, g) in PAIRWISE:
                    coded = both(encode_pair, op, g)
                    for i in range(2):
                        wire(coded[i], pair(lift_rows, op, g, i), ("pair", (op, g, i)))
                else:
                    coded = [(encode_half, op, g)] * 2
                    wire(coded[0], four(lift_rows, op, g), half_key(op, g))
                for c in range(4):
                    key = (op, g, c)
                    if key in SNAP:
                        for i in range(2):
                            bank = ("bank", ("snap",) + key + (i,))
                            dot = (dot_snap,) + key + (i,)
                            wire(dot, [coded[i]], bank)
                            wire((add_bias,) + key + (i,), [dot, (lift_bias_row,)], bank, ("z", key))
                        wire((tanh_snap,) + key, both(add_bias, *key), ("z", key), ("th", key))
                        if key in POOL:
                            run = SHARED.get(key, key)
                            wire((repeat_weights,) + run, [], ("run", run))
                            sources = [(tanh_snap,) + key, (repeat_weights,) + run]
                            wire((weigh_snap,) + key, sources, ("th", key), f_key(*key), ("run", run))
                        else:
                            wire((weigh_snap,) + key, [(tanh_snap,) + key], ("th", key), f_key(*key))
                        continue
                    for m in (2 * c, 2 * c + 1):
                        tile = (op, g, m)
                        sums, turned = ("bank", ("obs",) + tile), ("bank", ("turned",) + tile)
                        wire((dot_obs,) + tile, coded, sums)
                        wire((tanh_obs,) + tile, [(dot_obs,) + tile, (lift_bias_column,)], sums, ("t", tile))
                        wire((turn_obs,) + tile, [(tanh_obs,) + tile], turned, ("t", tile))
                        wire((weigh_obs,) + tile, [(turn_obs,) + tile], turned, f_key(*key))
        coded_f = {}
        rounded = {}
        for step in vector + scalar + pool:
            if step[0] == encode_f:
                op, n, first, count = step[1:]
                parts = range(first, first + count)
                if op == "y":
                    keys = [(op, g, 2 * n + c) for g in parts for c in range(2)]
                else:
                    keys = [(op, g, 2 * n + c) for c in parts for g in range(2)]
                wire(step, [source for key in keys for source in weighed(*key)], ("f", (op, n)))
                for part in parts:
                    coded_f[op, n, part] = step
            if step[0] == round_cross:
                c, h, n = step[1:]
                wire(step, banks(lift_cross, c)[2 * h : 2 * (h + n)], ("half", (c,)), ("s", (c,)))
                for k in range(n):
                    rounded[c, h + k] = [step]
        laid = {}
        for c in range(4):
            for h in range(2):
                unit = (c, h)
                coded = [coded_f["x", c // 2, c % 2], coded_f["y", h, 0], coded_f["y", h, 1]]
                for k in range(2):
                    bank = ("bank", ("cross", c, h, k))
                    wire((cross, c, h, k), coded, bank)
                    if unit in FROM_BANK:
                        wire((round_bank, c, h, k), [(cross, c, h, k)], bank, ("s", (c,)))
                        rounded[unit] = both(round_bank, c, h)
                    first = round_bank if unit in FROM_BANK else cross
                    wire((lift_cross, c, h, k), [(first, c, h, k)], bank, ("half", (c,)))
                    if (send_cross, c, h, k) in sync:
                        wire((send_cross, c, h, k), [(lift_cross, c, h, k)], ("half", (c,)))
                if (send_rows, c, h) in sync:
                    wire((send_rows, c, h), [(lift_cross, c, n, h) for n in range(2)], ("half", (c,)))
                if (send_unit, c, h) in sync:
                    wire((send_unit, c, h), both(lift_cross, c, h), ("half", (c,)))
                bank = ("bank", ("plane", c, h))
                wire((turn_cross, c, h), rounded[unit], bank, ("s", (c,)))
                wire((lift_plane, c, h), [(turn_cross, c, h)], bank, ("u", (c // 2, h)))
                laid[unit] = [(lift_plane, c, h)]
        encoded = {}
        for step in vector:
            if step[0] == encode_plane:
                c, h, n = step[1:]
                wire(step, [source for k in range(n) for source in laid[c + k, h]], ("u", (c // 2, h)))
                for k in range(n):
                    encoded[c + k, h] = step
        for step in sync:
            if step[0] == send_pass:
                h, c, n = step[1:]
                wire(step, [encoded[c + k, h] for k in range(n)])
        wire((send_scales,), encoded.values())


        queues = {"V": vector, "S": scalar, "G": pool, "Q": sync, "T": tensor}
        assert sorted(map(str, reads)) == sorted(str(step) for queue in queues.values() for step in queue)
        given = {tag: [] for tag in DEPTH}
        written = set()

        def place_free(step):
            for tag in DEPTH:
                new = [tile for tile in touches[step] if tile[0] == tag and tile not in given[tag]]
                count = len(given[tag]) + len(new) - DEPTH[tag]
                for old in given[tag][: max(count, 0)]:
                    if not all(user in written for user in touches if old in touches[user]):
                        return False
            return True

        while any(queues.values()):
            progress = False
            for engine, queue in queues.items():
                while queue and all(source in written for source in reads[queue[0]]) and place_free(queue[0]):
                    step = queue.pop(0)
                    for tile in touches[step]:
                        if tile not in given[tile[0]]:
                            given[tile[0]].append(tile)
                    step[0](engine, *step[1:])
                    written.add(step)
                    progress = True
                    if engine == "T":
                        break
            assert progress, [(queue[0][0], queue[0][1:]) for queue in queues.values() if queue]
